import numpy as np, ml_dtypes
CORES = [2,6,10,14,18,22,26,30]
N = 8
BF = ml_dtypes.bfloat16
def gentries(a):
    return np.ascontiguousarray(a.reshape(8, 16, -1).transpose(0, 2, 1)).reshape(8, -1)
def gtable(e):
    e = np.asarray(e); return np.ascontiguousarray(e.reshape(8, -1, 16).transpose(0, 2, 1)).reshape(128, -1).astype(np.int32)
W, LW, M, K, CAP, RO = 4096, 12, 1024, 192, 160, 3
def h1(v):
    return ((v * v >> 3) + v) & (W - 1)
def h2(v):
    return ((v * v >> 5) + 37 * v + 1) & (W - 1)
def parts(rng):
    X = rng.integers(0, 16, (N, 8, 16, W)); F = rng.integers(0, W, (N, 8, 16, W)); LG = rng.integers(0, M, (N, 8, W))
    for q in range(N):
        for g in range(8):
            v = rng.permutation(M)[:7 * M // 10]
            LG[q, g, np.where(rng.random(len(v)) < 0.5, h1(v), h2(v))] = v
    LE = (rng.random((N, 8, W)) < rng.choice(np.array([0.3, 0.5, 0.7, 0.9]), (N, 8, 1))).astype(np.int64)
    XL = rng.integers(0, 16, (N, 8, 16, M)); LF = rng.integers(0, M, (N, 8, 16, M))
    return X, F, LG, LE, XL, LF, rng.integers(0, W, (N, 8, 16, K)), rng.integers(0, 16, (N, 8, 16, K))
def pack(X, F, LG, LE, XL, LF, C, Q):
    def bf(a): return np.ascontiguousarray(a).reshape(N, 128, -1).astype(np.float32).astype(BF)
    F = np.ascontiguousarray(F).reshape(N, 128, W)
    return {"xr": bf(X), "fd": (F[..., :W // 2] + W * F[..., W // 2:]).astype(np.int32), "tg": (2 * LG + LE).astype(np.int32), "xl": bf(XL),
            "lf": np.ascontiguousarray(LF).reshape(N, 128, M).astype(np.int32), "cx": np.stack([gtable(a.transpose(0, 2, 1).reshape(8, -1)) for a in C]), "qx": bf(Q)}
def setup_inputs(rng):
    return pack(*parts(rng))
def setup_inputs_spread(rng):
    X, F, LG, LE, XL, LF, C, Q = parts(rng)
    def small(n): return np.minimum((np.exp2(4.2 * rng.random((N, 8, 1, n))) * rng.random((N, 8, 16, n))).astype(np.int64), 15)
    def low(n, top): return np.minimum((top * rng.random((N, 8, 16, n)) ** rng.choice(np.array([1.0, 2.0, 4.0]), (N, 8, 1, n))).astype(np.int64), top - 1)
    LE = (rng.random((N, 8, W)) < rng.random((N, 8, 1))).astype(np.int64)
    return pack(small(W), low(W, W), LG, LE, small(M), low(M, M), low(K, W), small(K))
def setup_inputs_ends(rng):
    X, F, LG, LE, XL, LF, C, Q = parts(rng); h = W // 2
    def faces(n):
        kind = rng.integers(0, 3, (N, 8, 1, n)); a = 15 * np.where(kind == 2, rng.integers(0, 2, (N, 8, 16, n)), kind)
        near = (rng.random((N, 8, 1, n)) < 0.25) & (np.arange(16)[:, None] == rng.integers(0, 16, (N, 8, 1, n)))
        return np.abs(a - near.astype(np.int64))
    def ends(a, top): return np.where(rng.random(a.shape) < 0.66, top * rng.integers(0, 2, a.shape), a)
    X, XL, Q = faces(W), faces(M), faces(K)
    X[..., 0] = 0; X[..., W - 1] = 0; X[..., 1] = 15; X[..., W - 2] = 15
    X[..., 2] = 0; X[..., 0, 2] = 1; X[..., W - 3] = 0; X[..., 15, W - 3] = 1
    m = rng.random((N, 8, 16, h)) < 0.66; e = (W - 1) * rng.integers(0, 2, m.shape)
    F = np.concatenate([np.where(m, e, F[..., :h]), np.where(m, e, F[..., h:])], axis=-1)
    m = rng.random((N, 8, W)) < 0.66; e = (rng.random((N, 8, W)) < 0.6).astype(np.int64)
    LG = np.where(m, (M - 1) * e, LG); LE = np.where(m, e, LE)
    LG[..., 0] = 0; LE[..., 0] = 0; LG[..., W - 1] = M - 1; LE[..., W - 1] = 1
    LF = ends(LF, M - 1); C = ends(C, W - 1)
    for k in (0, 1, K - 1): Q[..., k] = 15; C[..., k] = (W - 1) * rng.integers(0, 2, (N, 8, 16))
    Q[..., K - 2] = 0; C[..., K - 2] = (W - 1) * rng.integers(0, 2, (N, 8, 16))
    for k in (2, K - 3): Q[..., k] = 0; C[..., :15, k] = 1; C[..., 15, k] = W - 1
    for k, v in ((3, 2), (K - 4, W - 3)): Q[..., k] = 15; C[..., :15, k] = (W - 1) * rng.integers(0, 2, (N, 8, 15)); C[..., 15, k] = v
    return pack(X, F, LG, LE, XL, LF, C, Q)
def setup_inputs_corners(rng):
    X, F, LG, LE, XL, LF, C, Q = parts(rng); cnt = (0, 1, CAP - 1, CAP, CAP + 1, K); a = np.arange(M)
    for g in (2, 7):
        LG[:, g] = LG[0, g]; res = a[(LG[0, g][h1(a)] == a) | (LG[0, g][h2(a)] == a)]; LF[:, g] = rng.choice(res, (N, 16, M))
    v = LG[:, 3]; c = np.arange(W)
    for _ in range(3): v = np.where((h1(v) == c) | (h2(v) == c), (v + 1) % M, v)
    LG[:, 3] = v
    few = np.array([0, 1, M - 2, M - 1]); LF[:, 5] = rng.choice(few, (N, 16, M)); LG[:, 6] = rng.choice(few, (N, W))
    LE[:, 4] = 1; LE[0, 0] = 0
    for q in range(N):
        for g in range(8):
            b = rng.permutation(W)[:4 * K].reshape(K, 4)
            C[q, g] = b[np.arange(K)[None, :], rng.integers(0, 4, (16, K))]
            ask = np.zeros(K, np.int64); ask[rng.permutation(K)[:cnt[(q + g) % 6]]] = 1
            if g == 7:
                o = C[q, g][np.argmin(far(X[q, g], C[q, g], Q[q, g]), axis=0), np.arange(K)]; LE[q, g] = 0; LE[q, g, o] = ask
            else: LE[q, g, b] = ask[:, None]
    return pack(X, F, LG, LE, XL, LF, C, Q)
def setup_inputs_ties(rng):
    X, F, LG, LE, XL, LF, C, Q = parts(rng)
    pal = rng.integers(6, 10, (N, 8, 16, 6))
    X = np.take_along_axis(pal, rng.integers(0, 6, (N, 8, 1, W)), 3); XL = np.take_along_axis(pal, rng.integers(0, 6, (N, 8, 1, M)), 3)
    for q in range(N):
        for g in range(8):
            v = rng.permutation(M)[:M // 2]; LG[q, g, h2(v)] = v; LG[q, g, h1(v)] = v
    return pack(X, F, LG, LE, XL, LF, C, Q)
def setup_inputs_alike(rng):
    X, F, LG, LE, XL, LF, C, Q = parts(rng)
    for g in range(8):
        s = rng.permutation(M); w = s[:64]; pl = np.concatenate([h1(w), h2(w)])
        pair = s[:6]; few = np.concatenate([pair, pair ^ 1])
        for q in range(N):
            if g % 2 == 0:
                pool = rng.permutation(W)[:40]; C[q, g] = rng.choice(pool, (16, K)); F[q, g, :, ::2] = rng.choice(pool, (16, W // 2))
                LE[q, g, pool] = rng.random(40) < 0.8; LG[q, g, pool] = rng.choice(few, 40); LF[q, g] = rng.choice(s[:24], (16, M))
            else:
                C[q, g] = rng.choice(pl, (16, K)); LE[q, g, pl] = 1; LG[q, g, pl] = rng.choice(s[64:], 128); LF[q, g] = rng.choice(w, (16, M))
    return pack(X, F, LG, LE, XL, LF, C, Q)
def check_inputs(d):
    bad = []
    for k, lo, hi in (("xr", 0, 15), ("fd", 0, W * W - 1), ("tg", 0, 2 * M - 1), ("xl", 0, 15), ("lf", 0, M - 1), ("cx", 0, W - 1), ("qx", 0, 15)):
        a = np.asarray(d[k]).astype(np.float64)
        if not (np.min(a) >= lo and np.max(a) <= hi): bad.append("range of " + k)
        elif np.any(a != np.floor(a)): bad.append("whole numbers of " + k)
    return bad
def lowest(key, use):
    ix = np.flatnonzero(use); m = np.zeros(len(key), bool); m[ix[np.unique(key[ix], return_index=True)[1]]] = True
    return m
def far(x, c, q):
    return np.add.reduce(np.abs(x[:, c] - q[:, None, :]), axis=0)
def reference(xr, fd, tg, xl, lf, cx, qx):
    def whole(a): return a.astype(np.float32).astype(np.int64).reshape(N, 8, 16, -1)
    X, XL, Q = whole(xr), whole(xl), whole(qx)
    fi = fd.astype(np.int64); F = np.concatenate([fi & (W - 1), fi >> LW], axis=-1).reshape(N, 8, 16, W)
    LG = tg.astype(np.int64) >> 1; LE = tg.astype(np.int64) & 1; LF = lf.astype(np.int64).reshape(N, 8, 16, M)
    C = np.ascontiguousarray(np.stack([gentries(a) for a in cx]).astype(np.int64).reshape(N, 8, K, 16).transpose(0, 1, 3, 2))
    lane = np.arange(K)
    for t in range(RO):
        asked = {}; back = {}
        for r in range(N):
            for g in range(8):
                c = C[r, g]; o = c[np.argmin(far(X[r, g], c, Q[r, g]), axis=0), lane]
                s = np.flatnonzero(lowest(o, LE[r, g][o] == 1))[:CAP]
                asked[r, g] = (o, s, LG[r, g][o[s]], LG[r, g][c[:, s]])
        for r in range(N):
            p = (r + 1 + t % (N - 1)) % N
            for g in range(8):
                o, s, n, sent = asked[r, g]
                back[r, g] = (XL[p, g][:, n], LF[p, g][:, n])
                w = lowest(n ^ 1, np.ones(len(n), bool)); LF[p, g][:, (n ^ 1)[w]] = sent[:, w]
        for r in range(N):
            for g in range(8):
                o, s, n, sent = asked[r, g]; a, v = back[r, g]; q = Q[r, g][:, s]; j = np.arange(len(s))
                c1, c2 = h1(v), h2(v); in1 = LG[r, g][c1] == v; in2 = LG[r, g][c2] == v
                sh = np.where(in1, c1, np.where(in2, c2, np.where(far(X[r, g], c2, q) > far(X[r, g], c1, q), c2, c1)))
                new = ~(in1 | in2); i = np.argmax(new, axis=0); pl = sh[i, j]; w = lowest(pl, np.any(new, axis=0))
                LG[r, g][pl[w]] = v[i, j][w]; LE[r, g][pl[w]] = 1
                F[r, g][:, o[s]] = sh; X[r, g][:, o[s]] = a; LE[r, g][o[s]] = 0
                C[r, g] = F[r, g][:, o]; Q[r, g] = (Q[r, g] + X[r, g][:, o]) >> 1
    return {"yc": C.reshape(N, 128, K).astype(np.float32), "yq": Q.reshape(N, 128, K).astype(np.float32).astype(BF), "yt": (2 * LG + LE).astype(np.float32), "yl": LF.reshape(N, 128, M).astype(np.float32)}

@@ -1,0 +1,699 @@
+from concourse.mybir import AluOpType as Op, ActivationFunctionType as AF
+
+W, M, K, CAP, RO, N = 4096, 1024, 192, 160, 3, 8
+H = 96
+BIG = 65536.0
+RES = 1048576.0
+NE = 8
+WAKE, SLACK = 0.3, 0.1
+VCOST = {"ma": 1.7, "mb": 1.7, "xw": 0.6, "pw": 0.6, "fw": 0.7, "lw": 0.7, "lh": 0.7, "lfu": 0.85, "pcs": 0.64, "sq": 0.2, "cf": 0.25, "qs": 0.25, "eqo": 0.07, "eqt": 0.07, "cc": 0.12, "dc": 0.32, "sp": 0.16, "sg": 0.32, "u": 0.11}
+SCOST = {"pa": 1.7, "pb": 1.7, "pw": 0.43, "g": 0.28, "at": 0.15, "wt": 0.06, "ltk": 0.11, "wm": 0.06, "wp": 0.06}
+
+_S = "sbuf"
+F32, B16, I32, U16, H16 = "float32", "bfloat16", "int32", "uint16", "float16"
+PACK = {
+    "tf": (F32, (("z", 24), ("lis", 24), ("req", 12), ("rk", 12), ("dwin", 12), ("w1", 12), ("w2", 12), ("w3", 12), ("w4", 12), ("w5", 12), ("w6", 12), ("nrq", 12), ("pls", 12),
+                 ("dm4", 12), ("dm1", 12), ("er", 24), ("lt", 16), ("pmf", 4))),
+    "tl": (U16, (("ln", 12), ("lo", 12), ("ld", 12), ("lcl", 12), ("lm", 12))),
+    "ti": (I32, (("ni", 12), ("ei", 12), ("pari", 12), ("dmi", 12), ("pmi", 4))),
+    "tb": (B16, (("wm", 24), ("wp", 24), ("wm1", 24), ("wm2", 24), ("wp1", 24), ("wp2", 24), ("cand", 12), ("exb", 16))),
+    "cb": (B16, (("idb", 128), ("blb", 128), ("bt", 128), ("dg1", 128), ("sa", 128), ("dgc0", 128), ("dgc1", 128), ("dgc2", 128), ("bm", K), ("ltk", 2048), ("pb16", 128), ("nb16", 128))),
+    "cff": (F32, (("one", 512), ("idf", 128), ("blf", 128), ("btf", 128), ("af0", 128), ("af1", 128), ("af2", 128), ("sam", 384), ("rpf", 512), ("vrf", 384))),
+    "chh": (H16, (("rp", 512), ("rpc", 128), ("vr", 128), ("bi", 384), ("idh", 128))),
+}
+PLACE, SCRATCH = {}, {}
+for _b in PACK:
+    _o = 0
+    for _n, _w in PACK[_b][1]:
+        PLACE[_n] = (_b, _o, _w)
+        _o += _w
+    SCRATCH[_b] = (_S, [128, _o], PACK[_b][0])
+for _d, _l in (
+    (B16, (("xw", W + K), ("pw", W + K), ("pcs", 768), ("xlh", M), ("q", K), ("qb", K), ("qrep", 16 * K), ("ma", 16 * K), ("mb", 16 * K), ("pa", 16 * K), ("pb", 16 * K),
+           ("at", K), ("g1", K), ("v1", K), ("g2", K), ("v2", K), ("row", 512), ("ro2", 512), ("wt", 512), ("xl1", M), ("xl2", M), ("xl3", M), ("xp1", 512), ("xp2", 512), ("xp3", 512), ("xlp", 512), ("xt", 512))),
+    (I32, (("fw", W + K), ("fdt", 2048), ("tgs", 256), ("pci", 768), ("lfi", M), ("cxi", K), ("sct", K), ("sco", K), ("scl", K), ("tt", 2 * K), ("cc", 2 * K), ("dc", K), ("sg", K), ("ia", K), ("ic", 512))),
+    (U16, (("lfu", M), ("lc", K), ("ru", 2 * K), ("ru2", K), ("l1", K), ("l2", K), ("lu1", M), ("lu2", M), ("lu3", M))),
+    (F32, (("lh", M + K), ("qs", K), ("cf", K), ("scd", K), ("sct2", K), ("sq", 2 * K), ("sp", K), ("yts", 512), ("s0", K), ("lw1", M), ("lw2", M + K), ("lw3", M + K),
+           ("msg1", K + 12), ("msg2", K + 12), ("msg3", K + 12), ("up1", K + 12), ("up2", K + 12), ("up3", K + 12), ("hm1", K + 12), ("hm2", K + 12), ("hm3", K + 12))),
+    (H16, (("gt", K), ("gu", K), ("b16", K), ("c16", K))),
+):
+    for _n, _w in _l:
+        SCRATCH[_n] = (_S, [128, _w], _d)
+for _n, _w, _d in (("co", 128, F32), ("t1", 128, F32), ("t2", 64, F32), ("t3", 32, F32), ("t4", 16, I32), ("fi", 16, I32), ("fl", 16, H16), ("sl", 128, F32), ("r1", 128, F32), ("r2", 128, F32), ("u1", 128, F32),
+                   ("u2", 128, F32), ("ub", 128, F32), ("pk", 128, B16), ("kk", 128, F32), ("k2", 128, F32), ("ka", 64, F32), ("kb", 32, F32), ("kc", 16, F32), ("kd", 8, I32), ("fe", 16, I32), ("fg", 16, F32), ("fh", 16, I32), ("fm", 32, H16), ("t5", 16, F32), ("t6", 32, F32), ("t7", 16, I32), ("fj", 16, I32)):
+    SCRATCH[_n] = (_S, [128, 2, _w], _d)
+SCRATCH["eqo"] = (_S, [128, 12, K], B16)
+SCRATCH["eqt"] = (_S, [128, 12, K], B16)
+for _n in ("psk", "psv"):
+    SCRATCH[_n] = ("psum", [128, 2, 512], F32)
+for _n in ("psm", "psu", "psd", "psg"):
+    SCRATCH[_n] = ("psum", [128, 512], F32)
+SEMAPHORES = ["qv", "qs", "qp", "qg"] + ["ld%d" % j for j in range(20)] + ["ls%d" % j for j in range(16)]
+SEMAPHORES += ["%s%d" % (a, j) for a in ("rl", "rx", "ru", "rh") for j in (1, 2, 3)]
+
+
+def tracker(g, T):
+    Q = {"v": g.vector, "s": g.scalar, "p": g.tensor, "g": g, "d": g.sync}
+    cnt = {"v": 0, "s": 0, "p": 0, "g": 0}
+    known = {q: {} for q in Q}
+    hist, wr, rd, total = {}, {}, {}, {}
+    nd = [0]
+
+    def learn(q, sem, val):
+        if known[q].get(sem, 0) < val:
+            known[q][sem] = val
+        for s2, v2 in hist.get((sem, val), {}).items():
+            if known[q].get(s2, 0) < v2:
+                known[q][s2] = v2
+
+    def needs(q, comp, R, Wt):
+        out = []
+        for k in R:
+            if k in wr:
+                out.append((k, wr[k]))
+            if k.startswith("ps"):
+                out += [(k, x) for x in rd.get(k, {}).values()]
+        for k in Wt:
+            if k in wr:
+                out.append((k, wr[k]))
+            out += [(k, x) for x in rd.get(k, {}).values()]
+        need = {}
+        for k, (sem, val, dq) in out:
+            if comp and dq == q and (q == "p" or k.startswith("ps")):
+                continue
+            if need.get(sem, 0) < val:
+                need[sem] = val
+        return need
+
+    def deps(q, comp, R, Wt):
+        need = needs(q, comp, R, Wt)
+        for sem in sorted(need, key=lambda s: -len(hist.get((s, need[s]), {}))):
+            if known[q].get(sem, 0) < need[sem]:
+                Q[q].wait_ge(T.sem[sem], need[sem])
+                learn(q, sem, need[sem])
+
+    def note(ev, q, R, Wt):
+        for k in Wt:
+            wr[k] = ev
+            rd[k] = {}
+        for k in R:
+            rd.setdefault(k, {})[ev[0] if ev[2] is None else q] = ev
+
+    def op_(q, fns, R, Wt):
+        R, Wt = R.split(), Wt.split()
+        deps(q, True, R, Wt)
+        for f in fns[:-1]:
+            f()
+        sem = "q" + q
+        cnt[q] += 1
+        fns[-1]().then_inc(T.sem[sem], 1)
+        total[sem] = cnt[q]
+        hist[(sem, cnt[q])] = dict(known[q])
+        if cnt[q] > 1:
+            hist[(sem, cnt[q])][sem] = cnt[q] - 1
+        note((sem, cnt[q], q), q, R, Wt)
+
+    def dma_(q, out, in_, R, Wt):
+        R, Wt = R.split(), Wt.split()
+        deps(q, False, R, Wt)
+        sem = "ld%d" % nd[0]
+        nd[0] += 1
+        Q[q].dma_start(out, in_).then_inc(T.sem[sem], 16)
+        total[sem] = 16
+        hist[(sem, 16)] = dict(known[q])
+        note((sem, 16, None), q, R, Wt)
+
+    def send_(call, R, local, n):
+        deps("g", False, R.split(), [])
+        call()
+        total[local] = n
+        note((local, n, None), "g", R.split(), [])
+
+    def arrives_(sem, n, key):
+        total[sem] = n
+        wr[key] = (sem, n, None)
+        rd[key] = {}
+
+    nodes = []
+
+    def op(q, fns, R="", Wt=""):
+        nodes.append((q, R.split(), Wt.split(), lambda: op_(q, fns, R, Wt), len(fns), 0.0, -1))
+
+    def dma(q, out, in_, R="", Wt="", lat=2.2):
+        nodes.append((q, R.split(), Wt.split(), lambda: dma_(q, out, in_, R, Wt), 0, lat, -1))
+
+    def send(call, R, local, n):
+        nodes.append(("g", R.split(), [], lambda: send_(call, R, local, n), 0, 0.0, -1))
+
+    def arrives(sem, n, key, lat):
+        nodes.append(("a", [], [key], lambda: arrives_(sem, n, key), 0, lat, len(nodes) - 1))
+
+    def cost(q, W1, n):
+        if q == "p":
+            return 0.05 * n
+        if n == 0:
+            return 0.3 if q == "g" else 0.1
+        if q == "g":
+            return 0.6
+        return (SCOST if q == "s" else VCOST).get(W1, 0.2 if q == "s" else 0.09)
+
+    def finish():
+        nn = len(nodes)
+        dep = [set() for _ in nodes]
+        w, rds, ps = {}, {}, {}
+        for x, (q, R, Wt, f, n, lat, after) in enumerate(nodes):
+            if after >= 0:
+                dep[x].add(after)
+            for k in sorted(set(R + Wt)):
+                if k.startswith("ps"):
+                    cur = ps.setdefault(k, [q, [], []])
+                    if cur[0] == q:
+                        dep[x].update(cur[2])
+                        if q == "p" and cur[1]:
+                            dep[x].add(cur[1][-1])
+                        cur[1].append(x)
+                    else:
+                        dep[x].update(cur[1])
+                        ps[k] = [q, [x], cur[1]]
+                    continue
+                if k in w:
+                    dep[x].add(w[k])
+                if k in Wt:
+                    dep[x].update(rds.get(k, []))
+            for k in Wt:
+                w[k], rds[k] = x, []
+            for k in R:
+                if k not in Wt:
+                    rds.setdefault(k, []).append(x)
+            dep[x].discard(x)
+        succ = [[] for _ in nodes]
+        for x in range(nn):
+            for d in dep[x]:
+                succ[d].append(x)
+        cs = [0.0 if nd_[0] == "a" else cost(nd_[0], (nd_[2] + nd_[1] + [""])[0].rstrip("0123456789"), nd_[4]) for nd_ in nodes]
+        pr = [0.0] * nn
+        for x in range(nn - 1, -1, -1):
+            pr[x] = cs[x] + nodes[x][5] + max([pr[y] + WAKE for y in succ[x]] + [0.0])
+        left = [len(d) for d in dep]
+        ready = {q: [] for q in "vspgda"}
+        fin, qt = [0.0] * nn, {q: 0.0 for q in "vspgda"}
+        early = [0.0] * nn
+        for x in range(nn):
+            if not left[x]:
+                ready[nodes[x][0]].append(x)
+        for _ in range(nn):
+            best = None
+            for q in "avspgd":
+                if not ready[q]:
+                    continue
+                st = {}
+                for x in ready[q]:
+                    e = early[x]
+                    st[x] = e if q == "a" else (e + WAKE if e > qt[q] - 0.001 else qt[q])
+                lo = min(st.values())
+                if q in "gd":
+                    x = min(ready[q])
+                else:
+                    x = max((y for y in st if st[y] <= lo + SLACK), key=lambda y: (pr[y], -y))
+                if best is None or st[x] < best[0]:
+                    best = (st[x], q, x)
+            t0, q, x = best
+            ready[q].remove(x)
+            e = t0 + cs[x]
+            qt[q] = e
+            fin[x] = e + nodes[x][5]
+            nodes[x][3]()
+            for y in succ[x]:
+                left[y] -= 1
+                early[y] = max(early[y], fin[x])
+                if not left[y]:
+                    ready[nodes[y][0]].append(y)
+        for sem in total:
+            if known["g"].get(sem, 0) < total[sem]:
+                g.wait_ge(T.sem[sem], total[sem])
+                learn("g", sem, total[sem])
+    return op, dma, send, arrives, finish
+
+
+def rank_program(g, core, T, topo):
+    r = T.rank_of(core)
+    if r is None:
+        return
+    v, s, p = g.vector, g.scalar, g.tensor
+    op, dma, put, arrives, finish = tracker(g, T)
+
+    def C(n, a=0, b=None, p0=0, p1=128, st=1):
+        bf, o, w = PLACE[n]
+        return T[bf][p0:p1, o + a:o + (w if b is None else b):st]
+
+    def tt(o, a, b, f, R, Wt):
+        op("v", [lambda: v.tensor_tensor(o, a, b, f)], R, Wt)
+
+    def ts(o, a, x, f, R, Wt, y=None, f2=None):
+        if f2 is None:
+            op("v", [lambda: v.tensor_scalar(o, a, x, None, f)], R, Wt)
+        else:
+            op("v", [lambda: v.tensor_scalar(o, a, x, y, f, f2)], R, Wt)
+
+    def cp(o, a, R, Wt):
+        op("v", [lambda: v.tensor_copy(o, a)], R, Wt)
+
+    def fill(o, c, Wt):
+        op("v", [lambda: v.memset(o, c)], "", Wt)
+
+    def act(o, a, R, Wt, f=AF.Identity, **kw):
+        op("s", [lambda: s.activation(o, a, f, **kw)], R, Wt)
+
+    def mm(o, l, x, st, sp):
+        return lambda: p.matmul(o, l, x, st, sp)
+
+    def scan(o, d, R, Wt, n=K):
+        op("v", [lambda: v.tensor_tensor_scan(o, T.s0[:, 0:n], d, 0.0, Op.add, Op.min)], R + " s0", Wt)
+
+    def send(src, key, dst_rank, dst, sem, local, bulk=False):
+        dst_core = T.cores[dst_rank % N]
+        rid, pid = topo.addr(dst_core)[0:2]
+        eng = topo.engines(core, dst_core)
+        eng = eng[-NE:] if bulk else eng[0:NE]
+        put(lambda: g.remote_dma(dst, src, T.sem[sem], T.sem[local], pid, rid, sum(1 << e for e in eng)), key, local, len(eng))
+
+    PWI = " ".join("pw%d" % c for c in range(8))
+    PW = PWI + " pwr0 pwr1 pwr2 pwd"
+    XW = "xw0 xw1"
+    FW = "fw0 fw1"
+    QR = " ".join("qr%d" % i for i in range(16))
+    dma("s", T.tgs[:], T.tg[:], "", "tgs", 2.7)
+    dma("d", T.xw[:, 0:2048], T.xr[:, 0:2048], "", "xw0", 5.0)
+    dma("s", T.cxi[:], T.cx[:], "", "cxi", 5.0)
+    dma("s", T.q[:], T.qx[:], "", "q", 5.0)
+    dma("d", T.xw[:, 2048:W], T.xr[:, 2048:W], "", "xw1", 7.5)
+    dma("s", T.lfi[:], T.lf[:], "", "lfi", 9.0)
+    dma("d", T.xlh[:], T.xl[:], "", "xlh", 10.5)
+    dma("d", T.fdt[:], T.fd[:], "", "fdt", 16.0)
+    fill(C("one"), 1.0, "one")
+    gop = lambda f, R, Wt: op("g", [f], R, Wt)
+    gop(lambda: g.iota(C("pmi", 0, 1), [[0, 1]], 0, 1), "", "pmi")
+    gop(lambda: g.affine_select(C("blf"), C("one", 0, 128), [[-16, 8], [0, 16]], Op.is_ge, 0.0, 0, 1), "one", "blf")
+    gop(lambda: g.affine_select(C("blf"), C("blf"), [[16, 8], [0, 16]], Op.is_ge, 0.0, 15, -1), "blf", "blf")
+    gop(lambda: g.iota(T.ic[:], [[1, 512]], 0, 0), "", "ic")
+    gop(lambda: g.affine_select(C("idf"), C("one", 0, 128), [[-1, 128]], Op.is_equal, 0.0, 0, 1), "one", "idf")
+    gop(lambda: g.iota(T.ia[:], [[-1, K]], 0, 1), "", "ia")
+    gop(lambda: g.affine_select(C("rpf", p1=32), C("one", p1=32), [[-8, 4], [-1, 8], [0, 16]], Op.is_equal, 0.0, 0, 1), "one", "rpf")
+    gop(lambda: g.affine_select(C("btf"), C("blf"), [[1, 128]], Op.is_ge, 0.0, 0, -1), "blf", "btf")
+    gop(lambda: g.iota(C("dmi"), [[16, 12]], 0, 0), "", "dmi")
+
+    def gaff(t):
+        gop(lambda: g.affine_select(C("af%d" % t), C("one", 0, 128), [[-1, 128]], Op.is_equal, 0.0, -(2 + t), 1), "one", "af%d" % t)
+    for t in range(RO):
+        gaff(t)
+    E = lambda i: C("er", i, i + 1)
+    b8 = C("blf", st=16)
+    ts(C("pmi", 0, 1), C("pmi", 0, 1), 15, Op.bitwise_and, "pmi", "pmi")
+    cp(C("pmf", 0, 1), C("pmi", 0, 1), "pmi", "pmf")
+    PM = C("pmf", 0, 1)
+    ts(T.ic[:], T.ic[:], 15, Op.bitwise_and, "ic", "ic")
+    ts(C("sam", 0, 128), T.ic[:, 0:128], 3.0, Op.is_equal, "ic", "sam0")
+    tt(C("sa"), C("blf"), C("sam", 0, 128), Op.mult, "blf sam0", "sa")
+    for j in range(7):
+        ts(E(j), PM, float(j), Op.is_equal, "pmf", "er%d" % j)
+    ts(E(8), E(0), 32.0, Op.mult, "er0", "er8")
+    ts(E(12), E(3), 32768.0, Op.mult, "er3", "er12")
+    tt(E(9), E(8), E(1), Op.add, "er8 er1", "er9")
+    ts(E(7), E(3), 65536.0, Op.mult, "er3", "er7")
+    ts(E(10), E(9), 2.0, Op.mult, "er9", "er10")
+    ts(E(18), E(3), -1.0, Op.mult, "er3", "er18")
+    tt(E(11), E(10), E(2), Op.add, "er10 er2", "er11")
+    ts(C("lt"), T.ic[:, 0:16], PM, Op.is_gt, "ic pmf", "lt")
+    tt(E(13), E(12), E(11), Op.add, "er12 er11", "er13")
+    act(C("wm", 0, 8), b8, "blf", "wm", scale=-65536.0)
+    act(C("wm", 8, 16), b8, "blf", "wm", scale=-131072.0)
+    act(C("wm", 16, 24), b8, "blf", "wm", scale=0.0)
+    act(C("wp", 0, 8), b8, "blf er13", "wp", scale=E(13))
+    act(C("wp", 8, 16), b8, "blf er7", "wp", scale=E(7))
+    act(C("wp", 16, 24), b8, "blf er9", "wp", scale=E(9))
+    ts(T.pci[:, 0:256], T.tgs[:], 6, Op.logical_shift_right, "tgs", "pci0")
+    ts(T.pci[:, 256:512], T.tgs[:], 1, Op.logical_shift_right, "tgs", "pci1", 31, Op.bitwise_and)
+    ts(T.pci[:, 512:768], T.tgs[:], 1, Op.bitwise_and, "tgs", "pci2")
+    cp(T.pcs[:], T.pci[:], "pci0 pci1 pci2", "pcs")
+    fill(T.pw[:, W:W + K], 0.0, "pwd")
+    cp(T.lc[:], T.cxi[:], "cxi", "lc")
+    cp(T.cf[:], T.cxi[:], "cxi", "cf")
+    ts(T.c16[:], T.cxi[:], -2048.0, Op.add, "cxi", "c16")
+    for i in range(16):
+        if i % 2:
+            act(T.qrep[:, i:16 * K:16], T.q[:], "q", "qr%d" % i)
+        else:
+            cp(T.qrep[:, i:16 * K:16], T.q[:], "q", "qr%d" % i)
+    banks = (("psk0", T.psk[:, 0, :]), ("psk1", T.psk[:, 1, :]), ("psv0", T.psv[:, 0, :]), ("psv1", T.psv[:, 1, :]), ("psm", T.psm[:]), ("psu", T.psu[:]), ("psd", T.psd[:]), ("psg", T.psg[:]))
+    for c in range(8):
+        bk, ap = banks[c]
+        op("p", [mm(ap, C("sa"), T.xw[:, 512 * c:512 * c + 512], True, True)], "sa xw%d" % (c // 4), bk)
+        if c % 2:
+            cp(T.pw[:, 512 * c:512 * c + 512], ap, bk, "pw%d" % c)
+        else:
+            act(T.pw[:, 512 * c:512 * c + 512], ap, bk, "pw%d" % c)
+    for j in range(3):
+        dma("d", T.pw[j:128:16, 0:W], T.pcs[:, 256 * j:256 * j + 256], "pcs " + PWI, "pwr%d" % j, 3.5)
+
+    def weights():
+        fill(T.row[:], 0.0, "row")
+        ts(T.row[0:1, 0:128], T.ic[0:1, 0:128], 2048.0, Op.mult, "ic", "row")
+        ts(T.row[0:1, 128:256], T.ic[0:1, 0:128], 4096.0, Op.mult, "ic", "row", 2048.0, Op.add)
+        fill(T.ro2[:], 1.0, "ro2")
+        cp(C("idh"), C("idf"), "idf", "idh")
+
+    def scalar_later():
+        act(C("idb"), C("idf"), "idf", "idb")
+        for nm, cols in (("wm1", (2.0, 0.0, 0.0)), ("wm2", (-2.0, 0.0, 0.0)), ("wp1", (18, 9, 0.0)), ("wp2", (3, 0.0, 9))):
+            for j, w in enumerate(cols):
+                if w in (18, 9, 3):
+                    act(C(nm, 8 * j, 8 * j + 8), b8, "blf er%d" % w, nm, scale=E(w))
+                else:
+                    act(C(nm, 8 * j, 8 * j + 8), b8, "blf", nm, scale=w)
+        act(C("blb"), C("blf"), "blf", "blb")
+        act(C("bt"), C("btf"), "btf", "bt")
+        for k in range(16):
+            act(C("ltk", 128 * k, 128 * k + 128), C("blf"), "blf lt", "ltk", scale=C("lt", k, k + 1))
+
+    def later():
+        cp(C("rp", p1=32), C("rpf", p1=32), "rpf", "rp")
+        ts(T.ia[:], T.ia[:], 15, Op.bitwise_and, "ia", "ia")
+        ts(C("bm"), T.ia[:], 0.0, Op.not_equal, "ia", "bm", BIG, Op.mult)
+        ts(T.s0[:], T.ic[:, 0:K], 0.0, Op.is_equal, "ic", "s0", RES, Op.mult)
+        for j, w in enumerate((-1.0, -1.0, 2.0)):
+            ts(C("bi", 128 * j, 128 * j + 128), C("idf"), w, Op.mult, "idf", "bi")
+        ts(T.row[32:33, 384:512], T.ic[32:33, 0:128], 2048.0, Op.mult, "ic row", "row1")
+
+    def latest():
+        ts(C("dm4"), C("dmi"), PM, Op.add, "dmi pmf", "dm4", float(W), Op.add)
+        ts(C("dm1"), C("dmi"), PM, Op.add, "dmi pmf", "dm1", float(M), Op.add)
+        fill(C("exb"), 0.0, "exb")
+
+    def claim_weights():
+        ts(T.row[0:1, 384:512], T.ic[0:1, 0:128], 2.0, Op.is_equal, "ic row", "row2")
+        for t in range(RO):
+            ts(T.row[96:97, 128 * t:128 * t + 128], T.ic[96:97, 0:128], 4.0 + t, Op.is_equal, "ic row", "row3")
+        ts(E(14), PM, 4.0, Op.is_ge, "pmf", "er14")
+        tt(E(15), E(0), E(1), Op.add, "er0 er1", "er15")
+        tt(E(16), E(15), E(14), Op.add, "er15 er14", "er16")
+        ts(C("dg1"), C("idf"), E(16), Op.mult, "idf er16", "dg1")
+        tt(E(17), E(14), E(3), Op.add, "er14 er3", "er17")
+        ts(C("sam", 0, 128), C("idf"), E(17), Op.mult, "idf er17", "sam0")
+        for t in range(RO):
+            ts(C("af%d" % t), C("af%d" % t), E(4 + t), Op.mult, "af%d er%d" % (t, 4 + t), "af%d" % t)
+            tt(C("dgc%d" % t), C("sam", 0, 128), C("af%d" % t), Op.subtract, "sam0 af%d" % t, "dgc%d" % t)
+        ts(C("sam", 128, 256), T.ic[:, 0:128], 1.0, Op.is_equal, "ic", "sam1")
+        ts(C("vrf", 0, 128), T.ic[:, 0:128], 1.0, Op.is_equal, "ic", "vrf", -32.0, Op.mult)
+        ts(C("vrf", 128, 256), T.ic[:, 0:128], 0.0, Op.is_equal, "ic", "vrf1")
+        tt(C("sam", 256, 384), C("vrf", 0, 128), C("vrf", 128, 256), Op.add, "vrf vrf1", "sam2")
+        tt(C("vrf", 0, 256, p1=32), C("rpf", 256, 512, p1=32), C("sam", 128, 384, p1=32), Op.mult, "rpf sam1 sam2", "vrf vrf1")
+        tt(C("vr", p1=32), C("vrf", 0, 128, p1=32), C("vrf", 128, 256, p1=32), Op.add, "vrf", "vr")
+        ts(C("vrf", 256, 384, p1=32), C("rpf", 128, 256, p1=32), float(W), Op.mult, "rpf", "vrf2")
+        tt(C("rpc", p1=32), C("vrf", 256, 384, p1=32), C("rpf", 0, 128, p1=32), Op.add, "vrf2 rpf", "rpc")
+
+    def yt_weights():
+        fill(T.wt[:], 0.0, "wt")
+        for c in range(8):
+            act(T.wt[:, 64 * c + c:64 * c + 64:8], b8, "blf er11 wt", "wt%d" % c, scale=E(11))
+
+    def disks_out():
+        cp(T.lfu[:], T.lfi[:], "lfi", "lfu")
+        chip = lambda x: topo.chip(T.cores[x % N])
+
+        def handed(src, j):
+            return j > 1 and chip(src - j) == chip(src - j + 1) != chip(src)
+        act(C("pb16"), C("idf"), "idf", "pb16", scale=16.0)
+        act(C("nb16"), C("idf"), "idf", "nb16", scale=-16.0)
+        op("p", [mm(T.psg[:], C("idb"), T.xlh[:, 0:512], True, False), mm(T.psg[:], C("pb16"), T.xlh[:, 512:M], False, True)], "idb pb16 xlh", "psg")
+        act(T.xlp[:], T.psg[:], "psg", "xlp")
+        for j in (1, 2, 3):
+            if not handed(r, j):
+                send(T.lfu[:], "lfu", r - j, T["lu%d" % j][:], "rl%d" % j, "ls%d" % (2 * j - 2), True)
+            arrives("rl%d" % j, NE, "lu%d" % j, (9.0, 30.0, 40.0)[j - 1])
+            if not handed(r, j):
+                send(T.xlp[:], "xlp", r - j, T["xp%d" % j][:], "rx%d" % j, "ls%d" % (2 * j - 1), True)
+            arrives("rx%d" % j, NE, "xp%d" % j, (13.0, 35.0, 45.0)[j - 1])
+        for i in (1, 2):
+            if handed(r + i, i + 1):
+                send(T["lu%d" % i][:], "lu%d" % i, r - 1, T["lu%d" % (i + 1)][:], "rl%d" % (i + 1), "ls%d" % (10 + 2 * i), True)
+                send(T["xp%d" % i][:], "xp%d" % i, r - 1, T["xp%d" % (i + 1)][:], "rx%d" % (i + 1), "ls%d" % (11 + 2 * i), True)
+
+    def features(j):
+        x, xl = T["xp%d" % j], T["xl%d" % j]
+        act(T.xt[:], x[:], "xp%d" % j, "xt", AF.Copy, scale=0.0625, bias=144.0 - 0.46875)
+        act(xl[:, 512:M], T.xt[:], "xt", "xh%d" % j, AF.Copy, bias=-144.0)
+        op("p", [mm(T.psg[:], C("idb"), x[:], True, False), mm(T.psg[:], C("nb16"), xl[:, 512:M], False, True)], "idb nb16 xp%d xh%d" % (j, j), "psg")
+        act(xl[:, 0:512], T.psg[:], "psg", "xl%d" % j)
+
+    def disk_window(j):
+        cp(T["lw%d" % j][:, 0:M], T["lu%d" % j][:], "lu%d" % j, "lw%d" % j)
+
+    def unpack(j):
+        if j == 0:
+            ts(T.fw[:, 0:2048], T.fdt[:], W - 1, Op.bitwise_and, "fdt", "fw0")
+        else:
+            ts(T.fw[:, 2048:W], T.fdt[:], 12, Op.logical_shift_right, "fdt", "fw1")
+
+    def apply(buf, win):
+        cp(C("lm"), T[buf][:, K:K + 12], buf, "lm")
+        cp(T[win][:].indirect(C("lm")), T[buf][:, 0:K], buf + " lm", win)
+
+    EQ = lambda eq: " ".join("%s%d" % (eq, kb) for kb in range(12))
+
+    def same(eq, src, sk, lst, lk):
+        for kb in range(11, -1, -1):
+            ts(T[eq][:, kb, 0:K - 16 * kb], src[:, 16 * kb:K], C(lst[0], lst[1] + kb, lst[1] + kb + 1), Op.is_equal, sk + " " + lk, eq + str(kb))
+
+    def lower(eq, ps, pk):
+        fs = [mm(ps[:, 0:K], C("idb"), C("bm"), True, False)]
+        fs += [mm(ps[:, 16 * kb + 16:K], C("blb"), T[eq][:, kb, 16:K - 16 * kb], False, False) for kb in range(10, -1, -1)]
+        fs += [mm(ps[:, k:K:16], C("ltk", 128 * k, 128 * k + 128), T[eq][:, :, k], False, k == 15) for k in range(1, 16)]
+        op("p", fs, "idb bm blb ltk " + EQ(eq), pk)
+
+    def xgather(dst, lst, lk, h):
+        a, b = H * h, H * h + H
+        tt(T[dst][:, 16 * a:16 * b], T.xw[:, 0:W].indirect(T[lst][:, a:b]), T.qrep[:, 16 * a:16 * b], Op.min, " ".join((XW, lk, QR)), dst + str(h))
+
+    def pgather(dst, lst, lk, h):
+        act(T[dst][:, 16 * H * h:16 * H * (h + 1)], T.pw[:].indirect(T[lst][:, H * h:H * h + H]), PW + " " + lk, dst + str(h))
+
+    def sums(ps, src, w, h, last=False):
+        op("p", [mm(T[ps][0:H, h, i:384:16], T[src][:, 16 * H * h + i:16 * H * (h + 1):16], C(w), False, last and i == 15) for i in range(16)],
+           "%s%d %s" % (src, h, w), "%s%d" % (ps, h))
+
+    def halves(o, l, R, Wt, n, ident):
+        op("p", [mm(o[0:n, H * h:H * h + H], l[0:H, h, 0:n], C(ident, 0, H, p1=H), True, True) for h in (0, 1)], R + " " + ident, Wt)
+
+    def message(t, part):
+        msg = "msg%d" % (t + 1)
+        if part == 0:
+            same("eqt", T.ru[:, 0:K], "rut0 rut1", ("lis", 0), "lisa0 lisa1")
+            ts(C("pari"), C("ni"), 1, Op.bitwise_and, "ni0 ni1", "pari")
+            ts(C("w5"), C("pari"), -2.0, Op.mult, "pari", "w5", 1.0, Op.add)
+            tt(C("w6"), C("w5"), C("ni"), Op.add, "w5 ni0 ni1", "w6")
+            tt(C("w5"), C("w6"), C("dm1"), Op.subtract, "w6 dm1", "w5")
+            return
+        lower("eqt", T.psd, "psd")
+        scan(T.sct2[:], T.psd[:, 0:K], "psd", "sct2")
+        ts(C("z", 12, 24), T.sct2[:, 15:K:16], 0.0, Op.is_equal, "sct2", "z1")
+        tt(C("dwin"), C("req"), C("z", 12, 24), Op.mult, "req z1", "dwin")
+        tt(C("w6"), C("w5"), C("dwin"), Op.mult, "w5 dwin", "w6")
+        tt(T[msg][:, K:K + 12], C("w6"), C("dm1"), Op.add, "w6 dm1", msg + "l")
+        mk = msg + " " + msg + "l"
+        if t == 0:
+            send(T[msg][:], mk, r - 1, T.up1[:], "ru1", "ls6")
+            arrives("ru1", NE, "up1", 7.0)
+            send(T[msg][:], mk, r - 2, T.up2[:], "ru2", "ls7")
+            arrives("ru2", NE, "up2", 20.0)
+        elif t == 1:
+            send(T[msg][:], mk, r - 1, T.up3[:], "ru3", "ls8")
+            arrives("ru3", NE, "up3", 7.0)
+        send(T[msg][:], mk, r + 1 + t, T["hm%d" % (t + 1)][:], "rh%d" % (t + 1), "ls%d" % (9 + t))
+        arrives("rh%d" % (t + 1), NE, "hm%d" % (t + 1), (50.0, 20.0, 8.0)[t])
+
+    L = lambda n: T[n][0:H, :, :]
+    X = lambda n, i: T[n][0:H, :, 8 * i:8 * i + 8]
+    for t in range(RO):
+        j = t + 1
+        lw, xl, msg = "lw%d" % j, "xl%d" % j, "msg%d" % j
+        if t == 0:
+            scalar_later()
+        if t == 0:
+            disks_out()
+            weights()
+            later()
+            latest()
+            claim_weights()
+            unpack(0)
+            unpack(1)
+            disk_window(1)
+        elif t == 1:
+            disk_window(2)
+            disk_window(3)
+            apply("up1", "lw2")
+            apply("up2", "lw3")
+        else:
+            apply("up3", "lw3")
+            cp(T.lh[:, 0:M], T.lfi[:], "lfi", "lh")
+        if t:
+            ts(T.c16[:], T.cf[:], -2048.0, Op.add, "cf", "c16")
+        R16 = lambda f: C("rp", 128 * f, 128 * f + 128, p1=16)
+        lnw = T[lw][:, 0:M]
+        for h in (0, 1):
+            a, b, x, y = H * h, H * h + H, 6 * h, 6 * h + 6
+            k = lambda names: " ".join("%s%d" % (n, h) for n in names.split())
+            pgather("pa", "lc", "lc", h)
+            xgather("ma", "lc", "lc", h)
+            op("p", [mm(T.psk[0:H, h, 0:384], T.ro2[0:1, 0:H], T.row[0:1, 0:384], True, False)], "ro2 row", k("psk"))
+            sums("psk", *(("pa", "wp") if t else ("ma", "wm")), h)
+            sums("psk", *(("ma", "wm") if t else ("pa", "wp")), h)
+            op("p", [mm(T.psk[0:H, h, 128:256], T.c16[:, a:b], C("idh"), False, True)], "c16 idh", k("psk"))
+            act(T.co[0:H, h, :], T.psk[0:H, h, 1:256:2], k("psk"), k("co"))
+            tt(T.t1[0:H, h, :], T.psk[0:H, h, 0:256:2], T.co[0:H, h, :], Op.min, k("psk co"), k("t1_"))
+            act(T.sl[0:H, h, :], T.psk[0:H, h, 256:384], k("psk"), k("sl"))
+            tt(T.t2[0:H, h, :], T.t1[0:H, h, 0:128:2], T.t1[0:H, h, 1:128:2], Op.min, k("t1_"), k("t2_"))
+            tt(T.t3[0:H, h, :], T.t2[0:H, h, 0:64:2], T.t2[0:H, h, 1:64:2], Op.min, k("t2_"), k("t3_"))
+            tt(T.t4[0:H, h, :], T.t3[0:H, h, 0:32:2], T.t3[0:H, h, 1:32:2], Op.min, k("t3_"), k("t4_"))
+            ts(T.fi[0:H, h, 8:16], T.t4[0:H, h, 8:16], W - 1, Op.bitwise_and, k("t4_"), k("fio"))
+            ts(T.fi[0:H, h, 0:8], T.t4[0:H, h, 0:8], 2047, Op.bitwise_and, k("t4_"), k("fit"))
+            ts(T.fl[0:H, h, 8:16], T.fi[0:H, h, 8:16], -2048.0, Op.add, k("fio"), k("flo"))
+            cp(T.fl[0:H, h, 0:8], T.fi[0:H, h, 0:8], k("fit"), k("flt"))
+            op("p", [mm(T.psk[0:16, h, 384:480], T.fl[0:H, h, :], C("idh", 0, H, p1=H), True, True)], k("flo flt") + " idh", k("psk"))
+            cp(T.gt[0:16, a:b], T.psk[0:16, h, 384:480], k("psk"), k("gt"))
+            pb, pk = ((T.psm, "psm"), (T.psu, "psu"))[h]
+            fs = []
+            for f in (0, 1):
+                fs += [mm(pb[:, H * f:H * f + H], R16(f), T.gt[0:16, a:b], True, False), mm(pb[:, H * f:H * f + H], C("idb"), C("bm", 0, H), False, True),
+                       mm(pb[:, H * f + K:H * f + K + H], R16(f), T.gt[0:16, a:b], True, True)]
+            op("p", fs, "rp idb bm " + k("gt"), pk)
+            scan(T.sct[:, a:b], pb[:, 0:H], pk, k("sct"), H)
+            ts(C("ni", x, y), T.sct[:, a + 15:b:16], 1, Op.logical_shift_right, k("sct"), k("ni"))
+            cp(C("ln", x, y), C("ni", x, y), k("ni"), k("ln"))
+            LN = C("ln", x, y)
+            act(T.sq[:, a:b], lnw.indirect(LN), lw + " " + k("ln"), k("sqa"), AF.Square, bias=4.0)
+            act(T.sq[:, K + a:K + b], lnw.indirect(LN), lw + " " + k("ln"), k("sqb"), AF.Square, bias=592.0)
+            cp(T.b16[:, a:b], lnw.indirect(LN), lw + " " + k("ln"), k("b16_"))
+            if h == 0:
+                features(j)
+            act(T.at[:, a:b], T[xl][:].indirect(LN), xl + " xh%d " % j + k("ln"), k("at"))
+            for c, (sc, of) in enumerate(((0.125, -2.4375), (0.03125, -10951.484375))):
+                u, w, n = K * c + a, K * c + b, "ab"[c]
+                ts(T.tt[:, u:w], T.sq[:, u:w], sc, Op.mult, k("sq" + n), k("tt" + n), of, Op.add)
+                ts(T.cc[:, u:w], T.tt[:, u:w], W - 1, Op.bitwise_and, k("tt" + n), k("cc" + n))
+                cp(T["l%d" % (c + 1)][:, a:b], T.cc[:, u:w], k("cc" + n), k("li" + n))
+            scan(T.sco[:, a:b], pb[:, H:K], pk, k("sco"), H)
+            ts(T.ru[:, a:b], pb[:, K:K + H], 2048.0, Op.add, pk, k("rut"))
+            ts(T.ru[:, K + a:K + b], pb[:, K + H:2 * K], 2048.0, Op.add, pk, k("ruo"))
+            ts(C("lis", 12 + x, 12 + y), T.sco[:, a + 15:b:16], 2048.0, Op.add, k("sco"), k("lisb"))
+            ts(C("lis", x, y), T.sct[:, a + 15:b:16], 2048.0, Op.add, k("sct"), k("lisa"))
+            op("p", [mm(T.psv[0:H, h, :], T.ro2[32:33, 0:H], T.row[32:33, :], True, False),
+                     mm(T.psv[0:H, h, 128:512], T.b16[:, a:b], C("bi"), False, False)], "ro2 row1 bi " + k("b16_"), k("psv"))
+        for h in (0, 1):
+            for c in "ab":
+                pgather("p" + c, "l%d" % ("ab".index(c) + 1), "li%s%d" % (c, h), h)
+                xgather("m" + c, "l%d" % ("ab".index(c) + 1), "li%s%d" % (c, h), h)
+                sums("psv", "m" + c, "wm%d" % ("ab".index(c) + 1), h)
+                sums("psv", "p" + c, "wp%d" % ("ab".index(c) + 1), h, c == "b")
+        cp(C("lo"), C("lis", 12, 24), "lisb0 lisb1", "lo")
+        same("eqo", T.ru[:, K:2 * K], "ruo0 ruo1", ("lis", 12), "lisb0 lisb1")
+        lower("eqo", T.psd, "psd")
+        message(t, 0)
+        scan(T.scd[:], T.psd[:, 0:K], "psd", "scd")
+        ts(C("ei"), T.sct[:, 15:K:16], 1, Op.bitwise_and, "sct0 sct1", "ei")
+        ts(C("z", 0, 12), T.scd[:, 15:K:16], 0.0, Op.is_equal, "scd", "z0")
+        tt(C("w1"), C("lis", 12, 24), C("dm4"), Op.subtract, "lisb0 lisb1 dm4", "w1")
+        tt(C("cand"), C("z", 0, 12), C("ei"), Op.mult, "z0 ei", "cand")
+        op("v", [lambda: v.tensor_tensor_scan(C("exb", 1, 13), C("one", 0, 12), C("cand"), 0.0, Op.mult, Op.add)], "one cand", "exb")
+        op("p", [mm(T.psg[:, 400:412], C("bt"), C("cand"), True, False), mm(T.psg[:, 400:412], C("blb"), C("exb", 0, 12), False, True)], "bt cand blb exb", "psg")
+        ts(C("rk"), T.psg[:, 400:412], float(CAP), Op.is_le, "psg", "rk")
+        halves(T.psk[:, 1, :], T.sl, "sl0 sl1", "psk1", 128, "idf")
+        tt(T.dc[:], T.cc[:, K:2 * K], T.cc[:, 0:K], Op.subtract, "cca0 cca1 ccb0 ccb1", "dc")
+        tt(C("req"), C("rk"), C("cand"), Op.mult, "rk cand", "req")
+        tt(C("w2"), C("w1"), C("req"), Op.mult, "w1 req", "w2")
+        ts(C("nrq"), C("req"), -8192.0, Op.mult, "req", "nrq", 8192.0 + 2048.0, Op.add)
+        tt(C("ld"), C("w2"), C("dm4"), Op.add, "w2 dm4", "ld")
+        act(T[msg][:, 0:K], T.psk[:, 1, 0:K], "psk1", msg)
+        message(t, 1)
+        act(T.g2[:], T.pw[:].indirect(C("ld")), PW + " ld", "g2")
+        op("p", [mm(T.psk[:, 0, 0:K], C("sa"), T.at[:], True, False), mm(T.psk[:, 0, 0:K], C("dg1"), T.g2[:], False, False),
+                 mm(T.psk[:, 0, 0:K], T.row[96:97, 128 * t:128 * t + 128], T.ro2[96:97, 0:K], False, True)], "sa at0 at1 dg1 g2 row3 ro2", "psk0")
+        act(T.v2[:], T.psk[:, 0, 0:K], "psk0", "v2")
+        cp(T.xw[:].indirect(C("ld")), T.at[:], "ld at0 at1", XW)
+        for h in (0, 1):
+            k = lambda names: " ".join("%s%d" % (n, h) for n in names.split())
+            U = lambda n: T[n][0:H, h, :]
+            ts(U("r1"), T.psv[0:H, h, 128:256], 0.0, Op.is_equal, k("psv"), k("ra"), -4096.0, Op.mult)
+            ts(T.psv[0:H, h, 256:384], T.psv[0:H, h, 256:384], 0.0, Op.is_equal, k("psv"), k("rb psv"), 1024.0, Op.mult)
+            tt(U("u1"), T.psv[0:H, h, 0:128], U("r1"), Op.add, k("psv ra"), k("ua"))
+            tt(U("u2"), T.psv[0:H, h, 256:384], U("u1"), Op.add, k("psv ua rb"), k("uc"))
+            act(U("ub"), U("u2"), k("uc"), k("ub"), AF.Abs)
+            ts(U("pk"), U("u2"), 0.0, Op.is_gt, k("uc"), k("pk"))
+            tt(U("kk"), T.psv[0:H, h, 384:512], U("pk"), Op.add, k("psv pk"), k("kk"))
+            ts(T.psv[0:H, h, 128:256], U("ub"), 512.0, Op.is_gt, k("ub ra"), k("rc psv"), RES, Op.mult)
+            tt(U("k2"), T.psv[0:H, h, 128:256], U("kk"), Op.add, k("psv kk rc"), k("kz"))
+            tt(U("ka"), T.k2[0:H, h, 0:128:2], T.k2[0:H, h, 1:128:2], Op.min, k("kz"), k("ka"))
+            tt(U("kb"), T.ka[0:H, h, 0:64:2], T.ka[0:H, h, 1:64:2], Op.min, k("ka"), k("kb"))
+            tt(U("kc"), T.kb[0:H, h, 0:32:2], T.kb[0:H, h, 1:32:2], Op.min, k("kb"), k("kc"))
+            tt(U("kd"), T.kc[0:H, h, 0:16:2], T.kc[0:H, h, 1:16:2], Op.min, k("kc"), k("kd"))
+        halves(T.psg, T.pk, "pk0 pk1", "psg", 128, "idb")
+        KD = "kd0 kd1"
+        ts(X("t7", 0), L("kd"), 1, Op.logical_shift_right, KD, "t7", 1023, Op.bitwise_and)
+        ts(X("t7", 1), L("kd"), 6, Op.logical_shift_right, KD, "t7p", 31, Op.bitwise_and)
+        ts(X("fg", 0), X("t7", 0), 4.0, Op.add, "t7", "fga")
+        ts(X("fg", 1), X("t7", 0), 592.0, Op.add, "t7", "fgb")
+        ts(X("fh", 0), L("kd"), 1, Op.bitwise_and, KD, "fh")
+        tt(L("t5"), L("fg"), L("fg"), Op.mult, "fga fgb", "t5")
+        cp(T.fm[0:H, :, 16:32], L("t7"), "t7 t7p", "fm1")
+        ts(X("fj", 0), X("t5", 0), 0.125, Op.mult, "t5", "fja", -2.4375, Op.add)
+        ts(X("fj", 1), X("t5", 1), 0.03125, Op.mult, "t5", "fjb", -10951.484375, Op.add)
+        ts(X("fm", 1), L("kd"), RES, Op.is_ge, KD, "fm2")
+        ts(L("fe"), L("fj"), W - 1, Op.bitwise_and, "fja fjb", "fe")
+        tt(X("t6", 1), X("fe", 1), X("fe", 0), Op.subtract, "fe", "t6")
+        ts(X("t6", 0), X("fe", 0), -2048.0, Op.add, "fe", "t6b")
+        tt(X("t6", 2), X("t6", 1), X("fh", 0), Op.mult, "t6 fh", "t6c")
+        tt(X("fm", 0), X("t6", 2), X("t6", 0), Op.add, "t6c t6b", "fm0")
+        halves(T.psm, T.fm, "fm0 fm1 fm2", "psm", 32, "idh")
+        tt(T.sp[:], T.psg[:, 0:K], T.dc[:], Op.mult, "psg dc", "sp")
+        cp(T.gu[0:32, :], T.psm[0:32, 0:K], "psm", "gu")
+        op("p", [mm(T.psu[:, 0:K], C("rpc", p1=32), T.gu[0:32, :], True, True)], "rpc gu", "psu")
+        op("p", [mm(T.psg[:, 0:K], C("rpc", p1=32), T.gu[0:32, :], True, False), mm(T.psg[:, 0:K], C("idb"), C("bm"), False, True)], "rpc gu idb bm", "psg")
+        tt(T.sg[:], T.sp[:], T.cc[:, 0:K], Op.add, "sp cca0 cca1", "sg")
+        cp(T.pw[:].indirect(C("ld")), T.v2[:], "ld v2", PW)
+        ts(T.ru2[:], T.psu[:, 0:K], 2048.0, Op.add, "psu", "ru2_")
+        scan(T.scl[:], T.psg[:, 0:K], "psg", "scl")
+        tt(C("pls"), C("nrq"), T.scl[:, 15:K:16], Op.add, "nrq scl", "pls")
+        same("eqo", T.ru2, "ru2_", ("pls", 0), "pls")
+        lower("eqo", T.psd, "psd")
+        ts(C("w3"), C("pls"), float(W), Op.is_lt, "pls", "w3")
+        tt(C("w4"), C("pls"), C("dm4"), Op.subtract, "pls dm4", "w4")
+        cp(T.fw[:].indirect(C("ld")), T.sg[:], "ld sg", FW)
+        tt(C("w2"), C("w3"), C("w4"), Op.mult, "w3 w4", "w2")
+        tt(T.qs[:], T.xw[:, 0:W].indirect(C("lo")), T.q[:], Op.add, XW + " lo q", "qs")
+        cp(T.cf[:], T.fw[:, 0:W].indirect(C("lo")), FW + " lo", "cf")
+        ts(T.qb[:], T.qs[:], 0.5, Op.mult, "qs", "qb", 127.8125, Op.add)
+        if t < RO - 1:
+            cp(T.lc[:], T.cf[:], "cf", "lc")
+            for i in range(16):
+                ts(T.qrep[:, i:16 * K:16], T.qb[:], -128.0, Op.add, "qb", "qr%d" % i)
+        ts(T.q[:], T.qb[:], -128.0, Op.add, "qb", "q")
+        scan(T.scd[:], T.psd[:, 0:K], "psd", "scd")
+        ts(C("z", 0, 12), T.scd[:, 15:K:16], 0.0, Op.is_equal, "scd", "z0")
+        tt(C("w1"), C("w2"), C("z", 0, 12), Op.mult, "w2 z0", "w1")
+        tt(C("lcl"), C("w1"), C("dm4"), Op.add, "w1 dm4", "lcl")
+        act(T.g1[:], T.pw[:].indirect(C("lcl")), PW + " lcl", "g1")
+        op("p", [mm(T.psm[:, 0:K], C("vr", p1=32), T.gu[0:32, :], True, False),
+                 mm(T.psm[:, 0:K], T.row[0:1, 384:512], T.ro2[0:1, 0:K], False, False),
+                 mm(T.psm[:, 0:K], C("dgc%d" % t), T.g1[:], False, True)], "vr gu row2 ro2 dgc%d g1" % t, "psm")
+        act(T.v1[:], T.psm[:, 0:K], "psm", "v1")
+        cp(T.pw[:].indirect(C("lcl")), T.v1[:], "lcl v1", PW)
+        if t == 1:
+            yt_weights()
+    dma("d", T.yc[:], T.cf[:], "cf", "yc")
+    dma("d", T.yq[:], T.q[:], "q", "yq")
+    op("p", [mm(T.psv[0:64, 0, :], T.wt[:, 64 * c:64 * c + 64], T.pw[:, 512 * c:512 * c + 512], c == 0, c == 7) for c in range(8)], " ".join("wt%d" % c for c in range(8)) + " " + PW, "psv0")
+    for j in (1, 2, 3):
+        apply("hm%d" % j, "lh")
+    act(T.yts[0:64, :], T.psv[0:64, 0, :], "psv0", "yts")
+    dma("d", T.yt[:], T.yts[0:64, :], "yts", "yt")
+    dma("d", T.yl[:], T.lh[:, 0:M], "lh", "yl")
+    finish()

@@ -3,23 +3,25 @@ from concourse.mybir import AluOpType as Op, ActivationFunctionType as AF
 W, M, K, CAP, RO, N = 4096, 1024, 192, 160, 3, 8
 H = 96
 BIG = 65536.0
-RES = 1048576.0
+RES = 67108864.0
+OUT = 8192.0
 NE = 8
-WAKE, SLACK = 0.3, 0.1
-VCOST = {"ma": 1.7, "mb": 1.7, "xw": 0.6, "pw": 0.6, "fw": 0.7, "lw": 0.7, "lh": 0.7, "lfu": 0.85, "pcs": 0.64, "sq": 0.2, "cf": 0.25, "qs": 0.25, "eqo": 0.07, "eqt": 0.07, "cc": 0.12, "dc": 0.32, "sp": 0.16, "sg": 0.32, "u": 0.11}
-SCOST = {"pa": 1.7, "pb": 1.7, "pw": 0.43, "g": 0.28, "at": 0.15, "wt": 0.06, "ltk": 0.11, "wm": 0.06, "wp": 0.06}
+ACT16 = True
+ACTU = True
+QG, QS = 5, 5
+WAKE, SLACK, LEAD, CYC, PCYC, GATH, SCAT = 0.2, 0.1, 0.15, 0.00083, 0.0006, 1.56, 3.8
 
 _S = "sbuf"
 F32, B16, I32, U16, H16 = "float32", "bfloat16", "int32", "uint16", "float16"
 PACK = {
-    "tf": (F32, (("z", 24), ("lis", 24), ("req", 12), ("rk", 12), ("dwin", 12), ("w1", 12), ("w2", 12), ("w3", 12), ("w4", 12), ("w5", 12), ("w6", 12), ("nrq", 12), ("pls", 12),
-                 ("dm4", 12), ("dm1", 12), ("er", 24), ("lt", 16), ("pmf", 4))),
-    "tl": (U16, (("ln", 12), ("lo", 12), ("ld", 12), ("lcl", 12), ("lm", 12))),
-    "ti": (I32, (("ni", 12), ("ei", 12), ("pari", 12), ("dmi", 12), ("pmi", 4))),
-    "tb": (B16, (("wm", 24), ("wp", 24), ("wm1", 24), ("wm2", 24), ("wp1", 24), ("wp2", 24), ("cand", 12), ("exb", 16))),
-    "cb": (B16, (("idb", 128), ("blb", 128), ("bt", 128), ("dg1", 128), ("sa", 128), ("dgc0", 128), ("dgc1", 128), ("dgc2", 128), ("bm", K), ("ltk", 2048), ("pb16", 128), ("nb16", 128))),
-    "cff": (F32, (("one", 512), ("idf", 128), ("blf", 128), ("btf", 128), ("af0", 128), ("af1", 128), ("af2", 128), ("sam", 384), ("rpf", 512), ("vrf", 384))),
-    "chh": (H16, (("rp", 512), ("rpc", 128), ("vr", 128), ("bi", 384), ("idh", 128))),
+    "tf": (F32, (("nqd", 12), ("own", 12), ("w1", 12), ("dm4", 12), ("dm1", 12), ("er", 16), ("lt", 16), ("ec", 16), ("pmf", 4))),
+    "tl": (U16, (("ld", 12), ("lcl", 12), ("lp", 12), ("lm", 12))),
+    "ti": (I32, (("dmi", 12), ("pmi", 4))),
+    "tb": (B16, (("wm", 24), ("wp", 24), ("wm1", 24), ("wm2", 24), ("wp1", 24), ("wp2", 24), ("cand", 12), ("exb", 16), ("nrq", 12))),
+    "cb": (B16, (("idb", 128), ("id2", 128), ("idn", 128), ("blb", 128), ("bl8", 128), ("bn8", 128), ("btr", 128), ("tri", 128), ("dg1", 128), ("sa", 128), ("se", 128), ("vh", 128), ("wt", 128),
+                 ("dgc0", 128), ("dgc1", 128), ("dgc2", 128), ("bm", K), ("bmc", K), ("zr", K), ("ltk", 2048), ("sel", 2048), ("pb16", 128), ("nb16", 128))),
+    "cff": (F32, (("one", 512), ("idf", 128), ("blf", 128), ("btf", 128), ("tmp", 256), ("rpf", 512))),
+    "chh": (H16, (("rnp", 128), ("rop", 128), ("rop0", 128), ("rnp0", 128), ("rm", 128), ("blh", 128), ("vr", 128), ("bi", 384), ("idh", 128))),
 }
 PLACE, SCRATCH = {}, {}
 for _b in PACK:
@@ -29,18 +31,18 @@ for _b in PACK:
         _o += _w
     SCRATCH[_b] = (_S, [128, _o], PACK[_b][0])
 for _d, _l in (
-    (B16, (("xw", W + K), ("pw", W + K), ("pcs", 768), ("xlh", M), ("q", K), ("qb", K), ("qrep", 16 * K), ("ma", 16 * K), ("mb", 16 * K), ("pa", 16 * K), ("pb", 16 * K),
-           ("at", K), ("g1", K), ("v1", K), ("g2", K), ("v2", K), ("row", 512), ("ro2", 512), ("wt", 512), ("xl1", M), ("xl2", M), ("xl3", M), ("xp1", 512), ("xp2", 512), ("xp3", 512), ("xlp", 512), ("xt", 512))),
-    (I32, (("fw", W + K), ("fdt", 2048), ("tgs", 256), ("pci", 768), ("lfi", M), ("cxi", K), ("sct", K), ("sco", K), ("scl", K), ("tt", 2 * K), ("cc", 2 * K), ("dc", K), ("sg", K), ("ia", K), ("ic", 512))),
-    (U16, (("lfu", M), ("lc", K), ("ru", 2 * K), ("ru2", K), ("l1", K), ("l2", K), ("lu1", M), ("lu2", M), ("lu3", M))),
-    (F32, (("lh", M + K), ("qs", K), ("cf", K), ("scd", K), ("sct2", K), ("sq", 2 * K), ("sp", K), ("yts", 512), ("s0", K), ("lw1", M), ("lw2", M + K), ("lw3", M + K),
+    (B16, (("xw", W + K), ("pt", W), ("pcs", 768), ("xlh", M), ("q", K), ("qb", K), ("qrep", 16 * K), ("ma", 16 * K), ("mb", 16 * K), ("pa", 16 * K), ("pb", 16 * K),
+           ("at", K), ("g1", K), ("g2", K), ("nr", K), ("fst", K), ("hi", K), ("row", 512), ("ro2", 512), ("xl1", M), ("xl2", M), ("xl3", M), ("xp1", 512), ("xp2", 512), ("xp3", 512), ("xlp", 512), ("xt", 512))),
+    (I32, (("fw", W + K), ("fdt", 2048), ("tgs", 256), ("pci", 768), ("lfi", M), ("cxi", K), ("ia", K), ("ic", 256))),
+    (U16, (("lfu", M), ("lc", K), ("lu1", M), ("lu2", M), ("lu3", M))),
+    (F32, (("pw", W + K), ("lh", M + K), ("qs", K), ("cf", K), ("scd", K), ("scm", K), ("scc", K), ("dc", K), ("sg", K), ("sh", K), ("v1", K), ("v2", K), ("s0", 256), ("lw1", M), ("lw2", M + K), ("lw3", M + K),
            ("msg1", K + 12), ("msg2", K + 12), ("msg3", K + 12), ("up1", K + 12), ("up2", K + 12), ("up3", K + 12), ("hm1", K + 12), ("hm2", K + 12), ("hm3", K + 12))),
-    (H16, (("gt", K), ("gu", K), ("b16", K), ("c16", K))),
+    (H16, (("gt", K), ("b16", K), ("c16", K), ("x1", K), ("x2", K), ("rc", K))),
 ):
     for _n, _w in _l:
         SCRATCH[_n] = (_S, [128, _w], _d)
-for _n, _w, _d in (("co", 128, F32), ("t1", 128, F32), ("t2", 64, F32), ("t3", 32, F32), ("t4", 16, I32), ("fi", 16, I32), ("fl", 16, H16), ("sl", 128, F32), ("r1", 128, F32), ("r2", 128, F32), ("u1", 128, F32),
-                   ("u2", 128, F32), ("ub", 128, F32), ("pk", 128, B16), ("kk", 128, F32), ("k2", 128, F32), ("ka", 64, F32), ("kb", 32, F32), ("kc", 16, F32), ("kd", 8, I32), ("fe", 16, I32), ("fg", 16, F32), ("fh", 16, I32), ("fm", 32, H16), ("t5", 16, F32), ("t6", 32, F32), ("t7", 16, I32), ("fj", 16, I32)):
+for _n, _w, _d in (("sc", K, F32), ("ru", K, H16), ("ll", 12, U16), ("sq", K, F32), ("tt", K, I32), ("cc", K, I32), ("l12", K, U16),
+                   ("t4", 256, I32), ("fi", 24, I32), ("fl", 24, H16), ("sl", 128, F32), ("nn", 384, B16)):
     SCRATCH[_n] = (_S, [128, 2, _w], _d)
 SCRATCH["eqo"] = (_S, [128, 12, K], B16)
 SCRATCH["eqt"] = (_S, [128, 12, K], B16)
@@ -100,7 +102,6 @@ def tracker(g, T):
             rd.setdefault(k, {})[ev[0] if ev[2] is None else q] = ev
 
     def op_(q, fns, R, Wt):
-        R, Wt = R.split(), Wt.split()
         deps(q, True, R, Wt)
         for f in fns[:-1]:
             f()
@@ -114,7 +115,6 @@ def tracker(g, T):
         note((sem, cnt[q], q), q, R, Wt)
 
     def dma_(q, out, in_, R, Wt):
-        R, Wt = R.split(), Wt.split()
         deps(q, False, R, Wt)
         sem = "ld%d" % nd[0]
         nd[0] += 1
@@ -124,10 +124,10 @@ def tracker(g, T):
         note((sem, 16, None), q, R, Wt)
 
     def send_(call, R, local, n):
-        deps("g", False, R.split(), [])
+        deps("g", False, R, [])
         call()
         total[local] = n
-        note((local, n, None), "g", R.split(), [])
+        note((local, n, None), "g", R, [])
 
     def arrives_(sem, n, key):
         total[sem] = n
@@ -136,26 +136,21 @@ def tracker(g, T):
 
     nodes = []
 
-    def op(q, fns, R="", Wt=""):
-        nodes.append((q, R.split(), Wt.split(), lambda: op_(q, fns, R, Wt), len(fns), 0.0, -1))
+    def op(q, fns, R, Wt, cost):
+        R, Wt = R.split(), Wt.split()
+        nodes.append((q, R, Wt, lambda: op_(q, fns, R, Wt), cost, 0.0, -1))
 
     def dma(q, out, in_, R="", Wt="", lat=2.2):
-        nodes.append((q, R.split(), Wt.split(), lambda: dma_(q, out, in_, R, Wt), 0, lat, -1))
+        R, Wt = R.split(), Wt.split()
+        nodes.append((q, R, Wt, lambda: dma_(q, out, in_, R, Wt), 0.1, lat, -1))
 
     def send(call, R, local, n):
-        nodes.append(("g", R.split(), [], lambda: send_(call, R, local, n), 0, 0.0, -1))
+        R = R.split()
+        nodes.append(("g", R, [], lambda: send_(call, R, local, n), 0.3, 0.0, -2))
+        return len(nodes) - 1
 
-    def arrives(sem, n, key, lat):
-        nodes.append(("a", [], [key], lambda: arrives_(sem, n, key), 0, lat, len(nodes) - 1))
-
-    def cost(q, W1, n):
-        if q == "p":
-            return 0.05 * n
-        if n == 0:
-            return 0.3 if q == "g" else 0.1
-        if q == "g":
-            return 0.6
-        return (SCOST if q == "s" else VCOST).get(W1, 0.2 if q == "s" else 0.09)
+    def arrives(sem, n, key, lat, after):
+        nodes.append(("a", [], [key], lambda: arrives_(sem, n, key), 0.0, lat, after))
 
     def finish():
         nn = len(nodes)
@@ -190,7 +185,7 @@ def tracker(g, T):
         for x in range(nn):
             for d in dep[x]:
                 succ[d].append(x)
-        cs = [0.0 if nd_[0] == "a" else cost(nd_[0], (nd_[2] + nd_[1] + [""])[0].rstrip("0123456789"), nd_[4]) for nd_ in nodes]
+        cs = [nd_[4] for nd_ in nodes]
         pr = [0.0] * nn
         for x in range(nn - 1, -1, -1):
             pr[x] = cs[x] + nodes[x][5] + max([pr[y] + WAKE for y in succ[x]] + [0.0])
@@ -201,24 +196,33 @@ def tracker(g, T):
         for x in range(nn):
             if not left[x]:
                 ready[nodes[x][0]].append(x)
+        todo = {q: [x for x in range(nn) if nodes[x][0] == q and (q == "d" or nodes[x][6] == -2)] for q in "gd"}
         for _ in range(nn):
             best = None
             for q in "avspgd":
-                if not ready[q]:
+                cand = ready[q]
+                if q in "gd":
+                    cand = [x for x in cand if x not in todo[q][1:]]
+                if not cand:
                     continue
                 st = {}
-                for x in ready[q]:
+                for x in cand:
                     e = early[x]
                     st[x] = e if q == "a" else (e + WAKE if e > qt[q] - 0.001 else qt[q])
                 lo = min(st.values())
-                if q in "gd":
-                    x = min(ready[q])
-                else:
-                    x = max((y for y in st if st[y] <= lo + SLACK), key=lambda y: (pr[y], -y))
+                x = max((y for y in st if st[y] <= lo + SLACK), key=lambda y: (pr[y], -y))
+                for y in sorted(st, key=lambda y: -pr[y]):
+                    if pr[y] <= pr[x]:
+                        break
+                    if max(st[y] + pr[y], st[y] + cs[y] + pr[x]) < max(st[x] + pr[x], max(st[y], st[x] + cs[x]) + pr[y]) - LEAD:
+                        x = y
+                        break
                 if best is None or st[x] < best[0]:
                     best = (st[x], q, x)
             t0, q, x = best
             ready[q].remove(x)
+            if q in "gd" and x in todo[q]:
+                todo[q].pop(0)
             e = t0 + cs[x]
             qt[q] = e
             fin[x] = e + nodes[x][5]
@@ -246,98 +250,116 @@ def rank_program(g, core, T, topo):
         bf, o, w = PLACE[n]
         return T[bf][p0:p1, o + a:o + (w if b is None else b):st]
 
-    def tt(o, a, b, f, R, Wt):
-        op("v", [lambda: v.tensor_tensor(o, a, b, f)], R, Wt)
+    def wid(a):
+        n = 1
+        for x in list(a.shape)[1:]:
+            n *= x
+        return n
+
+    def vcost(o, a, per=1.0):
+        if "16" in str(o.dtype) and "16" in str(a.dtype):
+            per *= 0.5
+        return 0.03 + CYC * max(64, per * wid(o))
+
+    def ncost(n):
+        return 0.05 + CYC * (GATH * n if n > 0 else -SCAT * n)
+
+    def tt(o, a, b, f, R, Wt, n=0):
+        op("v", [lambda: v.tensor_tensor(o, a, b, f)], R, Wt, ncost(n) if n else 0.03 + CYC * max(64, wid(o) * (1 if "ps" in R else 2)))
 
     def ts(o, a, x, f, R, Wt, y=None, f2=None):
         if f2 is None:
-            op("v", [lambda: v.tensor_scalar(o, a, x, None, f)], R, Wt)
+            op("v", [lambda: v.tensor_scalar(o, a, x, None, f)], R, Wt, vcost(o, a))
         else:
-            op("v", [lambda: v.tensor_scalar(o, a, x, y, f, f2)], R, Wt)
+            op("v", [lambda: v.tensor_scalar(o, a, x, y, f, f2)], R, Wt, vcost(o, a))
 
-    def cp(o, a, R, Wt):
-        op("v", [lambda: v.tensor_copy(o, a)], R, Wt)
+    def cp(o, a, R, Wt, n=0):
+        op("v", [lambda: v.tensor_copy(o, a)], R, Wt, ncost(n) if n else vcost(o, a))
 
     def fill(o, c, Wt):
-        op("v", [lambda: v.memset(o, c)], "", Wt)
+        op("v", [lambda: v.memset(o, c)], "", Wt, vcost(o, o))
 
-    def act(o, a, R, Wt, f=AF.Identity, **kw):
-        op("s", [lambda: s.activation(o, a, f, **kw)], R, Wt)
+    def act(o, a, R, Wt, f=AF.Identity, n=0, **kw):
+        op("s", [lambda: s.activation(o, a, f, **kw)], R, Wt, ncost(n) if n else 0.05 + CYC * max(64, wid(o)))
+
+    def cp16(o, a, R, Wt, n=0):
+        (act if ACT16 else cp)(o, a, R, Wt, n=n)
 
     def mm(o, l, x, st, sp):
-        return lambda: p.matmul(o, l, x, st, sp)
+        return (lambda: p.matmul(o, l, x, st, sp), PCYC * max(64, wid(x)) * (4 if "32" in str(x.dtype) else 1))
 
-    def scan(o, d, R, Wt, n=K):
-        op("v", [lambda: v.tensor_tensor_scan(o, T.s0[:, 0:n], d, 0.0, Op.add, Op.min)], R + " s0", Wt)
+    def pe(fs, R, Wt):
+        op("p", [f[0] for f in fs], R, Wt, sum(f[1] for f in fs))
+
+    def scan(o, d, R, Wt, n=K, p1=128):
+        op("v", [lambda: v.tensor_tensor_scan(o, T.s0[0:p1, 0:n], d, 0.0, Op.add, Op.min)], R + " s0", Wt, 0.03 + CYC * n)
+
+    def gop(f, R, Wt, n):
+        op("g", [f], R, Wt, 0.17 + 2 * CYC * n)
 
     def send(src, key, dst_rank, dst, sem, local, bulk=False):
         dst_core = T.cores[dst_rank % N]
         rid, pid = topo.addr(dst_core)[0:2]
         eng = topo.engines(core, dst_core)
         eng = eng[-NE:] if bulk else eng[0:NE]
-        put(lambda: g.remote_dma(dst, src, T.sem[sem], T.sem[local], pid, rid, sum(1 << e for e in eng)), key, local, len(eng))
+        return put(lambda: g.remote_dma(dst, src, T.sem[sem], T.sem[local], pid, rid, sum(1 << e for e in eng)), key, local, len(eng))
 
-    PWI = " ".join("pw%d" % c for c in range(8))
-    PW = PWI + " pwr0 pwr1 pwr2 pwd"
+    PW = " ".join("pw%d" % c for c in range(8)) + " pwd"
     XW = "xw0 xw1"
-    FW = "fw0 fw1"
+    FW = " ".join("fw%d" % c for c in range(8))
     QR = " ".join("qr%d" % i for i in range(16))
-    dma("s", T.tgs[:], T.tg[:], "", "tgs", 2.7)
-    dma("d", T.xw[:, 0:2048], T.xr[:, 0:2048], "", "xw0", 5.0)
-    dma("s", T.cxi[:], T.cx[:], "", "cxi", 5.0)
-    dma("s", T.q[:], T.qx[:], "", "q", 5.0)
-    dma("d", T.xw[:, 2048:W], T.xr[:, 2048:W], "", "xw1", 7.5)
-    dma("s", T.lfi[:], T.lf[:], "", "lfi", 9.0)
-    dma("d", T.xlh[:], T.xl[:], "", "xlh", 10.5)
-    dma("d", T.fdt[:], T.fd[:], "", "fdt", 16.0)
+    dma("d", T.tgs[:], T.tg[:], "", "tgs", 2.7)
+    dma("d", T.lfi[:], T.lf[:], "", "lfi", 5.3)
+    dma("d", T.cxi[:], T.cx[:], "", "cxi", 5.7)
+    dma("d", T.q[:], T.qx[:], "", "q", 5.9)
+    dma("d", T.xw[:, 0:2048], T.xr[:, 0:2048], "", "xw0", 8.5)
+    dma("d", T.xw[:, 2048:W], T.xr[:, 2048:W], "", "xw1", 11.2)
     fill(C("one"), 1.0, "one")
-    gop = lambda f, R, Wt: op("g", [f], R, Wt)
-    gop(lambda: g.iota(C("pmi", 0, 1), [[0, 1]], 0, 1), "", "pmi")
-    gop(lambda: g.affine_select(C("blf"), C("one", 0, 128), [[-16, 8], [0, 16]], Op.is_ge, 0.0, 0, 1), "one", "blf")
-    gop(lambda: g.affine_select(C("blf"), C("blf"), [[16, 8], [0, 16]], Op.is_ge, 0.0, 15, -1), "blf", "blf")
-    gop(lambda: g.iota(T.ic[:], [[1, 512]], 0, 0), "", "ic")
-    gop(lambda: g.affine_select(C("idf"), C("one", 0, 128), [[-1, 128]], Op.is_equal, 0.0, 0, 1), "one", "idf")
-    gop(lambda: g.iota(T.ia[:], [[-1, K]], 0, 1), "", "ia")
-    gop(lambda: g.affine_select(C("rpf", p1=32), C("one", p1=32), [[-8, 4], [-1, 8], [0, 16]], Op.is_equal, 0.0, 0, 1), "one", "rpf")
-    gop(lambda: g.affine_select(C("btf"), C("blf"), [[1, 128]], Op.is_ge, 0.0, 0, -1), "blf", "btf")
-    gop(lambda: g.iota(C("dmi"), [[16, 12]], 0, 0), "", "dmi")
-
-    def gaff(t):
-        gop(lambda: g.affine_select(C("af%d" % t), C("one", 0, 128), [[-1, 128]], Op.is_equal, 0.0, -(2 + t), 1), "one", "af%d" % t)
-    for t in range(RO):
-        gaff(t)
+    gop(lambda: g.iota(C("pmi", 0, 1), [[0, 1]], 0, 1), "", "pmi", 1)
+    gop(lambda: g.iota(T.ic[:], [[0, 16], [1, 16]], 0, 0), "", "ic", 256)
+    gop(lambda: g.affine_select(C("blf"), C("one", 0, 128), [[-16, 8], [0, 16]], Op.is_ge, 0.0, 0, 1), "one", "blf", 128)
+    gop(lambda: g.affine_select(C("blf"), C("blf"), [[16, 8], [0, 16]], Op.is_ge, 0.0, 15, -1), "blf", "blf", 128)
+    gop(lambda: g.affine_select(C("rpf", p1=32), C("one", p1=32), [[-8, 4], [-1, 8], [0, 16]], Op.is_equal, 0.0, 0, 1), "one", "rpf", 512)
+    gop(lambda: g.affine_select(C("idf"), C("one", 0, 128), [[-1, 128]], Op.is_equal, 0.0, 0, 1), "one", "idf", 128)
+    gop(lambda: g.affine_select(C("btf"), C("blf"), [[1, 128]], Op.is_ge, 0.0, 0, -1), "blf", "btf", 128)
+    gop(lambda: g.iota(C("dmi"), [[16, 12]], 0, 0), "", "dmi", 12)
     E = lambda i: C("er", i, i + 1)
+    D = lambda i, p1=128: C("ec", i, i + 1, p1=p1)
+    RP = lambda f, st=1: C("rpf", 128 * f, 128 * f + 128, p1=32, st=st)
     b8 = C("blf", st=16)
-    ts(C("pmi", 0, 1), C("pmi", 0, 1), 15, Op.bitwise_and, "pmi", "pmi")
-    cp(C("pmf", 0, 1), C("pmi", 0, 1), "pmi", "pmf")
+    ts(D(9), C("pmi", 0, 1), 24.0, Op.is_equal, "pmi", "ec9", 2048.0, Op.mult)
+    ts(D(10), C("pmi", 0, 1), 24.0, Op.is_equal, "pmi", "ec10", -2047.0, Op.mult)
+    ts(C("pmi", 1, 2), C("pmi", 0, 1), 15, Op.bitwise_and, "pmi", "pmj")
+    cp(C("pmf", 0, 1), C("pmi", 1, 2), "pmj", "pmf")
     PM = C("pmf", 0, 1)
-    ts(T.ic[:], T.ic[:], 15, Op.bitwise_and, "ic", "ic")
-    ts(C("sam", 0, 128), T.ic[:, 0:128], 3.0, Op.is_equal, "ic", "sam0")
-    tt(C("sa"), C("blf"), C("sam", 0, 128), Op.mult, "blf sam0", "sa")
-    for j in range(7):
-        ts(E(j), PM, float(j), Op.is_equal, "pmf", "er%d" % j)
-    ts(E(8), E(0), 32.0, Op.mult, "er0", "er8")
-    ts(E(12), E(3), 32768.0, Op.mult, "er3", "er12")
-    tt(E(9), E(8), E(1), Op.add, "er8 er1", "er9")
-    ts(E(7), E(3), 65536.0, Op.mult, "er3", "er7")
-    ts(E(10), E(9), 2.0, Op.mult, "er9", "er10")
-    ts(E(18), E(3), -1.0, Op.mult, "er3", "er18")
-    tt(E(11), E(10), E(2), Op.add, "er10 er2", "er11")
-    ts(C("lt"), T.ic[:, 0:16], PM, Op.is_gt, "ic pmf", "lt")
-    tt(E(13), E(12), E(11), Op.add, "er12 er11", "er13")
-    act(C("wm", 0, 8), b8, "blf", "wm", scale=-65536.0)
-    act(C("wm", 8, 16), b8, "blf", "wm", scale=-131072.0)
-    act(C("wm", 16, 24), b8, "blf", "wm", scale=0.0)
-    act(C("wp", 0, 8), b8, "blf er13", "wp", scale=E(13))
-    act(C("wp", 8, 16), b8, "blf er7", "wp", scale=E(7))
-    act(C("wp", 16, 24), b8, "blf er9", "wp", scale=E(9))
+    ts(C("er"), T.ic[:, 0:16], PM, Op.is_equal, "ic pmf", "er")
+    ts(C("lt"), T.ic[:, 0:16], PM, Op.is_gt, "ic pmf", "lt", OUT, Op.mult)
+    ts(D(0), E(0), 32.0, Op.mult, "er", "ec0", E(1), Op.add)
+    ts(D(1), E(3), 65536.0, Op.mult, "er ec0", "ec1", D(0), Op.add)
+    ts(D(2), E(3), 65536.0, Op.mult, "er", "ec2")
+    ts(D(3), E(3), -1.0, Op.mult, "er", "ec3")
+    fill(C("sa"), 0.0, "sa")
+    fill(C("wt", p1=32), 0.0, "wt")
+    act(C("sa", 3, 128, st=16), b8, "blf sa", "sa")
+    for j, w in enumerate((-131072.0, -131072.0, 0.0)):
+        act(C("wm", 8 * j, 8 * j + 8), b8, "blf", "wm", scale=w)
+    for j, w in enumerate((1, 2, 0)):
+        act(C("wp", 8 * j, 8 * j + 8), b8, "blf ec%d" % w, "wp", scale=D(w))
     ts(T.pci[:, 0:256], T.tgs[:], 6, Op.logical_shift_right, "tgs", "pci0")
     ts(T.pci[:, 256:512], T.tgs[:], 1, Op.logical_shift_right, "tgs", "pci1", 31, Op.bitwise_and)
     ts(T.pci[:, 512:768], T.tgs[:], 1, Op.bitwise_and, "tgs", "pci2")
-    cp(T.pcs[:], T.pci[:], "pci0 pci1 pci2", "pcs")
+    for j in range(3):
+        cp(T.pcs[:, 256 * j:256 * j + 256], T.pci[:, 256 * j:256 * j + 256], "pci%d" % j, "pcs%d" % j)
+        dma("d", T.pt[8 * j:8 * j + 8, :], T.pcs[:, 256 * j:256 * j + 256], "pcs%d" % j, "pt%d" % j, 7.5)
+        cp(C("wt", j, 128, p1=32, st=16), RP(j, 16), "rpf wt", "wt%d" % j)
+    dma("d", T.xlh[:], T.xl[:], "", "xlh", 9.0)
+    dma("d", T.fdt[:], T.fd[:], "", "fdt", 14.5)
+    ts(C("tmp", 0, 8, p1=32), RP(0, 16), 64.0, Op.mult, "rpf", "tmpa")
+    ts(C("tmp", 8, 16, p1=32), RP(1, 16), 2.0, Op.mult, "rpf", "tmpb")
+    tt(C("tmp", 16, 24, p1=32), C("tmp", 0, 8, p1=32), C("tmp", 8, 16, p1=32), Op.add, "tmpa tmpb", "tmpc")
+    tt(C("wt", 7, 128, p1=32, st=16), C("tmp", 16, 24, p1=32), RP(2, 16), Op.add, "tmpc rpf wt", "wt7")
     fill(T.pw[:, W:W + K], 0.0, "pwd")
     cp(T.lc[:], T.cxi[:], "cxi", "lc")
-    cp(T.cf[:], T.cxi[:], "cxi", "cf")
     ts(T.c16[:], T.cxi[:], -2048.0, Op.add, "cxi", "c16")
     for i in range(16):
         if i % 2:
@@ -347,74 +369,77 @@ def rank_program(g, core, T, topo):
     banks = (("psk0", T.psk[:, 0, :]), ("psk1", T.psk[:, 1, :]), ("psv0", T.psv[:, 0, :]), ("psv1", T.psv[:, 1, :]), ("psm", T.psm[:]), ("psu", T.psu[:]), ("psd", T.psd[:]), ("psg", T.psg[:]))
     for c in range(8):
         bk, ap = banks[c]
-        op("p", [mm(ap, C("sa"), T.xw[:, 512 * c:512 * c + 512], True, True)], "sa xw%d" % (c // 4), bk)
+        pe([mm(ap, C("sa"), T.xw[:, 512 * c:512 * c + 512], True, False), mm(ap, C("wt", p1=24), T.pt[0:24, 512 * c:512 * c + 512], False, True)],
+           "sa wt0 wt1 wt2 wt7 pt0 pt1 pt2 xw%d" % (c // 4), bk)
         if c % 2:
             cp(T.pw[:, 512 * c:512 * c + 512], ap, bk, "pw%d" % c)
         else:
             act(T.pw[:, 512 * c:512 * c + 512], ap, bk, "pw%d" % c)
-    for j in range(3):
-        dma("d", T.pw[j:128:16, 0:W], T.pcs[:, 256 * j:256 * j + 256], "pcs " + PWI, "pwr%d" % j, 3.5)
 
     def weights():
         fill(T.row[:], 0.0, "row")
-        ts(T.row[0:1, 0:128], T.ic[0:1, 0:128], 2048.0, Op.mult, "ic", "row")
-        ts(T.row[0:1, 128:256], T.ic[0:1, 0:128], 4096.0, Op.mult, "ic", "row", 2048.0, Op.add)
+        ts(T.row[0:1, 0:128], T.ic[0:1, 0:128], 4096.0, Op.mult, "ic row", "rowa")
+        ts(T.row[0:1, 128:256], T.ic[0:1, 0:128], 4096.0, Op.mult, "ic row", "rowb", 2048.0, Op.add)
         fill(T.ro2[:], 1.0, "ro2")
         cp(C("idh"), C("idf"), "idf", "idh")
-
-    def scalar_later():
+        ts(T.s0[:], T.ic[:], 0.0, Op.is_equal, "ic", "s0", RES, Op.mult)
+        ts(C("bm"), T.ic[:, 0:K], PM, Op.not_equal, "ic pmf", "bm", BIG, Op.mult)
+        cp(T.gt[0:32, :], C("one", 0, K, p1=32), "one", "gt0 gt1")
+        ts(C("rnp", p1=32), RP(0), D(9, 32), Op.add, "rpf ec9", "rnp")
+        ts(C("rop", p1=32), RP(1), D(9, 32), Op.add, "rpf ec9", "rop")
+        cp(C("rnp0", p1=32), RP(0), "rpf", "rnp0")
+        cp(C("rop0", p1=32), RP(1), "rpf", "rop0")
         act(C("idb"), C("idf"), "idf", "idb")
-        for nm, cols in (("wm1", (2.0, 0.0, 0.0)), ("wm2", (-2.0, 0.0, 0.0)), ("wp1", (18, 9, 0.0)), ("wp2", (3, 0.0, 9))):
+        ts(C("bi", 0, 128), C("idf"), 0.0, Op.mult, "idf", "bia")
+        ts(C("bi", 128, 256), C("idf"), -1.0, Op.mult, "idf", "bib")
+        ts(C("bi", 256, 384), C("idf"), -1.0, Op.mult, "idf", "bic")
+        for nm, cols in (("wm1", (2.0, 0.0, 0.0)), ("wm2", (-2.0, 0.0, 0.0)), ("wp1", (D(3), D(0), 0.0)), ("wp2", (E(3), 0.0, D(0)))):
             for j, w in enumerate(cols):
-                if w in (18, 9, 3):
-                    act(C(nm, 8 * j, 8 * j + 8), b8, "blf er%d" % w, nm, scale=E(w))
-                else:
-                    act(C(nm, 8 * j, 8 * j + 8), b8, "blf", nm, scale=w)
-        act(C("blb"), C("blf"), "blf", "blb")
-        act(C("bt"), C("btf"), "btf", "bt")
-        for k in range(16):
-            act(C("ltk", 128 * k, 128 * k + 128), C("blf"), "blf lt", "ltk", scale=C("lt", k, k + 1))
+                act(C(nm, 8 * j, 8 * j + 8), b8, "blf er ec0 ec3", nm, scale=w)
 
     def later():
-        cp(C("rp", p1=32), C("rpf", p1=32), "rpf", "rp")
-        ts(T.ia[:], T.ia[:], 15, Op.bitwise_and, "ia", "ia")
-        ts(C("bm"), T.ia[:], 0.0, Op.not_equal, "ia", "bm", BIG, Op.mult)
-        ts(T.s0[:], T.ic[:, 0:K], 0.0, Op.is_equal, "ic", "s0", RES, Op.mult)
-        for j, w in enumerate((-1.0, -1.0, 2.0)):
-            ts(C("bi", 128 * j, 128 * j + 128), C("idf"), w, Op.mult, "idf", "bi")
-        ts(T.row[32:33, 384:512], T.ic[32:33, 0:128], 2048.0, Op.mult, "ic row", "row1")
-
-    def latest():
+        act(C("blb"), C("blf"), "blf", "blb")
+        act(C("bl8"), C("blf"), "blf", "bl8", scale=OUT)
+        act(C("bn8"), C("blf"), "blf", "bn8", scale=-OUT)
+        act(C("id2"), C("idf"), "idf", "id2", scale=2.0)
+        act(C("idn"), C("idf"), "idf", "idn", scale=-1.0)
+        for k in range(1, 16):
+            act(C("ltk", 128 * k, 128 * k + 128), C("blf"), "blf lt", "ltk", scale=C("lt", k, k + 1))
+        for k in range(16):
+            act(C("sel", 128 * k, 128 * k + 128), C("blf"), "blf er", "sel", scale=E(k))
+        ts(D(4), E(2), -1.0, Op.mult, "er", "ec4")
+        act(C("se"), C("blf"), "blf ec4", "se", scale=D(4))
+        act(C("bmc"), C("bm"), "bm", "bmc", AF.Copy, bias=OUT + 2048.0)
+        act(C("zr"), C("bm"), "bm", "zr", scale=0.0)
+        for nm, w in (("btr", -256.0), ("tri", -2.0)):
+            act(C("tmp", 128, 256), C("idf"), "idf", "tmpd", scale=w)
+            tt(C(nm), C("tmp", 128, 256), C("btf"), Op.add, "tmpd btf", nm)
+        ts(C("tmp", 0, 128, p1=32), RP(2), -2.0, Op.mult, "rpf ec10 tmpa tmpb tmpc", "tmpa tmpb tmpc", D(10, 32), Op.add)
+        tt(C("rm", p1=32), C("tmp", 0, 128, p1=32), RP(0), Op.add, "tmpa rpf", "rm")
+        cp16(C("blh"), C("blf"), "blf", "blh")
         ts(C("dm4"), C("dmi"), PM, Op.add, "dmi pmf", "dm4", float(W), Op.add)
         ts(C("dm1"), C("dmi"), PM, Op.add, "dmi pmf", "dm1", float(M), Op.add)
         fill(C("exb"), 0.0, "exb")
-
-    def claim_weights():
-        ts(T.row[0:1, 384:512], T.ic[0:1, 0:128], 2.0, Op.is_equal, "ic row", "row2")
         for t in range(RO):
-            ts(T.row[96:97, 128 * t:128 * t + 128], T.ic[96:97, 0:128], 4.0 + t, Op.is_equal, "ic row", "row3")
-        ts(E(14), PM, 4.0, Op.is_ge, "pmf", "er14")
-        tt(E(15), E(0), E(1), Op.add, "er0 er1", "er15")
-        tt(E(16), E(15), E(14), Op.add, "er15 er14", "er16")
-        ts(C("dg1"), C("idf"), E(16), Op.mult, "idf er16", "dg1")
-        tt(E(17), E(14), E(3), Op.add, "er14 er3", "er17")
-        ts(C("sam", 0, 128), C("idf"), E(17), Op.mult, "idf er17", "sam0")
+            ts(T.row[96:97, 128 * t:128 * t + 128], T.ic[96:97, 0:128], 4.0 + t, Op.is_equal, "ic row", "row3%d" % t)
+        for j, w in ((0, -144.0), (1, 4608.0), (2, 1.0), (7, 1.0)):
+            ts(T.row[0:1, 384 + j:512:16], T.ic[0:1, 0:8], 0.0, Op.mult, "ic row", "row2%d" % j, w, Op.add)
+        ts(D(5), PM, 4.0, Op.is_ge, "pmf", "ec5")
+        ts(D(6), D(5), E(0), Op.add, "ec5 er", "ec6", E(1), Op.add)
+        ts(D(7), D(5), E(3), Op.add, "ec5 er", "ec7")
+        ts(D(8), D(0), 2.0, Op.mult, "ec0", "ec8")
+        ts(D(11), E(1), -32.0, Op.mult, "er", "ec11", E(0), Op.add)
+        act(C("dg1"), C("idf"), "idf ec6", "dg1", scale=D(6))
+        act(C("dg1", 7, 128, st=16), b8, "blf ec8 dg1", "dg1", scale=D(8))
+        act(C("vh"), C("idf"), "idf ec11", "vh", scale=D(11))
         for t in range(RO):
-            ts(C("af%d" % t), C("af%d" % t), E(4 + t), Op.mult, "af%d er%d" % (t, 4 + t), "af%d" % t)
-            tt(C("dgc%d" % t), C("sam", 0, 128), C("af%d" % t), Op.subtract, "sam0 af%d" % t, "dgc%d" % t)
-        ts(C("sam", 128, 256), T.ic[:, 0:128], 1.0, Op.is_equal, "ic", "sam1")
-        ts(C("vrf", 0, 128), T.ic[:, 0:128], 1.0, Op.is_equal, "ic", "vrf", -32.0, Op.mult)
-        ts(C("vrf", 128, 256), T.ic[:, 0:128], 0.0, Op.is_equal, "ic", "vrf1")
-        tt(C("sam", 256, 384), C("vrf", 0, 128), C("vrf", 128, 256), Op.add, "vrf vrf1", "sam2")
-        tt(C("vrf", 0, 256, p1=32), C("rpf", 256, 512, p1=32), C("sam", 128, 384, p1=32), Op.mult, "rpf sam1 sam2", "vrf vrf1")
-        tt(C("vr", p1=32), C("vrf", 0, 128, p1=32), C("vrf", 128, 256, p1=32), Op.add, "vrf", "vr")
-        ts(C("vrf", 256, 384, p1=32), C("rpf", 128, 256, p1=32), float(W), Op.mult, "rpf", "vrf2")
-        tt(C("rpc", p1=32), C("vrf", 256, 384, p1=32), C("rpf", 0, 128, p1=32), Op.add, "vrf2 rpf", "rpc")
-
-    def yt_weights():
-        fill(T.wt[:], 0.0, "wt")
-        for c in range(8):
-            act(T.wt[:, 64 * c + c:64 * c + 64:8], b8, "blf er11 wt", "wt%d" % c, scale=E(11))
+            ts(D(12 + t), E(4 + t), -1.0, Op.mult, "er", "ec%d" % (12 + t))
+            act(C("dgc%d" % t), C("idf"), "idf ec7", "dgc%d" % t, scale=D(7))
+            for j in (2, 7):
+                act(C("dgc%d" % t, j, 128, st=16), b8, "blf ec%d dgc%d" % (12 + t, t), "dgc%d" % t, scale=D(12 + t))
+        ts(C("vr"), C("blf"), 0.0, Op.mult, "blf", "vr")
+        ts(C("vr", 1, 128, st=16), b8, 1.0, Op.mult, "blf vr", "vr1")
+        ts(C("vr", 7, 128, st=16), b8, 2.0, Op.mult, "blf vr", "vr7")
 
     def disks_out():
         cp(T.lfu[:], T.lfi[:], "lfi", "lfu")
@@ -424,276 +449,220 @@ def rank_program(g, core, T, topo):
             return j > 1 and chip(src - j) == chip(src - j + 1) != chip(src)
         act(C("pb16"), C("idf"), "idf", "pb16", scale=16.0)
         act(C("nb16"), C("idf"), "idf", "nb16", scale=-16.0)
-        op("p", [mm(T.psg[:], C("idb"), T.xlh[:, 0:512], True, False), mm(T.psg[:], C("pb16"), T.xlh[:, 512:M], False, True)], "idb pb16 xlh", "psg")
+        pe([mm(T.psg[:], C("idb"), T.xlh[:, 0:512], True, False), mm(T.psg[:], C("pb16"), T.xlh[:, 512:M], False, True)], "idb pb16 xlh", "psg")
         act(T.xlp[:], T.psg[:], "psg", "xlp")
+        sent = []
         for j in (1, 2, 3):
             if not handed(r, j):
-                send(T.lfu[:], "lfu", r - j, T["lu%d" % j][:], "rl%d" % j, "ls%d" % (2 * j - 2), True)
-            arrives("rl%d" % j, NE, "lu%d" % j, (9.0, 30.0, 40.0)[j - 1])
-            if not handed(r, j):
-                send(T.xlp[:], "xlp", r - j, T["xp%d" % j][:], "rx%d" % j, "ls%d" % (2 * j - 1), True)
-            arrives("rx%d" % j, NE, "xp%d" % j, (13.0, 35.0, 45.0)[j - 1])
+                sent.append(send(T.lfu[:], "lfu", r - j, T["lu%d" % j][:], "rl%d" % j, "ls%d" % (2 * j - 2), True))
+                sent.append(send(T.xlp[:], "xlp", r - j, T["xp%d" % j][:], "rx%d" % j, "ls%d" % (2 * j - 1), True))
+            arrives("rl%d" % j, NE, "lu%d" % j, (9.0, 20.0, 26.0)[j - 1], sent[0])
+            arrives("rx%d" % j, NE, "xp%d" % j, (6.0, 15.0, 21.0)[j - 1], sent[1])
         for i in (1, 2):
             if handed(r + i, i + 1):
                 send(T["lu%d" % i][:], "lu%d" % i, r - 1, T["lu%d" % (i + 1)][:], "rl%d" % (i + 1), "ls%d" % (10 + 2 * i), True)
                 send(T["xp%d" % i][:], "xp%d" % i, r - 1, T["xp%d" % (i + 1)][:], "rx%d" % (i + 1), "ls%d" % (11 + 2 * i), True)
 
-    def features(j):
+    def features(j, ps, pk, after):
         x, xl = T["xp%d" % j], T["xl%d" % j]
-        act(T.xt[:], x[:], "xp%d" % j, "xt", AF.Copy, scale=0.0625, bias=144.0 - 0.46875)
+        act(T.xt[:], x[:], "xp%d %s" % (j, after), "xt", AF.Copy, scale=0.0625, bias=144.0 - 0.46875)
         act(xl[:, 512:M], T.xt[:], "xt", "xh%d" % j, AF.Copy, bias=-144.0)
-        op("p", [mm(T.psg[:], C("idb"), x[:], True, False), mm(T.psg[:], C("nb16"), xl[:, 512:M], False, True)], "idb nb16 xp%d xh%d" % (j, j), "psg")
-        act(xl[:, 0:512], T.psg[:], "psg", "xl%d" % j)
+        pe([mm(ps, C("idb"), x[:], True, False), mm(ps, C("nb16"), xl[:, 512:M], False, True)], "idb nb16 xp%d xh%d" % (j, j), pk)
+        act(xl[:, 0:512], ps, pk, "xl%d" % j)
 
-    def disk_window(j):
-        cp(T["lw%d" % j][:, 0:M], T["lu%d" % j][:], "lu%d" % j, "lw%d" % j)
+    def disk_window(j, after):
+        (act if ACTU else cp)(T["lw%d" % j][:, 0:M], T["lu%d" % j][:], "lu%d %s" % (j, after), "lw%d" % j)
 
-    def unpack(j):
-        if j == 0:
-            ts(T.fw[:, 0:2048], T.fdt[:], W - 1, Op.bitwise_and, "fdt", "fw0")
-        else:
-            ts(T.fw[:, 2048:W], T.fdt[:], 12, Op.logical_shift_right, "fdt", "fw1")
+    def unpack():
+        for c in range(4):
+            a, b = 512 * c, 512 * c + 512
+            ts(T.fw[:, a:b], T.fdt[:, a:b], W - 1, Op.bitwise_and, "fdt", "fw%d" % c)
+            ts(T.fw[:, 2048 + a:2048 + b], T.fdt[:, a:b], 12, Op.logical_shift_right, "fdt", "fw%d" % (4 + c))
 
-    def apply(buf, win):
-        cp(C("lm"), T[buf][:, K:K + 12], buf, "lm")
-        cp(T[win][:].indirect(C("lm")), T[buf][:, 0:K], buf + " lm", win)
+    def apply(buf, win, after=""):
+        cp(C("lm"), T[buf][:, K:K + 12], buf + " " + after, "lm")
+        cp(T[win][:].indirect(C("lm")), T[buf][:, 0:K], buf + " lm", win, -K)
 
-    EQ = lambda eq: " ".join("%s%d" % (eq, kb) for kb in range(12))
-
-    def same(eq, src, sk, lst, lk):
-        for kb in range(11, -1, -1):
-            ts(T[eq][:, kb, 0:K - 16 * kb], src[:, 16 * kb:K], C(lst[0], lst[1] + kb, lst[1] + kb + 1), Op.is_equal, sk + " " + lk, eq + str(kb))
+    def same(eq, src, sk, own, lk):
+        for kb in range(12):
+            ts(T[eq][:, kb, 0:K - 16 * kb], src[:, 16 * kb:K], 2048.0, Op.add, sk + " " + lk, eq + str(kb), own(kb), Op.is_equal)
 
     def lower(eq, ps, pk):
-        fs = [mm(ps[:, 0:K], C("idb"), C("bm"), True, False)]
-        fs += [mm(ps[:, 16 * kb + 16:K], C("blb"), T[eq][:, kb, 16:K - 16 * kb], False, False) for kb in range(10, -1, -1)]
-        fs += [mm(ps[:, k:K:16], C("ltk", 128 * k, 128 * k + 128), T[eq][:, :, k], False, k == 15) for k in range(1, 16)]
-        op("p", fs, "idb bm blb ltk " + EQ(eq), pk)
+        for kb in range(11):
+            pe([mm(ps[:, 16 * kb + 16:K], C("bl8"), T[eq][:, kb, 16:K - 16 * kb], False, False)], "bl8 %s%d" % (eq, kb), pk)
+        pe([mm(ps[:, k:K:16], C("ltk", 128 * k, 128 * k + 128), T[eq][:, :, k], False, k == 15) for k in range(1, 16)],
+           "ltk " + " ".join("%s%d" % (eq, kb) for kb in range(12)), pk)
 
     def xgather(dst, lst, lk, h):
         a, b = H * h, H * h + H
-        tt(T[dst][:, 16 * a:16 * b], T.xw[:, 0:W].indirect(T[lst][:, a:b]), T.qrep[:, 16 * a:16 * b], Op.min, " ".join((XW, lk, QR)), dst + str(h))
+        tt(T[dst][:, 16 * a:16 * b], T.xw[:, 0:W].indirect(lst[:, a:b]), T.qrep[:, 16 * a:16 * b], Op.min, " ".join((XW, lk, QR)), dst + str(h), 16 * H)
 
     def pgather(dst, lst, lk, h):
-        act(T[dst][:, 16 * H * h:16 * H * (h + 1)], T.pw[:].indirect(T[lst][:, H * h:H * h + H]), PW + " " + lk, dst + str(h))
+        act(T[dst][:, 16 * H * h:16 * H * (h + 1)], T.pw[:].indirect(lst[:, H * h:H * h + H]), PW + " " + lk, dst + str(h), n=16 * H)
 
     def sums(ps, src, w, h, last=False):
-        op("p", [mm(T[ps][0:H, h, i:384:16], T[src][:, 16 * H * h + i:16 * H * (h + 1):16], C(w), False, last and i == 15) for i in range(16)],
+        pe([mm(T[ps][0:H, h, i:384:16], T[src][:, 16 * H * h + i:16 * H * (h + 1):16], C(w), False, last and i == 15) for i in range(16)],
            "%s%d %s" % (src, h, w), "%s%d" % (ps, h))
 
-    def halves(o, l, R, Wt, n, ident):
-        op("p", [mm(o[0:n, H * h:H * h + H], l[0:H, h, 0:n], C(ident, 0, H, p1=H), True, True) for h in (0, 1)], R + " " + ident, Wt)
+    def turn(o, l, w, h, st, sp):
+        return mm(o[:, H * h:H * h + H], l, C(w, 0, H, p1=H), st, sp)
 
-    def message(t, part):
-        msg = "msg%d" % (t + 1)
-        if part == 0:
-            same("eqt", T.ru[:, 0:K], "rut0 rut1", ("lis", 0), "lisa0 lisa1")
-            ts(C("pari"), C("ni"), 1, Op.bitwise_and, "ni0 ni1", "pari")
-            ts(C("w5"), C("pari"), -2.0, Op.mult, "pari", "w5", 1.0, Op.add)
-            tt(C("w6"), C("w5"), C("ni"), Op.add, "w5 ni0 ni1", "w6")
-            tt(C("w5"), C("w6"), C("dm1"), Op.subtract, "w6 dm1", "w5")
-            return
-        lower("eqt", T.psd, "psd")
-        scan(T.sct2[:], T.psd[:, 0:K], "psd", "sct2")
-        ts(C("z", 12, 24), T.sct2[:, 15:K:16], 0.0, Op.is_equal, "sct2", "z1")
-        tt(C("dwin"), C("req"), C("z", 12, 24), Op.mult, "req z1", "dwin")
-        tt(C("w6"), C("w5"), C("dwin"), Op.mult, "w5 dwin", "w6")
-        tt(T[msg][:, K:K + 12], C("w6"), C("dm1"), Op.add, "w6 dm1", msg + "l")
-        mk = msg + " " + msg + "l"
-        if t == 0:
-            send(T[msg][:], mk, r - 1, T.up1[:], "ru1", "ls6")
-            arrives("ru1", NE, "up1", 7.0)
-            send(T[msg][:], mk, r - 2, T.up2[:], "ru2", "ls7")
-            arrives("ru2", NE, "up2", 20.0)
-        elif t == 1:
-            send(T[msg][:], mk, r - 1, T.up3[:], "ru3", "ls8")
-            arrives("ru3", NE, "up3", 7.0)
-        send(T[msg][:], mk, r + 1 + t, T["hm%d" % (t + 1)][:], "rh%d" % (t + 1), "ls%d" % (9 + t))
-        arrives("rh%d" % (t + 1), NE, "hm%d" % (t + 1), (50.0, 20.0, 8.0)[t])
-
-    L = lambda n: T[n][0:H, :, :]
-    X = lambda n, i: T[n][0:H, :, 8 * i:8 * i + 8]
+    LO = T.ll[:, 1, :]
+    GT = T.gt[0:32, :]
+    R32 = lambda n: C(n, p1=32)
     for t in range(RO):
         j = t + 1
         lw, xl, msg = "lw%d" % j, "xl%d" % j, "msg%d" % j
         if t == 0:
-            scalar_later()
-        if t == 0:
-            disks_out()
             weights()
+            disks_out()
             later()
-            latest()
-            claim_weights()
-            unpack(0)
-            unpack(1)
-            disk_window(1)
-        elif t == 1:
-            disk_window(2)
-            disk_window(3)
-            apply("up1", "lw2")
-            apply("up2", "lw3")
-        else:
-            apply("up3", "lw3")
+            unpack()
             cp(T.lh[:, 0:M], T.lfi[:], "lfi", "lh")
-        if t:
-            ts(T.c16[:], T.cf[:], -2048.0, Op.add, "cf", "c16")
-        R16 = lambda f: C("rp", 128 * f, 128 * f + 128, p1=16)
         lnw = T[lw][:, 0:M]
+        for h in (0, 1):
+            pgather("pa", T.lc[:], "lc", h)
+            xgather("ma", T.lc[:], "lc", h)
+        if t == 0:
+            disk_window(1, "pa1")
+        else:
+            if t == 2:
+                apply("up2", lw, "lc")
+            apply(("up1", "up3")[t - 1], lw, "ma1")
+        features(j, T.psg[:], "psg", "pa1")
         for h in (0, 1):
             a, b, x, y = H * h, H * h + H, 6 * h, 6 * h + 6
             k = lambda names: " ".join("%s%d" % (n, h) for n in names.split())
-            pgather("pa", "lc", "lc", h)
-            xgather("ma", "lc", "lc", h)
-            op("p", [mm(T.psk[0:H, h, 0:384], T.ro2[0:1, 0:H], T.row[0:1, 0:384], True, False)], "ro2 row", k("psk"))
-            sums("psk", *(("pa", "wp") if t else ("ma", "wm")), h)
-            sums("psk", *(("ma", "wm") if t else ("pa", "wp")), h)
-            op("p", [mm(T.psk[0:H, h, 128:256], T.c16[:, a:b], C("idh"), False, True)], "c16 idh", k("psk"))
-            act(T.co[0:H, h, :], T.psk[0:H, h, 1:256:2], k("psk"), k("co"))
-            tt(T.t1[0:H, h, :], T.psk[0:H, h, 0:256:2], T.co[0:H, h, :], Op.min, k("psk co"), k("t1_"))
+            pe([mm(T.psk[0:H, h, 0:384], T.ro2[0:1, 0:H], T.row[0:1, 0:384], True, False)], "ro2 rowa rowb", k("psk"))
+            sums("psk", "ma", "wm", h)
+            sums("psk", "pa", "wp", h)
+            pe([mm(T.psk[0:H, h, 128:256], T.c16[:, a:b], C("idh"), False, True)], "c16 idh", k("psk"))
+            scan(T.t4[0:H, h, :], T.psk[0:H, h, 0:256], k("psk"), k("t4_"), 256, H)
             act(T.sl[0:H, h, :], T.psk[0:H, h, 256:384], k("psk"), k("sl"))
-            tt(T.t2[0:H, h, :], T.t1[0:H, h, 0:128:2], T.t1[0:H, h, 1:128:2], Op.min, k("t1_"), k("t2_"))
-            tt(T.t3[0:H, h, :], T.t2[0:H, h, 0:64:2], T.t2[0:H, h, 1:64:2], Op.min, k("t2_"), k("t3_"))
-            tt(T.t4[0:H, h, :], T.t3[0:H, h, 0:32:2], T.t3[0:H, h, 1:32:2], Op.min, k("t3_"), k("t4_"))
-            ts(T.fi[0:H, h, 8:16], T.t4[0:H, h, 8:16], W - 1, Op.bitwise_and, k("t4_"), k("fio"))
-            ts(T.fi[0:H, h, 0:8], T.t4[0:H, h, 0:8], 2047, Op.bitwise_and, k("t4_"), k("fit"))
-            ts(T.fl[0:H, h, 8:16], T.fi[0:H, h, 8:16], -2048.0, Op.add, k("fio"), k("flo"))
-            cp(T.fl[0:H, h, 0:8], T.fi[0:H, h, 0:8], k("fit"), k("flt"))
-            op("p", [mm(T.psk[0:16, h, 384:480], T.fl[0:H, h, :], C("idh", 0, H, p1=H), True, True)], k("flo flt") + " idh", k("psk"))
-            cp(T.gt[0:16, a:b], T.psk[0:16, h, 384:480], k("psk"), k("gt"))
+            ts(T.fi[0:H, h, 0:16], T.t4[0:H, h, 15:256:16], W - 1, Op.bitwise_and, k("t4_"), k("fia"))
+            ts(T.fi[0:H, h, 16:24], T.t4[0:H, h, 15:128:16], 1, Op.bitwise_and, k("t4_"), k("fib"))
+            ts(T.fl[0:H, h, :], T.fi[0:H, h, :], -2048.0, Op.add, k("fia fib"), k("fl"))
+            pe([mm(T.psk[0:24, h, 384:480], T.fl[0:H, h, :], C("idh", 0, H, p1=H), True, True)], k("fl") + " idh", k("psk"))
+            cp(T.gt[0:24, a:b], T.psk[0:24, h, 384:480], k("psk"), k("gt"))
             pb, pk = ((T.psm, "psm"), (T.psu, "psu"))[h]
             fs = []
-            for f in (0, 1):
-                fs += [mm(pb[:, H * f:H * f + H], R16(f), T.gt[0:16, a:b], True, False), mm(pb[:, H * f:H * f + H], C("idb"), C("bm", 0, H), False, True),
-                       mm(pb[:, H * f + K:H * f + K + H], R16(f), T.gt[0:16, a:b], True, True)]
-            op("p", fs, "rp idb bm " + k("gt"), pk)
-            scan(T.sct[:, a:b], pb[:, 0:H], pk, k("sct"), H)
-            ts(C("ni", x, y), T.sct[:, a + 15:b:16], 1, Op.logical_shift_right, k("sct"), k("ni"))
-            cp(C("ln", x, y), C("ni", x, y), k("ni"), k("ln"))
-            LN = C("ln", x, y)
-            act(T.sq[:, a:b], lnw.indirect(LN), lw + " " + k("ln"), k("sqa"), AF.Square, bias=4.0)
-            act(T.sq[:, K + a:K + b], lnw.indirect(LN), lw + " " + k("ln"), k("sqb"), AF.Square, bias=592.0)
-            cp(T.b16[:, a:b], lnw.indirect(LN), lw + " " + k("ln"), k("b16_"))
-            if h == 0:
-                features(j)
-            act(T.at[:, a:b], T[xl][:].indirect(LN), xl + " xh%d " % j + k("ln"), k("at"))
-            for c, (sc, of) in enumerate(((0.125, -2.4375), (0.03125, -10951.484375))):
-                u, w, n = K * c + a, K * c + b, "ab"[c]
-                ts(T.tt[:, u:w], T.sq[:, u:w], sc, Op.mult, k("sq" + n), k("tt" + n), of, Op.add)
-                ts(T.cc[:, u:w], T.tt[:, u:w], W - 1, Op.bitwise_and, k("tt" + n), k("cc" + n))
-                cp(T["l%d" % (c + 1)][:, a:b], T.cc[:, u:w], k("cc" + n), k("li" + n))
-            scan(T.sco[:, a:b], pb[:, H:K], pk, k("sco"), H)
-            ts(T.ru[:, a:b], pb[:, K:K + H], 2048.0, Op.add, pk, k("rut"))
-            ts(T.ru[:, K + a:K + b], pb[:, K + H:2 * K], 2048.0, Op.add, pk, k("ruo"))
-            ts(C("lis", 12 + x, 12 + y), T.sco[:, a + 15:b:16], 2048.0, Op.add, k("sco"), k("lisb"))
-            ts(C("lis", x, y), T.sct[:, a + 15:b:16], 2048.0, Op.add, k("sct"), k("lisa"))
-            op("p", [mm(T.psv[0:H, h, :], T.ro2[32:33, 0:H], T.row[32:33, :], True, False),
-                     mm(T.psv[0:H, h, 128:512], T.b16[:, a:b], C("bi"), False, False)], "ro2 row1 bi " + k("b16_"), k("psv"))
+            for f, n in enumerate(("rnp", "rop")):
+                fs += [mm(pb[:, H * f:H * f + H], R32(n), T.gt[0:32, a:b], True, False), mm(pb[:, H * f:H * f + H], C("idb"), C("bm", 0, H), False, True)]
+            fs += [mm(pb[:, H * f + K:H * f + K + H], R32(n), T.gt[0:32, a:b], True, True) for f, n in enumerate(("rnp0", "rop0"))]
+            pe(fs, "rnp rop rnp0 rop0 idb bm " + k("gt"), pk)
+            scan(T.sc[:, h, :], pb[:, 0:K], pk, k("sc"))
+            cp(T.ll[:, :, x:y], T.sc[:, h, 15:K:16], k("sc"), k("ll"))
+            cp16(T.ru[:, :, a:b], pb[:, K:2 * K], pk, k("ru"))
+            LN = T.ll[:, 0, x:y]
+            act(T.sq[:, 0, a:b], lnw.indirect(LN), lw + " " + k("ll"), k("sqa"), AF.Square, H, scale=2.0, bias=8.0)
+            act(T.sq[:, 1, a:b], lnw.indirect(LN), lw + " " + k("ll"), k("sqb"), AF.Square, H, bias=592.0)
+            cp16(T.b16[:, a:b], lnw.indirect(LN), lw + " " + k("ll"), k("b16_"), H)
+            for c, of in enumerate((-2.484375, -10951.484375)):
+                ts(T.tt[:, c, a:b], T.sq[:, c, a:b], 0.03125, Op.mult, k("sq" + "ab"[c]), k("tt" + "ab"[c]), of, Op.add)
+            ts(T.cc[:, :, a:b], T.tt[:, :, a:b], W - 1, Op.bitwise_and, k("tta ttb"), k("cc"))
+            cp(T.l12[:, :, a:b], T.cc[:, :, a:b], k("cc"), k("li"))
+            pe([mm(T.psv[0:H, h, 0:384], T.b16[:, a:b], C("bi"), True, False)], "bia bib bic " + k("b16_"), k("psv"))
         for h in (0, 1):
-            for c in "ab":
-                pgather("p" + c, "l%d" % ("ab".index(c) + 1), "li%s%d" % (c, h), h)
-                xgather("m" + c, "l%d" % ("ab".index(c) + 1), "li%s%d" % (c, h), h)
-                sums("psv", "m" + c, "wm%d" % ("ab".index(c) + 1), h)
-                sums("psv", "p" + c, "wp%d" % ("ab".index(c) + 1), h, c == "b")
-        cp(C("lo"), C("lis", 12, 24), "lisb0 lisb1", "lo")
-        same("eqo", T.ru[:, K:2 * K], "ruo0 ruo1", ("lis", 12), "lisb0 lisb1")
+            for c in (0, 1):
+                pgather("p" + "ab"[c], T.l12[:, c, :], "li%d" % h, h)
+                xgather("m" + "ab"[c], T.l12[:, c, :], "li%d" % h, h)
+                sums("psv", "m" + "ab"[c], "wm%d" % (c + 1), h)
+                sums("psv", "p" + "ab"[c], "wp%d" % (c + 1), h, c == 1)
+        act(T.at[:], T[xl][:].indirect(T.ll[:, 0, :]), xl + " xh%d ll0 ll1" % j, "at0 at1", n=K)
+        act(T.g2[:], T.pw[:].indirect(LO), PW + " ll0 ll1", "g2", n=K)
+        same("eqo", T.ru[:, 1, :], "ru0 ru1", lambda kb: T.sc[:, kb // 6, H + 16 * (kb % 6) + 15:H + 16 * (kb % 6) + 16], "sc0 sc1")
+        pe([mm(T.psd[:, 0:K], C("idb"), C("bm"), True, False), mm(T.psd[:, 0:K], C("se"), T.g2[:], False, False)], "idb bm se g2", "psd")
         lower("eqo", T.psd, "psd")
-        message(t, 0)
         scan(T.scd[:], T.psd[:, 0:K], "psd", "scd")
-        ts(C("ei"), T.sct[:, 15:K:16], 1, Op.bitwise_and, "sct0 sct1", "ei")
-        ts(C("z", 0, 12), T.scd[:, 15:K:16], 0.0, Op.is_equal, "scd", "z0")
-        tt(C("w1"), C("lis", 12, 24), C("dm4"), Op.subtract, "lisb0 lisb1 dm4", "w1")
-        tt(C("cand"), C("z", 0, 12), C("ei"), Op.mult, "z0 ei", "cand")
-        op("v", [lambda: v.tensor_tensor_scan(C("exb", 1, 13), C("one", 0, 12), C("cand"), 0.0, Op.mult, Op.add)], "one cand", "exb")
-        op("p", [mm(T.psg[:, 400:412], C("bt"), C("cand"), True, False), mm(T.psg[:, 400:412], C("blb"), C("exb", 0, 12), False, True)], "bt cand blb exb", "psg")
-        ts(C("rk"), T.psg[:, 400:412], float(CAP), Op.is_le, "psg", "rk")
-        halves(T.psk[:, 1, :], T.sl, "sl0 sl1", "psk1", 128, "idf")
-        tt(T.dc[:], T.cc[:, K:2 * K], T.cc[:, 0:K], Op.subtract, "cca0 cca1 ccb0 ccb1", "dc")
-        tt(C("req"), C("rk"), C("cand"), Op.mult, "rk cand", "req")
-        tt(C("w2"), C("w1"), C("req"), Op.mult, "w1 req", "w2")
-        ts(C("nrq"), C("req"), -8192.0, Op.mult, "req", "nrq", 8192.0 + 2048.0, Op.add)
-        tt(C("ld"), C("w2"), C("dm4"), Op.add, "w2 dm4", "ld")
+        ts(C("cand"), T.scd[:, 15:K:16], -1.0, Op.is_equal, "scd", "cand")
+        op("v", [lambda: v.tensor_tensor_scan(C("exb", 1, 13), C("one", 0, 12), C("cand"), 0.0, Op.mult, Op.add)], "one cand", "exb", 0.09)
+        pe([mm(T.psd[:, 400:412], C("btr"), C("cand"), True, False), mm(T.psd[:, 400:412], C("blb"), C("exb", 0, 12), False, True)], "btr cand blb exb", "psd")
+        ts(C("nrq"), T.psd[:, 400:412], CAP - 256.0, Op.is_gt, "psd", "nrq")
+        tt(C("nqd"), C("nrq"), C("dm4"), Op.mult, "nrq dm4", "nqd")
+        tt(C("ld"), C("nqd"), T.sc[:, :, H + 15:K:16], Op.max, "nqd sc0 sc1", "ld")
+        pe([mm(T.psg[:, 0:K], C("idb"), C("zr"), True, False)] + [mm(T.psg[:, k:K:16], C("sel", 128 * k, 128 * k + 128), C("nrq"), False, False) for k in range(16)], "idb zr sel nrq", "psg")
+        tt(T.dc[:], T.cc[:, 1, :], T.cc[:, 0, :], Op.subtract, "cc0 cc1", "dc")
+        pe([turn(T.psk[:, 1, :], T.sl[0:H, h, :], "idf", h, True, True) for h in (0, 1)], "sl0 sl1 idf", "psk1")
         act(T[msg][:, 0:K], T.psk[:, 1, 0:K], "psk1", msg)
-        message(t, 1)
-        act(T.g2[:], T.pw[:].indirect(C("ld")), PW + " ld", "g2")
-        op("p", [mm(T.psk[:, 0, 0:K], C("sa"), T.at[:], True, False), mm(T.psk[:, 0, 0:K], C("dg1"), T.g2[:], False, False),
-                 mm(T.psk[:, 0, 0:K], T.row[96:97, 128 * t:128 * t + 128], T.ro2[96:97, 0:K], False, True)], "sa at0 at1 dg1 g2 row3 ro2", "psk0")
+        tt(C("own"), C("nqd"), T.sc[:, :, 15:H:16], Op.max, "nqd sc0 sc1", "own")
+        same("eqt", T.ru[:, 0, :], "ru0 ru1", lambda kb: C("own", kb, kb + 1), "own")
+        pe([mm(T.psd[:, 0:K], C("idb"), C("bm"), True, False), mm(T.psd[:, 0:K], R32("rm"), GT, False, False)], "idb bm rm gt0 gt1", "psd")
+        lower("eqt", T.psd, "psd")
+        scan(T.scm[:], T.psd[:, 0:K], "psd", "scm")
+        tt(C("w1"), C("nqd"), T.scm[:, 15:K:16], Op.max, "nqd scm", "w1")
+        tt(T[msg][:, K:K + 12], C("w1"), C("dm1"), Op.min, "w1 dm1", msg + "l")
+        mk = msg + " " + msg + "l"
+        if t == 0:
+            arrives("ru1", NE, "up1", 5.0, send(T[msg][:], mk, r - 1, T.up1[:], "ru1", "ls6"))
+            arrives("ru2", NE, "up2", 5.0, send(T[msg][:], mk, r - 2, T.up2[:], "ru2", "ls7"))
+        elif t == 1:
+            arrives("ru3", NE, "up3", 5.0, send(T[msg][:], mk, r - 1, T.up3[:], "ru3", "ls8"))
+        arrives("rh%d" % j, NE, "hm%d" % j, 5.0, send(T[msg][:], mk, r + 1 + t, T["hm%d" % j][:], "rh%d" % j, "ls%d" % (9 + t)))
+        if t:
+            apply("hm%d" % t, "lh", "mb1")
+        pe([mm(T.psk[:, 0, 0:K], C("sa"), T.at[:], True, False), mm(T.psk[:, 0, 0:K], C("dg1"), T.g2[:], False, False),
+            mm(T.psk[:, 0, 0:K], T.row[96:97, 128 * t:128 * t + 128], T.ro2[96:97, 0:K], False, True)], "sa at0 at1 dg1 g2 row3%d ro2" % t, "psk0")
         act(T.v2[:], T.psk[:, 0, 0:K], "psk0", "v2")
-        cp(T.xw[:].indirect(C("ld")), T.at[:], "ld at0 at1", XW)
-        for h in (0, 1):
-            k = lambda names: " ".join("%s%d" % (n, h) for n in names.split())
-            U = lambda n: T[n][0:H, h, :]
-            ts(U("r1"), T.psv[0:H, h, 128:256], 0.0, Op.is_equal, k("psv"), k("ra"), -4096.0, Op.mult)
-            ts(T.psv[0:H, h, 256:384], T.psv[0:H, h, 256:384], 0.0, Op.is_equal, k("psv"), k("rb psv"), 1024.0, Op.mult)
-            tt(U("u1"), T.psv[0:H, h, 0:128], U("r1"), Op.add, k("psv ra"), k("ua"))
-            tt(U("u2"), T.psv[0:H, h, 256:384], U("u1"), Op.add, k("psv ua rb"), k("uc"))
-            act(U("ub"), U("u2"), k("uc"), k("ub"), AF.Abs)
-            ts(U("pk"), U("u2"), 0.0, Op.is_gt, k("uc"), k("pk"))
-            tt(U("kk"), T.psv[0:H, h, 384:512], U("pk"), Op.add, k("psv pk"), k("kk"))
-            ts(T.psv[0:H, h, 128:256], U("ub"), 512.0, Op.is_gt, k("ub ra"), k("rc psv"), RES, Op.mult)
-            tt(U("k2"), T.psv[0:H, h, 128:256], U("kk"), Op.add, k("psv kk rc"), k("kz"))
-            tt(U("ka"), T.k2[0:H, h, 0:128:2], T.k2[0:H, h, 1:128:2], Op.min, k("kz"), k("ka"))
-            tt(U("kb"), T.ka[0:H, h, 0:64:2], T.ka[0:H, h, 1:64:2], Op.min, k("ka"), k("kb"))
-            tt(U("kc"), T.kb[0:H, h, 0:32:2], T.kb[0:H, h, 1:32:2], Op.min, k("kb"), k("kc"))
-            tt(U("kd"), T.kc[0:H, h, 0:16:2], T.kc[0:H, h, 1:16:2], Op.min, k("kc"), k("kd"))
-        halves(T.psg, T.pk, "pk0 pk1", "psg", 128, "idb")
-        KD = "kd0 kd1"
-        ts(X("t7", 0), L("kd"), 1, Op.logical_shift_right, KD, "t7", 1023, Op.bitwise_and)
-        ts(X("t7", 1), L("kd"), 6, Op.logical_shift_right, KD, "t7p", 31, Op.bitwise_and)
-        ts(X("fg", 0), X("t7", 0), 4.0, Op.add, "t7", "fga")
-        ts(X("fg", 1), X("t7", 0), 592.0, Op.add, "t7", "fgb")
-        ts(X("fh", 0), L("kd"), 1, Op.bitwise_and, KD, "fh")
-        tt(L("t5"), L("fg"), L("fg"), Op.mult, "fga fgb", "t5")
-        cp(T.fm[0:H, :, 16:32], L("t7"), "t7 t7p", "fm1")
-        ts(X("fj", 0), X("t5", 0), 0.125, Op.mult, "t5", "fja", -2.4375, Op.add)
-        ts(X("fj", 1), X("t5", 1), 0.03125, Op.mult, "t5", "fjb", -10951.484375, Op.add)
-        ts(X("fm", 1), L("kd"), RES, Op.is_ge, KD, "fm2")
-        ts(L("fe"), L("fj"), W - 1, Op.bitwise_and, "fja fjb", "fe")
-        tt(X("t6", 1), X("fe", 1), X("fe", 0), Op.subtract, "fe", "t6")
-        ts(X("t6", 0), X("fe", 0), -2048.0, Op.add, "fe", "t6b")
-        tt(X("t6", 2), X("t6", 1), X("fh", 0), Op.mult, "t6 fh", "t6c")
-        tt(X("fm", 0), X("t6", 2), X("t6", 0), Op.add, "t6c t6b", "fm0")
-        halves(T.psm, T.fm, "fm0 fm1 fm2", "psm", 32, "idh")
-        tt(T.sp[:], T.psg[:, 0:K], T.dc[:], Op.mult, "psg dc", "sp")
-        cp(T.gu[0:32, :], T.psm[0:32, 0:K], "psm", "gu")
-        op("p", [mm(T.psu[:, 0:K], C("rpc", p1=32), T.gu[0:32, :], True, True)], "rpc gu", "psu")
-        op("p", [mm(T.psg[:, 0:K], C("rpc", p1=32), T.gu[0:32, :], True, False), mm(T.psg[:, 0:K], C("idb"), C("bm"), False, True)], "rpc gu idb bm", "psg")
-        tt(T.sg[:], T.sp[:], T.cc[:, 0:K], Op.add, "sp cca0 cca1", "sg")
-        cp(T.pw[:].indirect(C("ld")), T.v2[:], "ld v2", PW)
-        ts(T.ru2[:], T.psu[:, 0:K], 2048.0, Op.add, "psu", "ru2_")
-        scan(T.scl[:], T.psg[:, 0:K], "psg", "scl")
-        tt(C("pls"), C("nrq"), T.scl[:, 15:K:16], Op.add, "nrq scl", "pls")
-        same("eqo", T.ru2, "ru2_", ("pls", 0), "pls")
-        lower("eqo", T.psd, "psd")
-        ts(C("w3"), C("pls"), float(W), Op.is_lt, "pls", "w3")
-        tt(C("w4"), C("pls"), C("dm4"), Op.subtract, "pls dm4", "w4")
-        cp(T.fw[:].indirect(C("ld")), T.sg[:], "ld sg", FW)
-        tt(C("w2"), C("w3"), C("w4"), Op.mult, "w3 w4", "w2")
-        tt(T.qs[:], T.xw[:, 0:W].indirect(C("lo")), T.q[:], Op.add, XW + " lo q", "qs")
-        cp(T.cf[:], T.fw[:, 0:W].indirect(C("lo")), FW + " lo", "cf")
-        ts(T.qb[:], T.qs[:], 0.5, Op.mult, "qs", "qb", 127.8125, Op.add)
+        cp(T.xw[:].indirect(C("ld")), T.at[:], "ld at0 at1", XW, -K)
+        cp(T.pw[:].indirect(C("ld")), T.v2[:], "ld v2", PW, -K)
+        tt(T.qs[:], T.xw[:, 0:W].indirect(LO), T.q[:], Op.add, XW + " ll0 ll1 q", "qs", K)
+        act(T.qb[:], T.qs[:], "qs", "qb", AF.Copy, scale=0.5, bias=127.8125)
+        act(T.q[:], T.qb[:], "qb", "q", AF.Copy, bias=-128.0)
         if t < RO - 1:
-            cp(T.lc[:], T.cf[:], "cf", "lc")
             for i in range(16):
-                ts(T.qrep[:, i:16 * K:16], T.qb[:], -128.0, Op.add, "qb", "qr%d" % i)
-        ts(T.q[:], T.qb[:], -128.0, Op.add, "qb", "q")
+                o = T.qrep[:, i:16 * K:16]
+                if i < QG:
+                    gop(lambda o=o: g.affine_select(o, T.q[:], [[0, K]], Op.is_ge, 0.0, 0, 0), "q", "qr%d" % i, K)
+                elif i < QG + QS:
+                    act(o, T.qb[:], "qb", "qr%d" % i, AF.Copy, bias=-128.0)
+                else:
+                    ts(o, T.qb[:], -128.0, Op.add, "qb", "qr%d" % i)
+        for h in (0, 1):
+            ts(T.nn[0:H, h, 128:384], T.psv[0:H, h, 128:384], 0.0, Op.not_equal, "psv%d" % h, "nna%d" % h)
+            ts(T.nn[0:H, h, 0:128], T.psv[0:H, h, 0:128], 0.0, Op.is_gt, "psv%d" % h, "nnb%d" % h)
+            pe([turn(T.psu, T.nn[0:H, h, 128:256], "idb", h, True, False), turn(T.psu, T.nn[0:H, h, 256:384], "idb", h, False, True)], "idb nna%d" % h, "psu")
+            pe([turn(T.psm, T.nn[0:H, h, 128:256], "id2", h, True, False), turn(T.psm, T.nn[0:H, h, 256:384], "idn", h, False, False),
+                turn(T.psm, T.nn[0:H, h, 0:128], "idb", h, False, True)], "id2 idn idb nna%d nnb%d" % (h, h), "psm")
+        act(T.nr[:], T.psu[:, 0:K], "psu", "nr", AF.Relu, bias=-1.0)
+        ts(T.psm[:, 0:K], T.psm[:, 0:K], 1.0, Op.is_gt, "psm", "psm pk")
+        tt(T.psm[:, K:2 * K], T.psm[:, 0:K], T.dc[:], Op.mult, "psm pk dc", "psm sp")
+        tt(T.sg[:], T.psm[:, K:2 * K], T.cc[:, 0, :], Op.add, "psm sp cc0 cc1", "sg")
+        pe([mm(T.psg[:, 0:K], C("tri"), T.nr[:], False, True)], "tri nr", "psg")
+        act(T.psu[:, K:2 * K], T.psg[:, 0:K], "psg psu", "psu", AF.Relu, scale=-1.0)
+        act(T.sh[:], T.sg[:], "sg", "sh", AF.Copy, bias=-2048.0)
+        act(T.fst[:], T.psg[:, 0:K], "psg", "fst", AF.Relu, scale=-1.0)
+        cp(T.fw[:].indirect(C("ld")), T.sg[:], "ld sg", FW, -K)
+        if t < RO - 1:
+            cp(T.lc[:], T.fw[:, 0:W].indirect(LO), FW + " ll0 ll1", "lc", K)
+            ts(T.c16[:], T.lc[:], -2048.0, Op.add, "lc", "c16")
+        else:
+            cp(T.cf[:], T.fw[:, 0:W].indirect(LO), FW + " ll0 ll1", "cf", K)
+        tt(T.x1[:], T.psu[:, K:2 * K], T.sh[:], Op.mult, "psu sh", "x1")
+        tt(T.x2[:], T.psu[:, K:2 * K], T.b16[:], Op.mult, "psu b16_0 b16_1", "x2")
+        place = lambda o, sp: [mm(o, C("idb"), C("bmc"), True, False), mm(o, C("bn8"), T.fst[:], False, False), mm(o, C("blh"), T.x1[:], False, sp)]
+        pe(place(T.psv[:, 1, 0:K], True), "idb bmc bn8 fst blh x1", "psv1")
+        pe([mm(T.psv[:, 0, 0:K], C("blh"), T.x1[:], True, True)], "blh x1", "psv0")
+        pe([mm(T.psv[:, 0, K:2 * K], C("blh"), T.x2[:], True, True)], "blh x2", "psv0")
+        pe(place(T.psd[:, 0:K], False), "idb bmc bn8 fst blh x1", "psd")
+        scan(T.scc[:], T.psv[:, 1, 0:K], "psv1", "scc")
+        cp16(T.rc[:], T.psv[:, 0, 0:K], "psv0", "rc")
+        act(T.hi[:], T.psv[:, 0, K:2 * K], "psv0", "hi", AF.Copy, scale=0.03125, bias=144.0 - 0.484375)
+        tt(C("lp"), T.scc[:, 15:K:16], C("dm4"), Op.min, "scc dm4", "lp")
+        same("eqo", T.rc, "rc", lambda kb: T.scc[:, 16 * kb + 15:16 * kb + 16], "scc")
+        lower("eqo", T.psd, "psd")
+        act(T.g1[:], T.pw[:].indirect(C("lp")), PW + " lp", "g1", n=K)
+        pe([mm(T.psg[:, 0:K], C("vr"), T.x2[:], True, False), mm(T.psg[:, 0:K], T.row[0:1, 384:512], T.ro2[0:1, 0:K], False, False),
+            mm(T.psg[:, 0:K], C("vh"), T.hi[:], False, False), mm(T.psg[:, 0:K], C("dgc%d" % t), T.g1[:], False, True)],
+           "vr1 vr7 x2 row20 row21 row22 row27 ro2 vh hi dgc%d g1" % t, "psg")
+        act(T.v1[:], T.psg[:, 0:K], "psg", "v1")
+        if t < RO - 1:
+            disk_window(j + 1, "g1")
         scan(T.scd[:], T.psd[:, 0:K], "psd", "scd")
-        ts(C("z", 0, 12), T.scd[:, 15:K:16], 0.0, Op.is_equal, "scd", "z0")
-        tt(C("w1"), C("w2"), C("z", 0, 12), Op.mult, "w2 z0", "w1")
-        tt(C("lcl"), C("w1"), C("dm4"), Op.add, "w1 dm4", "lcl")
-        act(T.g1[:], T.pw[:].indirect(C("lcl")), PW + " lcl", "g1")
-        op("p", [mm(T.psm[:, 0:K], C("vr", p1=32), T.gu[0:32, :], True, False),
-                 mm(T.psm[:, 0:K], T.row[0:1, 384:512], T.ro2[0:1, 0:K], False, False),
-                 mm(T.psm[:, 0:K], C("dgc%d" % t), T.g1[:], False, True)], "vr gu row2 ro2 dgc%d g1" % t, "psm")
-        act(T.v1[:], T.psm[:, 0:K], "psm", "v1")
-        cp(T.pw[:].indirect(C("lcl")), T.v1[:], "lcl v1", PW)
-        if t == 1:
-            yt_weights()
-    dma("d", T.yc[:], T.cf[:], "cf", "yc")
+        tt(C("lcl"), T.scd[:, 15:K:16], C("dm4"), Op.min, "scd dm4", "lcl")
+        cp(T.pw[:].indirect(C("lcl")), T.v1[:], "lcl v1", PW, -K)
+    apply("hm3", "lh", "x1")
     dma("d", T.yq[:], T.q[:], "q", "yq")
-    op("p", [mm(T.psv[0:64, 0, :], T.wt[:, 64 * c:64 * c + 64], T.pw[:, 512 * c:512 * c + 512], c == 0, c == 7) for c in range(8)], " ".join("wt%d" % c for c in range(8)) + " " + PW, "psv0")
-    for j in (1, 2, 3):
-        apply("hm%d" % j, "lh")
-    act(T.yts[0:64, :], T.psv[0:64, 0, :], "psv0", "yts")
-    dma("d", T.yt[:], T.yts[0:64, :], "yts", "yt")
     dma("d", T.yl[:], T.lh[:, 0:M], "lh", "yl")
+    dma("d", T.yc[:], T.cf[:], "cf", "yc")
+    dma("d", T.yt[:], T.pw[7:128:16, 0:W], PW, "yt")
     finish()

@@ -6,24 +6,22 @@ BIG = 65536.0
 RES = 67108864.0
 OUT = 8192.0
 NE = 8
-ACT16 = True
-ACTU = True
+ON_S = "fl gt msg lw pcs lh c16 lc l12".split()
 QG, QS = 5, 5
-WAKE, SLACK, LEAD, CYC, PCYC, GATH, SCAT = 0.2, 0.1, 0.15, 0.00083, 0.0006, 1.56, 3.8
+WAKE, PASSES, CYC, PCYC, GATH, SCAT = 0.2, 6, 0.00083, 0.00045, 1.56, 3.8
 
 _S = "sbuf"
 F32, B16, I32, U16, H16 = "float32", "bfloat16", "int32", "uint16", "float16"
 PACK = {
-    "tf": (F32, (("nqd", 12), ("own", 12), ("w1", 12), ("dm4", 12), ("dm1", 12), ("er", 16), ("lt", 16), ("ec", 16), ("pmf", 4))),
-    "tl": (U16, (("ld", 12), ("lcl", 12), ("lp", 12), ("lm", 12))),
+    "tf": (F32, (("w01", 8), ("nqd", 12), ("w1", 12), ("dm4", 12), ("dm1", 12), ("er", 16), ("lt", 16), ("ec", 16), ("pmf", 4))),
+    "tl": (U16, (("ld", 12), ("lcl", 12), ("lp", 12), ("lq", 12))),
     "ti": (I32, (("dmi", 12), ("pmi", 4))),
-    "tb": (B16, (("wm", 24), ("wp", 24), ("wm1", 24), ("wm2", 24), ("wp1", 24), ("wp2", 24), ("cand", 12), ("exb", 16), ("nrq", 12))),
-    "cb": (B16, (("idb", 128), ("id2", 128), ("idn", 128), ("blb", 128), ("bl8", 128), ("bn8", 128), ("btr", 128), ("tri", 128), ("dg1", 128), ("sa", 128), ("se", 128), ("vh", 128), ("wt", 128),
-                 ("dgc0", 128), ("dgc1", 128), ("dgc2", 128), ("bm", K), ("bmc", K), ("zr", K), ("ltk", 2048), ("sel", 2048), ("pb16", 128), ("nb16", 128))),
-    "cff": (F32, (("one", 512), ("idf", 128), ("blf", 128), ("btf", 128), ("tmp", 256), ("rpf", 512))),
-    "chh": (H16, (("rnp", 128), ("rop", 128), ("rop0", 128), ("rnp0", 128), ("rm", 128), ("blh", 128), ("vr", 128), ("bi", 384), ("idh", 128))),
+    "tb": (B16, (("wm", 16), ("wp", 16), ("wm1", 24), ("wm2", 24), ("wp1", 24), ("wp2", 24), ("cand", 12), ("exb", 16), ("nrq", 12))),
+    "cb": (B16, (("one", 256), ("zero", 256), ("bl", 128), ("bt", 128), ("rp", 256), ("id", 128), ("idu", 768), ("id4", 128), ("idm", 128), ("bi", 384), ("pb16", 128), ("nb16", 128),
+                 ("btr", 128), ("tri", 128), ("bl8", 128), ("bn8", 128), ("sa", 128), ("wt", 128), ("se", 128), ("dg1", 128), ("dgc", 384), ("vr", 128), ("rq", 256),
+                 ("bm", K), ("bmc", K), ("bm4", K), ("ltk", 2048), ("slt", 2048), ("row", 512))),
 }
-PLACE, SCRATCH = {}, {}
+PLACE, SCRATCH, ORDERS = {}, {}, {}
 for _b in PACK:
     _o = 0
     for _n, _w in PACK[_b][1]:
@@ -31,18 +29,20 @@ for _b in PACK:
         _o += _w
     SCRATCH[_b] = (_S, [128, _o], PACK[_b][0])
 for _d, _l in (
-    (B16, (("xw", W + K), ("pt", W), ("pcs", 768), ("xlh", M), ("q", K), ("qb", K), ("qrep", 16 * K), ("ma", 16 * K), ("mb", 16 * K), ("pa", 16 * K), ("pb", 16 * K),
-           ("at", K), ("g1", K), ("g2", K), ("nr", K), ("fst", K), ("hi", K), ("row", 512), ("ro2", 512), ("xl1", M), ("xl2", M), ("xl3", M), ("xp1", 512), ("xp2", 512), ("xp3", 512), ("xlp", 512), ("xt", 512))),
-    (I32, (("fw", W + K), ("fdt", 2048), ("tgs", 256), ("pci", 768), ("lfi", M), ("cxi", K), ("ia", K), ("ic", 256))),
-    (U16, (("lfu", M), ("lc", K), ("lu1", M), ("lu2", M), ("lu3", M))),
-    (F32, (("pw", W + K), ("lh", M + K), ("qs", K), ("cf", K), ("scd", K), ("scm", K), ("scc", K), ("dc", K), ("sg", K), ("sh", K), ("v1", K), ("v2", K), ("s0", 256), ("lw1", M), ("lw2", M + K), ("lw3", M + K),
-           ("msg1", K + 12), ("msg2", K + 12), ("msg3", K + 12), ("up1", K + 12), ("up2", K + 12), ("up3", K + 12), ("hm1", K + 12), ("hm2", K + 12), ("hm3", K + 12))),
-    (H16, (("gt", K), ("b16", K), ("c16", K), ("x1", K), ("x2", K), ("rc", K))),
+    (B16, (("xw", W + K), ("xlh", M), ("q", K), ("qb", K), ("qrep", 16 * K), ("ma", 16 * K), ("mb", 16 * K), ("at", K), ("nr", K), ("nq", K), ("fst", K),
+           ("xl1", M), ("xl2", M), ("xl3", M), ("xp1", 512), ("xp2", 512), ("xp3", 512), ("xlp", 512), ("xt", 512))),
+    (I32, (("fw", W + K), ("ci", K), ("tgs", 256), ("pci", 256), ("lfi", M), ("cxi", K), ("ic", 256))),
+    (U16, (("lfu", M), ("lc", K), ("lu1", M), ("lu2", M), ("lu3", M), ("msg1", K + 16), ("msg2", K + 16), ("msg3", K + 16), ("up1", K + 12), ("up2", K + 12), ("up3", K + 12),
+           ("hm1", K + 12), ("hm2", K + 12), ("hm3", K + 12))),
+    (F32, (("pw", W + K), ("lh", M + K), ("qs", K), ("cf", K), ("scd", K), ("scm", K), ("scc", K), ("dc", K), ("sg", K), ("sh", K), ("v1", K), ("v2", K), ("s0", 256),
+           ("lw1", M), ("lw2", M + K), ("lw3", M + K))),
+    (H16, (("pt", W), ("pcs", 512), ("pa", 16 * K), ("pb", 16 * K), ("pc", 16 * K), ("g1", K), ("g2", K), ("gt", K), ("b16", K), ("c16", K), ("x1", K), ("x2", K), ("rc", K),
+           ("ro", K), ("rt", K), ("hh", K))),
 ):
     for _n, _w in _l:
         SCRATCH[_n] = (_S, [128, _w], _d)
-for _n, _w, _d in (("sc", K, F32), ("ru", K, H16), ("ll", 12, U16), ("sq", K, F32), ("tt", K, I32), ("cc", K, I32), ("l12", K, U16),
-                   ("t4", 256, I32), ("fi", 24, I32), ("fl", 24, H16), ("sl", 128, F32), ("nn", 384, B16)):
+for _n, _w, _d in (("sc", K, F32), ("ll", 12, U16), ("sq", K, F32), ("tt", K, I32), ("cc", K, I32), ("l12", K, U16),
+                   ("t4", 256, I32), ("fi", 16, I32), ("fl", 16, H16), ("nn", 384, B16)):
     SCRATCH[_n] = (_S, [128, 2, _w], _d)
 SCRATCH["eqo"] = (_S, [128, 12, K], B16)
 SCRATCH["eqt"] = (_S, [128, 12, K], B16)
@@ -140,9 +140,9 @@ def tracker(g, T):
         R, Wt = R.split(), Wt.split()
         nodes.append((q, R, Wt, lambda: op_(q, fns, R, Wt), cost, 0.0, -1))
 
-    def dma(q, out, in_, R="", Wt="", lat=2.2):
+    def dma(q, out, in_, R, Wt, kb):
         R, Wt = R.split(), Wt.split()
-        nodes.append((q, R, Wt, lambda: dma_(q, out, in_, R, Wt), 0.1, lat, -1))
+        nodes.append((q, R, Wt, lambda: dma_(q, out, in_, R, Wt), kb / 190.0, 2.0, -1))
 
     def send(call, R, local, n):
         R = R.split()
@@ -186,52 +186,48 @@ def tracker(g, T):
             for d in dep[x]:
                 succ[d].append(x)
         cs = [nd_[4] for nd_ in nodes]
+        lat = [nd_[5] + (0.0 if nd_[0] == "a" else WAKE) for nd_ in nodes]
+        prev, nxt = [[] for _ in nodes], [[] for _ in nodes]
+        for q in "gd":
+            row = [x for x in range(nn) if nodes[x][0] == q and (q == "d" or nodes[x][6] == -2)]
+            for x, y in zip(row, row[1:]):
+                prev[y].append(x)
+                nxt[x].append(y)
+
+        def place(order, back):
+            st, busy = [0.0] * nn, {q: [] for q in "vspgd"}
+            for x in order:
+                if back:
+                    e = max([lat[x]] + [st[y] + cs[y] + lat[x] for y in succ[x]] + [st[y] + cs[y] for y in nxt[x]])
+                else:
+                    e = max([0.0] + [st[y] + cs[y] + lat[y] for y in dep[x]] + [st[y] + cs[y] for y in prev[x]])
+                q = nodes[x][0]
+                if q != "a":
+                    b = busy[q]
+                    i, hi = 0, len(b)
+                    while i < hi:
+                        m = (i + hi) // 2
+                        i, hi = (i, m) if b[m][1] > e else (m + 1, hi)
+                    while i < len(b) and b[i][0] < e + cs[x] - 1e-9:
+                        e = max(e, b[i][1])
+                        i += 1
+                    b.insert(i, (e, e + cs[x]))
+                st[x] = e
+            return st, max(st[x] + cs[x] + (0.0 if back else lat[x]) for x in range(nn))
         pr = [0.0] * nn
         for x in range(nn - 1, -1, -1):
-            pr[x] = cs[x] + nodes[x][5] + max([pr[y] + WAKE for y in succ[x]] + [0.0])
-        left = [len(d) for d in dep]
-        ready = {q: [] for q in "vspgda"}
-        fin, qt = [0.0] * nn, {q: 0.0 for q in "vspgda"}
-        early = [0.0] * nn
-        for x in range(nn):
-            if not left[x]:
-                ready[nodes[x][0]].append(x)
-        todo = {q: [x for x in range(nn) if nodes[x][0] == q and (q == "d" or nodes[x][6] == -2)] for q in "gd"}
-        for _ in range(nn):
-            best = None
-            for q in "avspgd":
-                cand = ready[q]
-                if q in "gd":
-                    cand = [x for x in cand if x not in todo[q][1:]]
-                if not cand:
-                    continue
-                st = {}
-                for x in cand:
-                    e = early[x]
-                    st[x] = e if q == "a" else (e + WAKE if e > qt[q] - 0.001 else qt[q])
-                lo = min(st.values())
-                x = max((y for y in st if st[y] <= lo + SLACK), key=lambda y: (pr[y], -y))
-                for y in sorted(st, key=lambda y: -pr[y]):
-                    if pr[y] <= pr[x]:
-                        break
-                    if max(st[y] + pr[y], st[y] + cs[y] + pr[x]) < max(st[x] + pr[x], max(st[y], st[x] + cs[x]) + pr[y]) - LEAD:
-                        x = y
-                        break
-                if best is None or st[x] < best[0]:
-                    best = (st[x], q, x)
-            t0, q, x = best
-            ready[q].remove(x)
-            if q in "gd" and x in todo[q]:
-                todo[q].pop(0)
-            e = t0 + cs[x]
-            qt[q] = e
-            fin[x] = e + nodes[x][5]
+            pr[x] = cs[x] + max([lat[x]] + [pr[y] + lat[x] for y in succ[x]] + [pr[y] for y in nxt[x]])
+        order = sorted(range(nn), key=lambda x: (-pr[x], x))
+        alike = tuple((nd_[0], tuple(nd_[1]), tuple(nd_[2])) for nd_ in nodes)
+        for _ in range(0 if alike in ORDERS else PASSES):
+            st, end = place(order, False)
+            if alike not in ORDERS or end < ORDERS[alike][0]:
+                ORDERS[alike] = (end, st)
+            bk = place(sorted(range(nn), key=lambda x: (-st[x] - cs[x], -x)), True)[0]
+            order = sorted(range(nn), key=lambda x: (-bk[x] - cs[x], x))
+        st = ORDERS[alike][1]
+        for x in sorted(range(nn), key=lambda x: (st[x], x)):
             nodes[x][3]()
-            for y in succ[x]:
-                left[y] -= 1
-                early[y] = max(early[y], fin[x])
-                if not left[y]:
-                    ready[nodes[y][0]].append(y)
         for sem in total:
             if known["g"].get(sem, 0) < total[sem]:
                 g.wait_ge(T.sem[sem], total[sem])
@@ -250,6 +246,9 @@ def rank_program(g, core, T, topo):
         bf, o, w = PLACE[n]
         return T[bf][p0:p1, o + a:o + (w if b is None else b):st]
 
+    def keys(n, count, first=0):
+        return " ".join("%s%d" % (n, i) for i in range(first, count))
+
     def wid(a):
         n = 1
         for x in list(a.shape)[1:]:
@@ -267,9 +266,9 @@ def rank_program(g, core, T, topo):
     def tt(o, a, b, f, R, Wt, n=0):
         op("v", [lambda: v.tensor_tensor(o, a, b, f)], R, Wt, ncost(n) if n else 0.03 + CYC * max(64, wid(o) * (1 if "ps" in R else 2)))
 
-    def ts(o, a, x, f, R, Wt, y=None, f2=None):
+    def ts(o, a, x, f, R, Wt, y=None, f2=None, n=0):
         if f2 is None:
-            op("v", [lambda: v.tensor_scalar(o, a, x, None, f)], R, Wt, vcost(o, a))
+            op("v", [lambda: v.tensor_scalar(o, a, x, None, f)], R, Wt, ncost(n) if n else vcost(o, a))
         else:
             op("v", [lambda: v.tensor_scalar(o, a, x, y, f, f2)], R, Wt, vcost(o, a))
 
@@ -282,11 +281,16 @@ def rank_program(g, core, T, topo):
     def act(o, a, R, Wt, f=AF.Identity, n=0, **kw):
         op("s", [lambda: s.activation(o, a, f, **kw)], R, Wt, ncost(n) if n else 0.05 + CYC * max(64, wid(o)))
 
-    def cp16(o, a, R, Wt, n=0):
-        (act if ACT16 else cp)(o, a, R, Wt, n=n)
+    def mv(name, o, a, R, Wt, scale=1.0, bias=0.0):
+        if name in ON_S:
+            act(o, a, R, Wt, AF.Copy, scale=scale, bias=bias)
+        elif scale == 1.0 and bias == 0.0:
+            cp(o, a, R, Wt)
+        else:
+            ts(o, a, scale, Op.mult, R, Wt, bias, Op.add)
 
     def mm(o, l, x, st, sp):
-        return (lambda: p.matmul(o, l, x, st, sp), PCYC * max(64, wid(x)) * (4 if "32" in str(x.dtype) else 1))
+        return (lambda: p.matmul(o, l, x, st, sp), PCYC * max(64, wid(x)))
 
     def pe(fs, R, Wt):
         op("p", [f[0] for f in fs], R, Wt, sum(f[1] for f in fs))
@@ -304,60 +308,73 @@ def rank_program(g, core, T, topo):
         eng = eng[-NE:] if bulk else eng[0:NE]
         return put(lambda: g.remote_dma(dst, src, T.sem[sem], T.sem[local], pid, rid, sum(1 << e for e in eng)), key, local, len(eng))
 
-    PW = " ".join("pw%d" % c for c in range(8)) + " pwd"
-    XW = "xw0 xw1"
-    FW = " ".join("fw%d" % c for c in range(8))
-    QR = " ".join("qr%d" % i for i in range(16))
-    dma("d", T.tgs[:], T.tg[:], "", "tgs", 2.7)
-    dma("d", T.lfi[:], T.lf[:], "", "lfi", 5.3)
-    dma("d", T.cxi[:], T.cx[:], "", "cxi", 5.7)
-    dma("d", T.q[:], T.qx[:], "", "q", 5.9)
-    dma("d", T.xw[:, 0:2048], T.xr[:, 0:2048], "", "xw0", 8.5)
-    dma("d", T.xw[:, 2048:W], T.xr[:, 2048:W], "", "xw1", 11.2)
+    PW = keys("pw", 8) + " pwd"
+    XW = keys("xw", 4)
+    FW = "fwl " + keys("fw", 4)
+    QR = keys("qr", 16)
+    dma("d", T.tgs[:], T.tg[:], "", "tgs", 128)
+    dma("d", T.lfi[:], T.lf[:], "", "lfi", 512)
+    dma("d", T.cxi[:], T.cx[:], "", "cxi", 96)
+    dma("d", T.q[:], T.qx[:], "", "q", 48)
+    ts(T.pci[:], T.tgs[:], 1, Op.bitwise_and, "tgs", "pci")
+    for j, (n, src) in enumerate((("tgs", T.tgs), ("pci", T.pci))):
+        mv("pcs", T.pcs[:, 256 * j:256 * j + 256], src[:], n, "pcs%d" % j)
+        dma("d", T.pt[8 * j:8 * j + 8, :], T.pcs[:, 256 * j:256 * j + 256], "pcs%d" % j, "pt%d" % j, 64)
+    for c in range(4):
+        dma("d", T.xw[:, 1024 * c:1024 * c + 1024], T.xr[:, 1024 * c:1024 * c + 1024], "", "xw%d" % c, 256)
+    dma("d", T.xlh[:], T.xl[:], "", "xlh", 256)
+    dma("d", T.fw[:, 0:2048], T.fd[:], "", "fwl", 1024)
     fill(C("one"), 1.0, "one")
+    fill(C("zero"), 0.0, "zero")
     gop(lambda: g.iota(C("pmi", 0, 1), [[0, 1]], 0, 1), "", "pmi", 1)
     gop(lambda: g.iota(T.ic[:], [[0, 16], [1, 16]], 0, 0), "", "ic", 256)
-    gop(lambda: g.affine_select(C("blf"), C("one", 0, 128), [[-16, 8], [0, 16]], Op.is_ge, 0.0, 0, 1), "one", "blf", 128)
-    gop(lambda: g.affine_select(C("blf"), C("blf"), [[16, 8], [0, 16]], Op.is_ge, 0.0, 15, -1), "blf", "blf", 128)
-    gop(lambda: g.affine_select(C("rpf", p1=32), C("one", p1=32), [[-8, 4], [-1, 8], [0, 16]], Op.is_equal, 0.0, 0, 1), "one", "rpf", 512)
-    gop(lambda: g.affine_select(C("idf"), C("one", 0, 128), [[-1, 128]], Op.is_equal, 0.0, 0, 1), "one", "idf", 128)
-    gop(lambda: g.affine_select(C("btf"), C("blf"), [[1, 128]], Op.is_ge, 0.0, 0, -1), "blf", "btf", 128)
+    gop(lambda: g.affine_select(C("bl"), C("one", 0, 128), [[-16, 8], [0, 16]], Op.is_ge, 0.0, 0, 1), "one", "bl", 128)
+    gop(lambda: g.affine_select(C("bl"), C("bl"), [[16, 8], [0, 16]], Op.is_ge, 0.0, 15, -1), "bl", "bl", 128)
+    gop(lambda: g.affine_select(C("rp", p1=32), C("one", p1=32), [[-8, 2], [-1, 8], [0, 16]], Op.is_equal, 0.0, 0, 1), "one", "rp", 256)
+    gop(lambda: g.affine_select(C("bt"), C("bl"), [[1, 128]], Op.is_ge, 0.0, 0, -1), "bl", "bt", 128)
     gop(lambda: g.iota(C("dmi"), [[16, 12]], 0, 0), "", "dmi", 12)
+
+    def diag(n, a, w, src="zero", key=None):
+        gop(lambda: g.affine_select(C(n, a, a + 128), C(src, 0, 128), [[-1, 128]], Op.not_equal, w, 0, 1), src, key or n, 128)
+    diag("id", 0, 1.0)
+    diag("btr", 0, -255.0, "bt")
+    diag("tri", 0, -1.0, "bt")
     E = lambda i: C("er", i, i + 1)
     D = lambda i, p1=128: C("ec", i, i + 1, p1=p1)
-    RP = lambda f, st=1: C("rpf", 128 * f, 128 * f + 128, p1=32, st=st)
-    b8 = C("blf", st=16)
-    ts(D(9), C("pmi", 0, 1), 24.0, Op.is_equal, "pmi", "ec9", 2048.0, Op.mult)
-    ts(D(10), C("pmi", 0, 1), 24.0, Op.is_equal, "pmi", "ec10", -2047.0, Op.mult)
-    ts(C("pmi", 1, 2), C("pmi", 0, 1), 15, Op.bitwise_and, "pmi", "pmj")
-    cp(C("pmf", 0, 1), C("pmi", 1, 2), "pmj", "pmf")
+    RP = lambda f, st=1: C("rp", 128 * f, 128 * f + 128, p1=32, st=st)
+    b8 = C("bl", st=16)
     PM = C("pmf", 0, 1)
+
+    def times(o, a, w, R, Wt):
+        if wid(o) < 64:
+            act(o, a, R, Wt, scale=w)
+        else:
+            ts(o, a, w, Op.mult, R, Wt)
+    ts(D(9), C("pmi", 0, 1), 24.0, Op.is_equal, "pmi", "ec9", 2048.0, Op.mult)
+    ts(C("pmi", 1, 2), C("pmi", 0, 1), 15, Op.bitwise_and, "pmi", "pmj")
+    cp(PM, C("pmi", 1, 2), "pmj", "pmf")
     ts(C("er"), T.ic[:, 0:16], PM, Op.is_equal, "ic pmf", "er")
     ts(C("lt"), T.ic[:, 0:16], PM, Op.is_gt, "ic pmf", "lt", OUT, Op.mult)
-    ts(D(0), E(0), 32.0, Op.mult, "er", "ec0", E(1), Op.add)
-    ts(D(1), E(3), 65536.0, Op.mult, "er ec0", "ec1", D(0), Op.add)
-    ts(D(2), E(3), 65536.0, Op.mult, "er", "ec2")
+    ts(D(1), E(2), -0.5, Op.mult, "er", "ec1")
+    ts(D(0), E(0), 0.5, Op.mult, "er ec1", "ec0", D(1), Op.add)
+    ts(D(2), E(1), E(3), Op.add, "er", "ec2", 32768.0, Op.mult)
+    ts(D(6), D(2), E(0), Op.add, "er ec2", "ec6")
     ts(D(3), E(3), -1.0, Op.mult, "er", "ec3")
-    fill(C("sa"), 0.0, "sa")
-    fill(C("wt", p1=32), 0.0, "wt")
-    act(C("sa", 3, 128, st=16), b8, "blf sa", "sa")
-    for j, w in enumerate((-131072.0, -131072.0, 0.0)):
-        act(C("wm", 8 * j, 8 * j + 8), b8, "blf", "wm", scale=w)
-    for j, w in enumerate((1, 2, 0)):
-        act(C("wp", 8 * j, 8 * j + 8), b8, "blf ec%d" % w, "wp", scale=D(w))
-    ts(T.pci[:, 0:256], T.tgs[:], 6, Op.logical_shift_right, "tgs", "pci0")
-    ts(T.pci[:, 256:512], T.tgs[:], 1, Op.logical_shift_right, "tgs", "pci1", 31, Op.bitwise_and)
-    ts(T.pci[:, 512:768], T.tgs[:], 1, Op.bitwise_and, "tgs", "pci2")
-    for j in range(3):
-        cp(T.pcs[:, 256 * j:256 * j + 256], T.pci[:, 256 * j:256 * j + 256], "pci%d" % j, "pcs%d" % j)
-        dma("d", T.pt[8 * j:8 * j + 8, :], T.pcs[:, 256 * j:256 * j + 256], "pcs%d" % j, "pt%d" % j, 7.5)
-        cp(C("wt", j, 128, p1=32, st=16), RP(j, 16), "rpf wt", "wt%d" % j)
-    dma("d", T.xlh[:], T.xl[:], "", "xlh", 9.0)
-    dma("d", T.fdt[:], T.fd[:], "", "fdt", 14.5)
-    ts(C("tmp", 0, 8, p1=32), RP(0, 16), 64.0, Op.mult, "rpf", "tmpa")
-    ts(C("tmp", 8, 16, p1=32), RP(1, 16), 2.0, Op.mult, "rpf", "tmpb")
-    tt(C("tmp", 16, 24, p1=32), C("tmp", 0, 8, p1=32), C("tmp", 8, 16, p1=32), Op.add, "tmpa tmpb", "tmpc")
-    tt(C("wt", 7, 128, p1=32, st=16), C("tmp", 16, 24, p1=32), RP(2, 16), Op.add, "tmpc rpf wt", "wt7")
+    ts(D(4), E(2), -1.0, Op.mult, "er", "ec4")
+    ts(D(5), PM, 4.0, Op.is_ge, "pmf", "ec5")
+    ts(D(7), D(5), E(3), Op.add, "ec5 er", "ec7", E(1), Op.add)
+    ts(D(8), D(0), 2.0, Op.mult, "ec0", "ec8")
+    for n in ("sa", "wt", "vr", "slt", "row"):
+        fill(C(n), 0.0, n)
+    for j in (0, 1):
+        times(C("sa", 1 + 2 * j, 128, st=16), b8, 1.0, "bl sa", "sa%d" % j)
+        times(C("wt", 2 * j, 128, p1=32, st=16), RP(j, 16), 1.0, "rp wt", "wt%d" % j)
+        times(C("wm", 8 * j, 8 * j + 8), b8, -131072.0, "bl", "wm%d" % j)
+        times(C("wp", 8 * j, 8 * j + 8), b8, D((6, 2)[j]), "bl ec2 ec6", "wp%d" % j)
+        ts(C("row", 128 * j, 128 * j + 128, p1=1), T.ic[0:1, 0:128], 4096.0, Op.mult, "ic row", "rowa%d" % j, 2048.0 * j, Op.add)
+        ts(C("rq", 128 * j, 128 * j + 128, p1=32), RP(j), D(9, 32), Op.add, "rp ec9", "rq%d" % j)
+        ts(C("row", 128 * j, 128 * j + 128, 64, 65), C("one", 0, 128, 64, 65), (-OUT, OUT)[j], Op.mult, "one row", "rowu%d" % j)
+        cp(C("row", 384 + 2 * j, 512, p1=1, st=16), C("one", 0, 8, p1=1), "one row", "rowc%d" % j)
     fill(T.pw[:, W:W + K], 0.0, "pwd")
     cp(T.lc[:], T.cxi[:], "cxi", "lc")
     ts(T.c16[:], T.cxi[:], -2048.0, Op.add, "cxi", "c16")
@@ -366,132 +383,94 @@ def rank_program(g, core, T, topo):
             act(T.qrep[:, i:16 * K:16], T.q[:], "q", "qr%d" % i)
         else:
             cp(T.qrep[:, i:16 * K:16], T.q[:], "q", "qr%d" % i)
-    banks = (("psk0", T.psk[:, 0, :]), ("psk1", T.psk[:, 1, :]), ("psv0", T.psv[:, 0, :]), ("psv1", T.psv[:, 1, :]), ("psm", T.psm[:]), ("psu", T.psu[:]), ("psd", T.psd[:]), ("psg", T.psg[:]))
+    ts(T.s0[:], T.ic[:], 0.0, Op.is_equal, "ic", "s0", RES, Op.mult)
+    ts(C("bm"), T.ic[:, 0:K], PM, Op.not_equal, "ic pmf", "bm", BIG, Op.mult)
+    ts(C("bmc"), C("bm"), OUT + 2048.0, Op.add, "bm", "bmc")
+    ts(C("bm4"), C("bm"), -4096.0, Op.add, "bm", "bm4")
+    cp(T.gt[0:32, :], C("one", 0, K, p1=32), "one", "gt0 gt1")
+    cp(C("w01"), T.ic[:, 0:8], "ic", "w01")
+    for j, w in enumerate((0.0, -1.0, -1.0)):
+        times(C("bi", 128 * j, 128 * j + 128), C("id"), w, "id", "bi%d" % j)
+    for nm, cols in (("wm1", (2.0, 0.0, 0.0)), ("wm2", (-2.0, 0.0, 0.0)), ("wp1", (D(3), D(0), 0.0)), ("wp2", (E(3), 0.0, D(0)))):
+        for j, w in enumerate(cols):
+            times(C(nm, 8 * j, 8 * j + 8), b8, w, "bl er ec0 ec3", "%s_%d" % (nm, j))
+    for n, w in (("pb16", 16.0), ("nb16", -16.0), ("id4", 4.0), ("idm", -0.5)):
+        times(C(n), C("id"), w, "id", n)
+    for j, w in enumerate((2.0, -1.0, 0.5, -2.0, 1.0, -0.5)):
+        times(C("idu", 128 * j, 128 * j + 128), C("id"), w * OUT, "id", "idu%d" % j)
+    times(C("bl8"), C("bl"), OUT, "bl", "bl8")
+    times(C("bn8"), C("bl"), -OUT, "bl", "bn8")
+    times(C("se"), C("bl"), D(4), "bl ec4", "se")
+    for k in range(16):
+        if k:
+            times(C("ltk", 128 * k, 128 * k + 128), C("bl"), C("lt", k, k + 1), "bl lt", "ltk%d" % k)
+        times(C("slt", 128 * k + k, 128 * k + 128, st=16), b8, D(0), "bl ec0 slt", "slt%d" % k)
+    ts(C("dm4"), C("dmi"), PM, Op.add, "dmi pmf", "dm4", float(W), Op.add)
+    ts(C("dm1"), C("dmi"), PM, Op.add, "dmi pmf", "dm1", float(M), Op.add)
+    fill(C("exb"), 0.0, "exb")
+    times(C("dg1"), C("id"), D(5), "id ec5", "dg1")
+    times(C("dg1", 0, 128, st=16), b8, D(8), "bl ec8 dg1", "dg1")
+    times(C("vr", 0, 128, st=16), b8, 2.0, "bl vr", "vr")
+    for t in range(RO):
+        ts(C("row", 128 * t, 128 * t + 128, 96, 97), T.ic[96:97, 0:128], 4.0 + t, Op.is_equal, "ic row", "rowm%d" % t)
+        ts(D(12 + t), E(4 + t), -1.0, Op.mult, "er", "ec%d" % (12 + t))
+        times(C("dgc", 128 * t, 128 * t + 128), C("id"), D(7), "id ec7", "dgc%d" % t)
+        for j in (0, 2):
+            times(C("dgc", 128 * t + j, 128 * t + 128, st=16), b8, D(12 + t), "bl ec%d dgc%d" % (12 + t, t), "dgc%d%d" % (t, j))
+    banks = (("psv0", T.psv[:, 0, :]), ("psv1", T.psv[:, 1, :]), ("psm", T.psm[:]), ("psu", T.psu[:]), ("psd", T.psd[:]), ("psg", T.psg[:]))
     for c in range(8):
-        bk, ap = banks[c]
-        pe([mm(ap, C("sa"), T.xw[:, 512 * c:512 * c + 512], True, False), mm(ap, C("wt", p1=24), T.pt[0:24, 512 * c:512 * c + 512], False, True)],
-           "sa wt0 wt1 wt2 wt7 pt0 pt1 pt2 xw%d" % (c // 4), bk)
+        bk, ap = banks[c % 6]
+        pe([mm(ap, C("wt", p1=16), T.pt[0:16, 512 * c:512 * c + 512], True, False), mm(ap, C("sa"), T.xw[:, 512 * c:512 * c + 512], False, True)],
+           "sa0 sa1 wt0 wt1 pt0 pt1 xw%d" % (c // 2), bk)
         if c % 2:
             cp(T.pw[:, 512 * c:512 * c + 512], ap, bk, "pw%d" % c)
         else:
             act(T.pw[:, 512 * c:512 * c + 512], ap, bk, "pw%d" % c)
 
-    def weights():
-        fill(T.row[:], 0.0, "row")
-        ts(T.row[0:1, 0:128], T.ic[0:1, 0:128], 4096.0, Op.mult, "ic row", "rowa")
-        ts(T.row[0:1, 128:256], T.ic[0:1, 0:128], 4096.0, Op.mult, "ic row", "rowb", 2048.0, Op.add)
-        fill(T.ro2[:], 1.0, "ro2")
-        cp(C("idh"), C("idf"), "idf", "idh")
-        ts(T.s0[:], T.ic[:], 0.0, Op.is_equal, "ic", "s0", RES, Op.mult)
-        ts(C("bm"), T.ic[:, 0:K], PM, Op.not_equal, "ic pmf", "bm", BIG, Op.mult)
-        cp(T.gt[0:32, :], C("one", 0, K, p1=32), "one", "gt0 gt1")
-        ts(C("rnp", p1=32), RP(0), D(9, 32), Op.add, "rpf ec9", "rnp")
-        ts(C("rop", p1=32), RP(1), D(9, 32), Op.add, "rpf ec9", "rop")
-        cp(C("rnp0", p1=32), RP(0), "rpf", "rnp0")
-        cp(C("rop0", p1=32), RP(1), "rpf", "rop0")
-        act(C("idb"), C("idf"), "idf", "idb")
-        ts(C("bi", 0, 128), C("idf"), 0.0, Op.mult, "idf", "bia")
-        ts(C("bi", 128, 256), C("idf"), -1.0, Op.mult, "idf", "bib")
-        ts(C("bi", 256, 384), C("idf"), -1.0, Op.mult, "idf", "bic")
-        for nm, cols in (("wm1", (2.0, 0.0, 0.0)), ("wm2", (-2.0, 0.0, 0.0)), ("wp1", (D(3), D(0), 0.0)), ("wp2", (E(3), 0.0, D(0)))):
-            for j, w in enumerate(cols):
-                act(C(nm, 8 * j, 8 * j + 8), b8, "blf er ec0 ec3", nm, scale=w)
+    mv("lfu", T.lfu[:], T.lfi[:], "lfi", "lfu")
+    chip = lambda x: topo.chip(T.cores[x % N])
 
-    def later():
-        act(C("blb"), C("blf"), "blf", "blb")
-        act(C("bl8"), C("blf"), "blf", "bl8", scale=OUT)
-        act(C("bn8"), C("blf"), "blf", "bn8", scale=-OUT)
-        act(C("id2"), C("idf"), "idf", "id2", scale=2.0)
-        act(C("idn"), C("idf"), "idf", "idn", scale=-1.0)
-        for k in range(1, 16):
-            act(C("ltk", 128 * k, 128 * k + 128), C("blf"), "blf lt", "ltk", scale=C("lt", k, k + 1))
-        for k in range(16):
-            act(C("sel", 128 * k, 128 * k + 128), C("blf"), "blf er", "sel", scale=E(k))
-        ts(D(4), E(2), -1.0, Op.mult, "er", "ec4")
-        act(C("se"), C("blf"), "blf ec4", "se", scale=D(4))
-        act(C("bmc"), C("bm"), "bm", "bmc", AF.Copy, bias=OUT + 2048.0)
-        act(C("zr"), C("bm"), "bm", "zr", scale=0.0)
-        for nm, w in (("btr", -256.0), ("tri", -2.0)):
-            act(C("tmp", 128, 256), C("idf"), "idf", "tmpd", scale=w)
-            tt(C(nm), C("tmp", 128, 256), C("btf"), Op.add, "tmpd btf", nm)
-        ts(C("tmp", 0, 128, p1=32), RP(2), -2.0, Op.mult, "rpf ec10 tmpa tmpb tmpc", "tmpa tmpb tmpc", D(10, 32), Op.add)
-        tt(C("rm", p1=32), C("tmp", 0, 128, p1=32), RP(0), Op.add, "tmpa rpf", "rm")
-        cp16(C("blh"), C("blf"), "blf", "blh")
-        ts(C("dm4"), C("dmi"), PM, Op.add, "dmi pmf", "dm4", float(W), Op.add)
-        ts(C("dm1"), C("dmi"), PM, Op.add, "dmi pmf", "dm1", float(M), Op.add)
-        fill(C("exb"), 0.0, "exb")
-        for t in range(RO):
-            ts(T.row[96:97, 128 * t:128 * t + 128], T.ic[96:97, 0:128], 4.0 + t, Op.is_equal, "ic row", "row3%d" % t)
-        for j, w in ((0, -144.0), (1, 4608.0), (2, 1.0), (7, 1.0)):
-            ts(T.row[0:1, 384 + j:512:16], T.ic[0:1, 0:8], 0.0, Op.mult, "ic row", "row2%d" % j, w, Op.add)
-        ts(D(5), PM, 4.0, Op.is_ge, "pmf", "ec5")
-        ts(D(6), D(5), E(0), Op.add, "ec5 er", "ec6", E(1), Op.add)
-        ts(D(7), D(5), E(3), Op.add, "ec5 er", "ec7")
-        ts(D(8), D(0), 2.0, Op.mult, "ec0", "ec8")
-        ts(D(11), E(1), -32.0, Op.mult, "er", "ec11", E(0), Op.add)
-        act(C("dg1"), C("idf"), "idf ec6", "dg1", scale=D(6))
-        act(C("dg1", 7, 128, st=16), b8, "blf ec8 dg1", "dg1", scale=D(8))
-        act(C("vh"), C("idf"), "idf ec11", "vh", scale=D(11))
-        for t in range(RO):
-            ts(D(12 + t), E(4 + t), -1.0, Op.mult, "er", "ec%d" % (12 + t))
-            act(C("dgc%d" % t), C("idf"), "idf ec7", "dgc%d" % t, scale=D(7))
-            for j in (2, 7):
-                act(C("dgc%d" % t, j, 128, st=16), b8, "blf ec%d dgc%d" % (12 + t, t), "dgc%d" % t, scale=D(12 + t))
-        ts(C("vr"), C("blf"), 0.0, Op.mult, "blf", "vr")
-        ts(C("vr", 1, 128, st=16), b8, 1.0, Op.mult, "blf vr", "vr1")
-        ts(C("vr", 7, 128, st=16), b8, 2.0, Op.mult, "blf vr", "vr7")
+    def handed(src, j):
+        return j > 1 and chip(src - j) == chip(src - j + 1) != chip(src)
+    pe([mm(T.psd[:], C("id"), T.xlh[:, 0:512], True, False), mm(T.psd[:], C("pb16"), T.xlh[:, 512:M], False, True)], "id pb16 xlh", "psd")
+    act(T.xlp[:], T.psd[:], "psd", "xlp")
+    sent = []
+    for j in (1, 2, 3):
+        if not handed(r, j):
+            sent.append(send(T.lfu[:], "lfu", r - j, T["lu%d" % j][:], "rl%d" % j, "ls%d" % (2 * j - 2), True))
+            sent.append(send(T.xlp[:], "xlp", r - j, T["xp%d" % j][:], "rx%d" % j, "ls%d" % (2 * j - 1), True))
+        arrives("rl%d" % j, NE, "lu%d" % j, (9.0, 26.0, 40.0)[j - 1], sent[0])
+        arrives("rx%d" % j, NE, "xp%d" % j, (8.0, 24.0, 40.0)[j - 1], sent[1])
+    for i in (1, 2):
+        if handed(r + i, i + 1):
+            send(T["lu%d" % i][:], "lu%d" % i, r - 1, T["lu%d" % (i + 1)][:], "rl%d" % (i + 1), "ls%d" % (10 + 2 * i), True)
+            send(T["xp%d" % i][:], "xp%d" % i, r - 1, T["xp%d" % (i + 1)][:], "rx%d" % (i + 1), "ls%d" % (11 + 2 * i), True)
+    for c in range(4):
+        a, b = 512 * c, 512 * c + 512
+        ts(T.fw[:, 2048 + a:2048 + b], T.fw[:, a:b], 12, Op.logical_shift_right, "fwl", "fw%d" % c)
+    mv("lh", T.lh[:, 0:M], T.lfi[:], "lfi", "lh")
 
-    def disks_out():
-        cp(T.lfu[:], T.lfi[:], "lfi", "lfu")
-        chip = lambda x: topo.chip(T.cores[x % N])
-
-        def handed(src, j):
-            return j > 1 and chip(src - j) == chip(src - j + 1) != chip(src)
-        act(C("pb16"), C("idf"), "idf", "pb16", scale=16.0)
-        act(C("nb16"), C("idf"), "idf", "nb16", scale=-16.0)
-        pe([mm(T.psg[:], C("idb"), T.xlh[:, 0:512], True, False), mm(T.psg[:], C("pb16"), T.xlh[:, 512:M], False, True)], "idb pb16 xlh", "psg")
-        act(T.xlp[:], T.psg[:], "psg", "xlp")
-        sent = []
-        for j in (1, 2, 3):
-            if not handed(r, j):
-                sent.append(send(T.lfu[:], "lfu", r - j, T["lu%d" % j][:], "rl%d" % j, "ls%d" % (2 * j - 2), True))
-                sent.append(send(T.xlp[:], "xlp", r - j, T["xp%d" % j][:], "rx%d" % j, "ls%d" % (2 * j - 1), True))
-            arrives("rl%d" % j, NE, "lu%d" % j, (9.0, 20.0, 26.0)[j - 1], sent[0])
-            arrives("rx%d" % j, NE, "xp%d" % j, (6.0, 15.0, 21.0)[j - 1], sent[1])
-        for i in (1, 2):
-            if handed(r + i, i + 1):
-                send(T["lu%d" % i][:], "lu%d" % i, r - 1, T["lu%d" % (i + 1)][:], "rl%d" % (i + 1), "ls%d" % (10 + 2 * i), True)
-                send(T["xp%d" % i][:], "xp%d" % i, r - 1, T["xp%d" % (i + 1)][:], "rx%d" % (i + 1), "ls%d" % (11 + 2 * i), True)
-
-    def features(j, ps, pk, after):
+    def features(j, after):
         x, xl = T["xp%d" % j], T["xl%d" % j]
         act(T.xt[:], x[:], "xp%d %s" % (j, after), "xt", AF.Copy, scale=0.0625, bias=144.0 - 0.46875)
         act(xl[:, 512:M], T.xt[:], "xt", "xh%d" % j, AF.Copy, bias=-144.0)
-        pe([mm(ps, C("idb"), x[:], True, False), mm(ps, C("nb16"), xl[:, 512:M], False, True)], "idb nb16 xp%d xh%d" % (j, j), pk)
-        act(xl[:, 0:512], ps, pk, "xl%d" % j)
+        pe([mm(T.psg[:], C("id"), x[:], True, False), mm(T.psg[:], C("nb16"), xl[:, 512:M], False, True)], "id nb16 xp%d xh%d" % (j, j), "psg")
+        act(xl[:, 0:512], T.psg[:], "psg", "xl%d" % j)
 
     def disk_window(j, after):
-        (act if ACTU else cp)(T["lw%d" % j][:, 0:M], T["lu%d" % j][:], "lu%d %s" % (j, after), "lw%d" % j)
+        mv("lw", T["lw%d" % j][:, 0:M], T["lu%d" % j][:], "lu%d %s" % (j, after), "lw%d" % j)
 
-    def unpack():
-        for c in range(4):
-            a, b = 512 * c, 512 * c + 512
-            ts(T.fw[:, a:b], T.fdt[:, a:b], W - 1, Op.bitwise_and, "fdt", "fw%d" % c)
-            ts(T.fw[:, 2048 + a:2048 + b], T.fdt[:, a:b], 12, Op.logical_shift_right, "fdt", "fw%d" % (4 + c))
+    def apply(buf, win, after):
+        cp(T[win][:].indirect(T[buf][:, K:K + 12]), T[buf][:, 0:K], buf + " " + after, win, -K)
 
-    def apply(buf, win, after=""):
-        cp(C("lm"), T[buf][:, K:K + 12], buf + " " + after, "lm")
-        cp(T[win][:].indirect(C("lm")), T[buf][:, 0:K], buf + " lm", win, -K)
-
-    def same(eq, src, sk, own, lk):
+    def same(eq, src, sk, own, lk, less=2048.0):
         for kb in range(12):
-            ts(T[eq][:, kb, 0:K - 16 * kb], src[:, 16 * kb:K], 2048.0, Op.add, sk + " " + lk, eq + str(kb), own(kb), Op.is_equal)
+            ts(T[eq][:, kb, 0:K - 16 * kb], src[:, 16 * kb:K], less, Op.add, sk + " " + lk, eq + str(kb), own(kb), Op.is_equal)
 
     def lower(eq, ps, pk):
         for kb in range(11):
             pe([mm(ps[:, 16 * kb + 16:K], C("bl8"), T[eq][:, kb, 16:K - 16 * kb], False, False)], "bl8 %s%d" % (eq, kb), pk)
-        pe([mm(ps[:, k:K:16], C("ltk", 128 * k, 128 * k + 128), T[eq][:, :, k], False, k == 15) for k in range(1, 16)],
-           "ltk " + " ".join("%s%d" % (eq, kb) for kb in range(12)), pk)
+        pe([mm(ps[:, k:K:16], C("ltk", 128 * k, 128 * k + 128), T[eq][:, :, k], False, k == 15) for k in range(1, 16)], keys("ltk", 16, 1) + " " + keys(eq, 12), pk)
 
     def xgather(dst, lst, lk, h):
         a, b = H * h, H * h + H
@@ -500,112 +479,104 @@ def rank_program(g, core, T, topo):
     def pgather(dst, lst, lk, h):
         act(T[dst][:, 16 * H * h:16 * H * (h + 1)], T.pw[:].indirect(lst[:, H * h:H * h + H]), PW + " " + lk, dst + str(h), n=16 * H)
 
-    def sums(ps, src, w, h, last=False):
-        pe([mm(T[ps][0:H, h, i:384:16], T[src][:, 16 * H * h + i:16 * H * (h + 1):16], C(w), False, last and i == 15) for i in range(16)],
-           "%s%d %s" % (src, h, w), "%s%d" % (ps, h))
-
-    def turn(o, l, w, h, st, sp):
-        return mm(o[:, H * h:H * h + H], l, C(w, 0, H, p1=H), st, sp)
+    def sums(ps, src, w, wk, h, n, last=False):
+        pe([mm(T[ps][0:H, h, i:n:16], T[src][:, 16 * H * h + i:16 * H * (h + 1):16], C(w), False, last and i == 15) for i in range(16)],
+           "%s%d %s" % (src, h, wk), "%s%d" % (ps, h))
 
     LO = T.ll[:, 1, :]
-    GT = T.gt[0:32, :]
-    R32 = lambda n: C(n, p1=32)
+    ID = C("id", 0, H, p1=H)
+    own = lambda f: (lambda kb: T.sc[:, kb // 6, H * f + 16 * (kb % 6) + 15:H * f + 16 * (kb % 6) + 16])
     for t in range(RO):
         j = t + 1
         lw, xl, msg = "lw%d" % j, "xl%d" % j, "msg%d" % j
-        if t == 0:
-            weights()
-            disks_out()
-            later()
-            unpack()
-            cp(T.lh[:, 0:M], T.lfi[:], "lfi", "lh")
         lnw = T[lw][:, 0:M]
         for h in (0, 1):
-            pgather("pa", T.lc[:], "lc", h)
+            pgather("pc", T.lc[:], "lc", h)
             xgather("ma", T.lc[:], "lc", h)
         if t == 0:
-            disk_window(1, "pa1")
+            disk_window(1, "pc1")
         else:
             if t == 2:
                 apply("up2", lw, "lc")
             apply(("up1", "up3")[t - 1], lw, "ma1")
-        features(j, T.psg[:], "psg", "pa1")
+        features(j, "pc1")
         for h in (0, 1):
             a, b, x, y = H * h, H * h + H, 6 * h, 6 * h + 6
             k = lambda names: " ".join("%s%d" % (n, h) for n in names.split())
-            pe([mm(T.psk[0:H, h, 0:384], T.ro2[0:1, 0:H], T.row[0:1, 0:384], True, False)], "ro2 rowa rowb", k("psk"))
-            sums("psk", "ma", "wm", h)
-            sums("psk", "pa", "wp", h)
-            pe([mm(T.psk[0:H, h, 128:256], T.c16[:, a:b], C("idh"), False, True)], "c16 idh", k("psk"))
+            pe([mm(T.psk[0:H, h, 0:256], C("one", 0, H, p1=1), C("row", 0, 256, p1=1), True, False)], "one rowa0 rowa1", k("psk"))
+            sums("psk", "ma", "wm", "wm0 wm1", h, 256)
+            sums("psk", "pc", "wp", "wp0 wp1", h, 256)
+            pe([mm(T.psk[0:H, h, 128:256], T.c16[:, a:b], C("id"), False, True)], "c16 id", k("psk"))
             scan(T.t4[0:H, h, :], T.psk[0:H, h, 0:256], k("psk"), k("t4_"), 256, H)
-            act(T.sl[0:H, h, :], T.psk[0:H, h, 256:384], k("psk"), k("sl"))
-            ts(T.fi[0:H, h, 0:16], T.t4[0:H, h, 15:256:16], W - 1, Op.bitwise_and, k("t4_"), k("fia"))
-            ts(T.fi[0:H, h, 16:24], T.t4[0:H, h, 15:128:16], 1, Op.bitwise_and, k("t4_"), k("fib"))
-            ts(T.fl[0:H, h, :], T.fi[0:H, h, :], -2048.0, Op.add, k("fia fib"), k("fl"))
-            pe([mm(T.psk[0:24, h, 384:480], T.fl[0:H, h, :], C("idh", 0, H, p1=H), True, True)], k("fl") + " idh", k("psk"))
-            cp(T.gt[0:24, a:b], T.psk[0:24, h, 384:480], k("psk"), k("gt"))
+            ts(T.fi[0:H, h, :], T.t4[0:H, h, 15:256:16], W - 1, Op.bitwise_and, k("t4_"), k("fi"))
+            mv("fl", T.fl[0:H, h, :], T.fi[0:H, h, :], k("fi"), k("fl"), bias=-2048.0)
+            pe([mm(T.psk[0:16, h, 256:352], T.fl[0:H, h, :], ID, True, True)], k("fl") + " id", k("psk"))
+            mv("gt", T.gt[0:16, a:b], T.psk[0:16, h, 256:352], k("psk"), k("gt"))
             pb, pk = ((T.psm, "psm"), (T.psu, "psu"))[h]
             fs = []
-            for f, n in enumerate(("rnp", "rop")):
-                fs += [mm(pb[:, H * f:H * f + H], R32(n), T.gt[0:32, a:b], True, False), mm(pb[:, H * f:H * f + H], C("idb"), C("bm", 0, H), False, True)]
-            fs += [mm(pb[:, H * f + K:H * f + K + H], R32(n), T.gt[0:32, a:b], True, True) for f, n in enumerate(("rnp0", "rop0"))]
-            pe(fs, "rnp rop rnp0 rop0 idb bm " + k("gt"), pk)
+            for f in (0, 1):
+                fs += [mm(pb[:, H * f:H * f + H], C("rq", 128 * f, 128 * f + 128, p1=32), T.gt[0:32, a:b], True, False), mm(pb[:, H * f:H * f + H], C("id"), C("bm", 0, H), False, True)]
+            fs += [mm(pb[:, H * f + K:H * f + K + H], RP(f), T.gt[0:32, a:b], True, True) for f in (0, 1)]
+            pe(fs, "rq0 rq1 rp id bm " + k("gt"), pk)
             scan(T.sc[:, h, :], pb[:, 0:K], pk, k("sc"))
-            cp(T.ll[:, :, x:y], T.sc[:, h, 15:K:16], k("sc"), k("ll"))
-            cp16(T.ru[:, :, a:b], pb[:, K:2 * K], pk, k("ru"))
+            mv("ll", T.ll[:, 0, x:y], T.sc[:, h, 15:H:16], k("sc"), k("ln"), 0.5, -0.25)
+            mv("ll", T.ll[:, 1, x:y], T.sc[:, h, H + 15:K:16], k("sc"), k("lo"))
+            act(T.ro[:, a:b], pb[:, K + H:2 * K], pk, k("ro"))
+            act(T.rt[:, a:b], pb[:, K:K + H], pk, k("rt"), AF.Copy, bias=2045.0)
+            act(T.hh[:, a:b], pb[:, K:K + H], pk, k("hh"), AF.Copy, scale=0.25, bias=1535.625)
             LN = T.ll[:, 0, x:y]
-            act(T.sq[:, 0, a:b], lnw.indirect(LN), lw + " " + k("ll"), k("sqa"), AF.Square, H, scale=2.0, bias=8.0)
-            act(T.sq[:, 1, a:b], lnw.indirect(LN), lw + " " + k("ll"), k("sqb"), AF.Square, H, bias=592.0)
-            cp16(T.b16[:, a:b], lnw.indirect(LN), lw + " " + k("ll"), k("b16_"), H)
+            act(T.sq[:, 0, a:b], lnw.indirect(LN), lw + " " + k("ln"), k("sqa"), AF.Square, H, scale=2.0, bias=8.0)
+            act(T.sq[:, 1, a:b], lnw.indirect(LN), lw + " " + k("ln"), k("sqb"), AF.Square, H, bias=592.0)
+            act(T.b16[:, a:b], lnw.indirect(LN), lw + " " + k("ln"), k("b16_"), n=H)
             for c, of in enumerate((-2.484375, -10951.484375)):
-                ts(T.tt[:, c, a:b], T.sq[:, c, a:b], 0.03125, Op.mult, k("sq" + "ab"[c]), k("tt" + "ab"[c]), of, Op.add)
+                mv("tt", T.tt[:, c, a:b], T.sq[:, c, a:b], k("sq" + "ab"[c]), k("tt" + "ab"[c]), 0.03125, of)
             ts(T.cc[:, :, a:b], T.tt[:, :, a:b], W - 1, Op.bitwise_and, k("tta ttb"), k("cc"))
-            cp(T.l12[:, :, a:b], T.cc[:, :, a:b], k("cc"), k("li"))
-            pe([mm(T.psv[0:H, h, 0:384], T.b16[:, a:b], C("bi"), True, False)], "bia bib bic " + k("b16_"), k("psv"))
+            mv("l12", T.l12[:, :, a:b], T.cc[:, :, a:b], k("cc"), k("li"))
+            pe([mm(T.psv[0:H, h, 0:384], T.b16[:, a:b], C("bi"), True, False)], "bi0 bi1 bi2 " + k("b16_"), k("psv"))
         for h in (0, 1):
             for c in (0, 1):
                 pgather("p" + "ab"[c], T.l12[:, c, :], "li%d" % h, h)
                 xgather("m" + "ab"[c], T.l12[:, c, :], "li%d" % h, h)
-                sums("psv", "m" + "ab"[c], "wm%d" % (c + 1), h)
-                sums("psv", "p" + "ab"[c], "wp%d" % (c + 1), h, c == 1)
-        act(T.at[:], T[xl][:].indirect(T.ll[:, 0, :]), xl + " xh%d ll0 ll1" % j, "at0 at1", n=K)
-        act(T.g2[:], T.pw[:].indirect(LO), PW + " ll0 ll1", "g2", n=K)
-        same("eqo", T.ru[:, 1, :], "ru0 ru1", lambda kb: T.sc[:, kb // 6, H + 16 * (kb % 6) + 15:H + 16 * (kb % 6) + 16], "sc0 sc1")
-        pe([mm(T.psd[:, 0:K], C("idb"), C("bm"), True, False), mm(T.psd[:, 0:K], C("se"), T.g2[:], False, False)], "idb bm se g2", "psd")
+                sums("psv", "m" + "ab"[c], "wm%d" % (c + 1), keys("wm%d_" % (c + 1), 3), h, 384)
+                sums("psv", "p" + "ab"[c], "wp%d" % (c + 1), keys("wp%d_" % (c + 1), 3), h, 384, c == 1)
+        act(T.at[:], T[xl][:].indirect(T.ll[:, 0, :]), xl + " xh%d ln0 ln1" % j, "at", n=K)
+        act(T.g2[:], T.pw[:].indirect(LO), PW + " lo0 lo1", "g2", n=K)
+        same("eqo", T.ro, "ro0 ro1", own(1), "sc0 sc1")
+        pe([mm(T.psd[:, 0:K], C("id"), C("bm"), True, False), mm(T.psd[:, 0:K], C("se"), T.g2[:], False, False)], "id bm se g2", "psd")
         lower("eqo", T.psd, "psd")
         scan(T.scd[:], T.psd[:, 0:K], "psd", "scd")
         ts(C("cand"), T.scd[:, 15:K:16], -1.0, Op.is_equal, "scd", "cand")
         op("v", [lambda: v.tensor_tensor_scan(C("exb", 1, 13), C("one", 0, 12), C("cand"), 0.0, Op.mult, Op.add)], "one cand", "exb", 0.09)
-        pe([mm(T.psd[:, 400:412], C("btr"), C("cand"), True, False), mm(T.psd[:, 400:412], C("blb"), C("exb", 0, 12), False, True)], "btr cand blb exb", "psd")
+        pe([mm(T.psd[:, 400:412], C("btr"), C("cand"), True, False), mm(T.psd[:, 400:412], C("bl"), C("exb", 0, 12), False, True)], "btr cand bl exb", "psd")
         ts(C("nrq"), T.psd[:, 400:412], CAP - 256.0, Op.is_gt, "psd", "nrq")
+        ts(C("lq"), T.psd[:, 400:412], CAP - 256.0, Op.is_gt, "psd", "lq")
         tt(C("nqd"), C("nrq"), C("dm4"), Op.mult, "nrq dm4", "nqd")
         tt(C("ld"), C("nqd"), T.sc[:, :, H + 15:K:16], Op.max, "nqd sc0 sc1", "ld")
-        pe([mm(T.psg[:, 0:K], C("idb"), C("zr"), True, False)] + [mm(T.psg[:, k:K:16], C("sel", 128 * k, 128 * k + 128), C("nrq"), False, False) for k in range(16)], "idb zr sel nrq", "psg")
-        tt(T.dc[:], T.cc[:, 1, :], T.cc[:, 0, :], Op.subtract, "cc0 cc1", "dc")
-        pe([turn(T.psk[:, 1, :], T.sl[0:H, h, :], "idf", h, True, True) for h in (0, 1)], "sl0 sl1 idf", "psk1")
-        act(T[msg][:, 0:K], T.psk[:, 1, 0:K], "psk1", msg)
-        tt(C("own"), C("nqd"), T.sc[:, :, 15:H:16], Op.max, "nqd sc0 sc1", "own")
-        same("eqt", T.ru[:, 0, :], "ru0 ru1", lambda kb: C("own", kb, kb + 1), "own")
-        pe([mm(T.psd[:, 0:K], C("idb"), C("bm"), True, False), mm(T.psd[:, 0:K], R32("rm"), GT, False, False)], "idb bm rm gt0 gt1", "psd")
-        lower("eqt", T.psd, "psd")
-        scan(T.scm[:], T.psd[:, 0:K], "psd", "scm")
+        act(T.nq[:], C("w01").indirect(C("lq")), "w01 lq", "nq", n=K)
+        pe([mm(T.psk[:, 1, 0:K], C("slt", 128 * i, 128 * i + 128), T.pc[:, i:16 * K:16], i == 0, i == 15) for i in range(16)], keys("slt", 16) + " pc0 pc1", "psk1")
+        mv("msg", T[msg][:, 0:K], T.psk[:, 1, 0:K], "psk1", msg)
+        same("eqt", T.rt, "rt0 rt1", own(0), "sc0 sc1", 3.0)
+        pe([mm(T.psk[:, 0, 0:K], C("id"), C("bm4"), True, False), mm(T.psk[:, 0, 0:K], C("id4"), T.hh[:], False, False),
+            mm(T.psk[:, 0, 0:K], C("idm"), T.rt[:], False, False)], "id bm4 id4 hh0 hh1 idm rt0 rt1", "psk0")
+        lower("eqt", T.psk[:, 0, :], "psk0")
+        scan(T.scm[:], T.psk[:, 0, 0:K], "psk0", "scm")
         tt(C("w1"), C("nqd"), T.scm[:, 15:K:16], Op.max, "nqd scm", "w1")
         tt(T[msg][:, K:K + 12], C("w1"), C("dm1"), Op.min, "w1 dm1", msg + "l")
         mk = msg + " " + msg + "l"
         if t == 0:
-            arrives("ru1", NE, "up1", 5.0, send(T[msg][:], mk, r - 1, T.up1[:], "ru1", "ls6"))
-            arrives("ru2", NE, "up2", 5.0, send(T[msg][:], mk, r - 2, T.up2[:], "ru2", "ls7"))
+            arrives("ru1", NE, "up1", 5.0, send(T[msg][:, 0:K + 12], mk, r - 1, T.up1[:], "ru1", "ls6"))
+            arrives("ru2", NE, "up2", 5.0, send(T[msg][:, 0:K + 12], mk, r - 2, T.up2[:], "ru2", "ls7"))
         elif t == 1:
-            arrives("ru3", NE, "up3", 5.0, send(T[msg][:], mk, r - 1, T.up3[:], "ru3", "ls8"))
-        arrives("rh%d" % j, NE, "hm%d" % j, 5.0, send(T[msg][:], mk, r + 1 + t, T["hm%d" % j][:], "rh%d" % j, "ls%d" % (9 + t)))
+            arrives("ru3", NE, "up3", 5.0, send(T[msg][:, 0:K + 12], mk, r - 1, T.up3[:], "ru3", "ls8"))
+        arrives("rh%d" % j, NE, "hm%d" % j, 5.0, send(T[msg][:, 0:K + 12], mk, r + 1 + t, T["hm%d" % j][:], "rh%d" % j, "ls%d" % (9 + t)))
         if t:
-            apply("hm%d" % t, "lh", "mb1")
-        pe([mm(T.psk[:, 0, 0:K], C("sa"), T.at[:], True, False), mm(T.psk[:, 0, 0:K], C("dg1"), T.g2[:], False, False),
-            mm(T.psk[:, 0, 0:K], T.row[96:97, 128 * t:128 * t + 128], T.ro2[96:97, 0:K], False, True)], "sa at0 at1 dg1 g2 row3%d ro2" % t, "psk0")
-        act(T.v2[:], T.psk[:, 0, 0:K], "psk0", "v2")
-        cp(T.xw[:].indirect(C("ld")), T.at[:], "ld at0 at1", XW, -K)
+            apply("hm%d" % t, "lh", "lo0")
+        pe([mm(T.psk[:, 1, 0:K], C("sa"), T.at[:], True, False), mm(T.psk[:, 1, 0:K], C("dg1"), T.g2[:], False, False),
+            mm(T.psk[:, 1, 0:K], C("row", 128 * t, 128 * t + 128, 96, 97), C("one", 0, K, 96, 97), False, True)], "sa0 sa1 at dg1 g2 rowm%d one" % t, "psk1")
+        act(T.v2[:], T.psk[:, 1, 0:K], "psk1", "v2")
+        cp(T.xw[:].indirect(C("ld")), T.at[:], "ld at", XW, -K)
         cp(T.pw[:].indirect(C("ld")), T.v2[:], "ld v2", PW, -K)
-        tt(T.qs[:], T.xw[:, 0:W].indirect(LO), T.q[:], Op.add, XW + " ll0 ll1 q", "qs", K)
+        tt(T.qs[:], T.xw[:, 0:W].indirect(LO), T.q[:], Op.add, XW + " lo0 lo1 q", "qs", K)
         act(T.qb[:], T.qs[:], "qs", "qb", AF.Copy, scale=0.5, bias=127.8125)
         act(T.q[:], T.qb[:], "qb", "q", AF.Copy, bias=-128.0)
         if t < RO - 1:
@@ -618,51 +589,53 @@ def rank_program(g, core, T, topo):
                 else:
                     ts(o, T.qb[:], -128.0, Op.add, "qb", "qr%d" % i)
         for h in (0, 1):
+            nn = lambda f: T.nn[0:H, h, 128 * f:128 * f + 128]
             ts(T.nn[0:H, h, 128:384], T.psv[0:H, h, 128:384], 0.0, Op.not_equal, "psv%d" % h, "nna%d" % h)
-            ts(T.nn[0:H, h, 0:128], T.psv[0:H, h, 0:128], 0.0, Op.is_gt, "psv%d" % h, "nnb%d" % h)
-            pe([turn(T.psu, T.nn[0:H, h, 128:256], "idb", h, True, False), turn(T.psu, T.nn[0:H, h, 256:384], "idb", h, False, True)], "idb nna%d" % h, "psu")
-            pe([turn(T.psm, T.nn[0:H, h, 128:256], "id2", h, True, False), turn(T.psm, T.nn[0:H, h, 256:384], "idn", h, False, False),
-                turn(T.psm, T.nn[0:H, h, 0:128], "idb", h, False, True)], "id2 idn idb nna%d nnb%d" % (h, h), "psm")
+            act(nn(0), T.psv[0:H, h, 0:128], "psv%d" % h, "nnb%d" % h, AF.Sign, bias=-0.5)
+            pe([mm(T.psu[:, H * h:H * h + H], nn(f), ID, f == 1, f == 2) for f in (1, 2)], "id nna%d" % h, "psu")
+            for u in (0, 1):
+                o = T.psm[:, K * u + H * h:K * u + H * h + H]
+                fs = [mm(o, C("row", 128 * u, 128 * u + 128, 64, 65), C("one", 0, H, 64, 65), True, False)]
+                fs += [mm(o, nn(f), C("idu", 128 * (3 * u + w), 128 * (3 * u + w) + H, p1=H), False, f == 0) for f, w in ((1, 0), (2, 1), (0, 2))]
+                pe(fs, "rowu0 rowu1 one %s nna%d nnb%d" % (keys("idu", 6), h, h), "psm")
         act(T.nr[:], T.psu[:, 0:K], "psu", "nr", AF.Relu, bias=-1.0)
-        ts(T.psm[:, 0:K], T.psm[:, 0:K], 1.0, Op.is_gt, "psm", "psm pk")
-        tt(T.psm[:, K:2 * K], T.psm[:, 0:K], T.dc[:], Op.mult, "psm pk dc", "psm sp")
-        tt(T.sg[:], T.psm[:, K:2 * K], T.cc[:, 0, :], Op.add, "psm sp cc0 cc1", "sg")
-        pe([mm(T.psg[:, 0:K], C("tri"), T.nr[:], False, True)], "tri nr", "psg")
+        tt(T.psm[:, 0:K], T.psm[:, 0:K], T.cc[:, 1, :], Op.min, "psm cc0 cc1", "psm pk")
+        tt(T.dc[:], T.psm[:, K:2 * K], T.cc[:, 0, :], Op.min, "psm cc0 cc1", "dc")
+        tt(T.sg[:], T.psm[:, 0:K], T.dc[:], Op.max, "psm pk dc", "sg")
+        pe([mm(T.psg[:, 0:K], C("id"), T.nq[:], True, False), mm(T.psg[:, 0:K], C("tri"), T.nr[:], False, True)], "id nq tri nr", "psg")
         act(T.psu[:, K:2 * K], T.psg[:, 0:K], "psg psu", "psu", AF.Relu, scale=-1.0)
         act(T.sh[:], T.sg[:], "sg", "sh", AF.Copy, bias=-2048.0)
         act(T.fst[:], T.psg[:, 0:K], "psg", "fst", AF.Relu, scale=-1.0)
         cp(T.fw[:].indirect(C("ld")), T.sg[:], "ld sg", FW, -K)
+        ts(T.ci[:], T.fw[:, 0:W].indirect(LO), W - 1, Op.bitwise_and, FW + " lo0 lo1", "ci", n=K)
         if t < RO - 1:
-            cp(T.lc[:], T.fw[:, 0:W].indirect(LO), FW + " ll0 ll1", "lc", K)
-            ts(T.c16[:], T.lc[:], -2048.0, Op.add, "lc", "c16")
+            mv("lc", T.lc[:], T.ci[:], "ci", "lc")
+            mv("c16", T.c16[:], T.ci[:], "ci", "c16", bias=-2048.0)
         else:
-            cp(T.cf[:], T.fw[:, 0:W].indirect(LO), FW + " ll0 ll1", "cf", K)
+            mv("lc", T.cf[:], T.ci[:], "ci", "cf")
         tt(T.x1[:], T.psu[:, K:2 * K], T.sh[:], Op.mult, "psu sh", "x1")
         tt(T.x2[:], T.psu[:, K:2 * K], T.b16[:], Op.mult, "psu b16_0 b16_1", "x2")
-        place = lambda o, sp: [mm(o, C("idb"), C("bmc"), True, False), mm(o, C("bn8"), T.fst[:], False, False), mm(o, C("blh"), T.x1[:], False, sp)]
-        pe(place(T.psv[:, 1, 0:K], True), "idb bmc bn8 fst blh x1", "psv1")
-        pe([mm(T.psv[:, 0, 0:K], C("blh"), T.x1[:], True, True)], "blh x1", "psv0")
-        pe([mm(T.psv[:, 0, K:2 * K], C("blh"), T.x2[:], True, True)], "blh x2", "psv0")
-        pe(place(T.psd[:, 0:K], False), "idb bmc bn8 fst blh x1", "psd")
+        place = lambda o, sp: [mm(o, C("id"), C("bmc"), True, False), mm(o, C("bn8"), T.fst[:], False, False), mm(o, C("bl"), T.x1[:], False, sp)]
+        pe(place(T.psv[:, 1, 0:K], True), "id bmc bn8 fst bl x1", "psv1")
+        pe([mm(T.psv[:, 0, 0:K], C("bl"), T.x1[:], True, True)], "bl x1", "psv0")
+        pe(place(T.psd[:, 0:K], False), "id bmc bn8 fst bl x1", "psd")
         scan(T.scc[:], T.psv[:, 1, 0:K], "psv1", "scc")
-        cp16(T.rc[:], T.psv[:, 0, 0:K], "psv0", "rc")
-        act(T.hi[:], T.psv[:, 0, K:2 * K], "psv0", "hi", AF.Copy, scale=0.03125, bias=144.0 - 0.484375)
+        act(T.rc[:], T.psv[:, 0, 0:K], "psv0", "rc")
         tt(C("lp"), T.scc[:, 15:K:16], C("dm4"), Op.min, "scc dm4", "lp")
         same("eqo", T.rc, "rc", lambda kb: T.scc[:, 16 * kb + 15:16 * kb + 16], "scc")
         lower("eqo", T.psd, "psd")
         act(T.g1[:], T.pw[:].indirect(C("lp")), PW + " lp", "g1", n=K)
-        pe([mm(T.psg[:, 0:K], C("vr"), T.x2[:], True, False), mm(T.psg[:, 0:K], T.row[0:1, 384:512], T.ro2[0:1, 0:K], False, False),
-            mm(T.psg[:, 0:K], C("vh"), T.hi[:], False, False), mm(T.psg[:, 0:K], C("dgc%d" % t), T.g1[:], False, True)],
-           "vr1 vr7 x2 row20 row21 row22 row27 ro2 vh hi dgc%d g1" % t, "psg")
+        pe([mm(T.psg[:, 0:K], C("vr"), T.x2[:], True, False), mm(T.psg[:, 0:K], C("row", 384, 512, p1=1), C("one", 0, K, p1=1), False, False),
+            mm(T.psg[:, 0:K], C("dgc", 128 * t, 128 * t + 128), T.g1[:], False, True)], "vr x2 rowc0 rowc1 one dgc%d0 dgc%d2 g1" % (t, t), "psg")
         act(T.v1[:], T.psg[:, 0:K], "psg", "v1")
         if t < RO - 1:
             disk_window(j + 1, "g1")
         scan(T.scd[:], T.psd[:, 0:K], "psd", "scd")
         tt(C("lcl"), T.scd[:, 15:K:16], C("dm4"), Op.min, "scd dm4", "lcl")
         cp(T.pw[:].indirect(C("lcl")), T.v1[:], "lcl v1", PW, -K)
-    apply("hm3", "lh", "x1")
-    dma("d", T.yq[:], T.q[:], "q", "yq")
-    dma("d", T.yl[:], T.lh[:, 0:M], "lh", "yl")
-    dma("d", T.yc[:], T.cf[:], "cf", "yc")
-    dma("d", T.yt[:], T.pw[7:128:16, 0:W], PW, "yt")
+    apply("hm3", "lh", "nna0")
+    dma("d", T.yq[:], T.q[:], "q", "yq", 48)
+    dma("d", T.yl[:], T.lh[:, 0:M], "lh", "yl", 512)
+    dma("d", T.yc[:], T.cf[:], "cf", "yc", 96)
+    dma("d", T.yt[:], T.pw[0:128:16, 0:W], PW, "yt", 128)
     finish()

@@ -6,19 +6,19 @@ BIG = 65536.0
 RES = 67108864.0
 OUT = 8192.0
 NE = 8
-ON_S = "fl gt msg lw pcs lh c16 lc l12".split()
-QG, QS = 5, 5
-WAKE, PASSES, CYC, PCYC, GATH, SCAT = 0.2, 6, 0.00083, 0.00045, 1.56, 3.8
+QG = 5
+WAKE, LAG, VFIX, SFIX, CYC, PCYC, GATH, SCAT, FAR = 0.2, 0.05, 0.02, 0.04, 0.00083, 0.00045, 1.56, 3.8, 6.0
+PASSES, NOISE, TRIES, HEAT, EPS = 30, 1.0, 6000, 0.05, 0.5
 
 _S = "sbuf"
 F32, B16, I32, U16, H16 = "float32", "bfloat16", "int32", "uint16", "float16"
 PACK = {
-    "tf": (F32, (("w01", 8), ("nqd", 12), ("w1", 12), ("dm4", 12), ("dm1", 12), ("er", 16), ("lt", 16), ("ec", 16), ("pmf", 4))),
+    "tf": (F32, (("nqd", 12), ("w1", 12), ("dm4", 12), ("dm1", 12), ("er", 16), ("lt", 16), ("ec", 16), ("pmf", 4))),
     "tl": (U16, (("ld", 12), ("lcl", 12), ("lp", 12), ("lq", 12))),
     "ti": (I32, (("dmi", 12), ("pmi", 4))),
-    "tb": (B16, (("wm", 16), ("wp", 16), ("wm1", 24), ("wm2", 24), ("wp1", 24), ("wp2", 24), ("cand", 12), ("exb", 16), ("nrq", 12))),
-    "cb": (B16, (("one", 256), ("zero", 256), ("bl", 128), ("bt", 128), ("rp", 256), ("id", 128), ("idu", 768), ("id4", 128), ("idm", 128), ("bi", 384), ("pb16", 128), ("nb16", 128),
-                 ("btr", 128), ("tri", 128), ("bl8", 128), ("bn8", 128), ("sa", 128), ("wt", 128), ("se", 128), ("dg1", 128), ("dgc", 384), ("vr", 128), ("rq", 256),
+    "tb": (B16, (("wm", 16), ("wp", 16), ("wm1", 24), ("wm2", 24), ("wp1", 24), ("wp2", 24), ("cand", 12), ("exb", 16))),
+    "cb": (B16, (("w01", 320), ("one", 256), ("zero", 256), ("bl", 128), ("bt", 128), ("rp", 256), ("id", 128), ("idu", 768), ("id4", 128), ("idm", 128), ("bi", 384), ("pb16", 128), ("nb16", 128),
+                 ("btr", 128), ("tri", 128), ("tr8", 128), ("bl8", 128), ("bn8", 128), ("sa", 128), ("wt", 128), ("se", 128), ("dg1", 128), ("dgc", 384), ("vr", 128), ("rq", 256),
                  ("bm", K), ("bmc", K), ("bm4", K), ("ltk", 2048), ("slt", 2048), ("row", 512))),
 }
 PLACE, SCRATCH, ORDERS = {}, {}, {}
@@ -29,12 +29,12 @@ for _b in PACK:
         _o += _w
     SCRATCH[_b] = (_S, [128, _o], PACK[_b][0])
 for _d, _l in (
-    (B16, (("xw", W + K), ("xlh", M), ("q", K), ("qb", K), ("qrep", 16 * K), ("ma", 16 * K), ("mb", 16 * K), ("at", K), ("nr", K), ("nq", K), ("fst", K),
+    (B16, (("xw", W + K), ("xlh", M), ("q", K), ("qb", K), ("qrep", 16 * K), ("ma", 16 * K), ("mb", 16 * K), ("at", K), ("nr", K), ("nq", K), ("xo", K), ("fst", K),
            ("xl1", M), ("xl2", M), ("xl3", M), ("xp1", 512), ("xp2", 512), ("xp3", 512), ("xlp", 512), ("xt", 512))),
     (I32, (("fw", W + K), ("ci", K), ("tgs", 256), ("pci", 256), ("lfi", M), ("cxi", K), ("ic", 256))),
     (U16, (("lfu", M), ("lc", K), ("lu1", M), ("lu2", M), ("lu3", M), ("msg1", K + 16), ("msg2", K + 16), ("msg3", K + 16), ("up1", K + 12), ("up2", K + 12), ("up3", K + 12),
            ("hm1", K + 12), ("hm2", K + 12), ("hm3", K + 12))),
-    (F32, (("pw", W + K), ("lh", M + K), ("qs", K), ("cf", K), ("scd", K), ("scm", K), ("scc", K), ("dc", K), ("sg", K), ("sh", K), ("v1", K), ("v2", K), ("s0", 256),
+    (F32, (("pw", W + K), ("lh", M + K), ("cf", K), ("scd", K), ("scm", K), ("scc", K), ("dc", K), ("sg", K), ("sh", K), ("v1", K), ("v2", K), ("s0", 256),
            ("lw1", M), ("lw2", M + K), ("lw3", M + K))),
     (H16, (("pt", W), ("pcs", 512), ("pa", 16 * K), ("pb", 16 * K), ("pc", 16 * K), ("g1", K), ("g2", K), ("gt", K), ("b16", K), ("c16", K), ("x1", K), ("x2", K), ("rc", K),
            ("ro", K), ("rt", K), ("hh", K))),
@@ -50,7 +50,7 @@ for _n in ("psk", "psv"):
     SCRATCH[_n] = ("psum", [128, 2, 512], F32)
 for _n in ("psm", "psu", "psd", "psg"):
     SCRATCH[_n] = ("psum", [128, 512], F32)
-SEMAPHORES = ["qv", "qs", "qp", "qg"] + ["ld%d" % j for j in range(20)] + ["ls%d" % j for j in range(16)]
+SEMAPHORES = ["qv", "qs", "qp", "qg"] + ["ld%d" % j for j in range(20)] + ["ls%d" % j for j in range(20)] + ["rl0"]
 SEMAPHORES += ["%s%d" % (a, j) for a in ("rl", "rx", "ru", "rh") for j in (1, 2, 3)]
 
 
@@ -134,11 +134,13 @@ def tracker(g, T):
         wr[key] = (sem, n, None)
         rd[key] = {}
 
-    nodes = []
+    nodes, alt = [], {}
 
-    def op(q, fns, R, Wt, cost):
+    def op(q, fns, R, Wt, cost, other=None):
         R, Wt = R.split(), Wt.split()
         nodes.append((q, R, Wt, lambda: op_(q, fns, R, Wt), cost, 0.0, -1))
+        if other:
+            alt[len(nodes) - 1] = (other[0], R, Wt, lambda: op_(other[0], other[1], R, Wt), other[2], 0.0, -1)
 
     def dma(q, out, in_, R, Wt, kb):
         R, Wt = R.split(), Wt.split()
@@ -161,15 +163,16 @@ def tracker(g, T):
                 dep[x].add(after)
             for k in sorted(set(R + Wt)):
                 if k.startswith("ps"):
-                    cur = ps.setdefault(k, [q, [], []])
-                    if cur[0] == q:
+                    who = x if x in alt else q
+                    cur = ps.setdefault(k, [who, [], []])
+                    if cur[0] == who:
                         dep[x].update(cur[2])
                         if q == "p" and cur[1]:
                             dep[x].add(cur[1][-1])
                         cur[1].append(x)
                     else:
                         dep[x].update(cur[1])
-                        ps[k] = [q, [x], cur[1]]
+                        ps[k] = [who, [x], cur[1]]
                     continue
                 if k in w:
                     dep[x].add(w[k])
@@ -181,13 +184,17 @@ def tracker(g, T):
                 if k not in Wt:
                     rds.setdefault(k, []).append(x)
             dep[x].discard(x)
-        succ = [[] for _ in nodes]
+        prev, nxt, succ = [[] for _ in nodes], [[] for _ in nodes], [[] for _ in nodes]
         for x in range(nn):
-            for d in dep[x]:
-                succ[d].append(x)
+            for d in sorted(dep[x]):
+                if nodes[x][0] == "p" == nodes[d][0]:
+                    dep[x].discard(d)
+                    prev[x].append(d)
+                    nxt[d].append(x)
+                else:
+                    succ[d].append(x)
         cs = [nd_[4] for nd_ in nodes]
         lat = [nd_[5] + (0.0 if nd_[0] == "a" else WAKE) for nd_ in nodes]
-        prev, nxt = [[] for _ in nodes], [[] for _ in nodes]
         for q in "gd":
             row = [x for x in range(nn) if nodes[x][0] == q and (q == "d" or nodes[x][6] == -2)]
             for x, y in zip(row, row[1:]):
@@ -214,19 +221,113 @@ def tracker(g, T):
                     b.insert(i, (e, e + cs[x]))
                 st[x] = e
             return st, max(st[x] + cs[x] + (0.0 if back else lat[x]) for x in range(nn))
+
+        def times(seq):
+            st, fin, free, last, why = [0.0] * nn, [0.0] * nn, dict.fromkeys("vspgda", 0.0), dict.fromkeys("vspgda", -1), [-1] * nn
+            for x in seq:
+                q, e, w = qof[x], 0.0, -1
+                for y in dl[x]:
+                    if fin[y] > e:
+                        e, w = fin[y], y
+                if q == "a":
+                    st[x], why[x] = e, w
+                else:
+                    if e > free[q]:
+                        e += WAKE - LAG
+                    else:
+                        e, w = free[q], last[q]
+                    st[x], why[x], free[q], last[q] = e, w, e + cs[x], x
+                fin[x] = e + cs[x] + tail[x]
+            end = max(fin)
+            return end + EPS * sum(fin) / nn, st, why, fin.index(end)
+
+        def swap(x):
+            nodes[x], alt[x] = alt[x], nodes[x]
+            qof[x], cs[x] = nodes[x][0], nodes[x][4]
+
+        def polish(st):
+            seq = sorted(range(nn), key=lambda x: (st[x], x))
+            cur = best = times(seq)
+            bseq, bq, rnd = seq, list(qof), 7
+            for it in range(TRIES):
+                path, x = [], cur[3]
+                while x >= 0:
+                    y = cur[2][x]
+                    if y >= 0 and qof[y] == qof[x] and y not in dep[x] and y not in prev[x]:
+                        path.append((y, x))
+                    x = y
+                if not path:
+                    break
+                rnd = (rnd * 1103515245 + 12345) % 2147483648
+                y, x = path[(rnd >> 8) % len(path)]
+                turn = [z for z in (x, y) if z in alt and (rnd >> 20) % 3 == 0][:1]
+                for z in turn:
+                    swap(z)
+                i, j = seq.index(y), seq.index(x)
+                rnd = (rnd * 1103515245 + 12345) % 2147483648
+                more = (rnd >> 8) % 4
+                if turn:
+                    new = seq
+                elif (rnd >> 12) % 2:
+                    while more and i > 0:
+                        i -= 1
+                        more -= qof[seq[i]] == qof[x]
+                    need = {x}
+                    for z in reversed(seq[i:j]):
+                        if any(u in need for u in sl[z]):
+                            need.add(z)
+                    new = seq[:i] + [z for z in seq[i:j + 1] if z in need] + [z for z in seq[i:j + 1] if z not in need] + seq[j + 1:]
+                else:
+                    while more and j < nn - 1:
+                        j += 1
+                        more -= qof[seq[j]] == qof[x]
+                    need = {y}
+                    for z in seq[i + 1:j + 1]:
+                        if any(u in need for u in dp[z]):
+                            need.add(z)
+                    new = seq[:i] + [z for z in seq[i:j + 1] if z not in need] + [z for z in seq[i:j + 1] if z in need] + seq[j + 1:]
+                tr = times(new)
+                rnd = (rnd * 1103515245 + 12345) % 2147483648
+                if tr[0] < cur[0] + HEAT * (1.0 - it / TRIES) * (rnd >> 8) / 8388608:
+                    cur = tr
+                    pos = {z: n for n, z in enumerate(new)}
+                    seq = sorted(new, key=lambda z: (tr[1][z], pos[z]))
+                    if tr[0] < best[0]:
+                        best, bseq, bq = tr, seq, list(qof)
+                else:
+                    for z in turn:
+                        swap(z)
+            return bseq, bq
+        qof = [nd_[0] for nd_ in nodes]
+        dl = [sorted(d) for d in dep]
+        dp = [dl[x] + prev[x] for x in range(nn)]
+        sl = [succ[x] + nxt[x] for x in range(nn)]
+        tail = [nd_[5] + (0.0 if nd_[0] == "a" else LAG) for nd_ in nodes]
         pr = [0.0] * nn
         for x in range(nn - 1, -1, -1):
             pr[x] = cs[x] + max([lat[x]] + [pr[y] + lat[x] for y in succ[x]] + [pr[y] for y in nxt[x]])
         order = sorted(range(nn), key=lambda x: (-pr[x], x))
         alike = tuple((nd_[0], tuple(nd_[1]), tuple(nd_[2])) for nd_ in nodes)
-        for _ in range(0 if alike in ORDERS else PASSES):
-            st, end = place(order, False)
-            if alike not in ORDERS or end < ORDERS[alike][0]:
-                ORDERS[alike] = (end, st)
-            bk = place(sorted(range(nn), key=lambda x: (-st[x] - cs[x], -x)), True)[0]
-            order = sorted(range(nn), key=lambda x: (-bk[x] - cs[x], x))
-        st = ORDERS[alike][1]
-        for x in sorted(range(nn), key=lambda x: (st[x], x)):
+        if alike not in ORDERS:
+            seed, best = 1, None
+            for rnd in range(PASSES):
+                st, end = place(order, False)
+                if best is None or end < best[0]:
+                    best = (end, st)
+                shake = NOISE if rnd % 3 == 2 else 0.0
+                if shake:
+                    st = best[1]
+                bk = place(sorted(range(nn), key=lambda x: (-st[x] - cs[x], -x)), True)[0]
+                key = [0.0] * nn
+                for x in range(nn - 1, -1, -1):
+                    seed = (seed * 1103515245 + 12345) % 2147483648
+                    key[x] = max([bk[x] + cs[x] + shake * seed / 2147483648] + [key[y] + 1e-6 for y in sl[x]])
+                order = sorted(range(nn), key=lambda x: (-key[x], x))
+            ORDERS[alike] = polish(best[1])
+        seq, queue = ORDERS[alike]
+        for x in seq:
+            if qof[x] != queue[x]:
+                swap(x)
             nodes[x][3]()
         for sem in total:
             if known["g"].get(sem, 0) < total[sem]:
@@ -258,13 +359,13 @@ def rank_program(g, core, T, topo):
     def vcost(o, a, per=1.0):
         if "16" in str(o.dtype) and "16" in str(a.dtype):
             per *= 0.5
-        return 0.03 + CYC * max(64, per * wid(o))
+        return VFIX + CYC * max(64, per * wid(o))
 
-    def ncost(n):
-        return 0.05 + CYC * (GATH * n if n > 0 else -SCAT * n)
+    def ncost(n, fix=VFIX):
+        return fix + CYC * (GATH * n if n > 0 else -SCAT * n)
 
     def tt(o, a, b, f, R, Wt, n=0):
-        op("v", [lambda: v.tensor_tensor(o, a, b, f)], R, Wt, ncost(n) if n else 0.03 + CYC * max(64, wid(o) * (1 if "ps" in R else 2)))
+        op("v", [lambda: v.tensor_tensor(o, a, b, f)], R, Wt, ncost(n) if n else VFIX + CYC * max(64, wid(o) * (1 if "ps" in R else 2)))
 
     def ts(o, a, x, f, R, Wt, y=None, f2=None, n=0):
         if f2 is None:
@@ -279,15 +380,18 @@ def rank_program(g, core, T, topo):
         op("v", [lambda: v.memset(o, c)], "", Wt, vcost(o, o))
 
     def act(o, a, R, Wt, f=AF.Identity, n=0, **kw):
-        op("s", [lambda: s.activation(o, a, f, **kw)], R, Wt, ncost(n) if n else 0.05 + CYC * max(64, wid(o)))
+        op("s", [lambda: s.activation(o, a, f, **kw)], R, Wt, ncost(n, SFIX) if n else SFIX + CYC * max(64, wid(o)))
 
-    def mv(name, o, a, R, Wt, scale=1.0, bias=0.0):
-        if name in ON_S:
-            act(o, a, R, Wt, AF.Copy, scale=scale, bias=bias)
-        elif scale == 1.0 and bias == 0.0:
-            cp(o, a, R, Wt)
+    def mv(q, o, a, R, Wt, scale=1.0, bias=0.0):
+        if q == "g":
+            return gop(lambda: g.affine_select(o, a, [[0, wid(o)]], Op.is_ge, 0.0, 0, 0), R, Wt, wid(o))
+        on_s = ("s", [lambda: s.activation(o, a, AF.Copy, scale=scale, bias=bias)], SFIX + CYC * max(64, wid(o)))
+        if scale == 1.0 and bias == 0.0:
+            on_v = ("v", [lambda: v.tensor_copy(o, a)], vcost(o, a))
         else:
-            ts(o, a, scale, Op.mult, R, Wt, bias, Op.add)
+            on_v = ("v", [lambda: v.tensor_scalar(o, a, scale, bias, Op.mult, Op.add)], vcost(o, a))
+        x, y = (on_s, on_v) if q == "s" else (on_v, on_s)
+        op(x[0], x[1], R, Wt, x[2], y)
 
     def mm(o, l, x, st, sp):
         return (lambda: p.matmul(o, l, x, st, sp), PCYC * max(64, wid(x)))
@@ -296,7 +400,7 @@ def rank_program(g, core, T, topo):
         op("p", [f[0] for f in fs], R, Wt, sum(f[1] for f in fs))
 
     def scan(o, d, R, Wt, n=K, p1=128):
-        op("v", [lambda: v.tensor_tensor_scan(o, T.s0[0:p1, 0:n], d, 0.0, Op.add, Op.min)], R + " s0", Wt, 0.03 + CYC * n)
+        op("v", [lambda: v.tensor_tensor_scan(o, T.s0[0:p1, 0:n], d, 0.0, Op.add, Op.min)], R + " s0", Wt, VFIX + CYC * n)
 
     def gop(f, R, Wt, n):
         op("g", [f], R, Wt, 0.17 + 2 * CYC * n)
@@ -312,16 +416,18 @@ def rank_program(g, core, T, topo):
     XW = keys("xw", 4)
     FW = "fwl " + keys("fw", 4)
     QR = keys("qr", 16)
+    dma("d", T.lfi[:, 0:512], T.lf[:, 0:512], "", "lfi0", 256)
     dma("d", T.tgs[:], T.tg[:], "", "tgs", 128)
-    dma("d", T.lfi[:], T.lf[:], "", "lfi", 512)
     dma("d", T.cxi[:], T.cx[:], "", "cxi", 96)
     dma("d", T.q[:], T.qx[:], "", "q", 48)
+    dma("d", T.xw[:, 0:1024], T.xr[:, 0:1024], "", "xw0", 256)
     ts(T.pci[:], T.tgs[:], 1, Op.bitwise_and, "tgs", "pci")
     for j, (n, src) in enumerate((("tgs", T.tgs), ("pci", T.pci))):
-        mv("pcs", T.pcs[:, 256 * j:256 * j + 256], src[:], n, "pcs%d" % j)
+        mv("s", T.pcs[:, 256 * j:256 * j + 256], src[:], n, "pcs%d" % j)
         dma("d", T.pt[8 * j:8 * j + 8, :], T.pcs[:, 256 * j:256 * j + 256], "pcs%d" % j, "pt%d" % j, 64)
-    for c in range(4):
-        dma("d", T.xw[:, 1024 * c:1024 * c + 1024], T.xr[:, 1024 * c:1024 * c + 1024], "", "xw%d" % c, 256)
+    for c, (a, b) in enumerate(((1024, 2560), (2560, 3584), (3584, W))):
+        dma("d", T.xw[:, a:b], T.xr[:, a:b], "", "xw%d" % (c + 1), (b - a) / 4)
+    dma("d", T.lfi[:, 512:M], T.lf[:, 512:M], "", "lfi1", 256)
     dma("d", T.xlh[:], T.xl[:], "", "xlh", 256)
     dma("d", T.fw[:, 0:2048], T.fd[:], "", "fwl", 1024)
     fill(C("one"), 1.0, "one")
@@ -379,16 +485,14 @@ def rank_program(g, core, T, topo):
     cp(T.lc[:], T.cxi[:], "cxi", "lc")
     ts(T.c16[:], T.cxi[:], -2048.0, Op.add, "cxi", "c16")
     for i in range(16):
-        if i % 2:
-            act(T.qrep[:, i:16 * K:16], T.q[:], "q", "qr%d" % i)
-        else:
-            cp(T.qrep[:, i:16 * K:16], T.q[:], "q", "qr%d" % i)
+        mv("vs"[i % 2], T.qrep[:, i:16 * K:16], T.q[:], "q", "qr%d" % i)
     ts(T.s0[:], T.ic[:], 0.0, Op.is_equal, "ic", "s0", RES, Op.mult)
     ts(C("bm"), T.ic[:, 0:K], PM, Op.not_equal, "ic pmf", "bm", BIG, Op.mult)
     ts(C("bmc"), C("bm"), OUT + 2048.0, Op.add, "bm", "bmc")
     ts(C("bm4"), C("bm"), -4096.0, Op.add, "bm", "bm4")
     cp(T.gt[0:32, :], C("one", 0, K, p1=32), "one", "gt0 gt1")
-    cp(C("w01"), T.ic[:, 0:8], "ic", "w01")
+    fill(C("w01", 0, 1), 0.0, "w01")
+    fill(C("w01", 1), 1.0, "w02")
     for j, w in enumerate((0.0, -1.0, -1.0)):
         times(C("bi", 128 * j, 128 * j + 128), C("id"), w, "id", "bi%d" % j)
     for nm, cols in (("wm1", (2.0, 0.0, 0.0)), ("wm2", (-2.0, 0.0, 0.0)), ("wp1", (D(3), D(0), 0.0)), ("wp2", (E(3), 0.0, D(0)))):
@@ -398,6 +502,7 @@ def rank_program(g, core, T, topo):
         times(C(n), C("id"), w, "id", n)
     for j, w in enumerate((2.0, -1.0, 0.5, -2.0, 1.0, -0.5)):
         times(C("idu", 128 * j, 128 * j + 128), C("id"), w * OUT, "id", "idu%d" % j)
+    times(C("tr8"), C("tri"), -OUT, "tri", "tr8")
     times(C("bl8"), C("bl"), OUT, "bl", "bl8")
     times(C("bn8"), C("bl"), -OUT, "bl", "bn8")
     times(C("se"), C("bl"), D(4), "bl ec4", "se")
@@ -421,44 +526,44 @@ def rank_program(g, core, T, topo):
     for c in range(8):
         bk, ap = banks[c % 6]
         pe([mm(ap, C("wt", p1=16), T.pt[0:16, 512 * c:512 * c + 512], True, False), mm(ap, C("sa"), T.xw[:, 512 * c:512 * c + 512], False, True)],
-           "sa0 sa1 wt0 wt1 pt0 pt1 xw%d" % (c // 2), bk)
-        if c % 2:
-            cp(T.pw[:, 512 * c:512 * c + 512], ap, bk, "pw%d" % c)
-        else:
-            act(T.pw[:, 512 * c:512 * c + 512], ap, bk, "pw%d" % c)
+           "sa0 sa1 wt0 wt1 pt0 pt1 xw%d" % (0, 0, 1, 1, 1, 2, 2, 3)[c], bk)
+        mv("sv"[c % 2], T.pw[:, 512 * c:512 * c + 512], ap, bk, "pw%d" % c)
 
-    mv("lfu", T.lfu[:], T.lfi[:], "lfi", "lfu")
+    mv("v", T.lfu[:, 0:512], T.lfi[:, 0:512], "lfi0", "lfu0")
+    mv("g", T.lfu[:, 512:M], T.lfi[:, 512:M], "lfi1", "lfu1")
     chip = lambda x: topo.chip(T.cores[x % N])
 
     def handed(src, j):
         return j > 1 and chip(src - j) == chip(src - j + 1) != chip(src)
     pe([mm(T.psd[:], C("id"), T.xlh[:, 0:512], True, False), mm(T.psd[:], C("pb16"), T.xlh[:, 512:M], False, True)], "id pb16 xlh", "psd")
-    act(T.xlp[:], T.psd[:], "psd", "xlp")
-    sent = []
-    for j in (1, 2, 3):
+    mv("s", T.xlp[:], T.psd[:], "psd", "xlp")
+    arrives("rl0", NE, "lu0", 2 * FAR, send(T.lfu[:, 0:512], "lfu0", r - 1, T.lu1[:, 0:512], "rl0", "ls15", True))
+    arrives("rl1", NE, "lu1", FAR, send(T.lfu[:, 512:M], "lfu1", r - 1, T.lu1[:, 512:M], "rl1", "ls0", True))
+    sent = send(T.xlp[:], "xlp", r - 1, T.xp1[:], "rx1", "ls1", True)
+    arrives("rx1", NE, "xp1", 10.0, sent)
+    for j in (2, 3):
         if not handed(r, j):
-            sent.append(send(T.lfu[:], "lfu", r - j, T["lu%d" % j][:], "rl%d" % j, "ls%d" % (2 * j - 2), True))
-            sent.append(send(T.xlp[:], "xlp", r - j, T["xp%d" % j][:], "rx%d" % j, "ls%d" % (2 * j - 1), True))
-        arrives("rl%d" % j, NE, "lu%d" % j, (9.0, 26.0, 40.0)[j - 1], sent[0])
-        arrives("rx%d" % j, NE, "xp%d" % j, (8.0, 24.0, 40.0)[j - 1], sent[1])
-    for i in (1, 2):
+            send(T.lfu[:], "lfu0 lfu1", r - j, T["lu%d" % j][:], "rl%d" % j, "ls%d" % (2 * j - 2), True)
+            send(T.xlp[:], "xlp", r - j, T["xp%d" % j][:], "rx%d" % j, "ls%d" % (2 * j - 1), True)
+        arrives("rl%d" % j, NE, "lu%d" % j, 12.0 * j, sent)
+        arrives("rx%d" % j, NE, "xp%d" % j, 12.0 * j + 4.0, sent)
+
+    def hand_on(i):
         if handed(r + i, i + 1):
-            send(T["lu%d" % i][:], "lu%d" % i, r - 1, T["lu%d" % (i + 1)][:], "rl%d" % (i + 1), "ls%d" % (10 + 2 * i), True)
-            send(T["xp%d" % i][:], "xp%d" % i, r - 1, T["xp%d" % (i + 1)][:], "rx%d" % (i + 1), "ls%d" % (11 + 2 * i), True)
+            send(T["lu%d" % i][:], ("lu0 lu1", "lu2")[i - 1], r - 1, T["lu%d" % (i + 1)][:], "rl%d" % (i + 1), "ls%d" % (14 + 2 * i), True)
+            send(T["xp%d" % i][:], "xp%d" % i, r - 1, T["xp%d" % (i + 1)][:], "rx%d" % (i + 1), "ls%d" % (15 + 2 * i), True)
+    hand_on(1)
     for c in range(4):
         a, b = 512 * c, 512 * c + 512
         ts(T.fw[:, 2048 + a:2048 + b], T.fw[:, a:b], 12, Op.logical_shift_right, "fwl", "fw%d" % c)
-    mv("lh", T.lh[:, 0:M], T.lfi[:], "lfi", "lh")
+    mv("g", T.lh[:, 0:M], T.lfi[:], "lfi0 lfi1", "lh")
 
     def features(j, after):
         x, xl = T["xp%d" % j], T["xl%d" % j]
-        act(T.xt[:], x[:], "xp%d %s" % (j, after), "xt", AF.Copy, scale=0.0625, bias=144.0 - 0.46875)
-        act(xl[:, 512:M], T.xt[:], "xt", "xh%d" % j, AF.Copy, bias=-144.0)
+        mv("s", T.xt[:], x[:], "xp%d %s" % (j, after), "xt", 0.0625, 144.0 - 0.46875)
+        mv("s", xl[:, 512:M], T.xt[:], "xt", "xh%d" % j, bias=-144.0)
         pe([mm(T.psg[:], C("id"), x[:], True, False), mm(T.psg[:], C("nb16"), xl[:, 512:M], False, True)], "id nb16 xp%d xh%d" % (j, j), "psg")
-        act(xl[:, 0:512], T.psg[:], "psg", "xl%d" % j)
-
-    def disk_window(j, after):
-        mv("lw", T["lw%d" % j][:, 0:M], T["lu%d" % j][:], "lu%d %s" % (j, after), "lw%d" % j)
+        mv("s", xl[:, 0:512], T.psg[:], "psg", "xl%d" % j)
 
     def apply(buf, win, after):
         cp(T[win][:].indirect(T[buf][:, K:K + 12]), T[buf][:, 0:K], buf + " " + after, win, -K)
@@ -467,10 +572,10 @@ def rank_program(g, core, T, topo):
         for kb in range(12):
             ts(T[eq][:, kb, 0:K - 16 * kb], src[:, 16 * kb:K], less, Op.add, sk + " " + lk, eq + str(kb), own(kb), Op.is_equal)
 
-    def lower(eq, ps, pk):
+    def lower(eq, ps, pk, stop=True):
         for kb in range(11):
             pe([mm(ps[:, 16 * kb + 16:K], C("bl8"), T[eq][:, kb, 16:K - 16 * kb], False, False)], "bl8 %s%d" % (eq, kb), pk)
-        pe([mm(ps[:, k:K:16], C("ltk", 128 * k, 128 * k + 128), T[eq][:, :, k], False, k == 15) for k in range(1, 16)], keys("ltk", 16, 1) + " " + keys(eq, 12), pk)
+        pe([mm(ps[:, k:K:16], C("ltk", 128 * k, 128 * k + 128), T[eq][:, :, k], False, stop and k == 15) for k in range(1, 16)], keys("ltk", 16, 1) + " " + keys(eq, 12), pk)
 
     def xgather(dst, lst, lk, h):
         a, b = H * h, H * h + H
@@ -489,12 +594,13 @@ def rank_program(g, core, T, topo):
     for t in range(RO):
         j = t + 1
         lw, xl, msg = "lw%d" % j, "xl%d" % j, "msg%d" % j
-        lnw = T[lw][:, 0:M]
+        lnw, lk = T[lw][:, 0:M], lw if t else "lw0 lw1"
         for h in (0, 1):
             pgather("pc", T.lc[:], "lc", h)
             xgather("ma", T.lc[:], "lc", h)
         if t == 0:
-            disk_window(1, "pc1")
+            for h in (0, 1):
+                mv("s", T.lw1[:, 512 * h:512 * h + 512], T.lu1[:, 512 * h:512 * h + 512], "lu%d pc%d" % (h, h), "lw%d" % h)
         else:
             if t == 2:
                 apply("up2", lw, "lc")
@@ -509,9 +615,9 @@ def rank_program(g, core, T, topo):
             pe([mm(T.psk[0:H, h, 128:256], T.c16[:, a:b], C("id"), False, True)], "c16 id", k("psk"))
             scan(T.t4[0:H, h, :], T.psk[0:H, h, 0:256], k("psk"), k("t4_"), 256, H)
             ts(T.fi[0:H, h, :], T.t4[0:H, h, 15:256:16], W - 1, Op.bitwise_and, k("t4_"), k("fi"))
-            mv("fl", T.fl[0:H, h, :], T.fi[0:H, h, :], k("fi"), k("fl"), bias=-2048.0)
+            mv("s", T.fl[0:H, h, :], T.fi[0:H, h, :], k("fi"), k("fl"), bias=-2048.0)
             pe([mm(T.psk[0:16, h, 256:352], T.fl[0:H, h, :], ID, True, True)], k("fl") + " id", k("psk"))
-            mv("gt", T.gt[0:16, a:b], T.psk[0:16, h, 256:352], k("psk"), k("gt"))
+            mv("s", T.gt[0:16, a:b], T.psk[0:16, h, 256:352], k("psk"), k("gt"))
             pb, pk = ((T.psm, "psm"), (T.psu, "psu"))[h]
             fs = []
             for f in (0, 1):
@@ -519,19 +625,19 @@ def rank_program(g, core, T, topo):
             fs += [mm(pb[:, H * f + K:H * f + K + H], RP(f), T.gt[0:32, a:b], True, True) for f in (0, 1)]
             pe(fs, "rq0 rq1 rp id bm " + k("gt"), pk)
             scan(T.sc[:, h, :], pb[:, 0:K], pk, k("sc"))
-            mv("ll", T.ll[:, 0, x:y], T.sc[:, h, 15:H:16], k("sc"), k("ln"), 0.5, -0.25)
-            mv("ll", T.ll[:, 1, x:y], T.sc[:, h, H + 15:K:16], k("sc"), k("lo"))
-            act(T.ro[:, a:b], pb[:, K + H:2 * K], pk, k("ro"))
-            act(T.rt[:, a:b], pb[:, K:K + H], pk, k("rt"), AF.Copy, bias=2045.0)
-            act(T.hh[:, a:b], pb[:, K:K + H], pk, k("hh"), AF.Copy, scale=0.25, bias=1535.625)
+            mv("v", T.ll[:, 0, x:y], T.sc[:, h, 15:H:16], k("sc"), k("ln"), 0.5, -0.25)
+            mv("v", T.ll[:, 1, x:y], T.sc[:, h, H + 15:K:16], k("sc"), k("lo"))
+            mv("s", T.ro[:, a:b], pb[:, K + H:2 * K], pk, k("ro"))
+            mv("s", T.rt[:, a:b], pb[:, K:K + H], pk, k("rt"), bias=2045.0)
+            mv("s", T.hh[:, a:b], pb[:, K:K + H], pk, k("hh"), 0.25, 1535.625)
             LN = T.ll[:, 0, x:y]
-            act(T.sq[:, 0, a:b], lnw.indirect(LN), lw + " " + k("ln"), k("sqa"), AF.Square, H, scale=2.0, bias=8.0)
-            act(T.sq[:, 1, a:b], lnw.indirect(LN), lw + " " + k("ln"), k("sqb"), AF.Square, H, bias=592.0)
-            act(T.b16[:, a:b], lnw.indirect(LN), lw + " " + k("ln"), k("b16_"), n=H)
+            act(T.sq[:, 0, a:b], lnw.indirect(LN), lk + " " + k("ln"), k("sqa"), AF.Square, H, scale=2.0, bias=8.0)
+            act(T.sq[:, 1, a:b], lnw.indirect(LN), lk + " " + k("ln"), k("sqb"), AF.Square, H, bias=592.0)
+            act(T.b16[:, a:b], lnw.indirect(LN), lk + " " + k("ln"), k("b16_"), n=H)
             for c, of in enumerate((-2.484375, -10951.484375)):
-                mv("tt", T.tt[:, c, a:b], T.sq[:, c, a:b], k("sq" + "ab"[c]), k("tt" + "ab"[c]), 0.03125, of)
+                mv("s", T.tt[:, c, a:b], T.sq[:, c, a:b], k("sq" + "ab"[c]), k("tt" + "ab"[c]), 0.03125, of)
             ts(T.cc[:, :, a:b], T.tt[:, :, a:b], W - 1, Op.bitwise_and, k("tta ttb"), k("cc"))
-            mv("l12", T.l12[:, :, a:b], T.cc[:, :, a:b], k("cc"), k("li"))
+            mv("s", T.l12[:, :, a:b], T.cc[:, :, a:b], k("cc"), k("li"))
             pe([mm(T.psv[0:H, h, 0:384], T.b16[:, a:b], C("bi"), True, False)], "bi0 bi1 bi2 " + k("b16_"), k("psv"))
         for h in (0, 1):
             for c in (0, 1):
@@ -545,49 +651,48 @@ def rank_program(g, core, T, topo):
         pe([mm(T.psd[:, 0:K], C("id"), C("bm"), True, False), mm(T.psd[:, 0:K], C("se"), T.g2[:], False, False)], "id bm se g2", "psd")
         lower("eqo", T.psd, "psd")
         scan(T.scd[:], T.psd[:, 0:K], "psd", "scd")
-        ts(C("cand"), T.scd[:, 15:K:16], -1.0, Op.is_equal, "scd", "cand")
-        op("v", [lambda: v.tensor_tensor_scan(C("exb", 1, 13), C("one", 0, 12), C("cand"), 0.0, Op.mult, Op.add)], "one cand", "exb", 0.09)
+        act(C("cand"), T.scd[:, 15:K:16], "scd", "cand", AF.Relu, scale=-1.0)
+        op("v", [lambda: v.tensor_tensor_scan(C("exb", 1, 13), C("one", 0, 12), C("cand"), 0.0, Op.mult, Op.add)], "one cand", "exb", VFIX + 64 * CYC)
         pe([mm(T.psd[:, 400:412], C("btr"), C("cand"), True, False), mm(T.psd[:, 400:412], C("bl"), C("exb", 0, 12), False, True)], "btr cand bl exb", "psd")
-        ts(C("nrq"), T.psd[:, 400:412], CAP - 256.0, Op.is_gt, "psd", "nrq")
-        ts(C("lq"), T.psd[:, 400:412], CAP - 256.0, Op.is_gt, "psd", "lq")
-        tt(C("nqd"), C("nrq"), C("dm4"), Op.mult, "nrq dm4", "nqd")
-        tt(C("ld"), C("nqd"), T.sc[:, :, H + 15:K:16], Op.max, "nqd sc0 sc1", "ld")
-        act(T.nq[:], C("w01").indirect(C("lq")), "w01 lq", "nq", n=K)
+        act(C("nqd"), T.psd[:, 400:412], "psd", "nqd", AF.Relu, scale=OUT, bias=(256.0 - CAP) * OUT)
+        act(C("lq"), T.psd[:, 400:412], "psd", "lq", AF.Relu, bias=256.0 - CAP)
+        tt(C("w1"), C("nqd"), T.sc[:, :, H + 15:K:16], Op.add, "nqd sc0 sc1", "w1")
+        tt(C("ld"), C("w1"), C("dm4"), Op.min, "w1 dm4", "ld")
+        act(T.nq[:], C("w01").indirect(C("lq")), "w01 w02 lq", "nq", n=K)
         pe([mm(T.psk[:, 1, 0:K], C("slt", 128 * i, 128 * i + 128), T.pc[:, i:16 * K:16], i == 0, i == 15) for i in range(16)], keys("slt", 16) + " pc0 pc1", "psk1")
-        mv("msg", T[msg][:, 0:K], T.psk[:, 1, 0:K], "psk1", msg)
+        mv("s", T[msg][:, 0:K], T.psk[:, 1, 0:K], "psk1", msg)
         same("eqt", T.rt, "rt0 rt1", own(0), "sc0 sc1", 3.0)
         pe([mm(T.psk[:, 0, 0:K], C("id"), C("bm4"), True, False), mm(T.psk[:, 0, 0:K], C("id4"), T.hh[:], False, False),
             mm(T.psk[:, 0, 0:K], C("idm"), T.rt[:], False, False)], "id bm4 id4 hh0 hh1 idm rt0 rt1", "psk0")
-        lower("eqt", T.psk[:, 0, :], "psk0")
+        lower("eqt", T.psk[:, 0, :], "psk0", False)
+        pe([mm(T.psk[:, 0, 0:K], C("idu", 512, 640), T.nq[:], False, True)], "idu4 nq", "psk0")
         scan(T.scm[:], T.psk[:, 0, 0:K], "psk0", "scm")
-        tt(C("w1"), C("nqd"), T.scm[:, 15:K:16], Op.max, "nqd scm", "w1")
-        tt(T[msg][:, K:K + 12], C("w1"), C("dm1"), Op.min, "w1 dm1", msg + "l")
+        tt(T[msg][:, K:K + 12], T.scm[:, 15:K:16], C("dm1"), Op.min, "scm dm1", msg + "l")
         mk = msg + " " + msg + "l"
         if t == 0:
-            arrives("ru1", NE, "up1", 5.0, send(T[msg][:, 0:K + 12], mk, r - 1, T.up1[:], "ru1", "ls6"))
-            arrives("ru2", NE, "up2", 5.0, send(T[msg][:, 0:K + 12], mk, r - 2, T.up2[:], "ru2", "ls7"))
+            arrives("ru1", NE, "up1", FAR, send(T[msg][:, 0:K + 12], mk, r - 1, T.up1[:], "ru1", "ls6"))
+            arrives("ru2", NE, "up2", FAR, send(T[msg][:, 0:K + 12], mk, r - 2, T.up2[:], "ru2", "ls7"))
         elif t == 1:
-            arrives("ru3", NE, "up3", 5.0, send(T[msg][:, 0:K + 12], mk, r - 1, T.up3[:], "ru3", "ls8"))
-        arrives("rh%d" % j, NE, "hm%d" % j, 5.0, send(T[msg][:, 0:K + 12], mk, r + 1 + t, T["hm%d" % j][:], "rh%d" % j, "ls%d" % (9 + t)))
-        if t:
+            arrives("ru3", NE, "up3", FAR, send(T[msg][:, 0:K + 12], mk, r - 1, T.up3[:], "ru3", "ls8"))
+        arrives("rh%d" % j, NE, "hm%d" % j, FAR, send(T[msg][:, 0:K + 12], mk, r + 1 + t, T["hm%d" % j][:], "rh%d" % j, "ls%d" % (9 + t)))
+        if t == 0:
+            hand_on(2)
+        else:
             apply("hm%d" % t, "lh", "lo0")
         pe([mm(T.psk[:, 1, 0:K], C("sa"), T.at[:], True, False), mm(T.psk[:, 1, 0:K], C("dg1"), T.g2[:], False, False),
             mm(T.psk[:, 1, 0:K], C("row", 128 * t, 128 * t + 128, 96, 97), C("one", 0, K, 96, 97), False, True)], "sa0 sa1 at dg1 g2 rowm%d one" % t, "psk1")
-        act(T.v2[:], T.psk[:, 1, 0:K], "psk1", "v2")
+        mv("s", T.v2[:], T.psk[:, 1, 0:K], "psk1", "v2")
         cp(T.xw[:].indirect(C("ld")), T.at[:], "ld at", XW, -K)
         cp(T.pw[:].indirect(C("ld")), T.v2[:], "ld v2", PW, -K)
-        tt(T.qs[:], T.xw[:, 0:W].indirect(LO), T.q[:], Op.add, XW + " lo0 lo1 q", "qs", K)
-        act(T.qb[:], T.qs[:], "qs", "qb", AF.Copy, scale=0.5, bias=127.8125)
-        act(T.q[:], T.qb[:], "qb", "q", AF.Copy, bias=-128.0)
-        if t < RO - 1:
-            for i in range(16):
-                o = T.qrep[:, i:16 * K:16]
-                if i < QG:
-                    gop(lambda o=o: g.affine_select(o, T.q[:], [[0, K]], Op.is_ge, 0.0, 0, 0), "q", "qr%d" % i, K)
-                elif i < QG + QS:
-                    act(o, T.qb[:], "qb", "qr%d" % i, AF.Copy, bias=-128.0)
-                else:
-                    ts(o, T.qb[:], -128.0, Op.add, "qb", "qr%d" % i)
+        act(T.xo[:], T.xw[:, 0:W].indirect(LO), XW + " lo0 lo1", "xo", n=K)
+        pe([mm(T.psk[:, 0, 0:K], C("id"), T.q[:], True, False), mm(T.psk[:, 0, 0:K], C("id"), T.xo[:], False, True)], "id q xo", "psk0")
+        mv("s", T.qb[:], T.psk[:, 0, 0:K], "psk0", "qb", 0.5, 127.8125)
+        mv("s", T.q[:], T.qb[:], "qb", "q", bias=-128.0)
+        for i in range(16 if t < RO - 1 else 0):
+            if i < QG:
+                mv("g", T.qrep[:, i:16 * K:16], T.q[:], "q", "qr%d" % i)
+            else:
+                mv("s" if i < 2 * QG else "v", T.qrep[:, i:16 * K:16], T.qb[:], "qb", "qr%d" % i, bias=-128.0)
         for h in (0, 1):
             nn = lambda f: T.nn[0:H, h, 128 * f:128 * f + 128]
             ts(T.nn[0:H, h, 128:384], T.psv[0:H, h, 128:384], 0.0, Op.not_equal, "psv%d" % h, "nna%d" % h)
@@ -604,32 +709,35 @@ def rank_program(g, core, T, topo):
         tt(T.sg[:], T.psm[:, 0:K], T.dc[:], Op.max, "psm pk dc", "sg")
         pe([mm(T.psg[:, 0:K], C("id"), T.nq[:], True, False), mm(T.psg[:, 0:K], C("tri"), T.nr[:], False, True)], "id nq tri nr", "psg")
         act(T.psu[:, K:2 * K], T.psg[:, 0:K], "psg psu", "psu", AF.Relu, scale=-1.0)
-        act(T.sh[:], T.sg[:], "sg", "sh", AF.Copy, bias=-2048.0)
+        mv("s", T.sh[:], T.sg[:], "sg", "sh", bias=-2048.0)
         act(T.fst[:], T.psg[:, 0:K], "psg", "fst", AF.Relu, scale=-1.0)
         cp(T.fw[:].indirect(C("ld")), T.sg[:], "ld sg", FW, -K)
         ts(T.ci[:], T.fw[:, 0:W].indirect(LO), W - 1, Op.bitwise_and, FW + " lo0 lo1", "ci", n=K)
         if t < RO - 1:
-            mv("lc", T.lc[:], T.ci[:], "ci", "lc")
-            mv("c16", T.c16[:], T.ci[:], "ci", "c16", bias=-2048.0)
+            mv("s", T.lc[:], T.ci[:], "ci", "lc")
+            mv("s", T.c16[:], T.ci[:], "ci", "c16", bias=-2048.0)
         else:
-            mv("lc", T.cf[:], T.ci[:], "ci", "cf")
+            mv("s", T.cf[:], T.ci[:], "ci", "cf")
         tt(T.x1[:], T.psu[:, K:2 * K], T.sh[:], Op.mult, "psu sh", "x1")
-        tt(T.x2[:], T.psu[:, K:2 * K], T.b16[:], Op.mult, "psu b16_0 b16_1", "x2")
+        o = T.psv[:, 0, K:2 * K]
+        pe([mm(o, C("row", 0, 128, 64, 65), C("one", 0, K, 64, 65), True, False), mm(o, C("id"), T.b16[:], False, False),
+            mm(o, C("idu", 128, 256), T.nq[:], False, False), mm(o, C("tr8"), T.nr[:], False, True)], "rowu0 one id b16_0 b16_1 idu1 nq tr8 nr", "psv0")
+        act(T.x2[:], o, "psv0", "x2", AF.Relu)
         place = lambda o, sp: [mm(o, C("id"), C("bmc"), True, False), mm(o, C("bn8"), T.fst[:], False, False), mm(o, C("bl"), T.x1[:], False, sp)]
         pe(place(T.psv[:, 1, 0:K], True), "id bmc bn8 fst bl x1", "psv1")
         pe([mm(T.psv[:, 0, 0:K], C("bl"), T.x1[:], True, True)], "bl x1", "psv0")
         pe(place(T.psd[:, 0:K], False), "id bmc bn8 fst bl x1", "psd")
         scan(T.scc[:], T.psv[:, 1, 0:K], "psv1", "scc")
-        act(T.rc[:], T.psv[:, 0, 0:K], "psv0", "rc")
+        mv("s", T.rc[:], T.psv[:, 0, 0:K], "psv0", "rc")
         tt(C("lp"), T.scc[:, 15:K:16], C("dm4"), Op.min, "scc dm4", "lp")
         same("eqo", T.rc, "rc", lambda kb: T.scc[:, 16 * kb + 15:16 * kb + 16], "scc")
         lower("eqo", T.psd, "psd")
         act(T.g1[:], T.pw[:].indirect(C("lp")), PW + " lp", "g1", n=K)
         pe([mm(T.psg[:, 0:K], C("vr"), T.x2[:], True, False), mm(T.psg[:, 0:K], C("row", 384, 512, p1=1), C("one", 0, K, p1=1), False, False),
             mm(T.psg[:, 0:K], C("dgc", 128 * t, 128 * t + 128), T.g1[:], False, True)], "vr x2 rowc0 rowc1 one dgc%d0 dgc%d2 g1" % (t, t), "psg")
-        act(T.v1[:], T.psg[:, 0:K], "psg", "v1")
+        mv("s", T.v1[:], T.psg[:, 0:K], "psg", "v1")
         if t < RO - 1:
-            disk_window(j + 1, "g1")
+            mv("g", T["lw%d" % (j + 1)][:, 0:M], T["lu%d" % (j + 1)][:], "lu%d g1" % (j + 1), "lw%d" % (j + 1))
         scan(T.scd[:], T.psd[:, 0:K], "psd", "scd")
         tt(C("lcl"), T.scd[:, 15:K:16], C("dm4"), Op.min, "scd dm4", "lcl")
         cp(T.pw[:].indirect(C("lcl")), T.v1[:], "lcl v1", PW, -K)

@@ -1,25 +1,32 @@
 from concourse.mybir import AluOpType as Op, ActivationFunctionType as AF
 
 W, M, K, CAP, RO, N = 4096, 1024, 192, 160, 3, 8
-H = 96
+CUT = (0, 96, K)
+PIECES = (1, 1, 1, 1, 1, 1)
+XCUT = (0, 1536, 2560, 3584, W)
+LCUT, LQ, LW = 768, "g", "gs"
+LOADS = "tgs lfi0 cxi q pt xw0 xw1 xw2 xw3 lfi1 fwl0 fwl1 xlh fwl2 fwl3"
+HINT = ("",) * 8
+SPLIT, SEED, ROAM, BULK, VLOAD = 2, 3, 6, 9.0, 0.05
+SWEEPS, WIDE, RQ = 4, 140, "vv"
 BIG = 65536.0
 RES = 67108864.0
 OUT = 8192.0
 NE = 8
 QG = 5
-WAKE, LAG, VFIX, SFIX, CYC, PCYC, GATH, SCAT, FAR = 0.2, 0.05, 0.02, 0.04, 0.00083, 0.00045, 1.56, 3.8, 6.0
-PASSES, NOISE, TRIES, HEAT, EPS = 30, 1.0, 6000, 0.05, 0.5
+WAKE, LAG, VFIX, SFIX, CYC, PCYC, GATH, SCAT, FAR = 0.2, 0.05, 0.02, 0.04, 0.00083, 0.00045, 1.56, 3.8, 3.0
+PASSES, NOISE, TRIES, HEAT, EPS, REACH = 30, 1.0, 2500, 0.2, 0.05, 24
 
 _S = "sbuf"
 F32, B16, I32, U16, H16 = "float32", "bfloat16", "int32", "uint16", "float16"
 PACK = {
-    "tf": (F32, (("nqd", 12), ("w1", 12), ("dm4", 12), ("dm1", 12), ("er", 16), ("lt", 16), ("ec", 16), ("pmf", 4))),
-    "tl": (U16, (("ld", 12), ("lcl", 12), ("lp", 12), ("lq", 12))),
+    "tf": (F32, (("nqd", 12), ("w1", 12), ("w2", 12), ("dm4", 12), ("dm1", 12), ("er", 16), ("ec", 16), ("pmf", 4))),
+    "tl": (U16, (("ld", 12), ("lcl", 12), ("lp", 12), ("lk", 12))),
     "ti": (I32, (("dmi", 12), ("pmi", 4))),
     "tb": (B16, (("wm", 16), ("wp", 16), ("wm1", 24), ("wm2", 24), ("wp1", 24), ("wp2", 24), ("cand", 12), ("exb", 16))),
-    "cb": (B16, (("w01", 320), ("one", 256), ("zero", 256), ("bl", 128), ("bt", 128), ("rp", 256), ("id", 128), ("idu", 768), ("id4", 128), ("idm", 128), ("bi", 384), ("pb16", 128), ("nb16", 128),
-                 ("btr", 128), ("tri", 128), ("tr8", 128), ("bl8", 128), ("bn8", 128), ("sa", 128), ("wt", 128), ("se", 128), ("dg1", 128), ("dgc", 384), ("vr", 128), ("rq", 256),
-                 ("bm", K), ("bmc", K), ("bm4", K), ("ltk", 2048), ("slt", 2048), ("row", 512))),
+    "cb": (B16, (("one", 256), ("zero", 256), ("bl", 128), ("bt", 128), ("rp", 256), ("id", 128), ("idu", 768), ("id4", 128), ("idm", 128), ("bi", 384), ("sel", 1024), ("bj", 2048), ("gm", 128),
+                 ("btr", 128), ("tri", 128), ("tr8", 128), ("tr4", 128), ("cmp", 128), ("bl8", 128), ("bn8", 128), ("sa", 128), ("wt", 128), ("se", 128), ("dg1", 128), ("dgc", 384), ("vr", 128), ("up8", 128),
+                 ("bm", K), ("bmc", K), ("bm4", K), ("slt", 144), ("row", 512), ("c15", 128))),
 }
 PLACE, SCRATCH, ORDERS = {}, {}, {}
 for _b in PACK:
@@ -29,19 +36,19 @@ for _b in PACK:
         _o += _w
     SCRATCH[_b] = (_S, [128, _o], PACK[_b][0])
 for _d, _l in (
-    (B16, (("xw", W + K), ("xlh", M), ("q", K), ("qb", K), ("qrep", 16 * K), ("ma", 16 * K), ("mb", 16 * K), ("at", K), ("nr", K), ("nq", K), ("xo", K), ("fst", K),
-           ("xl1", M), ("xl2", M), ("xl3", M), ("xp1", 512), ("xp2", 512), ("xp3", 512), ("xlp", 512), ("xt", 512))),
-    (I32, (("fw", W + K), ("ci", K), ("tgs", 256), ("pci", 256), ("lfi", M), ("cxi", K), ("ic", 256))),
-    (U16, (("lfu", M), ("lc", K), ("lu1", M), ("lu2", M), ("lu3", M), ("msg1", K + 16), ("msg2", K + 16), ("msg3", K + 16), ("up1", K + 12), ("up2", K + 12), ("up3", K + 12),
-           ("hm1", K + 12), ("hm2", K + 12), ("hm3", K + 12))),
-    (F32, (("pw", W + K), ("lh", M + K), ("cf", K), ("scd", K), ("scm", K), ("scc", K), ("dc", K), ("sg", K), ("sh", K), ("v1", K), ("v2", K), ("s0", 256),
+    (B16, (("xw", W + K), ("xlh", M), ("q", K), ("qb", K), ("qrep", 16 * K), ("ma", 16 * K), ("mb", 16 * K), ("mc", 16 * K), ("at", K), ("nr", K), ("nq", K), ("xo", K), ("fst", K),
+           ("xl1", M), ("xl2", M), ("xl3", M))),
+    (I32, (("fw", W + K), ("ci", K), ("tgs", 256), ("pci", 256), ("lfi", M), ("cxi", K), ("ic", 256), ("ixi", 256))),
+    (U16, (("lfu", M), ("lc", K), ("lu1", M), ("lu2", M), ("lu3", M), ("lus", M), ("st", M), ("msg1", K + 16), ("msg2", K + 16), ("msg3", K + 16), ("up1", K + 12), ("up3", K + 12),
+           ("hm2", K + 12), ("hm3", K + 12))),
+    (F32, (("pw", W + K), ("lh", M + K), ("cf", K), ("sc", K), ("scd", K), ("scm", K), ("scc", K), ("dc", K), ("sg", K), ("v1", K), ("v2", K), ("s0", 256),
            ("lw1", M), ("lw2", M + K), ("lw3", M + K))),
-    (H16, (("pt", W), ("pcs", 512), ("pa", 16 * K), ("pb", 16 * K), ("pc", 16 * K), ("g1", K), ("g2", K), ("gt", K), ("b16", K), ("c16", K), ("x1", K), ("x2", K), ("rc", K),
-           ("ro", K), ("rt", K), ("hh", K))),
+    (H16, (("pt", W), ("pcs", 512), ("pa", 16 * K), ("pb", 16 * K), ("pc", 16 * K), ("g1", K), ("g2", K), ("lv", 24), ("b16", K), ("ixh", 256), ("x1", K), ("x2", K), ("rc", K),
+           ("hh", K), ("sh", K))),
 ):
     for _n, _w in _l:
         SCRATCH[_n] = (_S, [128, _w], _d)
-for _n, _w, _d in (("sc", K, F32), ("ll", 12, U16), ("sq", K, F32), ("tt", K, I32), ("cc", K, I32), ("l12", K, U16),
+for _n, _w, _d in (("rr", K, H16), ("cm", K, H16), ("ll", 12, U16), ("sq", K, F32), ("tt", K, I32), ("cc", K, I32), ("l12", K, U16),
                    ("t4", 256, I32), ("fi", 16, I32), ("fl", 16, H16), ("nn", 384, B16)):
     SCRATCH[_n] = (_S, [128, 2, _w], _d)
 SCRATCH["eqo"] = (_S, [128, 12, K], B16)
@@ -50,7 +57,7 @@ for _n in ("psk", "psv"):
     SCRATCH[_n] = ("psum", [128, 2, 512], F32)
 for _n in ("psm", "psu", "psd", "psg"):
     SCRATCH[_n] = ("psum", [128, 512], F32)
-SEMAPHORES = ["qv", "qs", "qp", "qg"] + ["ld%d" % j for j in range(20)] + ["ls%d" % j for j in range(20)] + ["rl0"]
+SEMAPHORES = ["qv", "qs", "qp", "qg"] + ["ld%d" % j for j in range(24)] + ["ls%d" % j for j in range(20)] + ["rl0", "rs"]
 SEMAPHORES += ["%s%d" % (a, j) for a in ("rl", "rx", "ru", "rh") for j in (1, 2, 3)]
 
 
@@ -134,21 +141,22 @@ def tracker(g, T):
         wr[key] = (sem, n, None)
         rd[key] = {}
 
-    nodes, alt = [], {}
+    nodes, alt, behind = [], {}, {}
 
     def op(q, fns, R, Wt, cost, other=None):
-        R, Wt = R.split(), Wt.split()
+        behind[len(nodes)] = [k[1:] for k in R.split() if k[0] == ">"]
+        R, Wt = [k for k in R.split() if k[0] != ">"], Wt.split()
         nodes.append((q, R, Wt, lambda: op_(q, fns, R, Wt), cost, 0.0, -1))
         if other:
             alt[len(nodes) - 1] = (other[0], R, Wt, lambda: op_(other[0], other[1], R, Wt), other[2], 0.0, -1)
 
     def dma(q, out, in_, R, Wt, kb):
         R, Wt = R.split(), Wt.split()
-        nodes.append((q, R, Wt, lambda: dma_(q, out, in_, R, Wt), kb / 190.0, 2.0, -1))
+        nodes.append((q, R, Wt, lambda: dma_(q, out, in_, R, Wt), kb / 190.0, 1.6, -1))
 
-    def send(call, R, local, n):
+    def send(call, R, local, n, on):
         R = R.split()
-        nodes.append(("g", R, [], lambda: send_(call, R, local, n), 0.3, 0.0, -2))
+        nodes.append(("g", R, [], lambda: on and send_(call, R, local, n), 0.3, 0.0, -2))
         return len(nodes) - 1
 
     def arrives(sem, n, key, lat, after):
@@ -161,6 +169,7 @@ def tracker(g, T):
         for x, (q, R, Wt, f, n, lat, after) in enumerate(nodes):
             if after >= 0:
                 dep[x].add(after)
+            behind[x] = [w[k] for k in behind.get(x, []) if k in w]
             for k in sorted(set(R + Wt)):
                 if k.startswith("ps"):
                     who = x if x in alt else q
@@ -193,6 +202,9 @@ def tracker(g, T):
                     nxt[d].append(x)
                 else:
                     succ[d].append(x)
+            for d in behind[x]:
+                prev[x].append(d)
+                nxt[d].append(x)
         cs = [nd_[4] for nd_ in nodes]
         lat = [nd_[5] + (0.0 if nd_[0] == "a" else WAKE) for nd_ in nodes]
         for q in "gd":
@@ -222,54 +234,76 @@ def tracker(g, T):
                 st[x] = e
             return st, max(st[x] + cs[x] + (0.0 if back else lat[x]) for x in range(nn))
 
-        def times(seq):
-            st, fin, free, last, why = [0.0] * nn, [0.0] * nn, dict.fromkeys("vspgda", 0.0), dict.fromkeys("vspgda", -1), [-1] * nn
-            for x in seq:
+        def times(seq, lo, hi, rest, old=None, i=0):
+            st, why, fin = (dict(old[1]), old[2][:], old[4][:]) if old else ({}, [-1] * nn, [0.0] * nn)
+            free, last = dict.fromkeys("vspgd", 0.0), dict.fromkeys("vspgd", -1)
+            todo = set("vspgd")
+            for j in range(i - 1, -1, -1):
+                x = seq[j]
+                if qof[x] in todo:
+                    todo.discard(qof[x])
+                    free[qof[x]], last[qof[x]] = st[x] + cs[x], x
+                    if not todo:
+                        break
+            for x in seq[i:hi]:
                 q, e, w = qof[x], 0.0, -1
                 for y in dl[x]:
                     if fin[y] > e:
                         e, w = fin[y], y
-                if q == "a":
-                    st[x], why[x] = e, w
-                else:
+                if q != "a":
                     if e > free[q]:
                         e += WAKE - LAG
                     else:
                         e, w = free[q], last[q]
-                    st[x], why[x], free[q], last[q] = e, w, e + cs[x], x
-                fin[x] = e + cs[x] + tail[x]
-            end = max(fin)
-            return end + EPS * sum(fin) / nn, st, why, fin.index(end)
+                    free[q], last[q] = e + cs[x], x
+                st[x], why[x], fin[x] = e, w, e + cs[x] + tail[x]
+            end, at = max([(fin[x] + rest[x], x) for x in seq[lo:hi]] + [(free[q] + rest[q], last[q]) for q in free])
+            return end + EPS * sum(fin[x] for x in seq[lo:hi]) / (hi - lo) + VLOAD * sum(cs[x] for x in seq[lo:hi] if qof[x] == "v"), st, why, at, fin
+
+        def beyond(seq, hi):
+            rest, left = dict.fromkeys(list(range(nn)) + list("vspgda"), 0.0), {}
+            for x in reversed(seq):
+                rest[x] = max([0.0] + [left[y] + (qof[y] != "a") * (WAKE - LAG) for y in succ[x] if y in left])
+                if len(left) < nn - hi:
+                    left[x] = cs[x] + max(tail[x] + rest[x], rest[qof[x]])
+                    rest[qof[x]] = left[x] * (qof[x] != "a")
+            return rest
 
         def swap(x):
             nodes[x], alt[x] = alt[x], nodes[x]
             qof[x], cs[x] = nodes[x][0], nodes[x][4]
 
-        def polish(st):
-            seq = sorted(range(nn), key=lambda x: (st[x], x))
-            cur = best = times(seq)
-            bseq, bq, rnd = seq, list(qof), 7
+        def polish(seq, lo, hi, heat, rnd):
+            rest, inside = beyond(seq, hi), set(seq[lo:hi])
+            cur = best = times(seq, lo, hi, rest)
+            bseq, bq = seq, list(qof)
             for it in range(TRIES):
                 path, x = [], cur[3]
-                while x >= 0:
+                while x in inside:
                     y = cur[2][x]
-                    if y >= 0 and qof[y] == qof[x] and y not in dep[x] and y not in prev[x]:
+                    if y in inside and qof[y] == qof[x] and y not in dp[x]:
                         path.append((y, x))
                     x = y
-                if not path:
-                    break
                 rnd = (rnd * 1103515245 + 12345) % 2147483648
+                if (rnd >> 4) % 16 < ROAM or not path:
+                    j = lo + (rnd >> 8) % (hi - lo)
+                    i = j - 1
+                    while i >= lo and qof[seq[i]] != qof[seq[j]]:
+                        i -= 1
+                    if i < lo or qof[seq[j]] not in "vspg" or seq[i] in dp[seq[j]]:
+                        continue
+                    path = [(seq[i], seq[j])]
                 y, x = path[(rnd >> 8) % len(path)]
                 turn = [z for z in (x, y) if z in alt and (rnd >> 20) % 3 == 0][:1]
                 for z in turn:
                     swap(z)
                 i, j = seq.index(y), seq.index(x)
                 rnd = (rnd * 1103515245 + 12345) % 2147483648
-                more = (rnd >> 8) % 4
+                more = (rnd >> 8) % 4 if (rnd >> 16) % 4 else (rnd >> 8) % REACH
                 if turn:
                     new = seq
                 elif (rnd >> 12) % 2:
-                    while more and i > 0:
+                    while more and i > lo:
                         i -= 1
                         more -= qof[seq[i]] == qof[x]
                     need = {x}
@@ -278,7 +312,7 @@ def tracker(g, T):
                             need.add(z)
                     new = seq[:i] + [z for z in seq[i:j + 1] if z in need] + [z for z in seq[i:j + 1] if z not in need] + seq[j + 1:]
                 else:
-                    while more and j < nn - 1:
+                    while more and j < hi - 1:
                         j += 1
                         more -= qof[seq[j]] == qof[x]
                     need = {y}
@@ -286,18 +320,21 @@ def tracker(g, T):
                         if any(u in need for u in dp[z]):
                             need.add(z)
                     new = seq[:i] + [z for z in seq[i:j + 1] if z not in need] + [z for z in seq[i:j + 1] if z in need] + seq[j + 1:]
-                tr = times(new)
+                tr = times(new, lo, hi, rest, cur, i)
                 rnd = (rnd * 1103515245 + 12345) % 2147483648
-                if tr[0] < cur[0] + HEAT * (1.0 - it / TRIES) * (rnd >> 8) / 8388608:
+                if tr[0] < cur[0] + heat * (1.0 - it / TRIES) * (rnd >> 8) / 8388608:
                     cur = tr
-                    pos = {z: n for n, z in enumerate(new)}
-                    seq = sorted(new, key=lambda z: (tr[1][z], pos[z]))
+                    seq = new[:lo] + sorted(new[lo:hi], key=tr[1].get) + new[hi:]
                     if tr[0] < best[0]:
                         best, bseq, bq = tr, seq, list(qof)
                 else:
                     for z in turn:
                         swap(z)
-            return bseq, bq
+            for x in alt:
+                if qof[x] != bq[x]:
+                    swap(x)
+            st = times(bseq, 0, nn, beyond(bseq, nn))[1]
+            return sorted(bseq, key=st.get)
         qof = [nd_[0] for nd_ in nodes]
         dl = [sorted(d) for d in dep]
         dp = [dl[x] + prev[x] for x in range(nn)]
@@ -323,8 +360,17 @@ def tracker(g, T):
                     seed = (seed * 1103515245 + 12345) % 2147483648
                     key[x] = max([bk[x] + cs[x] + shake * seed / 2147483648] + [key[y] + 1e-6 for y in sl[x]])
                 order = sorted(range(nn), key=lambda x: (-key[x], x))
-            ORDERS[alike] = polish(best[1])
-        seq, queue = ORDERS[alike]
+            seq = sorted(range(nn), key=lambda x: (best[1][x], x))
+            for rnd in range(SWEEPS):
+                for lo in range(-WIDE // 2 + rnd % 2 * WIDE // 4, nn - WIDE // 2, WIDE // 2):
+                    seq = polish(seq, max(lo, 0), min(lo + WIDE, nn), HEAT * (1.0 - rnd / SWEEPS), SEED + lo + rnd)
+            best = times(seq, 0, nn, beyond(seq, nn))
+            path, x = [], best[3]
+            while x >= 0:
+                path.append((round(best[1][x], 1), qof[x], nodes[x][2][:1]))
+                x = best[2][x]
+            ORDERS[alike] = (seq, list(qof), max(best[4]), path[::-1])
+        seq, queue = ORDERS[alike][0:2]
         for x in seq:
             if qof[x] != queue[x]:
                 swap(x)
@@ -362,7 +408,7 @@ def rank_program(g, core, T, topo):
         return VFIX + CYC * max(64, per * wid(o))
 
     def ncost(n, fix=VFIX):
-        return fix + CYC * (GATH * n if n > 0 else -SCAT * n)
+        return fix + 0.03 + CYC * (GATH * n if n > 0 else -SCAT * n)
 
     def tt(o, a, b, f, R, Wt, n=0):
         op("v", [lambda: v.tensor_tensor(o, a, b, f)], R, Wt, ncost(n) if n else VFIX + CYC * max(64, wid(o) * (1 if "ps" in R else 2)))
@@ -393,6 +439,12 @@ def rank_program(g, core, T, topo):
         x, y = (on_s, on_v) if q == "s" else (on_v, on_s)
         op(x[0], x[1], R, Wt, x[2], y)
 
+    def relu(q, o, a, R, Wt, scale=1.0, bias=0.0):
+        on_s = ("s", [lambda: s.activation(o, a, AF.Relu, scale=scale, bias=bias)], SFIX + CYC * max(64, wid(o)))
+        on_v = ("v", [lambda: v.tensor_scalar(o, a, bias or scale, 0.0, Op.add if bias else Op.mult, Op.max)], vcost(o, a))
+        x, y = (on_s, on_v) if q == "s" else (on_v, on_s)
+        op(x[0], x[1], R, Wt, x[2], y)
+
     def mm(o, l, x, st, sp):
         return (lambda: p.matmul(o, l, x, st, sp), PCYC * max(64, wid(x)))
 
@@ -405,31 +457,36 @@ def rank_program(g, core, T, topo):
     def gop(f, R, Wt, n):
         op("g", [f], R, Wt, 0.17 + 2 * CYC * n)
 
-    def send(src, key, dst_rank, dst, sem, local, bulk=False):
+    def send(src, key, dst_rank, dst, sem, local, bulk=False, on=True):
         dst_core = T.cores[dst_rank % N]
         rid, pid = topo.addr(dst_core)[0:2]
         eng = topo.engines(core, dst_core)
         eng = eng[-NE:] if bulk else eng[0:NE]
-        return put(lambda: g.remote_dma(dst, src, T.sem[sem], T.sem[local], pid, rid, sum(1 << e for e in eng)), key, local, len(eng))
+        return put(lambda: g.remote_dma(dst, src, T.sem[sem], T.sem[local], pid, rid, sum(1 << e for e in eng)), key, local, len(eng), on)
 
     PW = keys("pw", 8) + " pwd"
     XW = keys("xw", 4)
-    FW = "fwl " + keys("fw", 4)
+    FW = keys("fwl", 4) + " " + keys("fw", 4)
     QR = keys("qr", 16)
-    dma("d", T.lfi[:, 0:512], T.lf[:, 0:512], "", "lfi0", 256)
-    dma("d", T.tgs[:], T.tg[:], "", "tgs", 128)
-    dma("d", T.cxi[:], T.cx[:], "", "cxi", 96)
-    dma("d", T.q[:], T.qx[:], "", "q", 48)
-    dma("d", T.xw[:, 0:1024], T.xr[:, 0:1024], "", "xw0", 256)
-    ts(T.pci[:], T.tgs[:], 1, Op.bitwise_and, "tgs", "pci")
-    for j, (n, src) in enumerate((("tgs", T.tgs), ("pci", T.pci))):
-        mv("s", T.pcs[:, 256 * j:256 * j + 256], src[:], n, "pcs%d" % j)
-        dma("d", T.pt[8 * j:8 * j + 8, :], T.pcs[:, 256 * j:256 * j + 256], "pcs%d" % j, "pt%d" % j, 64)
-    for c, (a, b) in enumerate(((1024, 2560), (2560, 3584), (3584, W))):
-        dma("d", T.xw[:, a:b], T.xr[:, a:b], "", "xw%d" % (c + 1), (b - a) / 4)
-    dma("d", T.lfi[:, 512:M], T.lf[:, 512:M], "", "lfi1", 256)
-    dma("d", T.xlh[:], T.xl[:], "", "xlh", 256)
-    dma("d", T.fw[:, 0:2048], T.fd[:], "", "fwl", 1024)
+    def tags():
+        gop(lambda: g.iota(T.ixi[0:16, :], [[1, 256]], -2048, 256), "", "ixi", 256)
+        mv("s", T.ixh[0:16, :], T.ixi[0:16, :], "ixi", "ixh")
+        dma("d", T.pt[16:17, :], T.ixh[0:16, :], "ixh", "pt2", 8)
+        ts(T.pci[:], T.tgs[:], 1, Op.bitwise_and, "tgs", "pci")
+        for j, (n, src) in enumerate((("tgs", T.tgs), ("pci", T.pci))):
+            mv("s", T.pcs[:, 256 * j:256 * j + 256], src[:], n, "pcs%d" % j)
+            dma("d", T.pt[8 * j:8 * j + 8, :], T.pcs[:, 256 * j:256 * j + 256], "pcs%d" % j, "pt%d" % j, 64)
+    parts = {"tgs": (T.tgs[:], T.tg[:], 128), "cxi": (T.cxi[:], T.cx[:], 96), "q": (T.q[:], T.qx[:], 48), "xlh": (T.xlh[:], T.xl[:], 256),
+             "lfi0": (T.lfi[:, 0:LCUT], T.lf[:, 0:LCUT], LCUT / 2), "lfi1": (T.lfi[:, LCUT:M], T.lf[:, LCUT:M], (M - LCUT) / 2)}
+    for c in range(4):
+        a, b = XCUT[c:c + 2]
+        parts["xw%d" % c] = (T.xw[:, a:b], T.xr[:, a:b], (b - a) / 4)
+        parts["fwl%d" % c] = (T.fw[:, 512 * c:512 * c + 512], T.fd[:, 512 * c:512 * c + 512], 256)
+    for n in LOADS.split():
+        if n == "pt":
+            tags()
+        else:
+            dma("d", parts[n][0], parts[n][1], "", n, parts[n][2])
     fill(C("one"), 1.0, "one")
     fill(C("zero"), 0.0, "zero")
     gop(lambda: g.iota(C("pmi", 0, 1), [[0, 1]], 0, 1), "", "pmi", 1)
@@ -443,7 +500,9 @@ def rank_program(g, core, T, topo):
     def diag(n, a, w, src="zero", key=None):
         gop(lambda: g.affine_select(C(n, a, a + 128), C(src, 0, 128), [[-1, 128]], Op.not_equal, w, 0, 1), src, key or n, 128)
     diag("id", 0, 1.0)
-    diag("btr", 0, -255.0, "bt")
+    ts(C("bl8"), C("bl"), OUT, Op.mult, "bl", "bl8")
+    gop(lambda: g.affine_select(C("up8"), C("bl8"), [[1, 128]], Op.is_gt, 0.0, 0, -1), "bl8", "up8", 128)
+    diag("btr", 0, -255.0 * OUT, "up8")
     diag("tri", 0, -1.0, "bt")
     E = lambda i: C("er", i, i + 1)
     D = lambda i, p1=128: C("ec", i, i + 1, p1=p1)
@@ -456,11 +515,15 @@ def rank_program(g, core, T, topo):
             act(o, a, R, Wt, scale=w)
         else:
             ts(o, a, w, Op.mult, R, Wt)
-    ts(D(9), C("pmi", 0, 1), 24.0, Op.is_equal, "pmi", "ec9", 2048.0, Op.mult)
+
+    def scaled(n, a, w, key):
+        o = C(n, a, a + 128)
+        op("g", [lambda: g.affine_select(o, C("zero", 0, 128), [[-1, 128]], Op.not_equal, w, 0, 1)], "id zero", key, 0.17 + 256 * CYC,
+           ("v", [lambda: v.tensor_scalar(o, C("id"), w, None, Op.mult)], VFIX + 64 * CYC))
+    ts(D(9), C("pmi", 0, 1), 16.0, Op.is_equal, "pmi", "ec9")
     ts(C("pmi", 1, 2), C("pmi", 0, 1), 15, Op.bitwise_and, "pmi", "pmj")
     cp(PM, C("pmi", 1, 2), "pmj", "pmf")
     ts(C("er"), T.ic[:, 0:16], PM, Op.is_equal, "ic pmf", "er")
-    ts(C("lt"), T.ic[:, 0:16], PM, Op.is_gt, "ic pmf", "lt", OUT, Op.mult)
     ts(D(1), E(2), -0.5, Op.mult, "er", "ec1")
     ts(D(0), E(0), 0.5, Op.mult, "er ec1", "ec0", D(1), Op.add)
     ts(D(2), E(1), E(3), Op.add, "er", "ec2", 32768.0, Op.mult)
@@ -470,46 +533,51 @@ def rank_program(g, core, T, topo):
     ts(D(5), PM, 4.0, Op.is_ge, "pmf", "ec5")
     ts(D(7), D(5), E(3), Op.add, "ec5 er", "ec7", E(1), Op.add)
     ts(D(8), D(0), 2.0, Op.mult, "ec0", "ec8")
+    ts(D(10), D(2), E(7), Op.add, "er ec2", "ec10")
     for n in ("sa", "wt", "vr", "slt", "row"):
         fill(C(n), 0.0, n)
+    times(C("wt", 7, 128, p1=32, st=16), C("one", 0, 8, p1=32), D(9, 32), "one ec9 wt", "wt2")
+    times(C("slt", 15, 143, st=16), b8, D(0), "bl ec0 slt", "slt")
+    fill(C("c15", p1=1), 1.5, "c15")
+    for i in range(max(CUT[1], K - CUT[1]) // 16):
+        gop(lambda i=i: g.affine_select(C("sel", 128 * i, 128 * i + 128), C("one", 0, 128), [[0, 8], [-1, 16]], Op.is_equal, 0.0, -16 * i, 1), "one", "sel%d" % i, 128)
+    for i in range(16):
+        times(C("bj", 128 * i, 128 * i + 128), C("bl"), E(i), "bl er", "bj%d" % i)
+    ts(D(15), C("pmi", 0, 1), PM, Op.subtract, "pmi pmf", "ec15", 0.125, Op.mult)
+    ts(C("gm"), T.ic[:, 0:256:2], D(15), Op.not_equal, "ic ec15", "gm", BIG, Op.mult)
+    ts(C("gm"), C("gm"), 2048.0, Op.add, "gm", "gm")
     for j in (0, 1):
         times(C("sa", 1 + 2 * j, 128, st=16), b8, 1.0, "bl sa", "sa%d" % j)
         times(C("wt", 2 * j, 128, p1=32, st=16), RP(j, 16), 1.0, "rp wt", "wt%d" % j)
         times(C("wm", 8 * j, 8 * j + 8), b8, -131072.0, "bl", "wm%d" % j)
-        times(C("wp", 8 * j, 8 * j + 8), b8, D((6, 2)[j]), "bl ec2 ec6", "wp%d" % j)
+        times(C("wp", 8 * j, 8 * j + 8), b8, D((6, 10)[j]), "bl ec10 ec6", "wp%d" % j)
         ts(C("row", 128 * j, 128 * j + 128, p1=1), T.ic[0:1, 0:128], 4096.0, Op.mult, "ic row", "rowa%d" % j, 2048.0 * j, Op.add)
-        ts(C("rq", 128 * j, 128 * j + 128, p1=32), RP(j), D(9, 32), Op.add, "rp ec9", "rq%d" % j)
-        ts(C("row", 128 * j, 128 * j + 128, 64, 65), C("one", 0, 128, 64, 65), (-OUT, OUT)[j], Op.mult, "one row", "rowu%d" % j)
+        ts(C("row", 128 * j, 128 * j + 128, 64, 65), C("one", 0, 128, 64, 65), (-OUT, -2048.0)[j], Op.mult, "one row", "rowu%d" % j)
         cp(C("row", 384 + 2 * j, 512, p1=1, st=16), C("one", 0, 8, p1=1), "one row", "rowc%d" % j)
     fill(T.pw[:, W:W + K], 0.0, "pwd")
     cp(T.lc[:], T.cxi[:], "cxi", "lc")
-    ts(T.c16[:], T.cxi[:], -2048.0, Op.add, "cxi", "c16")
     for i in range(16):
         mv("vs"[i % 2], T.qrep[:, i:16 * K:16], T.q[:], "q", "qr%d" % i)
     ts(T.s0[:], T.ic[:], 0.0, Op.is_equal, "ic", "s0", RES, Op.mult)
     ts(C("bm"), T.ic[:, 0:K], PM, Op.not_equal, "ic pmf", "bm", BIG, Op.mult)
-    ts(C("bmc"), C("bm"), OUT + 2048.0, Op.add, "bm", "bmc")
-    ts(C("bm4"), C("bm"), -4096.0, Op.add, "bm", "bm4")
-    cp(T.gt[0:32, :], C("one", 0, K, p1=32), "one", "gt0 gt1")
-    fill(C("w01", 0, 1), 0.0, "w01")
-    fill(C("w01", 1), 1.0, "w02")
+    ts(C("bmc"), C("bm"), OUT + 34816.0, Op.add, "bm", "bmc")
+    ts(C("bm4"), C("bm"), -5120.0, Op.add, "bm", "bm4")
     for j, w in enumerate((0.0, -1.0, -1.0)):
-        times(C("bi", 128 * j, 128 * j + 128), C("id"), w, "id", "bi%d" % j)
+        scaled("bi", 128 * j, w, "bi%d" % j)
     for nm, cols in (("wm1", (2.0, 0.0, 0.0)), ("wm2", (-2.0, 0.0, 0.0)), ("wp1", (D(3), D(0), 0.0)), ("wp2", (E(3), 0.0, D(0)))):
         for j, w in enumerate(cols):
             times(C(nm, 8 * j, 8 * j + 8), b8, w, "bl er ec0 ec3", "%s_%d" % (nm, j))
-    for n, w in (("pb16", 16.0), ("nb16", -16.0), ("id4", 4.0), ("idm", -0.5)):
-        times(C(n), C("id"), w, "id", n)
-    for j, w in enumerate((2.0, -1.0, 0.5, -2.0, 1.0, -0.5)):
-        times(C("idu", 128 * j, 128 * j + 128), C("id"), w * OUT, "id", "idu%d" % j)
+    for n, w in (("id4", 4.0), ("idm", -0.5)):
+        scaled(n, 0, w, n)
+    for j, w in enumerate((-2.0, 1.0, 0.5, 2.0, -1.0, -0.5)):
+        scaled("idu", 128 * j, w * OUT, "idu%d" % j)
     times(C("tr8"), C("tri"), -OUT, "tri", "tr8")
-    times(C("bl8"), C("bl"), OUT, "bl", "bl8")
-    times(C("bn8"), C("bl"), -OUT, "bl", "bn8")
+    times(C("tr4"), C("tri"), -4096.0, "tri", "tr4")
+    ts(D(11), PM, -4096.0, Op.mult, "pmf", "ec11", 14 * 4096.0, Op.add)
+    times(C("cmp"), C("bl"), D(11), "bl ec11", "cmp")
+    times(C("bn8"), C("bl"), 2048.0 - OUT, "bl", "bn8")
+    mv("s", C("lk"), C("dmi"), "dmi", "lk", 0.0625)
     times(C("se"), C("bl"), D(4), "bl ec4", "se")
-    for k in range(16):
-        if k:
-            times(C("ltk", 128 * k, 128 * k + 128), C("bl"), C("lt", k, k + 1), "bl lt", "ltk%d" % k)
-        times(C("slt", 128 * k + k, 128 * k + 128, st=16), b8, D(0), "bl ec0 slt", "slt%d" % k)
     ts(C("dm4"), C("dmi"), PM, Op.add, "dmi pmf", "dm4", float(W), Op.add)
     ts(C("dm1"), C("dmi"), PM, Op.add, "dmi pmf", "dm1", float(M), Op.add)
     fill(C("exb"), 0.0, "exb")
@@ -522,48 +590,35 @@ def rank_program(g, core, T, topo):
         times(C("dgc", 128 * t, 128 * t + 128), C("id"), D(7), "id ec7", "dgc%d" % t)
         for j in (0, 2):
             times(C("dgc", 128 * t + j, 128 * t + 128, st=16), b8, D(12 + t), "bl ec%d dgc%d" % (12 + t, t), "dgc%d%d" % (t, j))
-    banks = (("psv0", T.psv[:, 0, :]), ("psv1", T.psv[:, 1, :]), ("psm", T.psm[:]), ("psu", T.psu[:]), ("psd", T.psd[:]), ("psg", T.psg[:]))
-    for c in range(8):
-        bk, ap = banks[c % 6]
-        pe([mm(ap, C("wt", p1=16), T.pt[0:16, 512 * c:512 * c + 512], True, False), mm(ap, C("sa"), T.xw[:, 512 * c:512 * c + 512], False, True)],
-           "sa0 sa1 wt0 wt1 pt0 pt1 xw%d" % (0, 0, 1, 1, 1, 2, 2, 3)[c], bk)
+    banks = (("psv0", T.psv[:, 0, :]), ("psv1", T.psv[:, 1, :]), ("psm", T.psm[:]), ("psu", T.psu[:]), ("psd", T.psd[:]), ("psg", T.psg[:]),
+             ("psk0", T.psk[:, 0, :]), ("psk1", T.psk[:, 1, :]))
+    for c, (bk, ap) in enumerate(banks):
+        pe([mm(ap, C("wt", p1=17), T.pt[0:17, 512 * c:512 * c + 512], True, False)], "wt0 wt1 wt2 pt0 pt1 pt2", bk)
+        pe([mm(ap, C("sa"), T.xw[:, 512 * c:512 * c + 512], False, True)], "sa0 sa1 xw%d" % sum(x <= 512 * c for x in XCUT[1:]), bk)
         mv("sv"[c % 2], T.pw[:, 512 * c:512 * c + 512], ap, bk, "pw%d" % c)
 
-    mv("v", T.lfu[:, 0:512], T.lfi[:, 0:512], "lfi0", "lfu0")
-    mv("g", T.lfu[:, 512:M], T.lfi[:, 512:M], "lfi1", "lfu1")
+    mv("v", T.lfu[:, 0:LCUT], T.lfi[:, 0:LCUT], "lfi0", "lfu0")
+    mv(LQ, T.lfu[:, LCUT:M], T.lfi[:, LCUT:M], "lfi1", "lfu1")
     chip = lambda x: topo.chip(T.cores[x % N])
 
     def handed(src, j):
         return j > 1 and chip(src - j) == chip(src - j + 1) != chip(src)
-    pe([mm(T.psd[:], C("id"), T.xlh[:, 0:512], True, False), mm(T.psd[:], C("pb16"), T.xlh[:, 512:M], False, True)], "id pb16 xlh", "psd")
-    mv("s", T.xlp[:], T.psd[:], "psd", "xlp")
-    arrives("rl0", NE, "lu0", 2 * FAR, send(T.lfu[:, 0:512], "lfu0", r - 1, T.lu1[:, 0:512], "rl0", "ls15", True))
-    arrives("rl1", NE, "lu1", FAR, send(T.lfu[:, 512:M], "lfu1", r - 1, T.lu1[:, 512:M], "rl1", "ls0", True))
-    sent = send(T.xlp[:], "xlp", r - 1, T.xp1[:], "rx1", "ls1", True)
-    arrives("rx1", NE, "xp1", 10.0, sent)
+    arrives("rl0", NE, "lu0", BULK, send(T.lfu[:, 0:LCUT], "lfu0", r - 1, T.lu1[:, 0:LCUT], "rl0", "ls15", True))
+    arrives("rl1", NE, "lu1", FAR + (M - LCUT) / 240, send(T.lfu[:, LCUT:M], "lfu1", r - 1, T.lu1[:, LCUT:M], "rl1", "ls0", True))
+    arrives("rx1", NE, "xl1", BULK, send(T.xlh[:], "xlh", r - 1, T.xl1[:], "rx1", "ls1", True))
+    send(T.lfu[:], "lfu0 lfu1", r - 2, T.lu2[:], "rl2", "ls2", True, not handed(r, 2))
     for j in (2, 3):
-        if not handed(r, j):
-            send(T.lfu[:], "lfu0 lfu1", r - j, T["lu%d" % j][:], "rl%d" % j, "ls%d" % (2 * j - 2), True)
-            send(T.xlp[:], "xlp", r - j, T["xp%d" % j][:], "rx%d" % j, "ls%d" % (2 * j - 1), True)
-        arrives("rl%d" % j, NE, "lu%d" % j, 12.0 * j, sent)
-        arrives("rx%d" % j, NE, "xp%d" % j, 12.0 * j + 4.0, sent)
+        send(T.xlh[:], "xlh", r - j, T["xl%d" % j][:], "rx%d" % j, "ls%d" % (2 * j - 1), True, not handed(r, j))
 
     def hand_on(i):
-        if handed(r + i, i + 1):
-            send(T["lu%d" % i][:], ("lu0 lu1", "lu2")[i - 1], r - 1, T["lu%d" % (i + 1)][:], "rl%d" % (i + 1), "ls%d" % (14 + 2 * i), True)
-            send(T["xp%d" % i][:], "xp%d" % i, r - 1, T["xp%d" % (i + 1)][:], "rx%d" % (i + 1), "ls%d" % (15 + 2 * i), True)
+        if i == 1:
+            arrives("rl2", NE, "lu2", BULK, send(T.lu1[:], "lu0 lu1", r - 1, T.lu2[:], "rl2", "ls16", True, handed(r + i, i + 1)))
+        a, b = "xl%d" % i, "xl%d" % (i + 1)
+        arrives("rx%d" % (i + 1), NE, b, BULK, send(T[a][:], a, r - 1, T[b][:], "rx%d" % (i + 1), "ls%d" % (15 + 2 * i), True, handed(r + i, i + 1)))
     hand_on(1)
     for c in range(4):
         a, b = 512 * c, 512 * c + 512
-        ts(T.fw[:, 2048 + a:2048 + b], T.fw[:, a:b], 12, Op.logical_shift_right, "fwl", "fw%d" % c)
-    mv("g", T.lh[:, 0:M], T.lfi[:], "lfi0 lfi1", "lh")
-
-    def features(j, after):
-        x, xl = T["xp%d" % j], T["xl%d" % j]
-        mv("s", T.xt[:], x[:], "xp%d %s" % (j, after), "xt", 0.0625, 144.0 - 0.46875)
-        mv("s", xl[:, 512:M], T.xt[:], "xt", "xh%d" % j, bias=-144.0)
-        pe([mm(T.psg[:], C("id"), x[:], True, False), mm(T.psg[:], C("nb16"), xl[:, 512:M], False, True)], "id nb16 xp%d xh%d" % (j, j), "psg")
-        mv("s", xl[:, 0:512], T.psg[:], "psg", "xl%d" % j)
+        ts(T.fw[:, 2048 + a:2048 + b], T.fw[:, a:b], 12, Op.logical_shift_right, "fwl%d" % c, "fw%d" % c)
 
     def apply(buf, win, after):
         cp(T[win][:].indirect(T[buf][:, K:K + 12]), T[buf][:, 0:K], buf + " " + after, win, -K)
@@ -575,110 +630,120 @@ def rank_program(g, core, T, topo):
     def lower(eq, ps, pk, stop=True):
         for kb in range(11):
             pe([mm(ps[:, 16 * kb + 16:K], C("bl8"), T[eq][:, kb, 16:K - 16 * kb], False, False)], "bl8 %s%d" % (eq, kb), pk)
-        pe([mm(ps[:, k:K:16], C("ltk", 128 * k, 128 * k + 128), T[eq][:, :, k], False, stop and k == 15) for k in range(1, 16)], keys("ltk", 16, 1) + " " + keys(eq, 12), pk)
+        pe([mm(ps[:, 0:K], C("up8"), T[eq][:, :, 0:16], False, stop)], "up8 " + keys(eq, 12), pk)
+
+    def pieces(dst, h):
+        n, m = PIECES[2 * "cab".index(dst[1]) + h], CUT[h + 1] - CUT[h]
+        return [(CUT[h] + m * i // n // 2 * 2, CUT[h] + m * (i + 1) // n // 2 * 2, "%s%d%d" % (dst, h, i)) for i in range(n)]
+
+    def made(dst, *hs):
+        return " ".join(x[2] for h in hs for x in pieces(dst, h))
 
     def xgather(dst, lst, lk, h):
-        a, b = H * h, H * h + H
-        tt(T[dst][:, 16 * a:16 * b], T.xw[:, 0:W].indirect(lst[:, a:b]), T.qrep[:, 16 * a:16 * b], Op.min, " ".join((XW, lk, QR)), dst + str(h), 16 * H)
+        for a, b, key in pieces(dst, h):
+            tt(T[dst][:, 16 * a:16 * b], T.xw[:, 0:W].indirect(lst[:, a:b]), T.qrep[:, 16 * a:16 * b], Op.min, " ".join((XW, lk, QR)), key, 16 * (b - a))
 
     def pgather(dst, lst, lk, h):
-        act(T[dst][:, 16 * H * h:16 * H * (h + 1)], T.pw[:].indirect(lst[:, H * h:H * h + H]), PW + " " + lk, dst + str(h), n=16 * H)
+        for a, b, key in pieces(dst, h):
+            act(T[dst][:, 16 * a:16 * b], T.pw[:].indirect(lst[:, a:b]), PW + " " + lk, key, n=16 * (b - a))
 
     def sums(ps, src, w, wk, h, n, last=False):
-        pe([mm(T[ps][0:H, h, i:n:16], T[src][:, 16 * H * h + i:16 * H * (h + 1):16], C(w), False, last and i == 15) for i in range(16)],
-           "%s%d %s" % (src, h, wk), "%s%d" % (ps, h))
+        a, b = CUT[h], CUT[h + 1]
+        pe([mm(T[ps][0:b - a, h, i:n:16], T[src][:, 16 * a + i:16 * b:16], C(w), False, last and i == 15) for i in range(16)],
+           made(src, h) + " " + wk, "%s%d" % (ps, h))
 
     LO = T.ll[:, 1, :]
-    ID = C("id", 0, H, p1=H)
-    own = lambda f: (lambda kb: T.sc[:, kb // 6, H * f + 16 * (kb % 6) + 15:H * f + 16 * (kb % 6) + 16])
+    own = lambda f: (lambda kb: T.sc[:, 16 * kb + 8 * f + 7:16 * kb + 8 * f + 8])
     for t in range(RO):
         j = t + 1
         lw, xl, msg = "lw%d" % j, "xl%d" % j, "msg%d" % j
         lnw, lk = T[lw][:, 0:M], lw if t else "lw0 lw1"
         for h in (0, 1):
             pgather("pc", T.lc[:], "lc", h)
-            xgather("ma", T.lc[:], "lc", h)
+            xgather("mc", T.lc[:], "lc", h)
         if t == 0:
             for h in (0, 1):
-                mv("s", T.lw1[:, 512 * h:512 * h + 512], T.lu1[:, 512 * h:512 * h + 512], "lu%d pc%d" % (h, h), "lw%d" % h)
+                a, b = (0, LCUT, M)[h:h + 2]
+                mv(LW[h], T.lw1[:, a:b], T.lu1[:, a:b], "lu%d %s" % (h, made("pc", h) if h else "lfu1"), "lw%d" % h)
         else:
-            if t == 2:
-                apply("up2", lw, "lc")
-            apply(("up1", "up3")[t - 1], lw, "ma1")
-        features(j, "pc1")
+            apply(("up1", "up3")[t - 1], lw, made("mc", 1))
+        if t == 1:
+            mv("g", T.st[:], T.lw2[:, 0:M], "lw2", "st")
+            arrives("rl3", NE, "lu3", BULK, send(T.st[:], "st", r - 1, T.lu3[:], "rl3", "ls4", True))
+            arrives("rs", NE, "lus", 1.5 * BULK, send(T.st[:], "st", r + 2, T.lus[:], "rs", "ls7", True))
+        if t == 2:
+            mv("g", T.lh[:, 0:M], T.lus[:], "lus lc", "lh")
+            apply("hm2", "lh", made("mc", 1))
         for h in (0, 1):
-            a, b, x, y = H * h, H * h + H, 6 * h, 6 * h + 6
+            a, b = CUT[h], CUT[h + 1]
+            H, x, y = b - a, a // 16, b // 16
             k = lambda names: " ".join("%s%d" % (n, h) for n in names.split())
             pe([mm(T.psk[0:H, h, 0:256], C("one", 0, H, p1=1), C("row", 0, 256, p1=1), True, False)], "one rowa0 rowa1", k("psk"))
-            sums("psk", "ma", "wm", "wm0 wm1", h, 256)
-            sums("psk", "pc", "wp", "wp0 wp1", h, 256)
-            pe([mm(T.psk[0:H, h, 128:256], T.c16[:, a:b], C("id"), False, True)], "c16 id", k("psk"))
+            sums("psk", "mc", "wm", "wm0 wm1", h, 256)
+            sums("psk", "pc", "wp", "wp0 wp1", h, 256, True)
             scan(T.t4[0:H, h, :], T.psk[0:H, h, 0:256], k("psk"), k("t4_"), 256, H)
             ts(T.fi[0:H, h, :], T.t4[0:H, h, 15:256:16], W - 1, Op.bitwise_and, k("t4_"), k("fi"))
             mv("s", T.fl[0:H, h, :], T.fi[0:H, h, :], k("fi"), k("fl"), bias=-2048.0)
-            pe([mm(T.psk[0:16, h, 256:352], T.fl[0:H, h, :], ID, True, True)], k("fl") + " id", k("psk"))
-            mv("s", T.gt[0:16, a:b], T.psk[0:16, h, 256:352], k("psk"), k("gt"))
             pb, pk = ((T.psm, "psm"), (T.psu, "psu"))[h]
-            fs = []
-            for f in (0, 1):
-                fs += [mm(pb[:, H * f:H * f + H], C("rq", 128 * f, 128 * f + 128, p1=32), T.gt[0:32, a:b], True, False), mm(pb[:, H * f:H * f + H], C("id"), C("bm", 0, H), False, True)]
-            fs += [mm(pb[:, H * f + K:H * f + K + H], RP(f), T.gt[0:32, a:b], True, True) for f in (0, 1)]
-            pe(fs, "rq0 rq1 rp id bm " + k("gt"), pk)
-            scan(T.sc[:, h, :], pb[:, 0:K], pk, k("sc"))
-            mv("v", T.ll[:, 0, x:y], T.sc[:, h, 15:H:16], k("sc"), k("ln"), 0.5, -0.25)
-            mv("v", T.ll[:, 1, x:y], T.sc[:, h, H + 15:K:16], k("sc"), k("lo"))
-            mv("s", T.ro[:, a:b], pb[:, K + H:2 * K], pk, k("ro"))
-            mv("s", T.rt[:, a:b], pb[:, K:K + H], pk, k("rt"), bias=2045.0)
-            mv("s", T.hh[:, a:b], pb[:, K:K + H], pk, k("hh"), 0.25, 1535.625)
+            pe([mm(pb[:, 0:H], C("id"), C("gm", 0, H), True, False)], "id gm", pk)
+            pe([mm(pb[:, 16 * i:16 * i + 16], C("sel", 128 * i, 128 * i + 128, p1=H), T.fl[0:H, h, :], False, i == y - x - 1) for i in range(y - x)],
+               keys("sel", y - x) + " " + k("fl"), pk)
+            op("v", [lambda a=a, b=b, pb=pb: v.tensor_tensor_scan(T.sc[:, a:b], T.s0[:, 0:2 * (b - a):2], pb[:, 0:b - a], 0.0, Op.add, Op.min)], pk + " s0", k("sc"), VFIX + CYC * H)
+            mv("v", T.ll[:, 0, x:y], T.sc[:, a + 7:b:16], k("sc"), k("ln"), 0.5, -0.25)
+            mv("s", T.ll[:, 1, x:y], T.sc[:, a + 15:b:16], k("sc"), k("lo"))
             LN = T.ll[:, 0, x:y]
             act(T.sq[:, 0, a:b], lnw.indirect(LN), lk + " " + k("ln"), k("sqa"), AF.Square, H, scale=2.0, bias=8.0)
             act(T.sq[:, 1, a:b], lnw.indirect(LN), lk + " " + k("ln"), k("sqb"), AF.Square, H, bias=592.0)
             act(T.b16[:, a:b], lnw.indirect(LN), lk + " " + k("ln"), k("b16_"), n=H)
             for c, of in enumerate((-2.484375, -10951.484375)):
                 mv("s", T.tt[:, c, a:b], T.sq[:, c, a:b], k("sq" + "ab"[c]), k("tt" + "ab"[c]), 0.03125, of)
-            ts(T.cc[:, :, a:b], T.tt[:, :, a:b], W - 1, Op.bitwise_and, k("tta ttb"), k("cc"))
-            mv("s", T.l12[:, :, a:b], T.cc[:, :, a:b], k("cc"), k("li"))
+            for c, d, n in ((0, 1, "a"), (1, 2, "b")) if h < SPLIT else ((0, 2, "ab"),):
+                ts(T.cc[:, c:d, a:b], T.tt[:, c:d, a:b], W - 1, Op.bitwise_and, k(" ".join("tt" + u for u in n)), k(" ".join("cc" + u for u in n)))
+                mv("s", T.l12[:, c:d, a:b], T.cc[:, c:d, a:b], k(" ".join("cc" + u for u in n)), k(" ".join("li" + u for u in n)))
+            mv("s", T.cm[:, :, a:b], T.cc[:, :, a:b], k("cca ccb"), k("cm"), bias=-2048.0)
             pe([mm(T.psv[0:H, h, 0:384], T.b16[:, a:b], C("bi"), True, False)], "bi0 bi1 bi2 " + k("b16_"), k("psv"))
-        for h in (0, 1):
-            for c in (0, 1):
-                pgather("p" + "ab"[c], T.l12[:, c, :], "li%d" % h, h)
-                xgather("m" + "ab"[c], T.l12[:, c, :], "li%d" % h, h)
-                sums("psv", "m" + "ab"[c], "wm%d" % (c + 1), keys("wm%d_" % (c + 1), 3), h, 384)
-                sums("psv", "p" + "ab"[c], "wp%d" % (c + 1), keys("wp%d_" % (c + 1), 3), h, 384, c == 1)
-        act(T.at[:], T[xl][:].indirect(T.ll[:, 0, :]), xl + " xh%d ln0 ln1" % j, "at", n=K)
+        for f in (0, 1):
+            mv("s", T.lv[:, 12 * f:12 * f + 12], T.sc[:, 7 + 8 * f:K:16], "sc0 sc1", "lv%d" % f, bias=-2048.0)
+        pe([mm(T.psg[:, i:2 * K:16], C("bj", 128 * i, 128 * i + 128), T.lv[:], True, True) for i in range(16)], keys("bj", 16) + " lv0 lv1", "psg")
+        mv("s", T.rr[:], T.psg[:, 0:2 * K], "psg", "rr")
+        act(T.at[:], T[xl][:].indirect(T.ll[:, 0, :]), xl + " ln0 ln1", "at", n=K)
         act(T.g2[:], T.pw[:].indirect(LO), PW + " lo0 lo1", "g2", n=K)
-        same("eqo", T.ro, "ro0 ro1", own(1), "sc0 sc1")
+        same("eqo", T.rr[:, 1, :], "rr", own(1), "sc0 sc1")
         pe([mm(T.psd[:, 0:K], C("id"), C("bm"), True, False), mm(T.psd[:, 0:K], C("se"), T.g2[:], False, False)], "id bm se g2", "psd")
         lower("eqo", T.psd, "psd")
         scan(T.scd[:], T.psd[:, 0:K], "psd", "scd")
-        act(C("cand"), T.scd[:, 15:K:16], "scd", "cand", AF.Relu, scale=-1.0)
+        relu(RQ[0], C("cand"), T.scd[:, 15:K:16], "scd", "cand", -1.0)
         op("v", [lambda: v.tensor_tensor_scan(C("exb", 1, 13), C("one", 0, 12), C("cand"), 0.0, Op.mult, Op.add)], "one cand", "exb", VFIX + 64 * CYC)
-        pe([mm(T.psd[:, 400:412], C("btr"), C("cand"), True, False), mm(T.psd[:, 400:412], C("bl"), C("exb", 0, 12), False, True)], "btr cand bl exb", "psd")
-        act(C("nqd"), T.psd[:, 400:412], "psd", "nqd", AF.Relu, scale=OUT, bias=(256.0 - CAP) * OUT)
-        act(C("lq"), T.psd[:, 400:412], "psd", "lq", AF.Relu, bias=256.0 - CAP)
-        tt(C("w1"), C("nqd"), T.sc[:, :, H + 15:K:16], Op.add, "nqd sc0 sc1", "w1")
+        pe([mm(T.psd[:, 400:412], C("btr"), C("cand"), True, False), mm(T.psd[:, 400:412], C("bl8"), C("exb", 0, 12), False, True)], "btr cand bl8 exb", "psd")
+        relu(RQ[1], C("nqd"), T.psd[:, 400:412], "psd", "nqd", bias=(256.0 - CAP) * OUT)
+        tt(C("w1"), C("nqd"), T.sc[:, 15:K:16], Op.add, "nqd sc0 sc1", "w1")
         tt(C("ld"), C("w1"), C("dm4"), Op.min, "w1 dm4", "ld")
-        act(T.nq[:], C("w01").indirect(C("lq")), "w01 w02 lq", "nq", n=K)
-        pe([mm(T.psk[:, 1, 0:K], C("slt", 128 * i, 128 * i + 128), T.pc[:, i:16 * K:16], i == 0, i == 15) for i in range(16)], keys("slt", 16) + " pc0 pc1", "psk1")
+        act(T.nq[:], C("nqd").indirect(C("lk")), "nqd lk", "nq", n=K)
+        pe([mm(T.psk[:, 1, 0:K], C("slt", 15 - i, 143 - i), T.pc[:, i:16 * K:16], i == 0, i == 15) for i in range(16)], "slt " + made("pc", 0, 1), "psk1")
         mv("s", T[msg][:, 0:K], T.psk[:, 1, 0:K], "psk1", msg)
-        same("eqt", T.rt, "rt0 rt1", own(0), "sc0 sc1", 3.0)
-        pe([mm(T.psk[:, 0, 0:K], C("id"), C("bm4"), True, False), mm(T.psk[:, 0, 0:K], C("id4"), T.hh[:], False, False),
-            mm(T.psk[:, 0, 0:K], C("idm"), T.rt[:], False, False)], "id bm4 id4 hh0 hh1 idm rt0 rt1", "psk0")
-        lower("eqt", T.psk[:, 0, :], "psk0", False)
-        pe([mm(T.psk[:, 0, 0:K], C("idu", 512, 640), T.nq[:], False, True)], "idu4 nq", "psk0")
+        same("eqt", T.rr[:, 0, :], "rr", own(0), "sc0 sc1")
+        mv("s", T.hh[:], T.rr[:, 0, :], "rr", "hh", 0.25, 1535.5)
+        pe([mm(T.psk[:, 0, 0:K], C("id"), C("bm4"), True, False), mm(T.psk[:, 0, 0:K], C("c15", p1=1), C("one", 0, K, p1=1), False, False),
+            mm(T.psk[:, 0, 0:K], C("id4"), T.hh[:], False, False), mm(T.psk[:, 0, 0:K], C("idm"), T.rr[:, 0, :], False, False)],
+           "id bm4 c15 one id4 hh idm rr", "psk0")
+        lower("eqt", T.psk[:, 0, :], "psk0")
         scan(T.scm[:], T.psk[:, 0, 0:K], "psk0", "scm")
-        tt(T[msg][:, K:K + 12], T.scm[:, 15:K:16], C("dm1"), Op.min, "scm dm1", msg + "l")
+        tt(C("w2"), T.scm[:, 15:K:16], C("nqd"), Op.add, "scm nqd", "w2")
+        tt(T[msg][:, K:K + 12], C("w2"), C("dm1"), Op.min, "w2 dm1", msg + "l")
         mk = msg + " " + msg + "l"
-        if t == 0:
-            arrives("ru1", NE, "up1", FAR, send(T[msg][:, 0:K + 12], mk, r - 1, T.up1[:], "ru1", "ls6"))
-            arrives("ru2", NE, "up2", FAR, send(T[msg][:, 0:K + 12], mk, r - 2, T.up2[:], "ru2", "ls7"))
-        elif t == 1:
-            arrives("ru3", NE, "up3", FAR, send(T[msg][:, 0:K + 12], mk, r - 1, T.up3[:], "ru3", "ls8"))
-        arrives("rh%d" % j, NE, "hm%d" % j, FAR, send(T[msg][:, 0:K + 12], mk, r + 1 + t, T["hm%d" % j][:], "rh%d" % j, "ls%d" % (9 + t)))
-        if t == 0:
-            hand_on(2)
+        if t < 2:
+            u = "up%d" % (1 + 2 * t)
+            arrives("r" + u[0::2], NE, u, FAR, send(T[msg][:, 0:K + 12], mk, r - 1, T[u][:], "r" + u[0::2], "ls%d" % (6 + 2 * t)))
+        if t:
+            arrives("rh%d" % j, NE, "hm%d" % j, FAR, send(T[msg][:, 0:K + 12], mk, r + 1 + t, T["hm%d" % j][:], "rh%d" % j, "ls%d" % (9 + t)))
         else:
-            apply("hm%d" % t, "lh", "lo0")
+            hand_on(2)
+        for h in (0, 1):
+            for c in (0, 1):
+                pgather("p" + "ab"[c], T.l12[:, c, :], "li%s%d %s" % ("ab"[c], h, HINT[4 + 2 * h + c]), h)
+                xgather("m" + "ab"[c], T.l12[:, c, :], "li%s%d %s" % ("ab"[c], h, HINT[2 * h + c].replace("msg", msg)), h)
+                sums("psv", "m" + "ab"[c], "wm%d" % (c + 1), keys("wm%d_" % (c + 1), 3), h, 384)
+                sums("psv", "p" + "ab"[c], "wp%d" % (c + 1), keys("wp%d_" % (c + 1), 3), h, 384, c == 1)
         pe([mm(T.psk[:, 1, 0:K], C("sa"), T.at[:], True, False), mm(T.psk[:, 1, 0:K], C("dg1"), T.g2[:], False, False),
             mm(T.psk[:, 1, 0:K], C("row", 128 * t, 128 * t + 128, 96, 97), C("one", 0, K, 96, 97), False, True)], "sa0 sa1 at dg1 g2 rowm%d one" % t, "psk1")
         mv("s", T.v2[:], T.psk[:, 1, 0:K], "psk1", "v2")
@@ -694,41 +759,46 @@ def rank_program(g, core, T, topo):
             else:
                 mv("s" if i < 2 * QG else "v", T.qrep[:, i:16 * K:16], T.qb[:], "qb", "qr%d" % i, bias=-128.0)
         for h in (0, 1):
+            a, b = CUT[h], CUT[h + 1]
+            H = b - a
             nn = lambda f: T.nn[0:H, h, 128 * f:128 * f + 128]
-            ts(T.nn[0:H, h, 128:384], T.psv[0:H, h, 128:384], 0.0, Op.not_equal, "psv%d" % h, "nna%d" % h)
-            act(nn(0), T.psv[0:H, h, 0:128], "psv%d" % h, "nnb%d" % h, AF.Sign, bias=-0.5)
-            pe([mm(T.psu[:, H * h:H * h + H], nn(f), ID, f == 1, f == 2) for f in (1, 2)], "id nna%d" % h, "psu")
+            ts(T.nn[0:H, h, 128:384], T.psv[0:H, h, 128:384], 0.0, Op.is_equal, "psv%d" % h, "nna%d" % h)
+            if h:
+                ts(nn(0), T.psv[0:H, h, 0:128], 0.5, Op.is_gt, "psv%d" % h, "nnb%d" % h, 0.5, Op.subtract)
+            else:
+                act(nn(0), T.psv[0:H, h, 0:128], "psv%d" % h, "nnb%d" % h, AF.Sign, bias=-0.5)
+            pe([mm(T.psu[:, a:b], nn(f), C("bi", 128, 128 + H, p1=H), f == 1, f == 2) for f in (1, 2)], "bi1 nna%d" % h, "psu")
             for u in (0, 1):
-                o = T.psm[:, K * u + H * h:K * u + H * h + H]
-                fs = [mm(o, C("row", 128 * u, 128 * u + 128, 64, 65), C("one", 0, H, 64, 65), True, False)]
-                fs += [mm(o, nn(f), C("idu", 128 * (3 * u + w), 128 * (3 * u + w) + H, p1=H), False, f == 0) for f, w in ((1, 0), (2, 1), (0, 2))]
-                pe(fs, "rowu0 rowu1 one %s nna%d nnb%d" % (keys("idu", 6), h, h), "psm")
-        act(T.nr[:], T.psu[:, 0:K], "psu", "nr", AF.Relu, bias=-1.0)
-        tt(T.psm[:, 0:K], T.psm[:, 0:K], T.cc[:, 1, :], Op.min, "psm cc0 cc1", "psm pk")
-        tt(T.dc[:], T.psm[:, K:2 * K], T.cc[:, 0, :], Op.min, "psm cc0 cc1", "dc")
-        tt(T.sg[:], T.psm[:, 0:K], T.dc[:], Op.max, "psm pk dc", "sg")
-        pe([mm(T.psg[:, 0:K], C("id"), T.nq[:], True, False), mm(T.psg[:, 0:K], C("tri"), T.nr[:], False, True)], "id nq tri nr", "psg")
-        act(T.psu[:, K:2 * K], T.psg[:, 0:K], "psg psu", "psu", AF.Relu, scale=-1.0)
-        mv("s", T.sh[:], T.sg[:], "sg", "sh", bias=-2048.0)
-        act(T.fst[:], T.psg[:, 0:K], "psg", "fst", AF.Relu, scale=-1.0)
+                pe([mm(T.psm[:, K * u + a:K * u + b], nn(f), C("idu", 128 * (3 * u + w), 128 * (3 * u + w) + H, p1=H), f == 1, f == 0) for f, w in ((1, 0), (2, 1), (0, 2 - h))],
+                   "%s nna%d nnb%d" % (keys("idu", 6), h, h), "psm")
+        relu("s", T.nr[:], T.psu[:, 0:K], "psu", "nr", bias=1.0)
+        tt(T.psm[:, 0:K], T.psm[:, 0:K], T.cm[:, 1, :], Op.min, "psm cm0 cm1", "psm pk")
+        tt(T.dc[:], T.psm[:, K:2 * K], T.cm[:, 0, :], Op.min, "psm cm0 cm1", "dc")
+        tt(T.sh[:], T.psm[:, 0:K], T.dc[:], Op.max, "psm pk dc", "sh")
+        pe([mm(T.psg[:, 0:K], C("row", 128, 256, 64, 65), C("one", 0, K, 64, 65), True, False)], "rowu1 one", "psg")
+        pe([mm(T.psg[:, 0:K], C("tr4"), T.nr[:], False, True)], "tr4 nr", "psg")
+        mv("s", T.sg[:], T.sh[:], "sh", "sg", bias=2048.0)
+        relu("s", T.fst[:], T.psg[:, 0:K], "psg", "fst", 1.0 / 2048)
         cp(T.fw[:].indirect(C("ld")), T.sg[:], "ld sg", FW, -K)
         ts(T.ci[:], T.fw[:, 0:W].indirect(LO), W - 1, Op.bitwise_and, FW + " lo0 lo1", "ci", n=K)
         if t < RO - 1:
             mv("s", T.lc[:], T.ci[:], "ci", "lc")
-            mv("s", T.c16[:], T.ci[:], "ci", "c16", bias=-2048.0)
         else:
             mv("s", T.cf[:], T.ci[:], "ci", "cf")
-        tt(T.x1[:], T.psu[:, K:2 * K], T.sh[:], Op.mult, "psu sh", "x1")
+        tt(T.x1[:], T.psg[:, 0:K], T.sh[:], Op.min, "psg sh", "x1")
         o = T.psv[:, 0, K:2 * K]
         pe([mm(o, C("row", 0, 128, 64, 65), C("one", 0, K, 64, 65), True, False), mm(o, C("id"), T.b16[:], False, False),
-            mm(o, C("idu", 128, 256), T.nq[:], False, False), mm(o, C("tr8"), T.nr[:], False, True)], "rowu0 one id b16_0 b16_1 idu1 nq tr8 nr", "psv0")
+            mm(o, C("tr8"), T.nr[:], False, True)], "rowu0 one id b16_0 b16_1 tr8 nr", "psv0")
         act(T.x2[:], o, "psv0", "x2", AF.Relu)
-        place = lambda o, sp: [mm(o, C("id"), C("bmc"), True, False), mm(o, C("bn8"), T.fst[:], False, False), mm(o, C("bl"), T.x1[:], False, sp)]
-        pe(place(T.psv[:, 1, 0:K], True), "id bmc bn8 fst bl x1", "psv1")
-        pe([mm(T.psv[:, 0, 0:K], C("bl"), T.x1[:], True, True)], "bl x1", "psv0")
-        pe(place(T.psd[:, 0:K], False), "id bmc bn8 fst bl x1", "psd")
+        for o, pk, stop in ((T.psv[:, 1, 0:K], "psv1", True), (T.psd[:, 0:K], "psd", False)):
+            pe([mm(o, C("id"), C("bmc"), True, False), mm(o, C("id"), T.nq[:], False, False)], "id bmc nq", pk)
+            pe([mm(o, C("cmp"), T.nr[:], False, False)], "cmp nr", pk)
+            pe([mm(o, C("bn8"), T.fst[:], False, False)], "bn8 fst", pk)
+            pe([mm(o, C("bl"), T.x1[:], False, stop)], "bl x1", pk)
+        pe([mm(T.psu[:, 0:K], C("cmp"), T.nr[:], True, False)], "cmp nr", "psu")
+        pe([mm(T.psu[:, 0:K], C("bl"), T.x1[:], False, True)], "bl x1", "psu")
         scan(T.scc[:], T.psv[:, 1, 0:K], "psv1", "scc")
-        mv("s", T.rc[:], T.psv[:, 0, 0:K], "psv0", "rc")
+        mv("s", T.rc[:], T.psu[:, 0:K], "psu", "rc", bias=34816.0)
         tt(C("lp"), T.scc[:, 15:K:16], C("dm4"), Op.min, "scc dm4", "lp")
         same("eqo", T.rc, "rc", lambda kb: T.scc[:, 16 * kb + 15:16 * kb + 16], "scc")
         lower("eqo", T.psd, "psd")
@@ -742,8 +812,8 @@ def rank_program(g, core, T, topo):
         tt(C("lcl"), T.scd[:, 15:K:16], C("dm4"), Op.min, "scd dm4", "lcl")
         cp(T.pw[:].indirect(C("lcl")), T.v1[:], "lcl v1", PW, -K)
     apply("hm3", "lh", "nna0")
-    dma("d", T.yq[:], T.q[:], "q", "yq", 48)
     dma("d", T.yl[:], T.lh[:, 0:M], "lh", "yl", 512)
+    dma("d", T.yq[:], T.q[:], "q", "yq", 48)
     dma("d", T.yc[:], T.cf[:], "cf", "yc", 96)
     dma("d", T.yt[:], T.pw[0:128:16, 0:W], PW, "yt", 128)
     finish()

@@ -1,32 +1,58 @@
+import numpy as np
 from concourse.mybir import AluOpType as Op, ActivationFunctionType as AF
 
 W, M, K, CAP, RO, N = 4096, 1024, 192, 160, 3, 8
-CUT = (0, 96, K)
-PIECES = (1, 1, 1, 1, 1, 1)
-XCUT = (0, 1536, 2560, 3584, W)
-LCUT, LQ, LW = 768, "g", "gs"
-LOADS = "tgs lfi0 cxi q pt xw0 xw1 xw2 xw3 lfi1 fwl0 fwl1 xlh fwl2 fwl3"
-HINT = ("",) * 8
-SPLIT, SEED, ROAM, BULK, VLOAD = 2, 3, 6, 9.0, 0.05
-SWEEPS, WIDE, RQ = 4, 140, "vv"
+CUT = (0, 64, K)
+PARTS = {"mc1": (64, 64), "pc1": (64, 64), "mb1": (96, 32), "pb1": (96, 32), "sb1": (96, 32)}
+LEND = ""
+EQ = (0, 4, 8, 12)
+ONG, PLAIN, OUTS = "lo0 lo1 lib1", "sqb0 sqa1 sqb1", "yq yl yc yt"
+_A = "mc10>mc00 mc11>mc10 pc10>pc00 pc11>pc10 ma10>mb00 mb00>ma00 pa10>pb00 pb00>pa00 mb10>ma10 pb10>pa10"
+AFTER = (_A + " pw2>pw0 pw4>pw2 pw6>pw4 pw3>pw1 pw5>pw3 pw7>pw5 mc00>pw7 lc>pw6", _A, _A)
+_V = "mc10 t4_0 fi0 mc11 sc0 lw t4_1 cca0 fi1 lia0 ccb0 ma00 sc1 mb00 ttb1 "
+_S = "pc00 pc10 fl0 pc11 ln0 b16_0 sqa0 sqb0 tta0 ttb0 fl1 lib0 pa00 lv1 ln1 lv0 b16_1 lo0 "
+_V0 = ("mc10 t4_0 fi0 mc11 sc0 fw0 fw1 t4_1 tta0 fi1 cca0 fl1 lia0 fw2 ccb0 sc1 ma00 mb00 hn eqo2 cca1 ccb1 eqo1 eqo0 eqt0 ma10 mb10 scd mb11 nna0 exb eqt2 eqt1 nna1 w1 nnb1 ld "
+       "xw0 psm dc scm sh msgl x1 fw3 scc qr0 eqo0 eqo1 eqo2 fwl0 scd ci qr5 +mc00")
+_S0 = ("pc00 pc10 fl0 pc11 ln0 lo0 lw sqa0 b16_0 sqb0 ttb0 pa00 ln1 lv1 lv0 lib0 b16_1 msg sqb1 sqa1 rr ttb1 tta1 pb00 hh lia1 at cm0 pa10 pb10 cand pb11 "
+       "cm1 nnb0 nqd v2 nq nr pw0 xo fst x2 sg qb rc qr1 qr2 lp g1 qr3 lcl v1 lc pw0")
+_V1 = _V + "cca1 ccb1 lia1 eqo0 eqo1 eqo2 ma10 mb10 scd mb11 exb nna0 eqt0 eqt1 w1 nna1 nnb1 ld eqt2 xw0 psm dc scm sh x1 fwl0 qr0 scc qr1 eqo0 eqo1 eqo2 ci qr5 scd v1 +mc00"
+_S1 = _S + "sqa1 sqb1 tta1 rr pb00 hh hn pa10 pb10 cand pb11 nnb0 cm0 nqd cm1 at nq nr msg fst xo msgl sg qb v2 rc pw0 qr2 lp x2 g1 qr3 lcl lc pw0"
+_V2 = (_V.replace("ttb1", "msg") + "eqo0 eqo1 eqo2 ccb1 eqt2 scd cca1 eqt0 exb eqt1 nqd ma10 w1 scm ld mb10 nna0 mb11 xw0 nna1 nnb1 "
+       "lh psm dc sh x1 yw scc eqo0 eqo1 eqo2 fwl0 scd ci yw")
+_S2 = (_S.replace("ln0", "ln0 yv").replace("lo0 ", "") + "sqa1 sqb1 rr ttb1 hn tta1 pb00 cand hh lia1 at cm0 nq pa10 msgl lh pb10 v2 pb11 lh nnb0 cm1 pw0 "
+       "nr xo fst x2 sg rc lp qb q g1 v1 lcl cf")
+PLAN = ((_V0, _V1, _V2), (_S0, _S1, _S2))
+QHOW = ("vvvvvv", "vsvsgs")
+NNB = "sv"
+PWV = (1, 3, 5, 7)
+XCUT, FCUT = (0, 2560, 3584, W), (0, 1024, 2048)
+LCUT, LQ, LW = 1024, "s", "gs"
+LOADS = "tgs lfi0 q pt xw0 xw1 xw2 cxi xlh fwl0 fwl1"
+LOFF = 64.0
+OFF = 2112.0
+WHOLE = 12582912.0
 BIG = 65536.0
 RES = 67108864.0
 OUT = 8192.0
 NE = 8
-QG = 5
-WAKE, LAG, VFIX, SFIX, CYC, PCYC, GATH, SCAT, FAR = 0.2, 0.05, 0.02, 0.04, 0.00083, 0.00045, 1.56, 3.8, 3.0
-PASSES, NOISE, TRIES, HEAT, EPS, REACH = 30, 1.0, 2500, 0.2, 0.05, 24
+SLOW = np.array([1.0, 1.3, 1.0])
+WAKE, LAG, VFIX, SFIX, CYC, PCYC = np.array([0.2, 0.2, 0.13]), 0.05, 0.02, 0.04, 0.00083 * SLOW, 0.00045 * SLOW
+GATH, SCAT, FAR, WEIGH = np.array([1.56, 1.7, 1.15]), np.array([3.8, 4.2, 2.2]), np.array([4.5, 6.0, 5.0]), (0.4, 0.25, 0.35)
+BULK = np.array([9.5, 12.0, 10.0])
+BULK2 = BULK + 1.0
+SEED, ROAM, VLOAD, MID, ENDS, FINE, WIDE = 12, 6, 0.1, 0, 4, 4, 70
+PASSES, NOISE, TRIES, HEAT, EPS, REACH = 6, 1.0, 1500, 0.2, 0.1, 24
 
 _S = "sbuf"
 F32, B16, I32, U16, H16 = "float32", "bfloat16", "int32", "uint16", "float16"
 PACK = {
-    "tf": (F32, (("nqd", 12), ("w1", 12), ("w2", 12), ("dm4", 12), ("dm1", 12), ("er", 16), ("ec", 16), ("pmf", 4))),
+    "tf": (F32, (("nqd", 12), ("w1", 12), ("dm4", 12), ("er", 16), ("ec", 16), ("pmf", 4))),
     "tl": (U16, (("ld", 12), ("lcl", 12), ("lp", 12), ("lk", 12))),
     "ti": (I32, (("dmi", 12), ("pmi", 4))),
-    "tb": (B16, (("wm", 16), ("wp", 16), ("wm1", 24), ("wm2", 24), ("wp1", 24), ("wp2", 24), ("cand", 12), ("exb", 16))),
-    "cb": (B16, (("one", 256), ("zero", 256), ("bl", 128), ("bt", 128), ("rp", 256), ("id", 128), ("idu", 768), ("id4", 128), ("idm", 128), ("bi", 384), ("sel", 1024), ("bj", 2048), ("gm", 128),
-                 ("btr", 128), ("tri", 128), ("tr8", 128), ("tr4", 128), ("cmp", 128), ("bl8", 128), ("bn8", 128), ("sa", 128), ("wt", 128), ("se", 128), ("dg1", 128), ("dgc", 384), ("vr", 128), ("up8", 128),
-                 ("bm", K), ("bmc", K), ("bm4", K), ("slt", 144), ("row", 512), ("c15", 128))),
+    "tb": (B16, (("wm", 16), ("wp", 16), ("wm1", 24), ("wm2", 24), ("wp1", 24), ("wp2", 24), ("cand", 12), ("exb", 16), ("rp", 8))),
+    "cb": (B16, (("one", 256), ("zero", 128), ("bl", 128), ("bt", 128), ("id", 128), ("idu", 768), ("id4", 128), ("idm", 128), ("bi", 384), ("sel", 1024), ("bj", 2048), ("gm", 128),
+                 ("btr", 128), ("tri", 128), ("tr8", 128), ("tr4", 128), ("cmp", 128), ("bl8", 128), ("bn8", 128), ("sa", 128), ("wt", 128), ("id2", 128), ("dg1", 128), ("dg7", 128),
+                 ("dgc", 384), ("vr", 128), ("up8", 128), ("bm", K), ("bmc", K), ("bm4", K), ("bme", K), ("slt", 144), ("row", 512), ("c15", 128))),
 }
 PLACE, SCRATCH, ORDERS = {}, {}, {}
 for _b in PACK:
@@ -36,29 +62,29 @@ for _b in PACK:
         _o += _w
     SCRATCH[_b] = (_S, [128, _o], PACK[_b][0])
 for _d, _l in (
-    (B16, (("xw", W + K), ("xlh", M), ("q", K), ("qb", K), ("qrep", 16 * K), ("ma", 16 * K), ("mb", 16 * K), ("mc", 16 * K), ("at", K), ("nr", K), ("nq", K), ("xo", K), ("fst", K),
+    (B16, (("xw", W + K), ("xlh", M), ("q", K), ("qb", K), ("ma", 16 * K), ("mb", 16 * K), ("mc", 16 * K), ("at", K), ("nr", K), ("nq", K), ("xo", K), ("fst", K),
            ("xl1", M), ("xl2", M), ("xl3", M))),
-    (I32, (("fw", W + K), ("ci", K), ("tgs", 256), ("pci", 256), ("lfi", M), ("cxi", K), ("ic", 256), ("ixi", 256))),
-    (U16, (("lfu", M), ("lc", K), ("lu1", M), ("lu2", M), ("lu3", M), ("lus", M), ("st", M), ("msg1", K + 16), ("msg2", K + 16), ("msg3", K + 16), ("up1", K + 12), ("up3", K + 12),
-           ("hm2", K + 12), ("hm3", K + 12))),
-    (F32, (("pw", W + K), ("lh", M + K), ("cf", K), ("sc", K), ("scd", K), ("scm", K), ("scc", K), ("dc", K), ("sg", K), ("v1", K), ("v2", K), ("s0", 256),
-           ("lw1", M), ("lw2", M + K), ("lw3", M + K))),
-    (H16, (("pt", W), ("pcs", 512), ("pa", 16 * K), ("pb", 16 * K), ("pc", 16 * K), ("g1", K), ("g2", K), ("lv", 24), ("b16", K), ("ixh", 256), ("x1", K), ("x2", K), ("rc", K),
+    (I32, (("fw", W + K), ("ci", K), ("tgs", 256), ("lfi", M), ("cxi", K), ("ic", 256), ("ixi", 256))),
+    (U16, (("lfu", M), ("lc", K), ("lu1", M), ("lu2", M), ("msg1", K + 16), ("msg2", K + 16), ("msg3", K + 16), ("up1", K + 12), ("up3", K + 12), ("hm2", K + 12), ("hm3", K + 12))),
+    (F32, (("pw", W + K), ("yw", W + K), ("yv", 256), ("lh", M + K), ("cf", K), ("sc", K), ("scd", K), ("scm", K), ("scc", K), ("dc", K), ("sg", K), ("v1", K), ("v2", K),
+           ("s0", 256), ("lw1", M), ("lw2", M + K), ("lw3", M + K))),
+    (H16, (("pt", W), ("pcs", 256), ("pa", 16 * K), ("pb", 16 * K), ("pc", 16 * K), ("g1", K), ("hn", K), ("lv", 24), ("b16", K), ("ixh", 256), ("x1", K), ("x2", K), ("rc", K),
            ("hh", K), ("sh", K))),
 ):
     for _n, _w in _l:
         SCRATCH[_n] = (_S, [128, _w], _d)
-for _n, _w, _d in (("rr", K, H16), ("cm", K, H16), ("ll", 12, U16), ("sq", K, F32), ("tt", K, I32), ("cc", K, I32), ("l12", K, U16),
+for _n, _w, _d in (("rr", K, H16), ("cm", K, H16), ("ll", 12, U16), ("sp", K, F32), ("sq", K, F32), ("tt", K, I32), ("cc", K, I32), ("l12", K, U16),
                    ("t4", 256, I32), ("fi", 16, I32), ("fl", 16, H16), ("nn", 384, B16)):
     SCRATCH[_n] = (_S, [128, 2, _w], _d)
+SCRATCH["qrep"] = (_S, [128, 16 * K], B16)
 SCRATCH["eqo"] = (_S, [128, 12, K], B16)
 SCRATCH["eqt"] = (_S, [128, 12, K], B16)
 for _n in ("psk", "psv"):
     SCRATCH[_n] = ("psum", [128, 2, 512], F32)
 for _n in ("psm", "psu", "psd", "psg"):
     SCRATCH[_n] = ("psum", [128, 512], F32)
-SEMAPHORES = ["qv", "qs", "qp", "qg"] + ["ld%d" % j for j in range(24)] + ["ls%d" % j for j in range(20)] + ["rl0", "rs"]
-SEMAPHORES += ["%s%d" % (a, j) for a in ("rl", "rx", "ru", "rh") for j in (1, 2, 3)]
+SEMAPHORES = ["qv", "qs", "qp", "qg"] + ["ld%d" % j for j in range(24)] + ["ls%d" % j for j in range(20)] + ["rl0", "rs", "rh2", "rh3"]
+SEMAPHORES += ["%s%d" % (a, j) for a in ("rl", "rx", "ru") for j in (1, 2, 3)]
 
 
 def tracker(g, T):
@@ -110,15 +136,15 @@ def tracker(g, T):
 
     def op_(q, fns, R, Wt):
         deps(q, True, R, Wt)
-        for f in fns[:-1]:
-            f()
         sem = "q" + q
-        cnt[q] += 1
-        fns[-1]().then_inc(T.sem[sem], 1)
+        for f in fns:
+            if q == "p" and f is not fns[-1]:
+                f()
+            else:
+                cnt[q] += 1
+                f().then_inc(T.sem[sem], 1)
         total[sem] = cnt[q]
         hist[(sem, cnt[q])] = dict(known[q])
-        if cnt[q] > 1:
-            hist[(sem, cnt[q])][sem] = cnt[q] - 1
         note((sem, cnt[q], q), q, R, Wt)
 
     def dma_(q, out, in_, R, Wt):
@@ -141,11 +167,10 @@ def tracker(g, T):
         wr[key] = (sem, n, None)
         rd[key] = {}
 
-    nodes, alt, behind = [], {}, {}
+    nodes, alt, steps = [], {}, []
 
     def op(q, fns, R, Wt, cost, other=None):
-        behind[len(nodes)] = [k[1:] for k in R.split() if k[0] == ">"]
-        R, Wt = [k for k in R.split() if k[0] != ">"], Wt.split()
+        R, Wt = R.split(), Wt.split()
         nodes.append((q, R, Wt, lambda: op_(q, fns, R, Wt), cost, 0.0, -1))
         if other:
             alt[len(nodes) - 1] = (other[0], R, Wt, lambda: op_(other[0], other[1], R, Wt), other[2], 0.0, -1)
@@ -156,7 +181,7 @@ def tracker(g, T):
 
     def send(call, R, local, n, on):
         R = R.split()
-        nodes.append(("g", R, [], lambda: on and send_(call, R, local, n), 0.3, 0.0, -2))
+        nodes.append(("g", R, ["sent"] if local == "ls15" else [], lambda: on and send_(call, R, local, n), 0.3, 0.0, -2))
         return len(nodes) - 1
 
     def arrives(sem, n, key, lat, after):
@@ -169,7 +194,6 @@ def tracker(g, T):
         for x, (q, R, Wt, f, n, lat, after) in enumerate(nodes):
             if after >= 0:
                 dep[x].add(after)
-            behind[x] = [w[k] for k in behind.get(x, []) if k in w]
             for k in sorted(set(R + Wt)):
                 if k.startswith("ps"):
                     who = x if x in alt else q
@@ -202,27 +226,42 @@ def tracker(g, T):
                     nxt[d].append(x)
                 else:
                     succ[d].append(x)
-            for d in behind[x]:
-                prev[x].append(d)
-                nxt[d].append(x)
-        cs = [nd_[4] for nd_ in nodes]
-        lat = [nd_[5] + (0.0 if nd_[0] == "a" else WAKE) for nd_ in nodes]
-        for q in "gd":
-            row = [x for x in range(nn) if nodes[x][0] == q and (q == "d" or nodes[x][6] == -2)]
-            for x, y in zip(row, row[1:]):
-                prev[y].append(x)
-                nxt[x].append(y)
+        nm = len(WAKE)
+        each = lambda c: [float(u) for u in c + 0.0 * WAKE]
+        qn = {q: i for i, q in enumerate("vspgda")}
+        qof = [qn[nd_[0]] for nd_ in nodes]
+        css = [list(u) for u in zip(*[each(nd_[4]) for nd_ in nodes])]
+        other = {x: (qn[alt[x][0]], each(alt[x][4])) for x in alt}
+        tails = [list(u) for u in zip(*[each(nd_[5] + (0.0 if nd_[0] == "a" else LAG)) for nd_ in nodes])]
+        wakes = each(WAKE - LAG)
+        cs = css[0]
+        lat = [tails[0][x] + (qof[x] != 5) * wakes[0] for x in range(nn)]
+        pairs = []
+        for q in (3, 4):
+            row = [x for x in range(nn) if qof[x] == q and (q == 4 or nodes[x][6] == -2)]
+            pairs += zip(row[1:], row)
+        edge = steps + [nn]
+        for u, rule in enumerate(AFTER):
+            for pair in rule.split():
+                pairs.append([[z for z in range(edge[u] * (u > 0), edge[u + 1]) if nodes[z][2][:1] == [n.strip("'")]][n.count("'")] for n in pair.split(">")])
+        first = [x for x in range(edge[0]) if nodes[x][2][:1] in (["pw0"], ["pw1"])]
+        pairs += [(x, y) for x in first for y in range(first[0]) if (qof[y] < 2 or y in other) and nodes[y][2] != ["lc"]]
+        for x, y in pairs:
+            prev[x].append(y)
+            nxt[y].append(x)
+        dl = [sorted(d) for d in dep]
+        dp = [set(dl[x] + prev[x]) for x in range(nn)]
+        sl = [set(succ[x] + nxt[x]) for x in range(nn)]
 
         def place(order, back):
-            st, busy = [0.0] * nn, {q: [] for q in "vspgd"}
+            st, busy = [0.0] * nn, [[] for q in qn]
             for x in order:
                 if back:
                     e = max([lat[x]] + [st[y] + cs[y] + lat[x] for y in succ[x]] + [st[y] + cs[y] for y in nxt[x]])
                 else:
-                    e = max([0.0] + [st[y] + cs[y] + lat[y] for y in dep[x]] + [st[y] + cs[y] for y in prev[x]])
-                q = nodes[x][0]
-                if q != "a":
-                    b = busy[q]
+                    e = max([0.0] + [st[y] + cs[y] + lat[y] for y in dl[x]] + [st[y] + cs[y] for y in prev[x]])
+                if qof[x] != 5:
+                    b = busy[qof[x]]
                     i, hi = 0, len(b)
                     while i < hi:
                         m = (i + hi) // 2
@@ -234,118 +273,179 @@ def tracker(g, T):
                 st[x] = e
             return st, max(st[x] + cs[x] + (0.0 if back else lat[x]) for x in range(nn))
 
-        def times(seq, lo, hi, rest, old=None, i=0):
-            st, why, fin = (dict(old[1]), old[2][:], old[4][:]) if old else ({}, [-1] * nn, [0.0] * nn)
-            free, last = dict.fromkeys("vspgd", 0.0), dict.fromkeys("vspgd", -1)
-            todo = set("vspgd")
-            for j in range(i - 1, -1, -1):
-                x = seq[j]
-                if qof[x] in todo:
-                    todo.discard(qof[x])
-                    free[qof[x]], last[qof[x]] = st[x] + cs[x], x
-                    if not todo:
-                        break
-            for x in seq[i:hi]:
+        def run(m, calls, fin, why, free, last):
+            c, tail, wake = css[m], tails[m], wakes[m]
+            for x in calls:
                 q, e, w = qof[x], 0.0, -1
                 for y in dl[x]:
                     if fin[y] > e:
                         e, w = fin[y], y
-                if q != "a":
+                if q != 5:
                     if e > free[q]:
-                        e += WAKE - LAG
+                        e += wake
                     else:
                         e, w = free[q], last[q]
-                    free[q], last[q] = e + cs[x], x
-                st[x], why[x], fin[x] = e, w, e + cs[x] + tail[x]
-            end, at = max([(fin[x] + rest[x], x) for x in seq[lo:hi]] + [(free[q] + rest[q], last[q]) for q in free])
-            return end + EPS * sum(fin[x] for x in seq[lo:hi]) / (hi - lo) + VLOAD * sum(cs[x] for x in seq[lo:hi] if qof[x] == "v"), st, why, at, fin
+                    e += c[x]
+                    free[q], last[q] = e, x
+                why[x], fin[x] = w, e + tail[x]
 
-        def beyond(seq, hi):
-            rest, left = dict.fromkeys(list(range(nn)) + list("vspgda"), 0.0), {}
+        def whole(seq, m=0):
+            fin, why = [0.0] * nn, [-1] * nn
+            run(m, seq, fin, why, [0.0] * 5, [-1] * 5)
+            return fin, why
+
+        def beyond(seq, hi, m):
+            rest, restq, left = [0.0] * nn, [0.0] * 6, {}
             for x in reversed(seq):
-                rest[x] = max([0.0] + [left[y] + (qof[y] != "a") * (WAKE - LAG) for y in succ[x] if y in left])
+                rest[x] = max([0.0] + [left[y] + (qof[y] != 5) * wakes[m] for y in succ[x] if y in left])
                 if len(left) < nn - hi:
-                    left[x] = cs[x] + max(tail[x] + rest[x], rest[qof[x]])
-                    rest[qof[x]] = left[x] * (qof[x] != "a")
-            return rest
+                    left[x] = css[m][x] + max(tails[m][x] + rest[x], restq[qof[x]])
+                    restq[qof[x]] = left[x] * (qof[x] != 5)
+            return rest, restq
 
         def swap(x):
-            nodes[x], alt[x] = alt[x], nodes[x]
-            qof[x], cs[x] = nodes[x][0], nodes[x][4]
+            q, c = other[x]
+            other[x] = (qof[x], [u[x] for u in css])
+            qof[x] = q
+            for m in range(nm):
+                css[m][x] = c[m]
 
-        def polish(seq, lo, hi, heat, rnd):
-            rest, inside = beyond(seq, hi), set(seq[lo:hi])
-            cur = best = times(seq, lo, hi, rest)
-            bseq, bq = seq, list(qof)
+        def polish(seq, lo, hi, heat, rnd, nm):
+            rests = [beyond(seq, hi, m) for m in range(nm)]
+            state = [whole(seq, m) for m in range(nm)]
+            scale = [WEIGH[m] / sum(WEIGH[0:nm]) * max(state[0][0]) / max(state[m][0]) for m in range(nm)]
+            win, n = seq[lo:hi], hi - lo
+            inside = set(win)
+            ends = [[x for x in win if rests[m][0][x] > 0.0 or not succ[x]] for m in range(nm)]
+            before = [-1] * 6
+            for x in seq[0:lo]:
+                before[qof[x]] = x
+
+            def value(new, i):
+                last0, todo, got = before[:], 5, [False] * 6
+                for j in range(i - 1, -1, -1):
+                    q = qof[new[j]]
+                    if not got[q]:
+                        got[q], last0[q] = True, new[j]
+                        todo -= q != 5
+                        if not todo:
+                            break
+                tot, ats, part = 0.0, [], new[i:]
+                for m in range(nm):
+                    fin, why = state[m]
+                    tail, (rest, restq) = tails[m], rests[m]
+                    free, last = [fin[x] - tail[x] if x >= 0 else 0.0 for x in last0], last0[:]
+                    run(m, part, fin, why, free, last)
+                    end, at = max([(fin[x] + rest[x], x) for x in ends[m]] + [(free[q] + restq[q], last[q]) for q in range(5)])
+                    tot += scale[m] * (end + EPS * sum([fin[x] for x in new]) / n)
+                    ats.append(at)
+                return tot + VLOAD * sum([cs[x] for x in new if qof[x] == 0 and x >= steps[0]]), ats
+            cur = best = value(win, 0)
+            bwin, bq = win, list(qof)
             for it in range(TRIES):
-                path, x = [], cur[3]
-                while x in inside:
-                    y = cur[2][x]
-                    if y in inside and qof[y] == qof[x] and y not in dp[x]:
-                        path.append((y, x))
-                    x = y
                 rnd = (rnd * 1103515245 + 12345) % 2147483648
-                if (rnd >> 4) % 16 < ROAM or not path:
-                    j = lo + (rnd >> 8) % (hi - lo)
+                path, x, why = [], cur[1][it % nm], state[it % nm][1]
+                if (rnd >> 4) % 16 >= ROAM:
+                    while x in inside:
+                        y = why[x]
+                        if y in inside and qof[y] == qof[x] and y not in dp[x]:
+                            path.append((y, x))
+                        x = y
+                if not path:
+                    j = (rnd >> 8) % n
                     i = j - 1
-                    while i >= lo and qof[seq[i]] != qof[seq[j]]:
+                    while i >= 0 and qof[win[i]] != qof[win[j]]:
                         i -= 1
-                    if i < lo or qof[seq[j]] not in "vspg" or seq[i] in dp[seq[j]]:
+                    if i < 0 or qof[win[j]] > 3 or win[i] in dp[win[j]]:
                         continue
-                    path = [(seq[i], seq[j])]
+                    path = [(win[i], win[j])]
                 y, x = path[(rnd >> 8) % len(path)]
-                turn = [z for z in (x, y) if z in alt and (rnd >> 20) % 3 == 0][:1]
+                turn = [z for z in (x, y) if z in other and (rnd >> 20) % 3 == 0][:1]
                 for z in turn:
                     swap(z)
-                i, j = seq.index(y), seq.index(x)
+                i, j = win.index(y), win.index(x)
                 rnd = (rnd * 1103515245 + 12345) % 2147483648
                 more = (rnd >> 8) % 4 if (rnd >> 16) % 4 else (rnd >> 8) % REACH
                 if turn:
-                    new = seq
+                    new = win
                 elif (rnd >> 12) % 2:
-                    while more and i > lo:
+                    while more and i > 0:
                         i -= 1
-                        more -= qof[seq[i]] == qof[x]
+                        more -= qof[win[i]] == qof[x]
                     need = {x}
-                    for z in reversed(seq[i:j]):
-                        if any(u in need for u in sl[z]):
+                    for z in reversed(win[i:j]):
+                        if not need.isdisjoint(sl[z]):
                             need.add(z)
-                    new = seq[:i] + [z for z in seq[i:j + 1] if z in need] + [z for z in seq[i:j + 1] if z not in need] + seq[j + 1:]
+                    new = win[:i] + [z for z in win[i:j + 1] if z in need] + [z for z in win[i:j + 1] if z not in need] + win[j + 1:]
                 else:
-                    while more and j < hi - 1:
+                    while more and j < n - 1:
                         j += 1
-                        more -= qof[seq[j]] == qof[x]
+                        more -= qof[win[j]] == qof[x]
                     need = {y}
-                    for z in seq[i + 1:j + 1]:
-                        if any(u in need for u in dp[z]):
+                    for z in win[i + 1:j + 1]:
+                        if not need.isdisjoint(dp[z]):
                             need.add(z)
-                    new = seq[:i] + [z for z in seq[i:j + 1] if z not in need] + [z for z in seq[i:j + 1] if z in need] + seq[j + 1:]
-                tr = times(new, lo, hi, rest, cur, i)
+                    new = win[:i] + [z for z in win[i:j + 1] if z not in need] + [z for z in win[i:j + 1] if z in need] + win[j + 1:]
+                part = win[i:]
+                keep = [([fin[z] for z in part], [why[z] for z in part]) for fin, why in state]
+                tr = value(new, i)
                 rnd = (rnd * 1103515245 + 12345) % 2147483648
                 if tr[0] < cur[0] + heat * (1.0 - it / TRIES) * (rnd >> 8) / 8388608:
                     cur = tr
-                    seq = new[:lo] + sorted(new[lo:hi], key=tr[1].get) + new[hi:]
+                    fin, tail = state[0][0], tails[0]
+                    win = sorted(new, key=lambda z: fin[z] - tail[z] - cs[z])
                     if tr[0] < best[0]:
-                        best, bseq, bq = tr, seq, list(qof)
+                        best, bwin, bq = tr, win, list(qof)
                 else:
                     for z in turn:
                         swap(z)
-            for x in alt:
+                    for (fin, why), (f0, w0) in zip(state, keep):
+                        for z, a, b in zip(part, f0, w0):
+                            fin[z], why[z] = a, b
+            for x in other:
                 if qof[x] != bq[x]:
                     swap(x)
-            st = times(bseq, 0, nn, beyond(bseq, nn))[1]
-            return sorted(bseq, key=st.get)
-        qof = [nd_[0] for nd_ in nodes]
-        dl = [sorted(d) for d in dep]
-        dp = [dl[x] + prev[x] for x in range(nn)]
-        sl = [succ[x] + nxt[x] for x in range(nn)]
-        tail = [nd_[5] + (0.0 if nd_[0] == "a" else LAG) for nd_ in nodes]
-        pr = [0.0] * nn
-        for x in range(nn - 1, -1, -1):
-            pr[x] = cs[x] + max([lat[x]] + [pr[y] + lat[x] for y in succ[x]] + [pr[y] for y in nxt[x]])
-        order = sorted(range(nn), key=lambda x: (-pr[x], x))
+            seq = seq[:lo] + bwin + seq[hi:]
+            fin = whole(seq)[0]
+            return sorted(seq, key=lambda z: fin[z] - tails[0][z] - cs[z])
+
+        def sweep(seq, a, b, count, heat, nm):
+            for rnd in range(count):
+                for lo in range(a - WIDE // 2 + rnd % 2 * WIDE // 4, b - WIDE // 2, WIDE // 2):
+                    seq = polish(seq, max(lo, 0), min(lo + WIDE, nn), heat * (1.0 - rnd / count), SEED + lo + rnd, nm)
+            return seq
         alike = tuple((nd_[0], tuple(nd_[1]), tuple(nd_[2])) for nd_ in nodes)
         if alike not in ORDERS:
+            named = [{} for u in edge]
+            for u in range(RO):
+                for x in range(edge[u], edge[u + 1]):
+                    n = (nodes[x][2] + [""])[0]
+                    named[u].setdefault("".join(c for c in n if c not in "123") if n[:2] in ("ms", "lw") else n, []).append(x)
+            for q, plan in enumerate(PLAN):
+                row = []
+                for u in range(-1, RO):
+                    for n in plan[max(u, 0)].split():
+                        have = named[u + (n[0] == "+")].get(n.strip("+"), [])
+                        got = [x for x in have if qof[x] == q or x in other and other[x][0] == q]
+                        if got and (u >= 0 or n[0] == "+"):
+                            row.append(got[0])
+                            have.remove(got[0])
+                for x, y in zip(row, row[1:] + [-1]):
+                    if qof[x] != q:
+                        swap(x)
+                    if y >= 0:
+                        nxt[x].append(y)
+                        prev[y].append(x)
+            topo, left = [x for x in range(nn) if not dl[x] and not prev[x]], [len(dl[x]) + len(prev[x]) for x in range(nn)]
+            for x in topo:
+                for y in succ[x] + nxt[x]:
+                    left[y] -= 1
+                    if not left[y]:
+                        topo.append(y)
+            pr = [0.0] * nn
+            for x in reversed(topo):
+                pr[x] = cs[x] + max([lat[x]] + [pr[y] + lat[x] for y in succ[x]] + [pr[y] for y in nxt[x]])
+            order = sorted(range(nn), key=lambda x: (-pr[x], x))
             seed, best = 1, None
             for rnd in range(PASSES):
                 st, end = place(order, False)
@@ -356,30 +456,28 @@ def tracker(g, T):
                     st = best[1]
                 bk = place(sorted(range(nn), key=lambda x: (-st[x] - cs[x], -x)), True)[0]
                 key = [0.0] * nn
-                for x in range(nn - 1, -1, -1):
+                for x in reversed(topo):
                     seed = (seed * 1103515245 + 12345) % 2147483648
-                    key[x] = max([bk[x] + cs[x] + shake * seed / 2147483648] + [key[y] + 1e-6 for y in sl[x]])
+                    key[x] = max([bk[x] + cs[x] + shake * seed / 2147483648] + [key[y] + 1e-6 for y in succ[x] + nxt[x]])
                 order = sorted(range(nn), key=lambda x: (-key[x], x))
             seq = sorted(range(nn), key=lambda x: (best[1][x], x))
-            for rnd in range(SWEEPS):
-                for lo in range(-WIDE // 2 + rnd % 2 * WIDE // 4, nn - WIDE // 2, WIDE // 2):
-                    seq = polish(seq, max(lo, 0), min(lo + WIDE, nn), HEAT * (1.0 - rnd / SWEEPS), SEED + lo + rnd)
-            best = times(seq, 0, nn, beyond(seq, nn))
-            path, x = [], best[3]
-            while x >= 0:
-                path.append((round(best[1][x], 1), qof[x], nodes[x][2][:1]))
-                x = best[2][x]
-            ORDERS[alike] = (seq, list(qof), max(best[4]), path[::-1])
-        seq, queue = ORDERS[alike][0:2]
+            seq = sweep(seq, steps[1] - WIDE // 2, steps[2] + WIDE, MID, HEAT, nm)
+            seq = sweep(seq, 0, steps[0] + WIDE, ENDS, HEAT, nm)
+            seq = sweep(seq, steps[0], steps[1], ENDS, HEAT, nm)
+            seq = sweep(seq, steps[2], nn, 2 * ENDS, HEAT, nm)
+            seq = sweep(seq, 0, nn, FINE, HEAT / 3, nm)
+            ORDERS[alike] = (seq, list(qof))
+        seq, queue = ORDERS[alike]
         for x in seq:
             if qof[x] != queue[x]:
                 swap(x)
-            nodes[x][3]()
+        for x in seq:
+            (nodes[x] if qn[nodes[x][0]] == qof[x] else alt[x])[3]()
         for sem in total:
             if known["g"].get(sem, 0) < total[sem]:
                 g.wait_ge(T.sem[sem], total[sem])
                 learn("g", sem, total[sem])
-    return op, dma, send, arrives, finish
+    return op, dma, send, arrives, finish, lambda: steps.append(len(nodes))
 
 
 def rank_program(g, core, T, topo):
@@ -387,7 +485,7 @@ def rank_program(g, core, T, topo):
     if r is None:
         return
     v, s, p = g.vector, g.scalar, g.tensor
-    op, dma, put, arrives, finish = tracker(g, T)
+    op, dma, put, arrives, finish, step = tracker(g, T)
 
     def C(n, a=0, b=None, p0=0, p1=128, st=1):
         bf, o, w = PLACE[n]
@@ -406,6 +504,9 @@ def rank_program(g, core, T, topo):
         if "16" in str(o.dtype) and "16" in str(a.dtype):
             per *= 0.5
         return VFIX + CYC * max(64, per * wid(o))
+
+    def scost(o):
+        return SFIX + CYC * max(64, wid(o))
 
     def ncost(n, fix=VFIX):
         return fix + 0.03 + CYC * (GATH * n if n > 0 else -SCAT * n)
@@ -426,33 +527,45 @@ def rank_program(g, core, T, topo):
         op("v", [lambda: v.memset(o, c)], "", Wt, vcost(o, o))
 
     def act(o, a, R, Wt, f=AF.Identity, n=0, **kw):
-        op("s", [lambda: s.activation(o, a, f, **kw)], R, Wt, ncost(n, SFIX) if n else SFIX + CYC * max(64, wid(o)))
+        op("s", [lambda: s.activation(o, a, f, **kw)], R, Wt, ncost(n, SFIX) if n else scost(o))
+
+    def either(q, on_s, on_v, R, Wt, cost_s, cost_v):
+        x, y = ("s", [on_s], cost_s), ("v", [on_v], cost_v)
+        if q == "v":
+            x, y = y, x
+        op(x[0], x[1], R, Wt, x[2], y)
 
     def mv(q, o, a, R, Wt, scale=1.0, bias=0.0):
-        if q == "g":
-            return gop(lambda: g.affine_select(o, a, [[0, wid(o)]], Op.is_ge, 0.0, 0, 0), R, Wt, wid(o))
-        on_s = ("s", [lambda: s.activation(o, a, AF.Copy, scale=scale, bias=bias)], SFIX + CYC * max(64, wid(o)))
+        on_s = lambda: s.activation(o, a, AF.Copy, scale=scale, bias=bias)
+        if q == "g" or Wt in ONG.split():
+            on_g = lambda: g.affine_select(o, a, [[0, n] for n in list(o.shape)[1:]], Op.is_ge, 0.0, 0, 0)
+            return op("g", [on_g], R, Wt, 0.17 + 2 * CYC * wid(o), None if q == "g" else ("s", [on_s], scost(o)))
         if scale == 1.0 and bias == 0.0:
-            on_v = ("v", [lambda: v.tensor_copy(o, a)], vcost(o, a))
+            on_v = lambda: v.tensor_copy(o, a)
         else:
-            on_v = ("v", [lambda: v.tensor_scalar(o, a, scale, bias, Op.mult, Op.add)], vcost(o, a))
-        x, y = (on_s, on_v) if q == "s" else (on_v, on_s)
-        op(x[0], x[1], R, Wt, x[2], y)
+            on_v = lambda: v.tensor_scalar(o, a, scale, bias, Op.mult, Op.add)
+        either(q, on_s, on_v, R, Wt, scost(o), vcost(o, a))
+
+    def take(o, a, R, Wt, bias=0.0, lend=True):
+        on_s = lambda: s.activation(o, a, AF.Copy, bias=bias)
+        on_v = (lambda: v.tensor_scalar(o, a, bias, None, Op.add)) if bias else (lambda: v.tensor_copy(o, a))
+        op("s", [on_s], R, Wt, ncost(wid(o), SFIX), ("v", [on_v], ncost(wid(o))) if lend else None)
 
     def relu(q, o, a, R, Wt, scale=1.0, bias=0.0):
-        on_s = ("s", [lambda: s.activation(o, a, AF.Relu, scale=scale, bias=bias)], SFIX + CYC * max(64, wid(o)))
-        on_v = ("v", [lambda: v.tensor_scalar(o, a, bias or scale, 0.0, Op.add if bias else Op.mult, Op.max)], vcost(o, a))
-        x, y = (on_s, on_v) if q == "s" else (on_v, on_s)
-        op(x[0], x[1], R, Wt, x[2], y)
+        either(q, lambda: s.activation(o, a, AF.Relu, scale=scale, bias=bias),
+               lambda: v.tensor_scalar(o, a, bias or scale, 0.0, Op.add if bias else Op.mult, Op.max), R, Wt, scost(o), vcost(o, a))
 
     def mm(o, l, x, st, sp):
-        return (lambda: p.matmul(o, l, x, st, sp), PCYC * max(64, wid(x)))
+        return (lambda: p.matmul(o, l, x, st, sp), PCYC * max(min(64, wid(l)), wid(x)))
 
     def pe(fs, R, Wt):
         op("p", [f[0] for f in fs], R, Wt, sum(f[1] for f in fs))
 
     def scan(o, d, R, Wt, n=K, p1=128):
         op("v", [lambda: v.tensor_tensor_scan(o, T.s0[0:p1, 0:n], d, 0.0, Op.add, Op.min)], R + " s0", Wt, VFIX + CYC * n)
+
+    def spare(o, d, j, R, Wt):
+        op("v", [lambda: v.tensor_tensor_scan(o, T.sp[:, j, :], d, 0.0, Op.max, Op.min)], R + " sp%d" % j, Wt, VFIX + CYC * K)
 
     def gop(f, R, Wt, n):
         op("g", [f], R, Wt, 0.17 + 2 * CYC * n)
@@ -467,33 +580,33 @@ def rank_program(g, core, T, topo):
     PW = keys("pw", 8) + " pwd"
     XW = keys("xw", 4)
     FW = keys("fwl", 4) + " " + keys("fw", 4)
-    QR = keys("qr", 16)
+    QR = keys("qr", 6)
     def tags():
         gop(lambda: g.iota(T.ixi[0:16, :], [[1, 256]], -2048, 256), "", "ixi", 256)
         mv("s", T.ixh[0:16, :], T.ixi[0:16, :], "ixi", "ixh")
-        dma("d", T.pt[16:17, :], T.ixh[0:16, :], "ixh", "pt2", 8)
-        ts(T.pci[:], T.tgs[:], 1, Op.bitwise_and, "tgs", "pci")
-        for j, (n, src) in enumerate((("tgs", T.tgs), ("pci", T.pci))):
-            mv("s", T.pcs[:, 256 * j:256 * j + 256], src[:], n, "pcs%d" % j)
-            dma("d", T.pt[8 * j:8 * j + 8, :], T.pcs[:, 256 * j:256 * j + 256], "pcs%d" % j, "pt%d" % j, 64)
+        dma("d", T.pt[8:9, :], T.ixh[0:16, :], "ixh", "pt2", 8)
+        mv("s", T.pcs[:], T.tgs[:], "tgs", "pcs")
+        dma("d", T.pt[0:8, :], T.pcs[:], "pcs", "pt0", 64)
     parts = {"tgs": (T.tgs[:], T.tg[:], 128), "cxi": (T.cxi[:], T.cx[:], 96), "q": (T.q[:], T.qx[:], 48), "xlh": (T.xlh[:], T.xl[:], 256),
              "lfi0": (T.lfi[:, 0:LCUT], T.lf[:, 0:LCUT], LCUT / 2), "lfi1": (T.lfi[:, LCUT:M], T.lf[:, LCUT:M], (M - LCUT) / 2)}
-    for c in range(4):
-        a, b = XCUT[c:c + 2]
+    for c, (a, b) in enumerate(zip(XCUT, XCUT[1:])):
         parts["xw%d" % c] = (T.xw[:, a:b], T.xr[:, a:b], (b - a) / 4)
-        parts["fwl%d" % c] = (T.fw[:, 512 * c:512 * c + 512], T.fd[:, 512 * c:512 * c + 512], 256)
+    for c, (a, b) in enumerate(zip(FCUT, FCUT[1:])):
+        parts["fwl%d" % c] = (T.fw[:, a:b], T.fd[:, a:b], (b - a) / 2)
     for n in LOADS.split():
         if n == "pt":
             tags()
-        else:
+        elif n != "lfi1" or LCUT < M:
             dma("d", parts[n][0], parts[n][1], "", n, parts[n][2])
+    ts(T.lfu[:, 0:LCUT], T.lfi[:, 0:LCUT], LOFF, Op.add, "lfi0", "lfu0")
+    arrives("rl0", NE, "lu0", BULK, send(T.lfu[:, 0:LCUT], "lfu0", r - 1, T.lu1[:, 0:LCUT], "rl0", "ls15", True))
     fill(C("one"), 1.0, "one")
     fill(C("zero"), 0.0, "zero")
     gop(lambda: g.iota(C("pmi", 0, 1), [[0, 1]], 0, 1), "", "pmi", 1)
     gop(lambda: g.iota(T.ic[:], [[0, 16], [1, 16]], 0, 0), "", "ic", 256)
     gop(lambda: g.affine_select(C("bl"), C("one", 0, 128), [[-16, 8], [0, 16]], Op.is_ge, 0.0, 0, 1), "one", "bl", 128)
     gop(lambda: g.affine_select(C("bl"), C("bl"), [[16, 8], [0, 16]], Op.is_ge, 0.0, 15, -1), "bl", "bl", 128)
-    gop(lambda: g.affine_select(C("rp", p1=32), C("one", p1=32), [[-8, 2], [-1, 8], [0, 16]], Op.is_equal, 0.0, 0, 1), "one", "rp", 256)
+    gop(lambda: g.affine_select(C("rp", p1=32), C("one", 0, 8, p1=32), [[-1, 8]], Op.is_equal, 0.0, 0, 1), "one", "rp", 8)
     gop(lambda: g.affine_select(C("bt"), C("bl"), [[1, 128]], Op.is_ge, 0.0, 0, -1), "bl", "bt", 128)
     gop(lambda: g.iota(C("dmi"), [[16, 12]], 0, 0), "", "dmi", 12)
 
@@ -506,33 +619,27 @@ def rank_program(g, core, T, topo):
     diag("tri", 0, -1.0, "bt")
     E = lambda i: C("er", i, i + 1)
     D = lambda i, p1=128: C("ec", i, i + 1, p1=p1)
-    RP = lambda f, st=1: C("rp", 128 * f, 128 * f + 128, p1=32, st=st)
     b8 = C("bl", st=16)
     PM = C("pmf", 0, 1)
 
     def times(o, a, w, R, Wt):
-        if wid(o) < 64:
-            act(o, a, R, Wt, scale=w)
-        else:
-            ts(o, a, w, Op.mult, R, Wt)
+        either("s" if wid(o) < 64 else "v", lambda: s.activation(o, a, AF.Identity, scale=w), lambda: v.tensor_scalar(o, a, w, None, Op.mult), R, Wt, scost(o), vcost(o, a))
 
     def scaled(n, a, w, key):
         o = C(n, a, a + 128)
-        op("g", [lambda: g.affine_select(o, C("zero", 0, 128), [[-1, 128]], Op.not_equal, w, 0, 1)], "id zero", key, 0.17 + 256 * CYC,
+        op("g", [lambda: g.affine_select(o, C("zero", 0, 128), [[-1, 128]], Op.not_equal, w, 0, 1)], "id zero sent", key, 0.17 + 256 * CYC,
            ("v", [lambda: v.tensor_scalar(o, C("id"), w, None, Op.mult)], VFIX + 64 * CYC))
-    ts(D(9), C("pmi", 0, 1), 16.0, Op.is_equal, "pmi", "ec9")
+    ts(D(9), C("pmi", 0, 1), 8.0, Op.is_equal, "pmi", "ec9")
     ts(C("pmi", 1, 2), C("pmi", 0, 1), 15, Op.bitwise_and, "pmi", "pmj")
     cp(PM, C("pmi", 1, 2), "pmj", "pmf")
     ts(C("er"), T.ic[:, 0:16], PM, Op.is_equal, "ic pmf", "er")
-    ts(D(1), E(2), -0.5, Op.mult, "er", "ec1")
+    ts(D(1), E(2), -0.25, Op.mult, "er", "ec1")
+    ts(D(8), E(2), OFF, Op.add, "er", "ec8")
     ts(D(0), E(0), 0.5, Op.mult, "er ec1", "ec0", D(1), Op.add)
     ts(D(2), E(1), E(3), Op.add, "er", "ec2", 32768.0, Op.mult)
     ts(D(6), D(2), E(0), Op.add, "er ec2", "ec6")
     ts(D(3), E(3), -1.0, Op.mult, "er", "ec3")
-    ts(D(4), E(2), -1.0, Op.mult, "er", "ec4")
-    ts(D(5), PM, 4.0, Op.is_ge, "pmf", "ec5")
-    ts(D(7), D(5), E(3), Op.add, "ec5 er", "ec7", E(1), Op.add)
-    ts(D(8), D(0), 2.0, Op.mult, "ec0", "ec8")
+    ts(D(7), PM, 1.0, Op.is_ge, "pmf", "ec7")
     ts(D(10), D(2), E(7), Op.add, "er ec2", "ec10")
     for n in ("sa", "wt", "vr", "slt", "row"):
         fill(C(n), 0.0, n)
@@ -540,34 +647,39 @@ def rank_program(g, core, T, topo):
     times(C("slt", 15, 143, st=16), b8, D(0), "bl ec0 slt", "slt")
     fill(C("c15", p1=1), 1.5, "c15")
     for i in range(max(CUT[1], K - CUT[1]) // 16):
-        gop(lambda i=i: g.affine_select(C("sel", 128 * i, 128 * i + 128), C("one", 0, 128), [[0, 8], [-1, 16]], Op.is_equal, 0.0, -16 * i, 1), "one", "sel%d" % i, 128)
-    for i in range(16):
-        times(C("bj", 128 * i, 128 * i + 128), C("bl"), E(i), "bl er", "bj%d" % i)
+        gop(lambda i=i: g.affine_select(C("sel", 128 * i, 128 * i + 128), C("one", 0, 128), [[0, 8], [-1, 16]], Op.is_equal, 0.0, -16 * i, 1), "one sent", "sel%d" % i, 128)
+    for i in range(0, 16, 4):
+        op("v", [lambda u=u: v.tensor_scalar(C("bj", 128 * u, 128 * u + 128), C("bl"), E(u), None, Op.mult) for u in range(i, i + 4)], "bl er", keys("bj", i + 4, i), 4 * (VFIX + 64 * CYC))
     ts(D(15), C("pmi", 0, 1), PM, Op.subtract, "pmi pmf", "ec15", 0.125, Op.mult)
     ts(C("gm"), T.ic[:, 0:256:2], D(15), Op.not_equal, "ic ec15", "gm", BIG, Op.mult)
     ts(C("gm"), C("gm"), 2048.0, Op.add, "gm", "gm")
     for j in (0, 1):
         times(C("sa", 1 + 2 * j, 128, st=16), b8, 1.0, "bl sa", "sa%d" % j)
-        times(C("wt", 2 * j, 128, p1=32, st=16), RP(j, 16), 1.0, "rp wt", "wt%d" % j)
         times(C("wm", 8 * j, 8 * j + 8), b8, -131072.0, "bl", "wm%d" % j)
         times(C("wp", 8 * j, 8 * j + 8), b8, D((6, 10)[j]), "bl ec10 ec6", "wp%d" % j)
         ts(C("row", 128 * j, 128 * j + 128, p1=1), T.ic[0:1, 0:128], 4096.0, Op.mult, "ic row", "rowa%d" % j, 2048.0 * j, Op.add)
         ts(C("row", 128 * j, 128 * j + 128, 64, 65), C("one", 0, 128, 64, 65), (-OUT, -2048.0)[j], Op.mult, "one row", "rowu%d" % j)
-        cp(C("row", 384 + 2 * j, 512, p1=1, st=16), C("one", 0, 8, p1=1), "one row", "rowc%d" % j)
-    fill(T.pw[:, W:W + K], 0.0, "pwd")
-    cp(T.lc[:], T.cxi[:], "cxi", "lc")
-    for i in range(16):
-        mv("vs"[i % 2], T.qrep[:, i:16 * K:16], T.q[:], "q", "qr%d" % i)
+    times(C("wt", 0, 128, p1=32, st=16), C("rp", p1=32), 1.0, "rp wt", "wt0")
+    cp(C("row", 384, 512, p1=1, st=16), C("one", 0, 8, p1=1), "one row", "rowc")
+    fill(T.pw[:, W:W + K], OFF, "pwd")
+    mv("s", T.lc[:], T.cxi[:], "cxi", "lc")
+
+    def spread(src, bias, how):
+        for i in (0, 1):
+            mv(how[i], T.qrep[:, 8 * i:16 * K:16], src[:], "qb" if bias else "q", "qr%d" % i, bias=bias)
+        for i, (a, n) in enumerate(((4, 8), (1, 4), (2, 4), (3, 4))):
+            mv(how[2 + i], T.qrep[:, a:16 * K:n], T.qrep[:, 0:16 * K:n], keys("qr", 2 + (i > 0)), "qr%d" % (2 + i))
+    spread(T.q, 0.0, QHOW[0])
     ts(T.s0[:], T.ic[:], 0.0, Op.is_equal, "ic", "s0", RES, Op.mult)
     ts(C("bm"), T.ic[:, 0:K], PM, Op.not_equal, "ic pmf", "bm", BIG, Op.mult)
-    ts(C("bmc"), C("bm"), OUT + 34816.0, Op.add, "bm", "bmc")
+    op("s", [lambda: s.activation(C("bmc"), C("bm"), AF.Silu, bias=OUT + 34816.0)], "bm", "bmc", SFIX + CYC * K + 1.3)
     ts(C("bm4"), C("bm"), -5120.0, Op.add, "bm", "bm4")
     for j, w in enumerate((0.0, -1.0, -1.0)):
         scaled("bi", 128 * j, w, "bi%d" % j)
-    for nm, cols in (("wm1", (2.0, 0.0, 0.0)), ("wm2", (-2.0, 0.0, 0.0)), ("wp1", (D(3), D(0), 0.0)), ("wp2", (E(3), 0.0, D(0)))):
-        for j, w in enumerate(cols):
-            times(C(nm, 8 * j, 8 * j + 8), b8, w, "bl er ec0 ec3", "%s_%d" % (nm, j))
-    for n, w in (("id4", 4.0), ("idm", -0.5)):
+    fill(T.tb[:, 32:128], 0.0, "wz")
+    for nm, j, w in (("wm1", 0, 2.0), ("wm2", 0, -2.0), ("wp1", 0, D(3)), ("wp1", 1, D(0)), ("wp2", 0, E(3)), ("wp2", 2, D(0))):
+        times(C(nm, 8 * j, 8 * j + 8), b8, w, "bl er ec0 ec3 wz", "%s_%d" % (nm, j))
+    for n, w in (("id4", 4.0), ("idm", -0.5), ("id2", 2.0)):
         scaled(n, 0, w, n)
     for j, w in enumerate((-2.0, 1.0, 0.5, 2.0, -1.0, -0.5)):
         scaled("idu", 128 * j, w * OUT, "idu%d" % j)
@@ -577,34 +689,39 @@ def rank_program(g, core, T, topo):
     times(C("cmp"), C("bl"), D(11), "bl ec11", "cmp")
     times(C("bn8"), C("bl"), 2048.0 - OUT, "bl", "bn8")
     mv("s", C("lk"), C("dmi"), "dmi", "lk", 0.0625)
-    times(C("se"), C("bl"), D(4), "bl ec4", "se")
+    mv("v", C("bme"), C("bm"), "bm", "bme", bias=-4096.0)
     ts(C("dm4"), C("dmi"), PM, Op.add, "dmi pmf", "dm4", float(W), Op.add)
-    ts(C("dm1"), C("dmi"), PM, Op.add, "dmi pmf", "dm1", float(M), Op.add)
+    for j, n in enumerate((W, M)):
+        fill(T.sp[:, j, :], 0.0, "sp%d" % j)
+        ts(T.sp[:, j, 0:K:16], C("dmi"), PM, Op.add, "dmi pmf sp%d" % j, "sp%d" % j, float(n), Op.add)
     fill(C("exb"), 0.0, "exb")
-    times(C("dg1"), C("id"), D(5), "id ec5", "dg1")
-    times(C("dg1", 0, 128, st=16), b8, D(8), "bl ec8 dg1", "dg1")
+    times(C("dg1"), C("id2"), E(0), "id2 er", "dg1")
+    times(C("dg7"), C("id"), E(7), "id er", "dg7")
     times(C("vr", 0, 128, st=16), b8, 2.0, "bl vr", "vr")
     for t in range(RO):
         ts(C("row", 128 * t, 128 * t + 128, 96, 97), T.ic[96:97, 0:128], 4.0 + t, Op.is_equal, "ic row", "rowm%d" % t)
+        fill(C("row", 128 * t, 128 * t + 128, 96, 97, 16), -2048.0, "rowm%d" % t)
         ts(D(12 + t), E(4 + t), -1.0, Op.mult, "er", "ec%d" % (12 + t))
         times(C("dgc", 128 * t, 128 * t + 128), C("id"), D(7), "id ec7", "dgc%d" % t)
-        for j in (0, 2):
-            times(C("dgc", 128 * t + j, 128 * t + 128, st=16), b8, D(12 + t), "bl ec%d dgc%d" % (12 + t, t), "dgc%d%d" % (t, j))
+        times(C("dgc", 128 * t, 128 * t + 128, st=16), b8, D(12 + t), "bl ec%d dgc%d" % (12 + t, t), "dgc%d0" % t)
     banks = (("psv0", T.psv[:, 0, :]), ("psv1", T.psv[:, 1, :]), ("psm", T.psm[:]), ("psu", T.psu[:]), ("psd", T.psd[:]), ("psg", T.psg[:]),
              ("psk0", T.psk[:, 0, :]), ("psk1", T.psk[:, 1, :]))
+    pe([mm(ap, C("wt", p1=9), T.pt[0:9, 512 * c:512 * c + 512], True, False) for c, (bk, ap) in enumerate(banks)], "wt0 wt2 pt0 pt2", " ".join(x[0] for x in banks))
     for c, (bk, ap) in enumerate(banks):
-        pe([mm(ap, C("wt", p1=17), T.pt[0:17, 512 * c:512 * c + 512], True, False)], "wt0 wt1 wt2 pt0 pt1 pt2", bk)
-        pe([mm(ap, C("sa"), T.xw[:, 512 * c:512 * c + 512], False, True)], "sa0 sa1 xw%d" % sum(x <= 512 * c for x in XCUT[1:]), bk)
-        mv("sv"[c % 2], T.pw[:, 512 * c:512 * c + 512], ap, bk, "pw%d" % c)
+        pe([mm(ap, C("sa"), T.xw[:, 512 * c:512 * c + 512], False, True)], "sa0 sa1 turn xw%d" % sum(x <= 512 * c for x in XCUT[1:]), bk + " turn")
+        o = T.pw[:, 512 * c:512 * c + 512]
+        if c in PWV:
+            ts(o, ap, D(8), Op.add, bk + " ec8", "pw%d" % c)
+        else:
+            act(o, ap, bk + " ec8 bmc", "pw%d" % c, bias=D(8))
 
-    mv("v", T.lfu[:, 0:LCUT], T.lfi[:, 0:LCUT], "lfi0", "lfu0")
-    mv(LQ, T.lfu[:, LCUT:M], T.lfi[:, LCUT:M], "lfi1", "lfu1")
     chip = lambda x: topo.chip(T.cores[x % N])
 
     def handed(src, j):
         return j > 1 and chip(src - j) == chip(src - j + 1) != chip(src)
-    arrives("rl0", NE, "lu0", BULK, send(T.lfu[:, 0:LCUT], "lfu0", r - 1, T.lu1[:, 0:LCUT], "rl0", "ls15", True))
-    arrives("rl1", NE, "lu1", FAR + (M - LCUT) / 240, send(T.lfu[:, LCUT:M], "lfu1", r - 1, T.lu1[:, LCUT:M], "rl1", "ls0", True))
+    if LCUT < M:
+        mv(LQ, T.lfu[:, LCUT:M], T.lfi[:, LCUT:M], "lfi1", "lfu1", bias=LOFF)
+        arrives("rl1", NE, "lu1", FAR + (M - LCUT) / 240, send(T.lfu[:, LCUT:M], "lfu1", r - 1, T.lu1[:, LCUT:M], "rl1", "ls0", True))
     arrives("rx1", NE, "xl1", BULK, send(T.xlh[:], "xlh", r - 1, T.xl1[:], "rx1", "ls1", True))
     send(T.lfu[:], "lfu0 lfu1", r - 2, T.lu2[:], "rl2", "ls2", True, not handed(r, 2))
     for j in (2, 3):
@@ -616,71 +733,82 @@ def rank_program(g, core, T, topo):
         a, b = "xl%d" % i, "xl%d" % (i + 1)
         arrives("rx%d" % (i + 1), NE, b, BULK, send(T[a][:], a, r - 1, T[b][:], "rx%d" % (i + 1), "ls%d" % (15 + 2 * i), True, handed(r + i, i + 1)))
     hand_on(1)
-    for c in range(4):
-        a, b = 512 * c, 512 * c + 512
-        ts(T.fw[:, 2048 + a:2048 + b], T.fw[:, a:b], 12, Op.logical_shift_right, "fwl%d" % c, "fw%d" % c)
 
     def apply(buf, win, after):
         cp(T[win][:].indirect(T[buf][:, K:K + 12]), T[buf][:, 0:K], buf + " " + after, win, -K)
 
     def same(eq, src, sk, own, lk, less=2048.0):
-        for kb in range(12):
-            ts(T[eq][:, kb, 0:K - 16 * kb], src[:, 16 * kb:K], less, Op.add, sk + " " + lk, eq + str(kb), own(kb), Op.is_equal)
+        for j, (a, b) in enumerate(zip(EQ, EQ[1:])):
+            op("v", [lambda kb=kb: v.tensor_scalar(T[eq][:, kb, 0:K - 16 * kb], src[:, 16 * kb:K], less, own(kb), Op.add, Op.is_equal) for kb in range(a, b)],
+               sk + " " + lk, eq + str(j), sum(VFIX + CYC * max(64, K // 2 - 8 * kb) for kb in range(a, b)))
 
     def lower(eq, ps, pk, stop=True):
-        for kb in range(11):
-            pe([mm(ps[:, 16 * kb + 16:K], C("bl8"), T[eq][:, kb, 16:K - 16 * kb], False, False)], "bl8 %s%d" % (eq, kb), pk)
-        pe([mm(ps[:, 0:K], C("up8"), T[eq][:, :, 0:16], False, stop)], "up8 " + keys(eq, 12), pk)
+        for j, (a, b) in enumerate(zip(EQ, EQ[1:])):
+            fs = [mm(ps[:, 16 * kb + 16:K], C("bl8"), T[eq][:, kb, 16:K - 16 * kb], False, False) for kb in range(a, min(b, 11))]
+            if b == 12:
+                fs.append(mm(ps[:, 0:K], C("up8"), T[eq][:, :, 0:16], False, stop))
+            pe(fs, "bl8 up8 " + keys(eq, j + 1, j * (b < 12)), pk)
 
     def pieces(dst, h):
-        n, m = PIECES[2 * "cab".index(dst[1]) + h], CUT[h + 1] - CUT[h]
-        return [(CUT[h] + m * i // n // 2 * 2, CUT[h] + m * (i + 1) // n // 2 * 2, "%s%d%d" % (dst, h, i)) for i in range(n)]
+        out, a = [], CUT[h]
+        for i, n in enumerate(PARTS.get(dst + str(h), (CUT[h + 1] - CUT[h],))):
+            out.append((a, a + n, "%s%d%d" % (dst, h, i)))
+            a += n
+        return out
 
     def made(dst, *hs):
         return " ".join(x[2] for h in hs for x in pieces(dst, h))
 
-    def xgather(dst, lst, lk, h):
-        for a, b, key in pieces(dst, h):
-            tt(T[dst][:, 16 * a:16 * b], T.xw[:, 0:W].indirect(lst[:, a:b]), T.qrep[:, 16 * a:16 * b], Op.min, " ".join((XW, lk, QR)), key, 16 * (b - a))
+    def gathers(x, lst, lk, h):
+        for a, b, key in pieces("p" + x, h):
+            take(T["p" + x][:, 16 * a:16 * b], T.pw[:].indirect(lst[:, a:b]), PW + " " + lk, key, -OFF, key in LEND.split())
+        for a, b, key in pieces("m" + x, h):
+            tt(T["m" + x][:, 16 * a:16 * b], T.xw[:, 0:W].indirect(lst[:, a:b]), T.qrep[:, 16 * a:16 * b], Op.min, " ".join((XW, lk, QR)), key, 16 * (b - a))
 
-    def pgather(dst, lst, lk, h):
-        for a, b, key in pieces(dst, h):
-            act(T[dst][:, 16 * a:16 * b], T.pw[:].indirect(lst[:, a:b]), PW + " " + lk, key, n=16 * (b - a))
+    def sums(ps, srcs, h, n, stop):
+        for a, b, key in pieces("s" + srcs[0][0][1], h):
+            for src, w, wk in srcs:
+                last = stop and src == srcs[-1][0]
+                pe([mm(T[ps][a - CUT[h]:b - CUT[h], h, i:n:16], T[src][:, 16 * a + i:16 * b:16], C(w), False, last and i == 15) for i in range(16)],
+                   " ".join(x[2] for x in pieces(src, h) if x[0] < b and a < x[1]) + " " + wk, "%s%d" % (ps, h))
 
-    def sums(ps, src, w, wk, h, n, last=False):
-        a, b = CUT[h], CUT[h + 1]
-        pe([mm(T[ps][0:b - a, h, i:n:16], T[src][:, 16 * a + i:16 * b:16], C(w), False, last and i == 15) for i in range(16)],
-           made(src, h) + " " + wk, "%s%d" % (ps, h))
+    def scatter(lst, src, end):
+        if end:
+            cp(T.yw[:].indirect(C(lst)), T[src][:], lst + " " + src, "yw", -K)
+        else:
+            act(T.pw[:].indirect(C(lst)), T[src][:], lst + " " + src, PW, AF.Silu, -K)
 
     LO = T.ll[:, 1, :]
     own = lambda f: (lambda kb: T.sc[:, 16 * kb + 8 * f + 7:16 * kb + 8 * f + 8])
     for t in range(RO):
-        j = t + 1
+        j, end = t + 1, t == RO - 1
+        step()
         lw, xl, msg = "lw%d" % j, "xl%d" % j, "msg%d" % j
         lnw, lk = T[lw][:, 0:M], lw if t else "lw0 lw1"
         for h in (0, 1):
-            pgather("pc", T.lc[:], "lc", h)
-            xgather("mc", T.lc[:], "lc", h)
+            gathers("c", T.lc[:], "lc", h)
         if t == 0:
+            for c in range(4):
+                a, b = 512 * c, 512 * c + 512
+                ts(T.fw[:, 2048 + a:2048 + b], T.fw[:, a:b], 12, Op.logical_shift_right, "fwl%d" % sum(x <= a for x in FCUT[1:]), "fw%d" % c)
             for h in (0, 1):
-                a, b = (0, LCUT, M)[h:h + 2]
-                mv(LW[h], T.lw1[:, a:b], T.lu1[:, a:b], "lu%d %s" % (h, made("pc", h) if h else "lfu1"), "lw%d" % h)
+                a, b = (0, 640, M)[h:h + 2]
+                mv(LW[h], T.lw1[:, a:b], T.lu1[:, a:b], "lu0 lu%d %s" % (h, made("pc", 0) if h else "lfu1"), "lw%d" % h)
         else:
-            apply(("up1", "up3")[t - 1], lw, made("mc", 1))
+            apply(("up1", "up3")[t - 1], lw, made("mc", 0))
         if t == 1:
-            mv("g", T.st[:], T.lw2[:, 0:M], "lw2", "st")
-            arrives("rl3", NE, "lu3", BULK, send(T.st[:], "st", r - 1, T.lu3[:], "rl3", "ls4", True))
-            arrives("rs", NE, "lus", 1.5 * BULK, send(T.st[:], "st", r + 2, T.lus[:], "rs", "ls7", True))
-        if t == 2:
-            mv("g", T.lh[:, 0:M], T.lus[:], "lus lc", "lh")
-            apply("hm2", "lh", made("mc", 1))
+            arrives("rl3", NE, "lw3", BULK2, send(lnw, lw, r - 1, T.lw3[:, 0:M], "rl3", "ls4", True))
+            arrives("rs", NE, "lh", 2 * BULK2, send(lnw, lw, r + 2, T.lh[:, 0:M], "rs", "ls7", True))
+        if end:
+            mv("g", T.cf[:], T.hm2[:, 0:K], "hm2", "cf")
+            act(T.lh[:].indirect(T.hm2[:, K:K + 12]), T.cf[:], "hm2 cf", "lh", AF.Silu, -K)
+            act(T.lh[:, 0:M], T.lh[:, 0:M], "lh", "lh", AF.Copy, bias=-LOFF)
         for h in (0, 1):
             a, b = CUT[h], CUT[h + 1]
             H, x, y = b - a, a // 16, b // 16
             k = lambda names: " ".join("%s%d" % (n, h) for n in names.split())
             pe([mm(T.psk[0:H, h, 0:256], C("one", 0, H, p1=1), C("row", 0, 256, p1=1), True, False)], "one rowa0 rowa1", k("psk"))
-            sums("psk", "mc", "wm", "wm0 wm1", h, 256)
-            sums("psk", "pc", "wp", "wp0 wp1", h, 256, True)
+            sums("psk", (("mc", "wm", "wm0 wm1"), ("pc", "wp", "wp0 wp1")), h, 256, True)
             scan(T.t4[0:H, h, :], T.psk[0:H, h, 0:256], k("psk"), k("t4_"), 256, H)
             ts(T.fi[0:H, h, :], T.t4[0:H, h, 15:256:16], W - 1, Op.bitwise_and, k("t4_"), k("fi"))
             mv("s", T.fl[0:H, h, :], T.fi[0:H, h, :], k("fi"), k("fl"), bias=-2048.0)
@@ -692,84 +820,92 @@ def rank_program(g, core, T, topo):
             mv("v", T.ll[:, 0, x:y], T.sc[:, a + 7:b:16], k("sc"), k("ln"), 0.5, -0.25)
             mv("s", T.ll[:, 1, x:y], T.sc[:, a + 15:b:16], k("sc"), k("lo"))
             LN = T.ll[:, 0, x:y]
-            act(T.sq[:, 0, a:b], lnw.indirect(LN), lk + " " + k("ln"), k("sqa"), AF.Square, H, scale=2.0, bias=8.0)
-            act(T.sq[:, 1, a:b], lnw.indirect(LN), lk + " " + k("ln"), k("sqb"), AF.Square, H, bias=592.0)
-            act(T.b16[:, a:b], lnw.indirect(LN), lk + " " + k("ln"), k("b16_"), n=H)
-            for c, of in enumerate((-2.484375, -10951.484375)):
-                mv("s", T.tt[:, c, a:b], T.sq[:, c, a:b], k("sq" + "ab"[c]), k("tt" + "ab"[c]), 0.03125, of)
-            for c, d, n in ((0, 1, "a"), (1, 2, "b")) if h < SPLIT else ((0, 2, "ab"),):
-                ts(T.cc[:, c:d, a:b], T.tt[:, c:d, a:b], W - 1, Op.bitwise_and, k(" ".join("tt" + u for u in n)), k(" ".join("cc" + u for u in n)))
-                mv("s", T.l12[:, c:d, a:b], T.cc[:, c:d, a:b], k(" ".join("cc" + u for u in n)), k(" ".join("li" + u for u in n)))
+            take(T.b16[:, a:b], lnw.indirect(LN), lk + " " + k("ln"), k("b16_"), -LOFF)
+            for c, (n, kw, of) in enumerate((("a", {"scale": 2.0, "bias": 8.0}, -2.484375), ("b", {"bias": 592.0}, -10951.484375))):
+                if k("sq" + n) in PLAIN.split():
+                    act(T.sq[:, c, a:b], T.b16[:, a:b], k("b16_"), k("sq" + n), AF.Square, **kw)
+                else:
+                    act(T.sq[:, c, a:b], lnw.indirect(LN), lk + " " + k("ln"), k("sq" + n), AF.Square, H, scale=2.0 - c, bias=kw["bias"] - (2.0 - c) * LOFF)
+                mv("s", T.tt[:, c, a:b], T.sq[:, c, a:b], k("sq" + n), k("tt" + n), 0.03125, of)
+                ts(T.cc[:, c, a:b], T.tt[:, c, a:b], W - 1, Op.bitwise_and, k("tt" + n), k("cc" + n))
+                mv("s", T.l12[:, c, a:b], T.cc[:, c, a:b], k("cc" + n), k("li" + n))
             mv("s", T.cm[:, :, a:b], T.cc[:, :, a:b], k("cca ccb"), k("cm"), bias=-2048.0)
             pe([mm(T.psv[0:H, h, 0:384], T.b16[:, a:b], C("bi"), True, False)], "bi0 bi1 bi2 " + k("b16_"), k("psv"))
         for f in (0, 1):
             mv("s", T.lv[:, 12 * f:12 * f + 12], T.sc[:, 7 + 8 * f:K:16], "sc0 sc1", "lv%d" % f, bias=-2048.0)
         pe([mm(T.psg[:, i:2 * K:16], C("bj", 128 * i, 128 * i + 128), T.lv[:], True, True) for i in range(16)], keys("bj", 16) + " lv0 lv1", "psg")
         mv("s", T.rr[:], T.psg[:, 0:2 * K], "psg", "rr")
-        act(T.at[:], T[xl][:].indirect(T.ll[:, 0, :]), xl + " ln0 ln1", "at", n=K)
-        act(T.g2[:], T.pw[:].indirect(LO), PW + " lo0 lo1", "g2", n=K)
+        take(T.at[:], T[xl][:].indirect(T.ll[:, 0, :]), xl + " ln0 ln1", "at")
+        if end:
+            dma("d", T.yv[:], T.pw[0:128:16, 0:W], PW, "yv", 128)
+            mv("s", T.yv[:], T.yv[:], "yv", "yv", bias=-OFF)
+            dma("d", T.yw[0:128:16, 0:W], T.yv[:], "yv", "yw", 128)
+        mv("s", T.hn[:], T.rr[:, 0, :], "rr", "hn", 0.5, 2047.75)
         same("eqo", T.rr[:, 1, :], "rr", own(1), "sc0 sc1")
-        pe([mm(T.psd[:, 0:K], C("id"), C("bm"), True, False), mm(T.psd[:, 0:K], C("se"), T.g2[:], False, False)], "id bm se g2", "psd")
+        pe([mm(T.psd[:, 0:K], C("id"), C("bme"), True, False), mm(T.psd[:, 0:K], C("bi", 128, 256), T.rr[:, 0, :], False, False),
+            mm(T.psd[:, 0:K], C("id2"), T.hn[:], False, False)], "id bme bi1 rr id2 hn", "psd")
         lower("eqo", T.psd, "psd")
         scan(T.scd[:], T.psd[:, 0:K], "psd", "scd")
-        relu(RQ[0], C("cand"), T.scd[:, 15:K:16], "scd", "cand", -1.0)
+        relu("v", C("cand"), T.scd[:, 15:K:16], "scd", "cand", -1.0)
         op("v", [lambda: v.tensor_tensor_scan(C("exb", 1, 13), C("one", 0, 12), C("cand"), 0.0, Op.mult, Op.add)], "one cand", "exb", VFIX + 64 * CYC)
         pe([mm(T.psd[:, 400:412], C("btr"), C("cand"), True, False), mm(T.psd[:, 400:412], C("bl8"), C("exb", 0, 12), False, True)], "btr cand bl8 exb", "psd")
-        relu(RQ[1], C("nqd"), T.psd[:, 400:412], "psd", "nqd", bias=(256.0 - CAP) * OUT)
+        relu("v", C("nqd"), T.psd[:, 400:412], "psd", "nqd", bias=(256.0 - CAP) * OUT)
         tt(C("w1"), C("nqd"), T.sc[:, 15:K:16], Op.add, "nqd sc0 sc1", "w1")
         tt(C("ld"), C("w1"), C("dm4"), Op.min, "w1 dm4", "ld")
-        act(T.nq[:], C("nqd").indirect(C("lk")), "nqd lk", "nq", n=K)
-        pe([mm(T.psk[:, 1, 0:K], C("slt", 15 - i, 143 - i), T.pc[:, i:16 * K:16], i == 0, i == 15) for i in range(16)], "slt " + made("pc", 0, 1), "psk1")
-        mv("s", T[msg][:, 0:K], T.psk[:, 1, 0:K], "psk1", msg)
+        take(T.nq[:], C("nqd").indirect(C("lk")), "nqd lk", "nq")
+        for e in range(0, 16, 4):
+            pe([mm(T.psk[:, 1, 0:K], C("slt", 15 - i, 143 - i), T.pc[:, i:16 * K:16], i == 0, i == 15) for i in range(e, e + 4)], "slt " + made("pc", 0, 1), "psk1")
+        mv("s", T[msg][:, 0:K], T.psk[:, 1, 0:K], "psk1", msg, bias=0.0 if end else LOFF)
         same("eqt", T.rr[:, 0, :], "rr", own(0), "sc0 sc1")
         mv("s", T.hh[:], T.rr[:, 0, :], "rr", "hh", 0.25, 1535.5)
         pe([mm(T.psk[:, 0, 0:K], C("id"), C("bm4"), True, False), mm(T.psk[:, 0, 0:K], C("c15", p1=1), C("one", 0, K, p1=1), False, False),
             mm(T.psk[:, 0, 0:K], C("id4"), T.hh[:], False, False), mm(T.psk[:, 0, 0:K], C("idm"), T.rr[:, 0, :], False, False)],
            "id bm4 c15 one id4 hh idm rr", "psk0")
-        lower("eqt", T.psk[:, 0, :], "psk0")
-        scan(T.scm[:], T.psk[:, 0, 0:K], "psk0", "scm")
-        tt(C("w2"), T.scm[:, 15:K:16], C("nqd"), Op.add, "scm nqd", "w2")
-        tt(T[msg][:, K:K + 12], C("w2"), C("dm1"), Op.min, "w2 dm1", msg + "l")
+        lower("eqt", T.psk[:, 0, :], "psk0", False)
+        pe([mm(T.psk[:, 0, 0:K], C("id"), T.nq[:], False, True)], "id nq", "psk0")
+        spare(T.scm[:], T.psk[:, 0, 0:K], 1, "psk0", "scm")
+        mv("s", T[msg][:, K:K + 12], T.scm[:, 15:K:16], "scm", msg + "l")
         mk = msg + " " + msg + "l"
-        if t < 2:
+        if end:
+            arrives("rh3", NE, "hm3", FAR, send(T[msg][:, 0:K + 12], mk, r + RO, T.hm3[:], "rh3", "ls11"))
+        else:
             u = "up%d" % (1 + 2 * t)
             arrives("r" + u[0::2], NE, u, FAR, send(T[msg][:, 0:K + 12], mk, r - 1, T[u][:], "r" + u[0::2], "ls%d" % (6 + 2 * t)))
-        if t:
-            arrives("rh%d" % j, NE, "hm%d" % j, FAR, send(T[msg][:, 0:K + 12], mk, r + 1 + t, T["hm%d" % j][:], "rh%d" % j, "ls%d" % (9 + t)))
-        else:
+        if t == 0:
             hand_on(2)
+        if t == 1:
+            arrives("rh2", NE, "hm2", FAR, send(T[msg][:, 0:K + 12], mk, r + 2, T.hm2[:], "rh2", "ls10"))
         for h in (0, 1):
-            for c in (0, 1):
-                pgather("p" + "ab"[c], T.l12[:, c, :], "li%s%d %s" % ("ab"[c], h, HINT[4 + 2 * h + c]), h)
-                xgather("m" + "ab"[c], T.l12[:, c, :], "li%s%d %s" % ("ab"[c], h, HINT[2 * h + c].replace("msg", msg)), h)
-                sums("psv", "m" + "ab"[c], "wm%d" % (c + 1), keys("wm%d_" % (c + 1), 3), h, 384)
-                sums("psv", "p" + "ab"[c], "wp%d" % (c + 1), keys("wp%d_" % (c + 1), 3), h, 384, c == 1)
-        pe([mm(T.psk[:, 1, 0:K], C("sa"), T.at[:], True, False), mm(T.psk[:, 1, 0:K], C("dg1"), T.g2[:], False, False),
-            mm(T.psk[:, 1, 0:K], C("row", 128 * t, 128 * t + 128, 96, 97), C("one", 0, K, 96, 97), False, True)], "sa0 sa1 at dg1 g2 rowm%d one" % t, "psk1")
-        mv("s", T.v2[:], T.psk[:, 1, 0:K], "psk1", "v2")
+            for c, n in enumerate("ab"):
+                gathers(n, T.l12[:, c, :], "li%s%d" % (n, h), h)
+                sums("psv", (("m" + n, "wm%d" % (c + 1), keys("wm%d_" % (c + 1), 3)), ("p" + n, "wp%d" % (c + 1), keys("wp%d_" % (c + 1), 3))), h, 384, c == 1)
+        pe([mm(T.psk[:, 1, 0:K], C("sa"), T.at[:], True, False), mm(T.psk[:, 1, 0:K], C("dg1"), T.hn[:], False, False), mm(T.psk[:, 1, 0:K], C("dg7"), T.rr[:, 1, :], False, False),
+            mm(T.psk[:, 1, 0:K], C("row", 128 * t, 128 * t + 128, 96, 97), C("one", 0, K, 96, 97), False, True)], "sa0 sa1 at dg1 hn dg7 rr rowm%d one" % t, "psk1")
+        either("s", lambda: s.activation(T.v2[:], T.psk[:, 1, 0:K], AF.Identity, bias=D(8)), lambda: v.tensor_scalar(T.v2[:], T.psk[:, 1, 0:K], D(8), None, Op.add),
+               "psk1 ec8", "v2", SFIX + K * CYC, VFIX + K * CYC)
         cp(T.xw[:].indirect(C("ld")), T.at[:], "ld at", XW, -K)
-        cp(T.pw[:].indirect(C("ld")), T.v2[:], "ld v2", PW, -K)
-        act(T.xo[:], T.xw[:, 0:W].indirect(LO), XW + " lo0 lo1", "xo", n=K)
-        pe([mm(T.psk[:, 0, 0:K], C("id"), T.q[:], True, False), mm(T.psk[:, 0, 0:K], C("id"), T.xo[:], False, True)], "id q xo", "psk0")
+        scatter("ld", "v2", False)
+        if end:
+            op("v", [lambda: v.tensor_scalar(T.yw[:].indirect(C("ld")), T.v2[:], 1.0, -OFF, Op.mult, Op.add)], "ld v2", "yw", ncost(-K))
+        take(T.xo[:], T.xw[:, 0:W].indirect(LO), XW + " lo0 lo1", "xo")
+        pe([mm(T.psk[:, 0, 0:K], C("id"), T.qrep[:, 0:16 * K:16], True, False), mm(T.psk[:, 0, 0:K], C("id"), T.xo[:], False, True)], "id qr0 xo", "psk0")
         mv("s", T.qb[:], T.psk[:, 0, 0:K], "psk0", "qb", 0.5, 127.8125)
-        mv("s", T.q[:], T.qb[:], "qb", "q", bias=-128.0)
-        for i in range(16 if t < RO - 1 else 0):
-            if i < QG:
-                mv("g", T.qrep[:, i:16 * K:16], T.q[:], "q", "qr%d" % i)
-            else:
-                mv("s" if i < 2 * QG else "v", T.qrep[:, i:16 * K:16], T.qb[:], "qb", "qr%d" % i, bias=-128.0)
+        if end:
+            mv("s", T.q[:], T.qb[:], "qb", "q", bias=-128.0)
+        else:
+            spread(T.qb, -128.0, QHOW[1])
         for h in (0, 1):
             a, b = CUT[h], CUT[h + 1]
             H = b - a
             nn = lambda f: T.nn[0:H, h, 128 * f:128 * f + 128]
-            ts(T.nn[0:H, h, 128:384], T.psv[0:H, h, 128:384], 0.0, Op.is_equal, "psv%d" % h, "nna%d" % h)
-            if h:
+            ts(T.nn[0:H, h, 128:384], T.psv[0:H, h, 128:384], WHOLE, Op.add, "psv%d" % h, "nna%d" % h, WHOLE, Op.is_equal)
+            if NNB[h] == "v":
                 ts(nn(0), T.psv[0:H, h, 0:128], 0.5, Op.is_gt, "psv%d" % h, "nnb%d" % h, 0.5, Op.subtract)
             else:
                 act(nn(0), T.psv[0:H, h, 0:128], "psv%d" % h, "nnb%d" % h, AF.Sign, bias=-0.5)
             pe([mm(T.psu[:, a:b], nn(f), C("bi", 128, 128 + H, p1=H), f == 1, f == 2) for f in (1, 2)], "bi1 nna%d" % h, "psu")
             for u in (0, 1):
-                pe([mm(T.psm[:, K * u + a:K * u + b], nn(f), C("idu", 128 * (3 * u + w), 128 * (3 * u + w) + H, p1=H), f == 1, f == 0) for f, w in ((1, 0), (2, 1), (0, 2 - h))],
+                pe([mm(T.psm[:, K * u + a:K * u + b], nn(f), C("idu", 128 * (3 * u + w), 128 * (3 * u + w) + H, p1=H), f == 1, f == 0) for f, w in ((1, 0), (2, 1), (0, 1 + (NNB[h] == "s")))],
                    "%s nna%d nnb%d" % (keys("idu", 6), h, h), "psm")
         relu("s", T.nr[:], T.psu[:, 0:K], "psu", "nr", bias=1.0)
         tt(T.psm[:, 0:K], T.psm[:, 0:K], T.cm[:, 1, :], Op.min, "psm cm0 cm1", "psm pk")
@@ -779,41 +915,37 @@ def rank_program(g, core, T, topo):
         pe([mm(T.psg[:, 0:K], C("tr4"), T.nr[:], False, True)], "tr4 nr", "psg")
         mv("s", T.sg[:], T.sh[:], "sh", "sg", bias=2048.0)
         relu("s", T.fst[:], T.psg[:, 0:K], "psg", "fst", 1.0 / 2048)
-        cp(T.fw[:].indirect(C("ld")), T.sg[:], "ld sg", FW, -K)
-        ts(T.ci[:], T.fw[:, 0:W].indirect(LO), W - 1, Op.bitwise_and, FW + " lo0 lo1", "ci", n=K)
-        if t < RO - 1:
-            mv("s", T.lc[:], T.ci[:], "ci", "lc")
-        else:
-            mv("s", T.cf[:], T.ci[:], "ci", "cf")
         tt(T.x1[:], T.psg[:, 0:K], T.sh[:], Op.min, "psg sh", "x1")
-        o = T.psv[:, 0, K:2 * K]
-        pe([mm(o, C("row", 0, 128, 64, 65), C("one", 0, K, 64, 65), True, False), mm(o, C("id"), T.b16[:], False, False),
-            mm(o, C("tr8"), T.nr[:], False, True)], "rowu0 one id b16_0 b16_1 tr8 nr", "psv0")
-        act(T.x2[:], o, "psv0", "x2", AF.Relu)
+        pe([mm(T.psu[:, 0:K], C("cmp"), T.nr[:], True, False)], "cmp nr", "psu")
+        pe([mm(T.psu[:, 0:K], C("bl"), T.x1[:], False, True)], "bl x1", "psu")
+        mv("s", T.rc[:], T.psu[:, 0:K], "psu", "rc", bias=34816.0)
         for o, pk, stop in ((T.psv[:, 1, 0:K], "psv1", True), (T.psd[:, 0:K], "psd", False)):
             pe([mm(o, C("id"), C("bmc"), True, False), mm(o, C("id"), T.nq[:], False, False)], "id bmc nq", pk)
             pe([mm(o, C("cmp"), T.nr[:], False, False)], "cmp nr", pk)
             pe([mm(o, C("bn8"), T.fst[:], False, False)], "bn8 fst", pk)
             pe([mm(o, C("bl"), T.x1[:], False, stop)], "bl x1", pk)
-        pe([mm(T.psu[:, 0:K], C("cmp"), T.nr[:], True, False)], "cmp nr", "psu")
-        pe([mm(T.psu[:, 0:K], C("bl"), T.x1[:], False, True)], "bl x1", "psu")
-        scan(T.scc[:], T.psv[:, 1, 0:K], "psv1", "scc")
-        mv("s", T.rc[:], T.psu[:, 0:K], "psu", "rc", bias=34816.0)
-        tt(C("lp"), T.scc[:, 15:K:16], C("dm4"), Op.min, "scc dm4", "lp")
+        spare(T.scc[:], T.psv[:, 1, 0:K], 0, "psv1", "scc")
+        cp(T.fw[:].indirect(C("ld")), T.sg[:], "ld sg", FW, -K)
+        ts(T.ci[:], T.fw[:, 0:W].indirect(LO), W - 1, Op.bitwise_and, FW + " lo0 lo1", "ci", n=K)
+        mv("s", T.cf[:] if end else T.lc[:], T.ci[:], "ci", "cf" if end else "lc")
+        o = T.psv[:, 0, K:2 * K]
+        pe([mm(o, C("row", 0, 128, 64, 65), C("one", 0, K, 64, 65), True, False), mm(o, C("id"), T.b16[:], False, False),
+            mm(o, C("tr8"), T.nr[:], False, True)], "rowu0 one id b16_0 b16_1 tr8 nr", "psv0")
+        act(T.x2[:], o, "psv0", "x2", AF.Relu)
+        mv("s", C("lp"), T.scc[:, 15:K:16], "scc", "lp")
         same("eqo", T.rc, "rc", lambda kb: T.scc[:, 16 * kb + 15:16 * kb + 16], "scc")
         lower("eqo", T.psd, "psd")
-        act(T.g1[:], T.pw[:].indirect(C("lp")), PW + " lp", "g1", n=K)
+        take(T.g1[:], T.pw[:].indirect(C("lp")), PW + " lp", "g1", -OFF)
         pe([mm(T.psg[:, 0:K], C("vr"), T.x2[:], True, False), mm(T.psg[:, 0:K], C("row", 384, 512, p1=1), C("one", 0, K, p1=1), False, False),
-            mm(T.psg[:, 0:K], C("dgc", 128 * t, 128 * t + 128), T.g1[:], False, True)], "vr x2 rowc0 rowc1 one dgc%d0 dgc%d2 g1" % (t, t), "psg")
-        mv("s", T.v1[:], T.psg[:, 0:K], "psg", "v1")
-        if t < RO - 1:
-            mv("g", T["lw%d" % (j + 1)][:, 0:M], T["lu%d" % (j + 1)][:], "lu%d g1" % (j + 1), "lw%d" % (j + 1))
-        scan(T.scd[:], T.psd[:, 0:K], "psd", "scd")
-        tt(C("lcl"), T.scd[:, 15:K:16], C("dm4"), Op.min, "scd dm4", "lcl")
-        cp(T.pw[:].indirect(C("lcl")), T.v1[:], "lcl v1", PW, -K)
+            mm(T.psg[:, 0:K], C("dgc", 128 * t, 128 * t + 128), T.g1[:], False, True)], "vr x2 rowc one dgc%d0 g1" % t, "psg")
+        mv("s", T.v1[:], T.psg[:, 0:K], "psg", "v1", bias=0.0 if end else OFF)
+        if t == 0:
+            mv("g", T.lw2[:, 0:M], T.lu2[:], "lu2 nna0", "lw2")
+        spare(T.scd[:], T.psd[:, 0:K], 0, "psd", "scd")
+        mv("s", C("lcl"), T.scd[:, 15:K:16], "scd", "lcl")
+        scatter("lcl", "v1", end)
     apply("hm3", "lh", "nna0")
-    dma("d", T.yl[:], T.lh[:, 0:M], "lh", "yl", 512)
-    dma("d", T.yq[:], T.q[:], "q", "yq", 48)
-    dma("d", T.yc[:], T.cf[:], "cf", "yc", 96)
-    dma("d", T.yt[:], T.pw[0:128:16, 0:W], PW, "yt", 128)
+    outs = {"yl": (T.lh[:, 0:M], "lh", 512), "yq": (T.q[:], "q", 48), "yc": (T.cf[:], "cf", 96), "yt": (T.yw[0:128:16, 0:W], "yw", 128)}
+    for n in OUTS.split():
+        dma("d", T[n][:], outs[n][0], outs[n][1], n, outs[n][2])
     finish()

import numpy as np
from concourse.mybir import AluOpType as Op, ActivationFunctionType as AF

W, M, K, CAP, RO, N = 4096, 1024, 192, 160, 3, 8
CUT = (0, 64, K)
PARTS = {"mc1": (64, 64), "pc1": (64, 64), "mb1": (96, 32), "pb1": (96, 32), "sb1": (96, 32)}
LEND = ""
EQ = (0, 4, 8, 12)
ONG, PLAIN, OUTS = "lo0 lo1 lib1", "sqb0 sqa1 sqb1", "yq yl yc yt"
_A = "mc10>mc00 mc11>mc10 pc10>pc00 pc11>pc10 ma10>mb00 mb00>ma00 pa10>pb00 pb00>pa00 mb10>ma10 pb10>pa10"
AFTER = (_A + " pw2>pw0 pw4>pw2 pw6>pw4 pw3>pw1 pw5>pw3 pw7>pw5 mc00>pw7 lc>pw6", _A, _A)
_V = "mc10 t4_0 fi0 mc11 sc0 lw t4_1 cca0 fi1 lia0 ccb0 ma00 sc1 mb00 ttb1 "
_S = "pc00 pc10 fl0 pc11 ln0 b16_0 sqa0 sqb0 tta0 ttb0 fl1 lib0 pa00 lv1 ln1 lv0 b16_1 lo0 "
_V0 = ("mc10 t4_0 fi0 mc11 sc0 fw0 fw1 t4_1 tta0 fi1 cca0 fl1 lia0 fw2 ccb0 sc1 ma00 mb00 hn eqo2 cca1 ccb1 eqo1 eqo0 eqt0 ma10 mb10 scd mb11 nna0 exb eqt2 eqt1 nna1 w1 nnb1 ld "
       "xw0 psm dc scm sh msgl x1 fw3 scc qr0 eqo0 eqo1 eqo2 fwl0 scd ci qr5 +mc00")
_S0 = ("pc00 pc10 fl0 pc11 ln0 lo0 lw sqa0 b16_0 sqb0 ttb0 pa00 ln1 lv1 lv0 lib0 b16_1 msg sqb1 sqa1 rr ttb1 tta1 pb00 hh lia1 at cm0 pa10 pb10 cand pb11 "
       "cm1 nnb0 nqd v2 nq nr pw0 xo fst x2 sg qb rc qr1 qr2 lp g1 qr3 lcl v1 lc pw0")
_V1 = _V + "cca1 ccb1 lia1 eqo0 eqo1 eqo2 ma10 mb10 scd mb11 exb nna0 eqt0 eqt1 w1 nna1 nnb1 ld eqt2 xw0 psm dc scm sh x1 fwl0 qr0 scc qr1 eqo0 eqo1 eqo2 ci qr5 scd v1 +mc00"
_S1 = _S + "sqa1 sqb1 tta1 rr pb00 hh hn pa10 pb10 cand pb11 nnb0 cm0 nqd cm1 at nq nr msg fst xo msgl sg qb v2 rc pw0 qr2 lp x2 g1 qr3 lcl lc pw0"
_V2 = (_V.replace("ttb1", "msg") + "eqo0 eqo1 eqo2 ccb1 eqt2 scd cca1 eqt0 exb eqt1 nqd ma10 w1 scm ld mb10 nna0 mb11 xw0 nna1 nnb1 "
       "lh psm dc sh x1 yw scc eqo0 eqo1 eqo2 fwl0 scd ci yw")
_S2 = (_S.replace("ln0", "ln0 yv").replace("lo0 ", "") + "sqa1 sqb1 rr ttb1 hn tta1 pb00 cand hh lia1 at cm0 nq pa10 msgl lh pb10 v2 pb11 lh nnb0 cm1 pw0 "
       "nr xo fst x2 sg rc lp qb q g1 v1 lcl cf")
PLAN = ((_V0, _V1, _V2), (_S0, _S1, _S2))
QHOW = ("vvvvvv", "vsvsgs")
NNB = "sv"
PWV = (1, 3, 5, 7)
XCUT, FCUT = (0, 2560, 3584, W), (0, 1024, 2048)
LCUT, LQ, LW = 1024, "s", "gs"
LOADS = "tgs lfi0 q pt xw0 xw1 xw2 cxi xlh fwl0 fwl1"
LOFF = 64.0
OFF = 2112.0
WHOLE = 12582912.0
BIG = 65536.0
RES = 67108864.0
OUT = 8192.0
NE = 8
SLOW = np.array([1.0, 1.3, 1.0])
WAKE, LAG, VFIX, SFIX, CYC, PCYC = np.array([0.2, 0.2, 0.13]), 0.05, 0.02, 0.04, 0.00083 * SLOW, 0.00045 * SLOW
GATH, SCAT, FAR, WEIGH = np.array([1.56, 1.7, 1.15]), np.array([3.8, 4.2, 2.2]), np.array([4.5, 6.0, 5.0]), (0.4, 0.25, 0.35)
BULK = np.array([9.5, 12.0, 10.0])
BULK2 = BULK + 1.0
SEED, ROAM, VLOAD, MID, ENDS, FINE, WIDE = 12, 6, 0.1, 0, 4, 4, 70
PASSES, NOISE, TRIES, HEAT, EPS, REACH = 6, 1.0, 1500, 0.2, 0.1, 24

_S = "sbuf"
F32, B16, I32, U16, H16 = "float32", "bfloat16", "int32", "uint16", "float16"
PACK = {
    "tf": (F32, (("nqd", 12), ("w1", 12), ("dm4", 12), ("er", 16), ("ec", 16), ("pmf", 4))),
    "tl": (U16, (("ld", 12), ("lcl", 12), ("lp", 12), ("lk", 12))),
    "ti": (I32, (("dmi", 12), ("pmi", 4))),
    "tb": (B16, (("wm", 16), ("wp", 16), ("wm1", 24), ("wm2", 24), ("wp1", 24), ("wp2", 24), ("cand", 12), ("exb", 16), ("rp", 8))),
    "cb": (B16, (("one", 256), ("zero", 128), ("bl", 128), ("bt", 128), ("id", 128), ("idu", 768), ("id4", 128), ("idm", 128), ("bi", 384), ("sel", 1024), ("bj", 2048), ("gm", 128),
                 ("btr", 128), ("tri", 128), ("tr8", 128), ("tr4", 128), ("cmp", 128), ("bl8", 128), ("bn8", 128), ("sa", 128), ("wt", 128), ("id2", 128), ("dg1", 128), ("dg7", 128),
                 ("dgc", 384), ("vr", 128), ("up8", 128), ("bm", K), ("bmc", K), ("bm4", K), ("bme", K), ("slt", 144), ("row", 512), ("c15", 128))),
}
PLACE, SCRATCH, ORDERS = {}, {}, {}
for _b in PACK:
    _o = 0
    for _n, _w in PACK[_b][1]:
        PLACE[_n] = (_b, _o, _w)
        _o += _w
    SCRATCH[_b] = (_S, [128, _o], PACK[_b][0])
for _d, _l in (
    (B16, (("xw", W + K), ("xlh", M), ("q", K), ("qb", K), ("ma", 16 * K), ("mb", 16 * K), ("mc", 16 * K), ("at", K), ("nr", K), ("nq", K), ("xo", K), ("fst", K),
           ("xl1", M), ("xl2", M), ("xl3", M))),
    (I32, (("fw", W + K), ("ci", K), ("tgs", 256), ("lfi", M), ("cxi", K), ("ic", 256), ("ixi", 256))),
    (U16, (("lfu", M), ("lc", K), ("lu1", M), ("lu2", M), ("msg1", K + 16), ("msg2", K + 16), ("msg3", K + 16), ("up1", K + 12), ("up3", K + 12), ("hm2", K + 12), ("hm3", K + 12))),
    (F32, (("pw", W + K), ("yw", W + K), ("yv", 256), ("lh", M + K), ("cf", K), ("sc", K), ("scd", K), ("scm", K), ("scc", K), ("dc", K), ("sg", K), ("v1", K), ("v2", K),
           ("s0", 256), ("lw1", M), ("lw2", M + K), ("lw3", M + K))),
    (H16, (("pt", W), ("pcs", 256), ("pa", 16 * K), ("pb", 16 * K), ("pc", 16 * K), ("g1", K), ("hn", K), ("lv", 24), ("b16", K), ("ixh", 256), ("x1", K), ("x2", K), ("rc", K),
           ("hh", K), ("sh", K))),
):
    for _n, _w in _l:
        SCRATCH[_n] = (_S, [128, _w], _d)
for _n, _w, _d in (("rr", K, H16), ("cm", K, H16), ("ll", 12, U16), ("sp", K, F32), ("sq", K, F32), ("tt", K, I32), ("cc", K, I32), ("l12", K, U16),
                   ("t4", 256, I32), ("fi", 16, I32), ("fl", 16, H16), ("nn", 384, B16)):
    SCRATCH[_n] = (_S, [128, 2, _w], _d)
SCRATCH["qrep"] = (_S, [128, 16 * K], B16)
SCRATCH["eqo"] = (_S, [128, 12, K], B16)
SCRATCH["eqt"] = (_S, [128, 12, K], B16)
for _n in ("psk", "psv"):
    SCRATCH[_n] = ("psum", [128, 2, 512], F32)
for _n in ("psm", "psu", "psd", "psg"):
    SCRATCH[_n] = ("psum", [128, 512], F32)
SEMAPHORES = ["qv", "qs", "qp", "qg"] + ["ld%d" % j for j in range(24)] + ["ls%d" % j for j in range(20)] + ["rl0", "rs", "rh2", "rh3"]
SEMAPHORES += ["%s%d" % (a, j) for a in ("rl", "rx", "ru") for j in (1, 2, 3)]


def tracker(g, T):
    Q = {"v": g.vector, "s": g.scalar, "p": g.tensor, "g": g, "d": g.sync}
    cnt = {"v": 0, "s": 0, "p": 0, "g": 0}
    known = {q: {} for q in Q}
    hist, wr, rd, total = {}, {}, {}, {}
    nd = [0]

    def learn(q, sem, val):
        if known[q].get(sem, 0) < val:
            known[q][sem] = val
        for s2, v2 in hist.get((sem, val), {}).items():
            if known[q].get(s2, 0) < v2:
                known[q][s2] = v2

    def needs(q, comp, R, Wt):
        out = []
        for k in R:
            if k in wr:
                out.append((k, wr[k]))
            if k.startswith("ps"):
                out += [(k, x) for x in rd.get(k, {}).values()]
        for k in Wt:
            if k in wr:
                out.append((k, wr[k]))
            out += [(k, x) for x in rd.get(k, {}).values()]
        need = {}
        for k, (sem, val, dq) in out:
            if comp and dq == q and (q == "p" or k.startswith("ps")):
                continue
            if need.get(sem, 0) < val:
                need[sem] = val
        return need

    def deps(q, comp, R, Wt):
        need = needs(q, comp, R, Wt)
        for sem in sorted(need, key=lambda s: -len(hist.get((s, need[s]), {}))):
            if known[q].get(sem, 0) < need[sem]:
                Q[q].wait_ge(T.sem[sem], need[sem])
                learn(q, sem, need[sem])

    def note(ev, q, R, Wt):
        for k in Wt:
            wr[k] = ev
            rd[k] = {}
        for k in R:
            rd.setdefault(k, {})[ev[0] if ev[2] is None else q] = ev

    def op_(q, fns, R, Wt):
        deps(q, True, R, Wt)
        sem = "q" + q
        for f in fns:
            if q == "p" and f is not fns[-1]:
                f()
            else:
                cnt[q] += 1
                f().then_inc(T.sem[sem], 1)
        total[sem] = cnt[q]
        hist[(sem, cnt[q])] = dict(known[q])
        note((sem, cnt[q], q), q, R, Wt)

    def dma_(q, out, in_, R, Wt):
        deps(q, False, R, Wt)
        sem = "ld%d" % nd[0]
        nd[0] += 1
        Q[q].dma_start(out, in_).then_inc(T.sem[sem], 16)
        total[sem] = 16
        hist[(sem, 16)] = dict(known[q])
        note((sem, 16, None), q, R, Wt)

    def send_(call, R, local, n):
        deps("g", False, R, [])
        call()
        total[local] = n
        note((local, n, None), "g", R, [])

    def arrives_(sem, n, key):
        total[sem] = n
        wr[key] = (sem, n, None)
        rd[key] = {}

    nodes, alt, steps = [], {}, []

    def op(q, fns, R, Wt, cost, other=None):
        R, Wt = R.split(), Wt.split()
        nodes.append((q, R, Wt, lambda: op_(q, fns, R, Wt), cost, 0.0, -1))
        if other:
            alt[len(nodes) - 1] = (other[0], R, Wt, lambda: op_(other[0], other[1], R, Wt), other[2], 0.0, -1)

    def dma(q, out, in_, R, Wt, kb):
        R, Wt = R.split(), Wt.split()
        nodes.append((q, R, Wt, lambda: dma_(q, out, in_, R, Wt), kb / 190.0, 1.6, -1))

    def send(call, R, local, n, on):
        R = R.split()
        nodes.append(("g", R, ["sent"] if local == "ls15" else [], lambda: on and send_(call, R, local, n), 0.3, 0.0, -2))
        return len(nodes) - 1

    def arrives(sem, n, key, lat, after):
        nodes.append(("a", [], [key], lambda: arrives_(sem, n, key), 0.0, lat, after))

    def finish():
        nn = len(nodes)
        dep = [set() for _ in nodes]
        w, rds, ps = {}, {}, {}
        for x, (q, R, Wt, f, n, lat, after) in enumerate(nodes):
            if after >= 0:
                dep[x].add(after)
            for k in sorted(set(R + Wt)):
                if k.startswith("ps"):
                    who = x if x in alt else q
                    cur = ps.setdefault(k, [who, [], []])
                    if cur[0] == who:
                        dep[x].update(cur[2])
                        if q == "p" and cur[1]:
                            dep[x].add(cur[1][-1])
                        cur[1].append(x)
                    else:
                        dep[x].update(cur[1])
                        ps[k] = [who, [x], cur[1]]
                    continue
                if k in w:
                    dep[x].add(w[k])
                if k in Wt:
                    dep[x].update(rds.get(k, []))
            for k in Wt:
                w[k], rds[k] = x, []
            for k in R:
                if k not in Wt:
                    rds.setdefault(k, []).append(x)
            dep[x].discard(x)
        prev, nxt, succ = [[] for _ in nodes], [[] for _ in nodes], [[] for _ in nodes]
        for x in range(nn):
            for d in sorted(dep[x]):
                if nodes[x][0] == "p" == nodes[d][0]:
                    dep[x].discard(d)
                    prev[x].append(d)
                    nxt[d].append(x)
                else:
                    succ[d].append(x)
        nm = len(WAKE)
        each = lambda c: [float(u) for u in c + 0.0 * WAKE]
        qn = {q: i for i, q in enumerate("vspgda")}
        qof = [qn[nd_[0]] for nd_ in nodes]
        css = [list(u) for u in zip(*[each(nd_[4]) for nd_ in nodes])]
        other = {x: (qn[alt[x][0]], each(alt[x][4])) for x in alt}
        tails = [list(u) for u in zip(*[each(nd_[5] + (0.0 if nd_[0] == "a" else LAG)) for nd_ in nodes])]
        wakes = each(WAKE - LAG)
        cs = css[0]
        lat = [tails[0][x] + (qof[x] != 5) * wakes[0] for x in range(nn)]
        pairs = []
        for q in (3, 4):
            row = [x for x in range(nn) if qof[x] == q and (q == 4 or nodes[x][6] == -2)]
            pairs += zip(row[1:], row)
        edge = steps + [nn]
        for u, rule in enumerate(AFTER):
            for pair in rule.split():
                pairs.append([[z for z in range(edge[u] * (u > 0), edge[u + 1]) if nodes[z][2][:1] == [n.strip("'")]][n.count("'")] for n in pair.split(">")])
        first = [x for x in range(edge[0]) if nodes[x][2][:1] in (["pw0"], ["pw1"])]
        pairs += [(x, y) for x in first for y in range(first[0]) if (qof[y] < 2 or y in other) and nodes[y][2] != ["lc"]]
        for x, y in pairs:
            prev[x].append(y)
            nxt[y].append(x)
        dl = [sorted(d) for d in dep]
        dp = [set(dl[x] + prev[x]) for x in range(nn)]
        sl = [set(succ[x] + nxt[x]) for x in range(nn)]

        def place(order, back):
            st, busy = [0.0] * nn, [[] for q in qn]
            for x in order:
                if back:
                    e = max([lat[x]] + [st[y] + cs[y] + lat[x] for y in succ[x]] + [st[y] + cs[y] for y in nxt[x]])
                else:
                    e = max([0.0] + [st[y] + cs[y] + lat[y] for y in dl[x]] + [st[y] + cs[y] for y in prev[x]])
                if qof[x] != 5:
                    b = busy[qof[x]]
                    i, hi = 0, len(b)
                    while i < hi:
                        m = (i + hi) // 2
                        i, hi = (i, m) if b[m][1] > e else (m + 1, hi)
                    while i < len(b) and b[i][0] < e + cs[x] - 1e-9:
                        e = max(e, b[i][1])
                        i += 1
                    b.insert(i, (e, e + cs[x]))
                st[x] = e
            return st, max(st[x] + cs[x] + (0.0 if back else lat[x]) for x in range(nn))

        def run(m, calls, fin, why, free, last):
            c, tail, wake = css[m], tails[m], wakes[m]
            for x in calls:
                q, e, w = qof[x], 0.0, -1
                for y in dl[x]:
                    if fin[y] > e:
                        e, w = fin[y], y
                if q != 5:
                    if e > free[q]:
                        e += wake
                    else:
                        e, w = free[q], last[q]
                    e += c[x]
                    free[q], last[q] = e, x
                why[x], fin[x] = w, e + tail[x]

        def whole(seq, m=0):
            fin, why = [0.0] * nn, [-1] * nn
            run(m, seq, fin, why, [0.0] * 5, [-1] * 5)
            return fin, why

        def beyond(seq, hi, m):
            rest, restq, left = [0.0] * nn, [0.0] * 6, {}
            for x in reversed(seq):
                rest[x] = max([0.0] + [left[y] + (qof[y] != 5) * wakes[m] for y in succ[x] if y in left])
                if len(left) < nn - hi:
                    left[x] = css[m][x] + max(tails[m][x] + rest[x], restq[qof[x]])
                    restq[qof[x]] = left[x] * (qof[x] != 5)
            return rest, restq

        def swap(x):
            q, c = other[x]
            other[x] = (qof[x], [u[x] for u in css])
            qof[x] = q
            for m in range(nm):
                css[m][x] = c[m]

        def polish(seq, lo, hi, heat, rnd, nm):
            rests = [beyond(seq, hi, m) for m in range(nm)]
            state = [whole(seq, m) for m in range(nm)]
            scale = [WEIGH[m] / sum(WEIGH[0:nm]) * max(state[0][0]) / max(state[m][0]) for m in range(nm)]
            win, n = seq[lo:hi], hi - lo
            inside = set(win)
            ends = [[x for x in win if rests[m][0][x] > 0.0 or not succ[x]] for m in range(nm)]
            before = [-1] * 6
            for x in seq[0:lo]:
                before[qof[x]] = x

            def value(new, i):
                last0, todo, got = before[:], 5, [False] * 6
                for j in range(i - 1, -1, -1):
                    q = qof[new[j]]
                    if not got[q]:
                        got[q], last0[q] = True, new[j]
                        todo -= q != 5
                        if not todo:
                            break
                tot, ats, part = 0.0, [], new[i:]
                for m in range(nm):
                    fin, why = state[m]
                    tail, (rest, restq) = tails[m], rests[m]
                    free, last = [fin[x] - tail[x] if x >= 0 else 0.0 for x in last0], last0[:]
                    run(m, part, fin, why, free, last)
                    end, at = max([(fin[x] + rest[x], x) for x in ends[m]] + [(free[q] + restq[q], last[q]) for q in range(5)])
                    tot += scale[m] * (end + EPS * sum([fin[x] for x in new]) / n)
                    ats.append(at)
                return tot + VLOAD * sum([cs[x] for x in new if qof[x] == 0 and x >= steps[0]]), ats
            cur = best = value(win, 0)
            bwin, bq = win, list(qof)
            for it in range(TRIES):
                rnd = (rnd * 1103515245 + 12345) % 2147483648
                path, x, why = [], cur[1][it % nm], state[it % nm][1]
                if (rnd >> 4) % 16 >= ROAM:
                    while x in inside:
                        y = why[x]
                        if y in inside and qof[y] == qof[x] and y not in dp[x]:
                            path.append((y, x))
                        x = y
                if not path:
                    j = (rnd >> 8) % n
                    i = j - 1
                    while i >= 0 and qof[win[i]] != qof[win[j]]:
                        i -= 1
                    if i < 0 or qof[win[j]] > 3 or win[i] in dp[win[j]]:
                        continue
                    path = [(win[i], win[j])]
                y, x = path[(rnd >> 8) % len(path)]
                turn = [z for z in (x, y) if z in other and (rnd >> 20) % 3 == 0][:1]
                for z in turn:
                    swap(z)
                i, j = win.index(y), win.index(x)
                rnd = (rnd * 1103515245 + 12345) % 2147483648
                more = (rnd >> 8) % 4 if (rnd >> 16) % 4 else (rnd >> 8) % REACH
                if turn:
                    new = win
                elif (rnd >> 12) % 2:
                    while more and i > 0:
                        i -= 1
                        more -= qof[win[i]] == qof[x]
                    need = {x}
                    for z in reversed(win[i:j]):
                        if not need.isdisjoint(sl[z]):
                            need.add(z)
                    new = win[:i] + [z for z in win[i:j + 1] if z in need] + [z for z in win[i:j + 1] if z not in need] + win[j + 1:]
                else:
                    while more and j < n - 1:
                        j += 1
                        more -= qof[win[j]] == qof[x]
                    need = {y}
                    for z in win[i + 1:j + 1]:
                        if not need.isdisjoint(dp[z]):
                            need.add(z)
                    new = win[:i] + [z for z in win[i:j + 1] if z not in need] + [z for z in win[i:j + 1] if z in need] + win[j + 1:]
                part = win[i:]
                keep = [([fin[z] for z in part], [why[z] for z in part]) for fin, why in state]
                tr = value(new, i)
                rnd = (rnd * 1103515245 + 12345) % 2147483648
                if tr[0] < cur[0] + heat * (1.0 - it / TRIES) * (rnd >> 8) / 8388608:
                    cur = tr
                    fin, tail = state[0][0], tails[0]
                    win = sorted(new, key=lambda z: fin[z] - tail[z] - cs[z])
                    if tr[0] < best[0]:
                        best, bwin, bq = tr, win, list(qof)
                else:
                    for z in turn:
                        swap(z)
                    for (fin, why), (f0, w0) in zip(state, keep):
                        for z, a, b in zip(part, f0, w0):
                            fin[z], why[z] = a, b
            for x in other:
                if qof[x] != bq[x]:
                    swap(x)
            seq = seq[:lo] + bwin + seq[hi:]
            fin = whole(seq)[0]
            return sorted(seq, key=lambda z: fin[z] - tails[0][z] - cs[z])

        def sweep(seq, a, b, count, heat, nm):
            for rnd in range(count):
                for lo in range(a - WIDE // 2 + rnd % 2 * WIDE // 4, b - WIDE // 2, WIDE // 2):
                    seq = polish(seq, max(lo, 0), min(lo + WIDE, nn), heat * (1.0 - rnd / count), SEED + lo + rnd, nm)
            return seq
        alike = tuple((nd_[0], tuple(nd_[1]), tuple(nd_[2])) for nd_ in nodes)
        if alike not in ORDERS:
            named = [{} for u in edge]
            for u in range(RO):
                for x in range(edge[u], edge[u + 1]):
                    n = (nodes[x][2] + [""])[0]
                    named[u].setdefault("".join(c for c in n if c not in "123") if n[:2] in ("ms", "lw") else n, []).append(x)
            for q, plan in enumerate(PLAN):
                row = []
                for u in range(-1, RO):
                    for n in plan[max(u, 0)].split():
                        have = named[u + (n[0] == "+")].get(n.strip("+"), [])
                        got = [x for x in have if qof[x] == q or x in other and other[x][0] == q]
                        if got and (u >= 0 or n[0] == "+"):
                            row.append(got[0])
                            have.remove(got[0])
                for x, y in zip(row, row[1:] + [-1]):
                    if qof[x] != q:
                        swap(x)
                    if y >= 0:
                        nxt[x].append(y)
                        prev[y].append(x)
            topo, left = [x for x in range(nn) if not dl[x] and not prev[x]], [len(dl[x]) + len(prev[x]) for x in range(nn)]
            for x in topo:
                for y in succ[x] + nxt[x]:
                    left[y] -= 1
                    if not left[y]:
                        topo.append(y)
            pr = [0.0] * nn
            for x in reversed(topo):
                pr[x] = cs[x] + max([lat[x]] + [pr[y] + lat[x] for y in succ[x]] + [pr[y] for y in nxt[x]])
            order = sorted(range(nn), key=lambda x: (-pr[x], x))
            seed, best = 1, None
            for rnd in range(PASSES):
                st, end = place(order, False)
                if best is None or end < best[0]:
                    best = (end, st)
                shake = NOISE if rnd % 3 == 2 else 0.0
                if shake:
                    st = best[1]
                bk = place(sorted(range(nn), key=lambda x: (-st[x] - cs[x], -x)), True)[0]
                key = [0.0] * nn
                for x in reversed(topo):
                    seed = (seed * 1103515245 + 12345) % 2147483648
                    key[x] = max([bk[x] + cs[x] + shake * seed / 2147483648] + [key[y] + 1e-6 for y in succ[x] + nxt[x]])
                order = sorted(range(nn), key=lambda x: (-key[x], x))
            seq = sorted(range(nn), key=lambda x: (best[1][x], x))
            seq = sweep(seq, steps[1] - WIDE // 2, steps[2] + WIDE, MID, HEAT, nm)
            seq = sweep(seq, 0, steps[0] + WIDE, ENDS, HEAT, nm)
            seq = sweep(seq, steps[0], steps[1], ENDS, HEAT, nm)
            seq = sweep(seq, steps[2], nn, 2 * ENDS, HEAT, nm)
            seq = sweep(seq, 0, nn, FINE, HEAT / 3, nm)
            ORDERS[alike] = (seq, list(qof))
        seq, queue = ORDERS[alike]
        for x in seq:
            if qof[x] != queue[x]:
                swap(x)
        for x in seq:
            (nodes[x] if qn[nodes[x][0]] == qof[x] else alt[x])[3]()
        for sem in total:
            if known["g"].get(sem, 0) < total[sem]:
                g.wait_ge(T.sem[sem], total[sem])
                learn("g", sem, total[sem])
    return op, dma, send, arrives, finish, lambda: steps.append(len(nodes))


def rank_program(g, core, T, topo):
    r = T.rank_of(core)
    if r is None:
        return
    v, s, p = g.vector, g.scalar, g.tensor
    op, dma, put, arrives, finish, step = tracker(g, T)

    def C(n, a=0, b=None, p0=0, p1=128, st=1):
        bf, o, w = PLACE[n]
        return T[bf][p0:p1, o + a:o + (w if b is None else b):st]

    def keys(n, count, first=0):
        return " ".join("%s%d" % (n, i) for i in range(first, count))

    def wid(a):
        n = 1
        for x in list(a.shape)[1:]:
            n *= x
        return n

    def vcost(o, a, per=1.0):
        if "16" in str(o.dtype) and "16" in str(a.dtype):
            per *= 0.5
        return VFIX + CYC * max(64, per * wid(o))

    def scost(o):
        return SFIX + CYC * max(64, wid(o))

    def ncost(n, fix=VFIX):
        return fix + 0.03 + CYC * (GATH * n if n > 0 else -SCAT * n)

    def tt(o, a, b, f, R, Wt, n=0):
        op("v", [lambda: v.tensor_tensor(o, a, b, f)], R, Wt, ncost(n) if n else VFIX + CYC * max(64, wid(o) * (1 if "ps" in R else 2)))

    def ts(o, a, x, f, R, Wt, y=None, f2=None, n=0):
        if f2 is None:
            op("v", [lambda: v.tensor_scalar(o, a, x, None, f)], R, Wt, ncost(n) if n else vcost(o, a))
        else:
            op("v", [lambda: v.tensor_scalar(o, a, x, y, f, f2)], R, Wt, vcost(o, a))

    def cp(o, a, R, Wt, n=0):
        op("v", [lambda: v.tensor_copy(o, a)], R, Wt, ncost(n) if n else vcost(o, a))

    def fill(o, c, Wt):
        op("v", [lambda: v.memset(o, c)], "", Wt, vcost(o, o))

    def act(o, a, R, Wt, f=AF.Identity, n=0, **kw):
        op("s", [lambda: s.activation(o, a, f, **kw)], R, Wt, ncost(n, SFIX) if n else scost(o))

    def either(q, on_s, on_v, R, Wt, cost_s, cost_v):
        x, y = ("s", [on_s], cost_s), ("v", [on_v], cost_v)
        if q == "v":
            x, y = y, x
        op(x[0], x[1], R, Wt, x[2], y)

    def mv(q, o, a, R, Wt, scale=1.0, bias=0.0):
        on_s = lambda: s.activation(o, a, AF.Copy, scale=scale, bias=bias)
        if q == "g" or Wt in ONG.split():
            on_g = lambda: g.affine_select(o, a, [[0, n] for n in list(o.shape)[1:]], Op.is_ge, 0.0, 0, 0)
            return op("g", [on_g], R, Wt, 0.17 + 2 * CYC * wid(o), None if q == "g" else ("s", [on_s], scost(o)))
        if scale == 1.0 and bias == 0.0:
            on_v = lambda: v.tensor_copy(o, a)
        else:
            on_v = lambda: v.tensor_scalar(o, a, scale, bias, Op.mult, Op.add)
        either(q, on_s, on_v, R, Wt, scost(o), vcost(o, a))

    def take(o, a, R, Wt, bias=0.0, lend=True):
        on_s = lambda: s.activation(o, a, AF.Copy, bias=bias)
        on_v = (lambda: v.tensor_scalar(o, a, bias, None, Op.add)) if bias else (lambda: v.tensor_copy(o, a))
        op("s", [on_s], R, Wt, ncost(wid(o), SFIX), ("v", [on_v], ncost(wid(o))) if lend else None)

    def relu(q, o, a, R, Wt, scale=1.0, bias=0.0):
        either(q, lambda: s.activation(o, a, AF.Relu, scale=scale, bias=bias),
               lambda: v.tensor_scalar(o, a, bias or scale, 0.0, Op.add if bias else Op.mult, Op.max), R, Wt, scost(o), vcost(o, a))

    def mm(o, l, x, st, sp):
        return (lambda: p.matmul(o, l, x, st, sp), PCYC * max(min(64, wid(l)), wid(x)))

    def pe(fs, R, Wt):
        op("p", [f[0] for f in fs], R, Wt, sum(f[1] for f in fs))

    def scan(o, d, R, Wt, n=K, p1=128):
        op("v", [lambda: v.tensor_tensor_scan(o, T.s0[0:p1, 0:n], d, 0.0, Op.add, Op.min)], R + " s0", Wt, VFIX + CYC * n)

    def spare(o, d, j, R, Wt):
        op("v", [lambda: v.tensor_tensor_scan(o, T.sp[:, j, :], d, 0.0, Op.max, Op.min)], R + " sp%d" % j, Wt, VFIX + CYC * K)

    def gop(f, R, Wt, n):
        op("g", [f], R, Wt, 0.17 + 2 * CYC * n)

    def send(src, key, dst_rank, dst, sem, local, bulk=False, on=True):
        dst_core = T.cores[dst_rank % N]
        rid, pid = topo.addr(dst_core)[0:2]
        eng = topo.engines(core, dst_core)
        eng = eng[-NE:] if bulk else eng[0:NE]
        return put(lambda: g.remote_dma(dst, src, T.sem[sem], T.sem[local], pid, rid, sum(1 << e for e in eng)), key, local, len(eng), on)

    PW = keys("pw", 8) + " pwd"
    XW = keys("xw", 4)
    FW = keys("fwl", 4) + " " + keys("fw", 4)
    QR = keys("qr", 6)
    def tags():
        gop(lambda: g.iota(T.ixi[0:16, :], [[1, 256]], -2048, 256), "", "ixi", 256)
        mv("s", T.ixh[0:16, :], T.ixi[0:16, :], "ixi", "ixh")
        dma("d", T.pt[8:9, :], T.ixh[0:16, :], "ixh", "pt2", 8)
        mv("s", T.pcs[:], T.tgs[:], "tgs", "pcs")
        dma("d", T.pt[0:8, :], T.pcs[:], "pcs", "pt0", 64)
    parts = {"tgs": (T.tgs[:], T.tg[:], 128), "cxi": (T.cxi[:], T.cx[:], 96), "q": (T.q[:], T.qx[:], 48), "xlh": (T.xlh[:], T.xl[:], 256),
             "lfi0": (T.lfi[:, 0:LCUT], T.lf[:, 0:LCUT], LCUT / 2), "lfi1": (T.lfi[:, LCUT:M], T.lf[:, LCUT:M], (M - LCUT) / 2)}
    for c, (a, b) in enumerate(zip(XCUT, XCUT[1:])):
        parts["xw%d" % c] = (T.xw[:, a:b], T.xr[:, a:b], (b - a) / 4)
    for c, (a, b) in enumerate(zip(FCUT, FCUT[1:])):
        parts["fwl%d" % c] = (T.fw[:, a:b], T.fd[:, a:b], (b - a) / 2)
    for n in LOADS.split():
        if n == "pt":
            tags()
        elif n != "lfi1" or LCUT < M:
            dma("d", parts[n][0], parts[n][1], "", n, parts[n][2])
    ts(T.lfu[:, 0:LCUT], T.lfi[:, 0:LCUT], LOFF, Op.add, "lfi0", "lfu0")
    arrives("rl0", NE, "lu0", BULK, send(T.lfu[:, 0:LCUT], "lfu0", r - 1, T.lu1[:, 0:LCUT], "rl0", "ls15", True))
    fill(C("one"), 1.0, "one")
    fill(C("zero"), 0.0, "zero")
    gop(lambda: g.iota(C("pmi", 0, 1), [[0, 1]], 0, 1), "", "pmi", 1)
    gop(lambda: g.iota(T.ic[:], [[0, 16], [1, 16]], 0, 0), "", "ic", 256)
    gop(lambda: g.affine_select(C("bl"), C("one", 0, 128), [[-16, 8], [0, 16]], Op.is_ge, 0.0, 0, 1), "one", "bl", 128)
    gop(lambda: g.affine_select(C("bl"), C("bl"), [[16, 8], [0, 16]], Op.is_ge, 0.0, 15, -1), "bl", "bl", 128)
    gop(lambda: g.affine_select(C("rp", p1=32), C("one", 0, 8, p1=32), [[-1, 8]], Op.is_equal, 0.0, 0, 1), "one", "rp", 8)
    gop(lambda: g.affine_select(C("bt"), C("bl"), [[1, 128]], Op.is_ge, 0.0, 0, -1), "bl", "bt", 128)
    gop(lambda: g.iota(C("dmi"), [[16, 12]], 0, 0), "", "dmi", 12)

    def diag(n, a, w, src="zero", key=None):
        gop(lambda: g.affine_select(C(n, a, a + 128), C(src, 0, 128), [[-1, 128]], Op.not_equal, w, 0, 1), src, key or n, 128)
    diag("id", 0, 1.0)
    ts(C("bl8"), C("bl"), OUT, Op.mult, "bl", "bl8")
    gop(lambda: g.affine_select(C("up8"), C("bl8"), [[1, 128]], Op.is_gt, 0.0, 0, -1), "bl8", "up8", 128)
    diag("btr", 0, -255.0 * OUT, "up8")
    diag("tri", 0, -1.0, "bt")
    E = lambda i: C("er", i, i + 1)
    D = lambda i, p1=128: C("ec", i, i + 1, p1=p1)
    b8 = C("bl", st=16)
    PM = C("pmf", 0, 1)

    def times(o, a, w, R, Wt):
        either("s" if wid(o) < 64 else "v", lambda: s.activation(o, a, AF.Identity, scale=w), lambda: v.tensor_scalar(o, a, w, None, Op.mult), R, Wt, scost(o), vcost(o, a))

    def scaled(n, a, w, key):
        o = C(n, a, a + 128)
        op("g", [lambda: g.affine_select(o, C("zero", 0, 128), [[-1, 128]], Op.not_equal, w, 0, 1)], "id zero sent", key, 0.17 + 256 * CYC,
           ("v", [lambda: v.tensor_scalar(o, C("id"), w, None, Op.mult)], VFIX + 64 * CYC))
    ts(D(9), C("pmi", 0, 1), 8.0, Op.is_equal, "pmi", "ec9")
    ts(C("pmi", 1, 2), C("pmi", 0, 1), 15, Op.bitwise_and, "pmi", "pmj")
    cp(PM, C("pmi", 1, 2), "pmj", "pmf")
    ts(C("er"), T.ic[:, 0:16], PM, Op.is_equal, "ic pmf", "er")
    ts(D(1), E(2), -0.25, Op.mult, "er", "ec1")
    ts(D(8), E(2), OFF, Op.add, "er", "ec8")
    ts(D(0), E(0), 0.5, Op.mult, "er ec1", "ec0", D(1), Op.add)
    ts(D(2), E(1), E(3), Op.add, "er", "ec2", 32768.0, Op.mult)
    ts(D(6), D(2), E(0), Op.add, "er ec2", "ec6")
    ts(D(3), E(3), -1.0, Op.mult, "er", "ec3")
    ts(D(7), PM, 1.0, Op.is_ge, "pmf", "ec7")
    ts(D(10), D(2), E(7), Op.add, "er ec2", "ec10")
    for n in ("sa", "wt", "vr", "slt", "row"):
        fill(C(n), 0.0, n)
    times(C("wt", 7, 128, p1=32, st=16), C("one", 0, 8, p1=32), D(9, 32), "one ec9 wt", "wt2")
    times(C("slt", 15, 143, st=16), b8, D(0), "bl ec0 slt", "slt")
    fill(C("c15", p1=1), 1.5, "c15")
    for i in range(max(CUT[1], K - CUT[1]) // 16):
        gop(lambda i=i: g.affine_select(C("sel", 128 * i, 128 * i + 128), C("one", 0, 128), [[0, 8], [-1, 16]], Op.is_equal, 0.0, -16 * i, 1), "one sent", "sel%d" % i, 128)
    for i in range(0, 16, 4):
        op("v", [lambda u=u: v.tensor_scalar(C("bj", 128 * u, 128 * u + 128), C("bl"), E(u), None, Op.mult) for u in range(i, i + 4)], "bl er", keys("bj", i + 4, i), 4 * (VFIX + 64 * CYC))
    ts(D(15), C("pmi", 0, 1), PM, Op.subtract, "pmi pmf", "ec15", 0.125, Op.mult)
    ts(C("gm"), T.ic[:, 0:256:2], D(15), Op.not_equal, "ic ec15", "gm", BIG, Op.mult)
    ts(C("gm"), C("gm"), 2048.0, Op.add, "gm", "gm")
    for j in (0, 1):
        times(C("sa", 1 + 2 * j, 128, st=16), b8, 1.0, "bl sa", "sa%d" % j)
        times(C("wm", 8 * j, 8 * j + 8), b8, -131072.0, "bl", "wm%d" % j)
        times(C("wp", 8 * j, 8 * j + 8), b8, D((6, 10)[j]), "bl ec10 ec6", "wp%d" % j)
        ts(C("row", 128 * j, 128 * j + 128, p1=1), T.ic[0:1, 0:128], 4096.0, Op.mult, "ic row", "rowa%d" % j, 2048.0 * j, Op.add)
        ts(C("row", 128 * j, 128 * j + 128, 64, 65), C("one", 0, 128, 64, 65), (-OUT, -2048.0)[j], Op.mult, "one row", "rowu%d" % j)
    times(C("wt", 0, 128, p1=32, st=16), C("rp", p1=32), 1.0, "rp wt", "wt0")
    cp(C("row", 384, 512, p1=1, st=16), C("one", 0, 8, p1=1), "one row", "rowc")
    fill(T.pw[:, W:W + K], OFF, "pwd")
    mv("s", T.lc[:], T.cxi[:], "cxi", "lc")

    def spread(src, bias, how):
        for i in (0, 1):
            mv(how[i], T.qrep[:, 8 * i:16 * K:16], src[:], "qb" if bias else "q", "qr%d" % i, bias=bias)
        for i, (a, n) in enumerate(((4, 8), (1, 4), (2, 4), (3, 4))):
            mv(how[2 + i], T.qrep[:, a:16 * K:n], T.qrep[:, 0:16 * K:n], keys("qr", 2 + (i > 0)), "qr%d" % (2 + i))
    spread(T.q, 0.0, QHOW[0])
    ts(T.s0[:], T.ic[:], 0.0, Op.is_equal, "ic", "s0", RES, Op.mult)
    ts(C("bm"), T.ic[:, 0:K], PM, Op.not_equal, "ic pmf", "bm", BIG, Op.mult)
    op("s", [lambda: s.activation(C("bmc"), C("bm"), AF.Silu, bias=OUT + 34816.0)], "bm", "bmc", SFIX + CYC * K + 1.3)
    ts(C("bm4"), C("bm"), -5120.0, Op.add, "bm", "bm4")
    for j, w in enumerate((0.0, -1.0, -1.0)):
        scaled("bi", 128 * j, w, "bi%d" % j)
    fill(T.tb[:, 32:128], 0.0, "wz")
    for nm, j, w in (("wm1", 0, 2.0), ("wm2", 0, -2.0), ("wp1", 0, D(3)), ("wp1", 1, D(0)), ("wp2", 0, E(3)), ("wp2", 2, D(0))):
        times(C(nm, 8 * j, 8 * j + 8), b8, w, "bl er ec0 ec3 wz", "%s_%d" % (nm, j))
    for n, w in (("id4", 4.0), ("idm", -0.5), ("id2", 2.0)):
        scaled(n, 0, w, n)
    for j, w in enumerate((-2.0, 1.0, 0.5, 2.0, -1.0, -0.5)):
        scaled("idu", 128 * j, w * OUT, "idu%d" % j)
    times(C("tr8"), C("tri"), -OUT, "tri", "tr8")
    times(C("tr4"), C("tri"), -4096.0, "tri", "tr4")
    ts(D(11), PM, -4096.0, Op.mult, "pmf", "ec11", 14 * 4096.0, Op.add)
    times(C("cmp"), C("bl"), D(11), "bl ec11", "cmp")
    times(C("bn8"), C("bl"), 2048.0 - OUT, "bl", "bn8")
    mv("s", C("lk"), C("dmi"), "dmi", "lk", 0.0625)
    mv("v", C("bme"), C("bm"), "bm", "bme", bias=-4096.0)
    ts(C("dm4"), C("dmi"), PM, Op.add, "dmi pmf", "dm4", float(W), Op.add)
    for j, n in enumerate((W, M)):
        fill(T.sp[:, j, :], 0.0, "sp%d" % j)
        ts(T.sp[:, j, 0:K:16], C("dmi"), PM, Op.add, "dmi pmf sp%d" % j, "sp%d" % j, float(n), Op.add)
    fill(C("exb"), 0.0, "exb")
    times(C("dg1"), C("id2"), E(0), "id2 er", "dg1")
    times(C("dg7"), C("id"), E(7), "id er", "dg7")
    times(C("vr", 0, 128, st=16), b8, 2.0, "bl vr", "vr")
    for t in range(RO):
        ts(C("row", 128 * t, 128 * t + 128, 96, 97), T.ic[96:97, 0:128], 4.0 + t, Op.is_equal, "ic row", "rowm%d" % t)
        fill(C("row", 128 * t, 128 * t + 128, 96, 97, 16), -2048.0, "rowm%d" % t)
        ts(D(12 + t), E(4 + t), -1.0, Op.mult, "er", "ec%d" % (12 + t))
        times(C("dgc", 128 * t, 128 * t + 128), C("id"), D(7), "id ec7", "dgc%d" % t)
        times(C("dgc", 128 * t, 128 * t + 128, st=16), b8, D(12 + t), "bl ec%d dgc%d" % (12 + t, t), "dgc%d0" % t)
    banks = (("psv0", T.psv[:, 0, :]), ("psv1", T.psv[:, 1, :]), ("psm", T.psm[:]), ("psu", T.psu[:]), ("psd", T.psd[:]), ("psg", T.psg[:]),
             ("psk0", T.psk[:, 0, :]), ("psk1", T.psk[:, 1, :]))
    pe([mm(ap, C("wt", p1=9), T.pt[0:9, 512 * c:512 * c + 512], True, False) for c, (bk, ap) in enumerate(banks)], "wt0 wt2 pt0 pt2", " ".join(x[0] for x in banks))
    for c, (bk, ap) in enumerate(banks):
        pe([mm(ap, C("sa"), T.xw[:, 512 * c:512 * c + 512], False, True)], "sa0 sa1 turn xw%d" % sum(x <= 512 * c for x in XCUT[1:]), bk + " turn")
        o = T.pw[:, 512 * c:512 * c + 512]
        if c in PWV:
            ts(o, ap, D(8), Op.add, bk + " ec8", "pw%d" % c)
        else:
            act(o, ap, bk + " ec8 bmc", "pw%d" % c, bias=D(8))

    chip = lambda x: topo.chip(T.cores[x % N])

    def handed(src, j):
        return j > 1 and chip(src - j) == chip(src - j + 1) != chip(src)
    if LCUT < M:
        mv(LQ, T.lfu[:, LCUT:M], T.lfi[:, LCUT:M], "lfi1", "lfu1", bias=LOFF)
        arrives("rl1", NE, "lu1", FAR + (M - LCUT) / 240, send(T.lfu[:, LCUT:M], "lfu1", r - 1, T.lu1[:, LCUT:M], "rl1", "ls0", True))
    arrives("rx1", NE, "xl1", BULK, send(T.xlh[:], "xlh", r - 1, T.xl1[:], "rx1", "ls1", True))
    send(T.lfu[:], "lfu0 lfu1", r - 2, T.lu2[:], "rl2", "ls2", True, not handed(r, 2))
    for j in (2, 3):
        send(T.xlh[:], "xlh", r - j, T["xl%d" % j][:], "rx%d" % j, "ls%d" % (2 * j - 1), True, not handed(r, j))

    def hand_on(i):
        if i == 1:
            arrives("rl2", NE, "lu2", BULK, send(T.lu1[:], "lu0 lu1", r - 1, T.lu2[:], "rl2", "ls16", True, handed(r + i, i + 1)))
        a, b = "xl%d" % i, "xl%d" % (i + 1)
        arrives("rx%d" % (i + 1), NE, b, BULK, send(T[a][:], a, r - 1, T[b][:], "rx%d" % (i + 1), "ls%d" % (15 + 2 * i), True, handed(r + i, i + 1)))
    hand_on(1)

    def apply(buf, win, after):
        cp(T[win][:].indirect(T[buf][:, K:K + 12]), T[buf][:, 0:K], buf + " " + after, win, -K)

    def same(eq, src, sk, own, lk, less=2048.0):
        for j, (a, b) in enumerate(zip(EQ, EQ[1:])):
            op("v", [lambda kb=kb: v.tensor_scalar(T[eq][:, kb, 0:K - 16 * kb], src[:, 16 * kb:K], less, own(kb), Op.add, Op.is_equal) for kb in range(a, b)],
               sk + " " + lk, eq + str(j), sum(VFIX + CYC * max(64, K // 2 - 8 * kb) for kb in range(a, b)))

    def lower(eq, ps, pk, stop=True):
        for j, (a, b) in enumerate(zip(EQ, EQ[1:])):
            fs = [mm(ps[:, 16 * kb + 16:K], C("bl8"), T[eq][:, kb, 16:K - 16 * kb], False, False) for kb in range(a, min(b, 11))]
            if b == 12:
                fs.append(mm(ps[:, 0:K], C("up8"), T[eq][:, :, 0:16], False, stop))
            pe(fs, "bl8 up8 " + keys(eq, j + 1, j * (b < 12)), pk)

    def pieces(dst, h):
        out, a = [], CUT[h]
        for i, n in enumerate(PARTS.get(dst + str(h), (CUT[h + 1] - CUT[h],))):
            out.append((a, a + n, "%s%d%d" % (dst, h, i)))
            a += n
        return out

    def made(dst, *hs):
        return " ".join(x[2] for h in hs for x in pieces(dst, h))

    def gathers(x, lst, lk, h):
        for a, b, key in pieces("p" + x, h):
            take(T["p" + x][:, 16 * a:16 * b], T.pw[:].indirect(lst[:, a:b]), PW + " " + lk, key, -OFF, key in LEND.split())
        for a, b, key in pieces("m" + x, h):
            tt(T["m" + x][:, 16 * a:16 * b], T.xw[:, 0:W].indirect(lst[:, a:b]), T.qrep[:, 16 * a:16 * b], Op.min, " ".join((XW, lk, QR)), key, 16 * (b - a))

    def sums(ps, srcs, h, n, stop):
        for a, b, key in pieces("s" + srcs[0][0][1], h):
            for src, w, wk in srcs:
                last = stop and src == srcs[-1][0]
                pe([mm(T[ps][a - CUT[h]:b - CUT[h], h, i:n:16], T[src][:, 16 * a + i:16 * b:16], C(w), False, last and i == 15) for i in range(16)],
                   " ".join(x[2] for x in pieces(src, h) if x[0] < b and a < x[1]) + " " + wk, "%s%d" % (ps, h))

    def scatter(lst, src, end):
        if end:
            cp(T.yw[:].indirect(C(lst)), T[src][:], lst + " " + src, "yw", -K)
        else:
            act(T.pw[:].indirect(C(lst)), T[src][:], lst + " " + src, PW, AF.Silu, -K)

    LO = T.ll[:, 1, :]
    own = lambda f: (lambda kb: T.sc[:, 16 * kb + 8 * f + 7:16 * kb + 8 * f + 8])
    for t in range(RO):
        j, end = t + 1, t == RO - 1
        step()
        lw, xl, msg = "lw%d" % j, "xl%d" % j, "msg%d" % j
        lnw, lk = T[lw][:, 0:M], lw if t else "lw0 lw1"
        for h in (0, 1):
            gathers("c", T.lc[:], "lc", h)
        if t == 0:
            for c in range(4):
                a, b = 512 * c, 512 * c + 512
                ts(T.fw[:, 2048 + a:2048 + b], T.fw[:, a:b], 12, Op.logical_shift_right, "fwl%d" % sum(x <= a for x in FCUT[1:]), "fw%d" % c)
            for h in (0, 1):
                a, b = (0, 640, M)[h:h + 2]
                mv(LW[h], T.lw1[:, a:b], T.lu1[:, a:b], "lu0 lu%d %s" % (h, made("pc", 0) if h else "lfu1"), "lw%d" % h)
        else:
            apply(("up1", "up3")[t - 1], lw, made("mc", 0))
        if t == 1:
            arrives("rl3", NE, "lw3", BULK2, send(lnw, lw, r - 1, T.lw3[:, 0:M], "rl3", "ls4", True))
            arrives("rs", NE, "lh", 2 * BULK2, send(lnw, lw, r + 2, T.lh[:, 0:M], "rs", "ls7", True))
        if end:
            mv("g", T.cf[:], T.hm2[:, 0:K], "hm2", "cf")
            act(T.lh[:].indirect(T.hm2[:, K:K + 12]), T.cf[:], "hm2 cf", "lh", AF.Silu, -K)
            act(T.lh[:, 0:M], T.lh[:, 0:M], "lh", "lh", AF.Copy, bias=-LOFF)
        for h in (0, 1):
            a, b = CUT[h], CUT[h + 1]
            H, x, y = b - a, a // 16, b // 16
            k = lambda names: " ".join("%s%d" % (n, h) for n in names.split())
            pe([mm(T.psk[0:H, h, 0:256], C("one", 0, H, p1=1), C("row", 0, 256, p1=1), True, False)], "one rowa0 rowa1", k("psk"))
            sums("psk", (("mc", "wm", "wm0 wm1"), ("pc", "wp", "wp0 wp1")), h, 256, True)
            scan(T.t4[0:H, h, :], T.psk[0:H, h, 0:256], k("psk"), k("t4_"), 256, H)
            ts(T.fi[0:H, h, :], T.t4[0:H, h, 15:256:16], W - 1, Op.bitwise_and, k("t4_"), k("fi"))
            mv("s", T.fl[0:H, h, :], T.fi[0:H, h, :], k("fi"), k("fl"), bias=-2048.0)
            pb, pk = ((T.psm, "psm"), (T.psu, "psu"))[h]
            pe([mm(pb[:, 0:H], C("id"), C("gm", 0, H), True, False)], "id gm", pk)
            pe([mm(pb[:, 16 * i:16 * i + 16], C("sel", 128 * i, 128 * i + 128, p1=H), T.fl[0:H, h, :], False, i == y - x - 1) for i in range(y - x)],
               keys("sel", y - x) + " " + k("fl"), pk)
            op("v", [lambda a=a, b=b, pb=pb: v.tensor_tensor_scan(T.sc[:, a:b], T.s0[:, 0:2 * (b - a):2], pb[:, 0:b - a], 0.0, Op.add, Op.min)], pk + " s0", k("sc"), VFIX + CYC * H)
            mv("v", T.ll[:, 0, x:y], T.sc[:, a + 7:b:16], k("sc"), k("ln"), 0.5, -0.25)
            mv("s", T.ll[:, 1, x:y], T.sc[:, a + 15:b:16], k("sc"), k("lo"))
            LN = T.ll[:, 0, x:y]
            take(T.b16[:, a:b], lnw.indirect(LN), lk + " " + k("ln"), k("b16_"), -LOFF)
            for c, (n, kw, of) in enumerate((("a", {"scale": 2.0, "bias": 8.0}, -2.484375), ("b", {"bias": 592.0}, -10951.484375))):
                if k("sq" + n) in PLAIN.split():
                    act(T.sq[:, c, a:b], T.b16[:, a:b], k("b16_"), k("sq" + n), AF.Square, **kw)
                else:
                    act(T.sq[:, c, a:b], lnw.indirect(LN), lk + " " + k("ln"), k("sq" + n), AF.Square, H, scale=2.0 - c, bias=kw["bias"] - (2.0 - c) * LOFF)
                mv("s", T.tt[:, c, a:b], T.sq[:, c, a:b], k("sq" + n), k("tt" + n), 0.03125, of)
                ts(T.cc[:, c, a:b], T.tt[:, c, a:b], W - 1, Op.bitwise_and, k("tt" + n), k("cc" + n))
                mv("s", T.l12[:, c, a:b], T.cc[:, c, a:b], k("cc" + n), k("li" + n))
            mv("s", T.cm[:, :, a:b], T.cc[:, :, a:b], k("cca ccb"), k("cm"), bias=-2048.0)
            pe([mm(T.psv[0:H, h, 0:384], T.b16[:, a:b], C("bi"), True, False)], "bi0 bi1 bi2 " + k("b16_"), k("psv"))
        for f in (0, 1):
            mv("s", T.lv[:, 12 * f:12 * f + 12], T.sc[:, 7 + 8 * f:K:16], "sc0 sc1", "lv%d" % f, bias=-2048.0)
        pe([mm(T.psg[:, i:2 * K:16], C("bj", 128 * i, 128 * i + 128), T.lv[:], True, True) for i in range(16)], keys("bj", 16) + " lv0 lv1", "psg")
        mv("s", T.rr[:], T.psg[:, 0:2 * K], "psg", "rr")
        take(T.at[:], T[xl][:].indirect(T.ll[:, 0, :]), xl + " ln0 ln1", "at")
        if end:
            dma("d", T.yv[:], T.pw[0:128:16, 0:W], PW, "yv", 128)
            mv("s", T.yv[:], T.yv[:], "yv", "yv", bias=-OFF)
            dma("d", T.yw[0:128:16, 0:W], T.yv[:], "yv", "yw", 128)
        mv("s", T.hn[:], T.rr[:, 0, :], "rr", "hn", 0.5, 2047.75)
        same("eqo", T.rr[:, 1, :], "rr", own(1), "sc0 sc1")
        pe([mm(T.psd[:, 0:K], C("id"), C("bme"), True, False), mm(T.psd[:, 0:K], C("bi", 128, 256), T.rr[:, 0, :], False, False),
            mm(T.psd[:, 0:K], C("id2"), T.hn[:], False, False)], "id bme bi1 rr id2 hn", "psd")
        lower("eqo", T.psd, "psd")
        scan(T.scd[:], T.psd[:, 0:K], "psd", "scd")
        relu("v", C("cand"), T.scd[:, 15:K:16], "scd", "cand", -1.0)
        op("v", [lambda: v.tensor_tensor_scan(C("exb", 1, 13), C("one", 0, 12), C("cand"), 0.0, Op.mult, Op.add)], "one cand", "exb", VFIX + 64 * CYC)
        pe([mm(T.psd[:, 400:412], C("btr"), C("cand"), True, False), mm(T.psd[:, 400:412], C("bl8"), C("exb", 0, 12), False, True)], "btr cand bl8 exb", "psd")
        relu("v", C("nqd"), T.psd[:, 400:412], "psd", "nqd", bias=(256.0 - CAP) * OUT)
        tt(C("w1"), C("nqd"), T.sc[:, 15:K:16], Op.add, "nqd sc0 sc1", "w1")
        tt(C("ld"), C("w1"), C("dm4"), Op.min, "w1 dm4", "ld")
        take(T.nq[:], C("nqd").indirect(C("lk")), "nqd lk", "nq")
        for e in range(0, 16, 4):
            pe([mm(T.psk[:, 1, 0:K], C("slt", 15 - i, 143 - i), T.pc[:, i:16 * K:16], i == 0, i == 15) for i in range(e, e + 4)], "slt " + made("pc", 0, 1), "psk1")
        mv("s", T[msg][:, 0:K], T.psk[:, 1, 0:K], "psk1", msg, bias=0.0 if end else LOFF)
        same("eqt", T.rr[:, 0, :], "rr", own(0), "sc0 sc1")
        mv("s", T.hh[:], T.rr[:, 0, :], "rr", "hh", 0.25, 1535.5)
        pe([mm(T.psk[:, 0, 0:K], C("id"), C("bm4"), True, False), mm(T.psk[:, 0, 0:K], C("c15", p1=1), C("one", 0, K, p1=1), False, False),
            mm(T.psk[:, 0, 0:K], C("id4"), T.hh[:], False, False), mm(T.psk[:, 0, 0:K], C("idm"), T.rr[:, 0, :], False, False)],
           "id bm4 c15 one id4 hh idm rr", "psk0")
        lower("eqt", T.psk[:, 0, :], "psk0", False)
        pe([mm(T.psk[:, 0, 0:K], C("id"), T.nq[:], False, True)], "id nq", "psk0")
        spare(T.scm[:], T.psk[:, 0, 0:K], 1, "psk0", "scm")
        mv("s", T[msg][:, K:K + 12], T.scm[:, 15:K:16], "scm", msg + "l")
        mk = msg + " " + msg + "l"
        if end:
            arrives("rh3", NE, "hm3", FAR, send(T[msg][:, 0:K + 12], mk, r + RO, T.hm3[:], "rh3", "ls11"))
        else:
            u = "up%d" % (1 + 2 * t)
            arrives("r" + u[0::2], NE, u, FAR, send(T[msg][:, 0:K + 12], mk, r - 1, T[u][:], "r" + u[0::2], "ls%d" % (6 + 2 * t)))
        if t == 0:
            hand_on(2)
        if t == 1:
            arrives("rh2", NE, "hm2", FAR, send(T[msg][:, 0:K + 12], mk, r + 2, T.hm2[:], "rh2", "ls10"))
        for h in (0, 1):
            for c, n in enumerate("ab"):
                gathers(n, T.l12[:, c, :], "li%s%d" % (n, h), h)
                sums("psv", (("m" + n, "wm%d" % (c + 1), keys("wm%d_" % (c + 1), 3)), ("p" + n, "wp%d" % (c + 1), keys("wp%d_" % (c + 1), 3))), h, 384, c == 1)
        pe([mm(T.psk[:, 1, 0:K], C("sa"), T.at[:], True, False), mm(T.psk[:, 1, 0:K], C("dg1"), T.hn[:], False, False), mm(T.psk[:, 1, 0:K], C("dg7"), T.rr[:, 1, :], False, False),
            mm(T.psk[:, 1, 0:K], C("row", 128 * t, 128 * t + 128, 96, 97), C("one", 0, K, 96, 97), False, True)], "sa0 sa1 at dg1 hn dg7 rr rowm%d one" % t, "psk1")
        either("s", lambda: s.activation(T.v2[:], T.psk[:, 1, 0:K], AF.Identity, bias=D(8)), lambda: v.tensor_scalar(T.v2[:], T.psk[:, 1, 0:K], D(8), None, Op.add),
               "psk1 ec8", "v2", SFIX + K * CYC, VFIX + K * CYC)
        cp(T.xw[:].indirect(C("ld")), T.at[:], "ld at", XW, -K)
        scatter("ld", "v2", False)
        if end:
            op("v", [lambda: v.tensor_scalar(T.yw[:].indirect(C("ld")), T.v2[:], 1.0, -OFF, Op.mult, Op.add)], "ld v2", "yw", ncost(-K))
        take(T.xo[:], T.xw[:, 0:W].indirect(LO), XW + " lo0 lo1", "xo")
        pe([mm(T.psk[:, 0, 0:K], C("id"), T.qrep[:, 0:16 * K:16], True, False), mm(T.psk[:, 0, 0:K], C("id"), T.xo[:], False, True)], "id qr0 xo", "psk0")
        mv("s", T.qb[:], T.psk[:, 0, 0:K], "psk0", "qb", 0.5, 127.8125)
        if end:
            mv("s", T.q[:], T.qb[:], "qb", "q", bias=-128.0)
        else:
            spread(T.qb, -128.0, QHOW[1])
        for h in (0, 1):
            a, b = CUT[h], CUT[h + 1]
            H = b - a
            nn = lambda f: T.nn[0:H, h, 128 * f:128 * f + 128]
            ts(T.nn[0:H, h, 128:384], T.psv[0:H, h, 128:384], WHOLE, Op.add, "psv%d" % h, "nna%d" % h, WHOLE, Op.is_equal)
            if NNB[h] == "v":
                ts(nn(0), T.psv[0:H, h, 0:128], 0.5, Op.is_gt, "psv%d" % h, "nnb%d" % h, 0.5, Op.subtract)
            else:
                act(nn(0), T.psv[0:H, h, 0:128], "psv%d" % h, "nnb%d" % h, AF.Sign, bias=-0.5)
            pe([mm(T.psu[:, a:b], nn(f), C("bi", 128, 128 + H, p1=H), f == 1, f == 2) for f in (1, 2)], "bi1 nna%d" % h, "psu")
            for u in (0, 1):
                pe([mm(T.psm[:, K * u + a:K * u + b], nn(f), C("idu", 128 * (3 * u + w), 128 * (3 * u + w) + H, p1=H), f == 1, f == 0) for f, w in ((1, 0), (2, 1), (0, 1 + (NNB[h] == "s")))],
                   "%s nna%d nnb%d" % (keys("idu", 6), h, h), "psm")
        relu("s", T.nr[:], T.psu[:, 0:K], "psu", "nr", bias=1.0)
        tt(T.psm[:, 0:K], T.psm[:, 0:K], T.cm[:, 1, :], Op.min, "psm cm0 cm1", "psm pk")
        tt(T.dc[:], T.psm[:, K:2 * K], T.cm[:, 0, :], Op.min, "psm cm0 cm1", "dc")
        tt(T.sh[:], T.psm[:, 0:K], T.dc[:], Op.max, "psm pk dc", "sh")
        pe([mm(T.psg[:, 0:K], C("row", 128, 256, 64, 65), C("one", 0, K, 64, 65), True, False)], "rowu1 one", "psg")
        pe([mm(T.psg[:, 0:K], C("tr4"), T.nr[:], False, True)], "tr4 nr", "psg")
        mv("s", T.sg[:], T.sh[:], "sh", "sg", bias=2048.0)
        relu("s", T.fst[:], T.psg[:, 0:K], "psg", "fst", 1.0 / 2048)
        tt(T.x1[:], T.psg[:, 0:K], T.sh[:], Op.min, "psg sh", "x1")
        pe([mm(T.psu[:, 0:K], C("cmp"), T.nr[:], True, False)], "cmp nr", "psu")
        pe([mm(T.psu[:, 0:K], C("bl"), T.x1[:], False, True)], "bl x1", "psu")
        mv("s", T.rc[:], T.psu[:, 0:K], "psu", "rc", bias=34816.0)
        for o, pk, stop in ((T.psv[:, 1, 0:K], "psv1", True), (T.psd[:, 0:K], "psd", False)):
            pe([mm(o, C("id"), C("bmc"), True, False), mm(o, C("id"), T.nq[:], False, False)], "id bmc nq", pk)
            pe([mm(o, C("cmp"), T.nr[:], False, False)], "cmp nr", pk)
            pe([mm(o, C("bn8"), T.fst[:], False, False)], "bn8 fst", pk)
            pe([mm(o, C("bl"), T.x1[:], False, stop)], "bl x1", pk)
        spare(T.scc[:], T.psv[:, 1, 0:K], 0, "psv1", "scc")
        cp(T.fw[:].indirect(C("ld")), T.sg[:], "ld sg", FW, -K)
        ts(T.ci[:], T.fw[:, 0:W].indirect(LO), W - 1, Op.bitwise_and, FW + " lo0 lo1", "ci", n=K)
        mv("s", T.cf[:] if end else T.lc[:], T.ci[:], "ci", "cf" if end else "lc")
        o = T.psv[:, 0, K:2 * K]
        pe([mm(o, C("row", 0, 128, 64, 65), C("one", 0, K, 64, 65), True, False), mm(o, C("id"), T.b16[:], False, False),
            mm(o, C("tr8"), T.nr[:], False, True)], "rowu0 one id b16_0 b16_1 tr8 nr", "psv0")
        act(T.x2[:], o, "psv0", "x2", AF.Relu)
        mv("s", C("lp"), T.scc[:, 15:K:16], "scc", "lp")
        same("eqo", T.rc, "rc", lambda kb: T.scc[:, 16 * kb + 15:16 * kb + 16], "scc")
        lower("eqo", T.psd, "psd")
        take(T.g1[:], T.pw[:].indirect(C("lp")), PW + " lp", "g1", -OFF)
        pe([mm(T.psg[:, 0:K], C("vr"), T.x2[:], True, False), mm(T.psg[:, 0:K], C("row", 384, 512, p1=1), C("one", 0, K, p1=1), False, False),
            mm(T.psg[:, 0:K], C("dgc", 128 * t, 128 * t + 128), T.g1[:], False, True)], "vr x2 rowc one dgc%d0 g1" % t, "psg")
        mv("s", T.v1[:], T.psg[:, 0:K], "psg", "v1", bias=0.0 if end else OFF)
        if t == 0:
            mv("g", T.lw2[:, 0:M], T.lu2[:], "lu2 nna0", "lw2")
        spare(T.scd[:], T.psd[:, 0:K], 0, "psd", "scd")
        mv("s", C("lcl"), T.scd[:, 15:K:16], "scd", "lcl")
        scatter("lcl", "v1", end)
    apply("hm3", "lh", "nna0")
    outs = {"yl": (T.lh[:, 0:M], "lh", 512), "yq": (T.q[:], "q", 48), "yc": (T.cf[:], "cf", 96), "yt": (T.yw[0:128:16, 0:W], "yw", 128)}
    for n in OUTS.split():
        dma("d", T[n][:], outs[n][0], outs[n][1], n, outs[n][2])
    finish()
